import numpy as np, ml_dtypes
CORES = [3,11,19,27,35,43]
N = 6
BF = ml_dtypes.bfloat16
P, V, C, PH, S, Z, CAP, RO = 3072, 1152, 512, 3, 8, 8, 96, 4
I = V // PH
def tail(rng, b, top):
    return np.where(np.arange(16)[:, None] >= rng.integers(0, 17, (N, 8, 1, V)), rng.integers(0, top, b.shape), b)
def parts(rng):
    e = rng.choice(np.array([10.0, 14.0, 18.0, 24.0]), (N, 8, 1, 1))
    x = np.minimum((256 * rng.random((N, 8, 16, P)) ** e).astype(np.int64), 255)
    m = rng.integers(0, 256, (N, 8, 16, V)); b = rng.integers(0, P, (N, 8, 16, V))
    return x, m, b, tail(rng, b, P), rng.integers(0, V, (N, 8, 16, C))
def tops(x, l):
    y = np.take_along_axis(x, l[:, :, 0][:, :, None, :], 3)
    for k in range(1, 16): y = np.maximum(y, np.take_along_axis(x, l[:, :, k][:, :, None, :], 3))
    return y
def late(rng, shape):
    return PH * rng.integers(0, I, shape) + 1 + rng.integers(0, PH - 1, shape)
def pack(x, m, b, d, u):
    r = {"mor": x.reshape(N, 128, P).astype(np.float32).astype(BF), "mea": m.reshape(N, 128, V).astype(np.float32).astype(BF)}
    r["bas"] = b.reshape(N, 128, V).astype(np.int32); r["der"] = d.reshape(N, 128, V).astype(np.int32); r["use"] = u.reshape(N, 128, C).astype(np.int32)
    return r
def setup_inputs(rng):
    x, m, b, d, u = parts(rng); h = rng.integers(0, 8, N)
    for q in range(N):
        g = int(h[q]); x[q, g, :, P - 1] = 255; m[q, g] = rng.integers(0, 151, (16, V)); u[q, g] = late(rng, (16, C))
        d[q, g, rng.integers(0, 16, I), PH * np.arange(I)] = P - 1
    near = rng.random((N, 8, 1, V)) < rng.choice(np.array([0.0, 0.2, 0.5, 0.8]), (N, 8, 1, 1)); near[np.arange(N), h] = False
    m = np.where(near, np.clip(tops(x, d) + rng.integers(-24, 25, m.shape), 0, 255), m)
    for q in range(N):
        for g in range(8):
            v = PH * rng.permutation(I)[:3]; u[q, g][:, b[q, g, 15, v] & (C - 1)] = v
    return pack(x, m, b, d, u)
def setup_inputs_corners(rng):
    x, m, b, d, u = parts(rng); x = np.minimum(x, 100); x[..., P - 1] = 255; m = rng.integers(0, 101, m.shape)
    b = rng.integers(0, P - 1, b.shape); d = tail(rng, b, P - 1); u = late(rng, u.shape)
    u = np.where(rng.random((N, 8, 1, C)) < 0.1, np.where(rng.random((N, 8, 1, C)) < 0.5, V - 1, 1), u); top = tops(x, d)
    for q in range(N):
        for g in range(8):
            if q == 3 and g % 2 == 1:
                n = (0, 1, CAP // 2, CAP - 1)[g // 2]; o = PH * np.arange(I); w = PH * rng.permutation(I) + 1
                m[q, g][:, o] = top[q, g][:, o]; m[q, g][:, w[:n]] = top[q, g][:, w[:n]]
                d[q, g, rng.integers(0, 16, I - n), w[n:]] = P - 1; u[q, g] = PH * rng.integers(0, I, (16, C))
                continue
            n = int(rng.choice(np.array([0, 1, CAP - 1, CAP, CAP + 1, I])))
            if q == 0: n = (CAP, CAP + 1, I, CAP - 1, 1, 0, CAP, CAP + 1)[g]
            if q == 1 or q == 2: n = (CAP, 1, CAP - 1, 0)[g % 4]
            if q == 2 and g == 7: n = CAP + 1
            o = PH * rng.permutation(I); nl = min(n, C // 2); lone, fit, ad = o[:nl], o[nl:n], o[n:]
            cols = 2 * rng.permutation(C // 2)[:nl] + q % 2
            b[q, g, 15, lone] = cols + C * rng.integers(0, P // C - 1, nl); u[q, g][:, cols] = lone
            b[q, g, 15, ad] = 2 * rng.integers(0, C // 2, I - n) + 1 - q % 2 + C * rng.integers(0, P // C - 1, I - n)
            bad = np.concatenate([lone, ad]); d[q, g, rng.integers(0, 16, len(bad)), bad] = P - 1
            m[q, g][:, fit] = top[q, g][:, fit]
            if q == 2:
                o = PH * np.arange(I); z = np.add.reduce(np.arange(1, 17)[:, None] * m[q, g][:, o], axis=0) & (Z - 1)
                left = np.ones(P, dtype=bool); left[P - 1] = False; left[S * np.arange(I) + z] = False
                l = d[q, g][:, o + 1]; l = np.where(left[l], l, rng.choice(np.flatnonzero(left), l.shape))
                d[q, g][:, o + 1] = l; m[q, g][:, o + 1] = np.maximum.reduce(x[q, g][:, l], axis=1)
    return pack(x, m, b, d, u)
def setup_inputs_ties(rng):
    x, m, b, d, u = parts(rng); x[:, 1::2] = x[:, 1::2] >> 6
    k = rng.integers(0, 8, (N, 8, 1, V)); m = np.take_along_axis(m[..., :8], k, 3); m[:, 1::2] = m[:, 1::2] >> 6
    b[:, :2] = np.take_along_axis(b[:, :2, :, :8], k[:, :2], 3); d[:, :2] = np.take_along_axis(d[:, :2, :, :8], k[:, :2], 3)
    lane = np.arange(V); a = rng.integers(40, 81, (N, 16, 1)); high = (np.arange(16)[:, None] == 15) & (lane >= V // 2)
    m[:, 6] = np.where(lane % PH == 0, rng.integers(215, 256, (N, 16, V)), a + high); u[:, 6] = late(rng, (N, 16, C))
    u[..., ::2] = u[:, :, np.arange(16) & 3, ::2]
    return pack(x, m, b, d, u)
def setup_inputs_alike(rng):
    x, m, b, d, u = parts(rng)
    d[:, :3] = b[:, :3]; d[:, 1, 0] = (b[:, 1, 0] + 1) % P; d[:, 2, 15] = (b[:, 2, 15] + 1) % P
    b[:, 3, 15] = rng.integers(0, P, (N, 1)); u[:, 4] = rng.integers(0, V, (N, 1, C))
    for q in range(N):
        v = PH * rng.permutation(I)[:I // 4]; u[q, 4][:, b[q, 4, 15, v] & (C - 1)] = v
    b[:, 5] = rng.integers(0, P, (N, 1, V)); d[:, 5] = rng.integers(0, P, (N, 1, V)); u[:, 6] = (V - 1) * rng.integers(0, 2, (N, 16, C))
    for q in range(N):
        v = PH * rng.permutation(I)[:I // 8]; c = b[q, 7, 15, v] & (C - 1); u[q, 7][:, c] = v; u[(q + 1) % N, 7][:, c] = v
    return pack(x, m, b, d, u)
def setup_inputs_spread(rng):
    x = (np.exp2(8 * rng.random((N, 8, 1, P))) * rng.random((N, 8, 16, P)) ** 3).astype(np.int64)
    m = (np.exp2(8 * rng.random((N, 8, 1, V))) * rng.random((N, 8, 16, V))).astype(np.int64)
    e = rng.choice(np.array([1.0, 2.0, 4.0, 8.0]), (3, N, 8, 1, 1))
    b = (P * rng.random((N, 8, 16, V)) ** e[0]).astype(np.int64); c = (P * rng.random((N, 8, 16, V)) ** e[1]).astype(np.int64)
    d = np.where(np.arange(16)[:, None] >= rng.integers(0, 17, (N, 8, 1, V)), c, b); u = (V * rng.random((N, 8, 16, C)) ** e[2]).astype(np.int64)
    return pack(np.clip(x, 0, 255), np.clip(m, 0, 255), np.clip(b, 0, P - 1), np.clip(d, 0, P - 1), np.clip(u, 0, V - 1))
def setup_inputs_ends(rng):
    def bits(p, n): return 255 * (rng.random((N, 8, 16, n)) < p)
    def lists(n, hi):
        k = rng.random((N, 8, 1, n)); a = hi * rng.integers(0, 2, (N, 8, 16, n))
        return np.where(k < 0.25, 0, np.where(k < 0.5, hi, np.where(k < 0.8, a, rng.integers(0, hi + 1, (N, 8, 16, n)))))
    k = rng.random((N, 8, 1, P)); x = np.where(k < 0.6, 0, np.where(k < 0.63, 255, bits(0.06, P)))
    k = rng.random((N, 8, 1, V)); m = np.where(k < 0.25, 0, np.where(k < 0.5, 255, bits(0.5, V)))
    b = lists(V, P - 1); d = np.where(np.arange(16)[:, None] >= rng.integers(0, 17, (N, 8, 1, V)), lists(V, P - 1), b); u = lists(C, V - 1)
    for t in range(RO):
        for c in (97 * t, 97 * t - 1):
            u[..., c & (C - 1)] = np.where(rng.random((N, 8, 16)) < 0.5, (V - 1) * rng.integers(0, 2, (N, 8, 16)), rng.integers(0, V, (N, 8, 16)))
    x[:, ::2, :, 0] = 255 * rng.integers(0, 2, (N, 4, 16)); x[:, ::2, :, P - 1] = 255 * rng.integers(0, 2, (N, 4, 16)); x[:, 1::2, :, 0] = 0; x[:, 1::2, :, P - 1] = 255
    lo, hi = PH - 1 + PH * (PH % 2), V - 1 - PH
    m[:, 1::2, :, :PH - 1] = 0; m[:, 1::2, :, V - PH:V - 1] = 255; m[..., V - 1] = 255
    m[:, 1::2, :, lo] = 0; m[:, 1::2, :, hi] = 0; m[:, ::2, :, lo] = 255; m[:, ::2, :, hi] = 255
    u[:, 1::2, :, 0] = np.where(np.arange(16) % 2 == 0, 0, V - 1); b[:, 1::2, :, 0] = 0; d[:, 1::2, :, 0] = P - 1
    u[..., C - 1] = np.where(np.arange(16) % 2 == 0, hi, lo)
    b[..., lo] = 0; d[..., lo] = P - 1; b[..., hi] = P - 1; d[..., hi] = 0; d[..., V - 1] = 0
    b[:, :, 15, V - 1] = ((C - 1 - 97 * (PH - 1)) & (C - 1)) + P - C
    return pack(x, m, b, d, u)
def check_inputs(d):
    bad = []
    for k, hi in (("mor", 255), ("mea", 255), ("bas", P - 1), ("der", P - 1), ("use", V - 1)):
        a = np.asarray(d[k]).astype(np.float64)
        if not np.all((a >= 0) & (a <= hi) & (a == np.floor(a))): bad.append("range of " + k)
    return bad
def pick(a, ix):
    return np.stack([np.take(a[g], ix[g], axis=1) for g in range(8)])
def model(kap, mv, own, m, b, d, u):
    c = pick(u, kap)
    s = np.add.reduce(np.abs(pick(m, c) - mv[:, :, None, :]), axis=1)
    k = np.minimum.reduce(np.where(c == own, 2 ** 24, s * 2048 + c), axis=1)
    ok = k < 2 ** 24; w = np.where(ok, k & 2047, 0); dm = pick(d, w)
    diff = pick(b, w) != dm; diff[:, 15] = True
    return ok, w, np.argmax(diff, axis=1), dm
def gap(x, l, mv):
    return np.add.reduce(np.abs(np.maximum.reduce(pick(x, l), axis=2) - mv), axis=1)
def reference(mor, mea, bas, der, use):
    x = mor.astype(np.float32).astype(np.int32).reshape(N, 8, 16, P); m = mea.astype(np.float32).astype(np.int32).reshape(N, 8, 16, V)
    b = bas.astype(np.int32).reshape(N, 8, 16, V); d = der.astype(np.int32).reshape(N, 8, 16, V); u = use.astype(np.int32).reshape(N, 8, 16, C)
    row = np.arange(16)[None, :, None]; i = np.arange(I); count = [0] * N
    for t in range(RO):
        v = PH * i + t % PH; todo = []
        for r in range(N):
            mv = m[r][:, :, v]; bv = b[r][:, :, v]; dv = d[r][:, :, v]; kap = (bv[:, 15] + 97 * t) & (C - 1); mar = count[r] & 127
            ok, w, f, dm = model(kap, mv, v, m[r], b[r], d[r], u[r])
            e = np.where(row < f[:, None, :], bv, dm); old = gap(x[r], dv, mv)
            ad = ok & (gap(x[r], e, mv) + mar < old)
            q = (r + 1 + t % (N - 1)) % N
            sel = np.argsort(ad, axis=1, kind="stable")[:, :CAP]
            asks = ~np.take_along_axis(ad, sel, 1); mv2 = pick(mv, sel)
            ok2, w2, f2, dm2 = model(np.take_along_axis(kap, sel, 1), mv2, -1, m[q], b[q], d[q], u[q])
            e2 = np.where(row < f2[:, None, :], pick(bv, sel), dm2)
            ad2 = asks & (gap(x[r], e2, mv2) + mar < np.take_along_axis(old, sel, 1))
            new = np.where(ad[:, None, :], e, dv); got = ad.copy()
            for g in range(8):
                new[g][:, sel[g][ad2[g]]] = e2[g][:, ad2[g]]; got[g, sel[g][ad2[g]]] = True
            todo.append((ad, w, new, got, (np.add.reduce((row + 1) * mv, axis=1) + t) & (Z - 1)))
        for r in range(N):
            ad, w, new, got, z = todo[r]; d[r][:, :, v] = new; count[r] = int(np.count_nonzero(got))
            for g in range(8):
                j = i[ad[g]]; u[r, g, (j + t) & 15, (j + 37 * t) & (C - 1)] = w[g][j] ^ 1
                j = i[got[g]]; x[r, g][:, S * j + z[g][j]] = m[r, g][:, v[j]]
    return {"yd": d.reshape(N, 128, V).astype(np.float32), "yu": u.reshape(N, 128, C).astype(np.float32), "ym": x.reshape(N, 128, P).astype(np.float32).astype(BF)}

@@ -1,0 +1,624 @@
+from concourse.mybir import AluOpType as OP, ActivationFunctionType as AF
+
+NR = 6
+P, V, C, PH, I, CAP, RO = 3072, 1152, 512, 3, 384, 96, 4
+IX = I + CAP
+VX = V + PH * CAP
+W16 = 16 * I
+CH = 96
+SC = 128
+VC, NVC = 64, 4
+EV = [0, 3, 3, 3]
+BIG = float(1 << 23)
+FIRST = "cvdewvfwvhwivwspq"
+ORDER = "bacadvawevfavwhviawaw"
+
+SCRATCH = {}
+
+
+def _sb(dtype, **kw):
+    for n, w in kw.items():
+        SCRATCH[n] = ("sbuf", [128, w], dtype)
+
+
+_sb("int32", bas_i=V, der_i=V, use_i=C, pi=8, clsi=96, zi=96, mi=24, ni=8, KUg=I, U=I, Ea=IX, nmi=8, KQs=CAP, uq=CAP, E2=CAP)
+_sb("uint16", cls=96, zof=96, use16=C, u16=I, d16=I, e16=I, m16=24, s16=8, sv16=8, n16=8, uq16=CAP, e216=CAP)
+_sb("float32", Bf=VX, Dv=V, W=V, KU=C, KLX=V, VR=V, onef=144, selr=144, swp=512, oall=128, pm=8, pw=8, cb=8, i8=96, dgf=400,
+    amask=I, acc=8, KEY=I, KT=I, KS=I, thr=IX, nm=8, cnt=8, KN=I, KQ=IX, KEY2=CAP, KT2=CAP, KS2=CAP, Bs=CAP, ths=CAP)
+_sb("bfloat16", meas=VX, morph=P, oneb=I, sel1=144, selm=144, selp=144, selq=144, selz=144, blk=128, blkn=128, blk2=128,
+    blk2n=128, tri=128, cst=128, idb=128, idn=128, idbig=128, blkK=128, dg=400, rmask=16 * SC, c128=IX, Z=16 * SC,
+    GM=16 * SC, RA=16 * SC, EQ=I, GD=W16, GE=W16, SD=W16, SE=W16, MD=I, ME=I, got=IX, non=IX, cum=IX, junk=IX, old=I, gx=I,
+    NEQ=V, GQ=16 * CAP, RQ=16 * CAP, S2=16 * CAP, MM2=CAP, ad2=CAP, x0=16 * VC * NVC, x1=16 * VC * NVC, x2=16 * VC * NVC)
+for _t in range(RO):
+    _sb("bfloat16", **{"qm%d" % _t: V})
+    _sb("float32", **{"qk%d" % _t: C, "qw%d" % _t: V})
+for _t in range(8):
+    SCRATCH["P%d" % _t] = ("psum", [128, 512], "float32")
+SEMAPHORES = ["q_v", "q_a", "q_t", "q_g"] + ["d%d" % k for k in range(9)] + ["l%d" % k for k in range(12)] + ["r%s%d" % (a, k) for a in "mkw" for k in range(RO)]
+
+
+def R(name, lo=0, hi=None, step=1):
+    return (name, lo, SCRATCH[name][1][1] if hi is None else hi, step)
+
+
+def make(g, T):
+    eng = {"v": g.vector, "a": g.scalar, "t": g.tensor, "g": g, "s": g.sync}
+    count, known, waited, hist, total = {}, {k: {} for k in eng}, {}, {}, {}
+
+    def ap(r):
+        if r[0] == "@":
+            return ap(r[1]).indirect(ap(r[2]))
+        n, lo, hi, st = r
+        return T[n][:, lo:hi] if st == 1 else T[n][:, lo:hi:st]
+
+    def acc(reads, writes):
+        a = []
+        for w, rs in ((0, reads), (1, writes)):
+            for r in rs:
+                if r[0] == "@":
+                    a += [(r[1], w), (r[2], 0)]
+                else:
+                    a.append((r, w))
+        return a
+
+    def sync(q, accs):
+        need = []
+        for (n, lo, hi, st), w in accs:
+            ps = SCRATCH[n][0] == "psum"
+            for e in hist.get(n, []):
+                if ps and q == "t" and e[3] == "t":
+                    continue
+                if (ps and e[3] != q) or ((w or e[2]) and lo < e[1] and e[0] < hi):
+                    need.append(e)
+        need.sort(key=lambda e: -e[5])
+        k = known[q]
+        for e in need:
+            if k.get(e[4], 0) >= e[5]:
+                continue
+            eng[q].wait_ge(T.sem[e[4]], e[5])
+            waited[e[4]] = max(waited.get(e[4], 0), e[5])
+            for s, v in e[6].items():
+                k[s] = max(k.get(s, 0), v)
+            k[e[4]] = max(k.get(e[4], 0), e[5])
+
+    def note(q, accs, sem, val):
+        clock = dict(known[q]) if q in known else {}
+        for (n, lo, hi, st), w in accs:
+            ps = SCRATCH[n][0] == "psum"
+            keep = []
+            for e in hist.get(n, []):
+                same = e[0] == lo and e[1] == hi and e[7] == st
+                if ps and e[3] != q:
+                    continue
+                if w and (same or (st == 1 and lo <= e[0] and e[1] <= hi)):
+                    continue
+                if not w and not e[2] and same and e[3] == q and e[4] == sem:
+                    continue
+                keep.append(e)
+            keep.append((lo, hi, w, q, sem, val, clock, st))
+            hist[n] = keep
+
+    def do(q, reads, writes, call):
+        a = acc(reads, writes)
+        sync(q, a)
+        s = "q_" + q
+        count[q] = total[s] = count.get(q, 0) + 1
+        call().then_inc(T.sem[s], 1)
+        note(q, a, s, count[q])
+
+    def isr(x):
+        return isinstance(x, tuple)
+
+    def tt(out, a, b, op):
+        do("v", [a, b], [out], lambda: g.vector.tensor_tensor(out=ap(out), in0=ap(a), in1=ap(b), op=op))
+
+    def ts(out, a, s1, s2, op0, op1=None):
+        rs = [a] + [s for s in (s1, s2) if isr(s)]
+        v = [ap(s) if isr(s) else s for s in (s1, s2)]
+        kw = {} if op1 is None else {"op1": op1}
+        do("v", rs, [out], lambda: g.vector.tensor_scalar(out=ap(out), in0=ap(a), scalar1=v[0], scalar2=v[1], op0=op0, **kw))
+
+    def cp(out, a):
+        do("v", [a], [out], lambda: g.vector.tensor_copy(out=ap(out), in_=ap(a)))
+
+    def ms(out, c):
+        do("v", [], [out], lambda: g.vector.memset(ap(out), c))
+
+    def scan(out, a, b, op0, op1):
+        do("v", [a, b], [out], lambda: g.vector.tensor_tensor_scan(out=ap(out), data0=ap(a), data1=ap(b), initial=0.0, op0=op0, op1=op1))
+
+    def tr(out, a):
+        do("v", [a], [out], lambda: g.vector.transpose(out=ap(out), in_=ap(a)))
+
+    def act(out, a, func=AF.Copy, bias=None, accum=None):
+        kw = {}
+        if bias is not None:
+            kw["bias"] = ap(bias)
+        if accum is not None:
+            kw["accum_out"] = ap(accum)
+        do("a", [a] + [b for b in [bias] if b], [out] + [b for b in [accum] if b],
+           lambda: g.scalar.activation(out=ap(out), in_=ap(a), func=func, **kw))
+
+    def mm(out, lhsT, rhs, start, stop):
+        do("t", [lhsT, rhs], [out], lambda: g.tensor.matmul(ap(out), ap(lhsT), ap(rhs), start, stop))
+
+    def iota(out, pattern, base, cm):
+        kw = {} if SCRATCH[out[0]][2] == "int32" else {"allow_small_or_imprecise_dtypes": True}
+        do("g", [], [out], lambda: g.iota(ap(out), pattern, base, cm, **kw))
+
+    def aff(out, a, pattern, op, base, cm):
+        do("g", [a], [out], lambda: g.affine_select(ap(out), ap(a), pattern, op, 0.0, base, cm))
+
+    nd, nl = [0], [0]
+
+    def dma(q, out, a):
+        accs = acc([a] if isr(a) else [], [out] if isr(out) else [])
+        sync(q, accs)
+        s = "d%d" % nd[0]
+        nd[0] += 1
+        total[s] = 16
+        eng[q].dma_start(out=ap(out) if isr(out) else out, in_=ap(a) if isr(a) else a).then_inc(T.sem[s], 16)
+        note("dma" + s, accs, s, 16)
+
+    def send(topo, src, dst, land, a, rsem):
+        accs = acc([a], [])
+        sync("g", accs)
+        s = "l%d" % nl[0]
+        nl[0] += 1
+        rid, pid, _ = topo.addr(dst)
+        total[s] = len(topo.engines(src, dst))
+        g.remote_dma(out_ap=T[land][:], in_ap=ap(a), remote_sem=T.sem[rsem], local_sem=T.sem[s], pid=pid, routing_id=rid, dma_engine_mask=topo.mask(src, dst))
+        note("rem" + s, accs, s, total[s])
+
+    def arrive(land, rsem, n):
+        total[rsem] = n
+        note("arr" + rsem, acc([], [R(land)]), rsem, n)
+
+    def finish():
+        for s, n in total.items():
+            if waited.get(s, 0) < n:
+                g.wait_ge(T.sem[s], n)
+
+    return {"tt": tt, "ts": ts, "cp": cp, "ms": ms, "scan": scan, "tr": tr, "act": act, "mm": mm, "iota": iota, "aff": aff,
+            "dma": dma, "send": send, "arrive": arrive, "finish": finish}
+
+
+def rank_program(g, core, T, topo):
+    rank = T.rank_of(core)
+    if rank is None:
+        return
+    F = make(g, T)
+    tt, ts, cp, ms, scan, tr, act, mm = (F[k] for k in ("tt", "ts", "cp", "ms", "scan", "tr", "act", "mm"))
+    iota, aff, dma, send, arrive = (F[k] for k in ("iota", "aff", "dma", "send", "arrive"))
+    asker = [T.cores[(rank - 1 - t) % NR] for t in range(RO)]
+    asked = [T.cores[(rank + 1 + t) % NR] for t in range(RO)]
+    for t in range(RO):
+        for a in "mkw":
+            arrive("q%s%d" % (a, t), "r%s%d" % (a, t), len(topo.engines(asked[t], core)))
+
+    def at(win, off):
+        return ("@", win, off)
+
+    def col(n, k=0):
+        return R(n, k, k + 1)
+
+    def lanes(n, ph):
+        return R(n, ph, V, PH)
+
+    def ch(n, k, w):
+        return R(n, w * k, w * (k + 1))
+
+    def sk(name, k):
+        return R(name, 15 - k, 15 - k + 128)
+
+    def cls(t):
+        return ch("cls", t, 24)
+
+    def zof(t):
+        return ch("zof", t, 24)
+
+    MO, MS = R("morph"), R("meas", 0, V)
+
+    dma("s", R("bas_i"), T.bas[:])
+    dma("a", MS, T.mea[:])
+    dma("s", R("use_i"), T.use[:])
+    dma("s", R("der_i"), T.der[:])
+    dma("s", MO, T.mor[:])
+
+    ms(R("onef"), 1.0)
+    aff(R("selr"), R("onef"), [[1, 144]], OP.is_equal, 0, -1)
+    aff(R("selr"), R("selr"), [[0, 9], [1, 16]], OP.is_equal, -15, 0)
+    ms(R("oneb"), 1.0)
+    aff(R("sel1"), R("oneb", 0, 144), [[0, 9], [1, 16]], OP.is_equal, -15, 0)
+    aff(R("sel1"), R("sel1"), [[-16, 9], [0, 16]], OP.is_ge, 0, 1)
+    aff(R("sel1"), R("sel1"), [[16, 9], [0, 16]], OP.is_ge, 15, -1)
+    iota(R("pi", 0, 1), [[0, 1]], 0, 1)
+    iota(R("i8"), [[0, 4], [128, 24]], 0, 0)
+    iota(R("cb", 0, 6), [[-16, 6]], 0, 0)
+    aff(R("idb"), R("oneb", 0, 128), [[1, 128]], OP.is_equal, 0, -1)
+    aff(R("blk"), R("oneb", 0, 128), [[-16, 8], [0, 16]], OP.is_ge, 0, 1)
+    aff(R("blk"), R("blk"), [[16, 8], [0, 16]], OP.is_ge, 15, -1)
+    aff(R("tri"), R("blk"), [[1, 128]], OP.is_ge, 0, -1)
+    iota(R("VR"), [[1, V]], 0, 0)
+    for h in range(2):
+        for y in range(2):
+            o = ch("swp", 2 * h + y, 128)
+            aff(o, R("onef", 0, 128), [[1, 128]], OP.is_equal, -16 * (h - y), -1)
+            aff(o, o, [[0, 4], [1, 2], [0, 16]], OP.is_equal, -h, 0)
+    iota(R("dgf"), [[0, 25], [1, 16]], 0, 0)
+    iota(R("KLX"), [[2, V // 2], [-1, 2]], 1, 0)
+    ms(R("rmask"), 1.0)
+    ms(R("rmask", 0, 16 * SC, 16), 0.0)
+    ms(R("Z"), 0.0)
+    ms(R("amask"), -2.0 * 2 ** 25)
+    ms(R("amask", 0, I, 16), 2.0 * 2 ** 25)
+    ms(R("Bf", V, VX), 0.0)
+    ms(R("meas", V, VX), 0.0)
+    ms(R("cst"), -32.0)
+    ms(R("cst", 15, 128, 16), 32.0)
+    ms(R("nm", 0, 1), 0.0)
+    ms(R("thr", I, IX), -1e9)
+    ms(R("non", I, IX), 1.0)
+    ms(R("c128"), 128.0)
+    ms(R("KQ", I, IX), 0.0)
+    ms(R("Ea", I, IX), 0)
+    ms(R("got", I, IX), 0.0)
+    ms(R("oall"), 0.0625)
+
+    def classes(rounds, ph):
+        for t in rounds:
+            c = ch("clsi", t, 24)
+            ts(c, ch("P2", ph, 24), float(97 * t), None, OP.add)
+            ts(c, c, 511, None, OP.bitwise_and)
+            cp(cls(t), c)
+
+    def class_rows(ph):
+        for x in range(16):
+            mm(ch("P2", ph, 24), sk("selr", x), R("Bf", 3 * x + ph, V, 48), x == 0, x == 15)
+
+    def spread(ph):
+        for k in range(VC * NVC // SC):
+            cp(R("Z", 0, 16 * SC, 16), R("meas", PH * SC * k + ph, PH * SC * (k + 1), PH))
+            scan(ch("x%d" % ph, k, 16 * SC), R("rmask"), R("Z"), OP.mult, OP.add)
+
+    def prelude(t):
+        if t:
+            cp(R("KUg"), at(R("KU"), cls(t)))
+            ts(R("U"), R("KUg"), 2047, None, OP.bitwise_and)
+            cp(R("u16"), R("U"))
+            tt(R("EQ"), R("U"), R("P6", 0, I), OP.is_equal)
+        else:
+            cp(R("U"), at(R("use_i"), cls(t)))
+            cp(R("u16"), R("U"))
+            tt(R("EQ"), R("U"), lanes("VR", t), OP.is_equal)
+
+    def vpiece(t, k):
+        tt(ch("GE", k, 16 * VC), at(MS, ch("u16", k, VC)), ch("x%d" % (t % PH), k, 16 * VC), OP.min)
+
+    def vsum(k):
+        mm(ch("P0", k, VC), R("idbig"), ch("EQ", k, VC), True, False)
+        for j in range(16):
+            mm(ch("P0", k, VC), sk("selm", j), R("GE", 16 * VC * k + j, 16 * VC * (k + 1), 16), False, j == 15)
+
+    def apiece(t, part):
+        n = VC * NVC
+
+        def sub(q):
+            b = "P3" if q % 2 else "P6"
+            for j in range(4):
+                mm(ch(b, j, SC), R("idb"), R("meas", PH * n + t % PH, V, PH), True, False)
+                mm(ch(b, j, SC), R("idn"), R("GM", 4 * q + j, 16 * SC, 16), False, True)
+            act(ch("RA", q, 4 * SC), R(b), AF.Relu)
+
+        def add(q):
+            for k in range(4 * q, 4 * q + 4):
+                mm(R("P4", n, I), sk("selq", k), ch("RA", k, SC), False, k == 15)
+
+        if part == 0:
+            act(R("GM"), at(MS, R("u16", n, I)))
+        elif part < 3:
+            sub(part - 1)
+        elif part == 3:
+            mm(R("P4", n, I), R("idbig"), R("EQ", n, I), True, False)
+            add(0)
+            sub(2)
+        elif part == 4:
+            add(1)
+            sub(3)
+        else:
+            add(2)
+            add(3)
+
+    def winners(keys, kt, ks, n, p2):
+        tr(kt, keys)
+        scan(ks, R("amask", 0, n), kt, OP.max, OP.min)
+        for y in range(2):
+            for h in range(2):
+                mm(R("P2", p2 + y, p2 + n // 16, 2), ch("swp", 2 * h + y, 128), R(ks[0], 15 + 16 * h, n, 32), h == 0, h == 1)
+
+    def numbers(lst, li, p2, n):
+        cp(R(li, 0, n), R("P2", p2, p2 + n))
+        ts(R(li, 0, n), R(li, 0, n), 2047, None, OP.bitwise_and)
+        cp(R(lst, 0, n), R(li, 0, n))
+
+    def keys(t):
+        if t == 0:
+            cp(R("KUg"), at(R("KU"), cls(t)))
+        n = VC * NVC
+        tt(R("KEY", 0, n), R("P0", 0, n), R("KUg", 0, n), OP.add)
+        tt(R("KEY", n, I), R("P4", n, I), R("KUg", n, I), OP.add)
+        winners(R("KEY"), R("KT"), R("KS"), I, 0)
+
+    def models():
+        numbers("m16", "mi", 0, 24)
+
+    def search(t):
+        n = {"v": 0, "w": 0}
+
+        def step(z):
+            if z == "b":
+                prelude(t)
+            elif z == "v":
+                vpiece(t, n["v"])
+            elif z == "w":
+                vsum(n["w"])
+            elif z in "cdefhi":
+                apiece(t, "cdefhi".index(z))
+            elif z == "s":
+                spread(1)
+                spread(2)
+            elif z == "p":
+                keys(t)
+            elif z == "q":
+                models()
+            if z in n:
+                n[z] += 1
+        return step
+
+    def gd(k):
+        act(ch("GD", k, 16 * CH), at(MO, ch("d16", k, CH)))
+
+    cp(lanes("Bf", 0), lanes("bas_i", 0))
+    cp(R("use16"), R("use_i"))
+    for ph in (1, 2):
+        cp(lanes("Bf", ph), lanes("bas_i", ph))
+    ts(R("selp"), R("sel1"), 2048.0, None, OP.mult)
+    for k in range(2):
+        act(R("SD" if k == 0 else "SE", 0, 4096), at(MS, ch("use16", k, 256)))
+    ts(R("pi", 0, 1), R("pi", 0, 1), 15, None, OP.bitwise_and)
+    cp(R("pm", 0, 1), R("pi", 0, 1))
+    ts(R("pw", 0, 1), R("pm", 0, 1), 1.0, None, OP.add)
+    ts(R("pw", 1, 2), R("pm", 0, 1), 8.0, None, OP.mult)
+    ts(R("cb", 0, 6), R("cb", 0, 6), col("pm"), 0.5, OP.subtract, OP.subtract)
+    ts(R("selz"), R("sel1"), col("pw"), None, OP.mult)
+    ts(R("i8"), R("i8"), col("pw", 1), None, OP.add)
+    spread(0)
+    class_rows(0)
+    classes([0, 3], 0)
+    ts(R("selm"), R("sel1"), -4096.0, None, OP.mult)
+    ts(R("idbig"), R("idb"), BIG, None, OP.mult)
+    ts(R("idn"), R("idb"), -1.0, None, OP.mult)
+    ts(R("selq"), R("sel1"), 4096.0, None, OP.mult)
+    ts(R("blkK"), R("blk"), 2048.0, None, OP.mult)
+    for k in range(2):
+        mm(R("P5" if k == 0 else "P7", 0, I), R("blkK"), ch("meas", k, I), True, True)
+    s0 = search(0)
+    s0("b")
+    cp(R("d16"), lanes("der_i", 0))
+    for k in range(2):
+        for j in range(16):
+            mm(ch("P1", k, 256), sk("selp", j), R("SD" if k == 0 else "SE", j, 4096, 16), j == 0, j == 15)
+    for z in FIRST:
+        if z == "p":
+            tt(R("NEQ"), R("bas_i"), R("der_i"), OP.not_equal)
+            for k in range(2):
+                for y in range(2):
+                    o = R("KLX", I * k + y, I * k + I, 2)
+                    tt(o, R("P5" if k == 0 else "P7", 1 - y, I, 2), o, OP.add)
+            tt(R("KU"), R("P1"), R("use_i"), OP.add)
+            ts(R("tri"), R("tri"), 8192.0, None, OP.mult)
+        s0(z)
+        for k in {"e": [0], "h": [1, 2, 3]}.get(z, []):
+            gd(k)
+        if z == "p":
+            for k in range(3):
+                p = R("P%d" % (4 + k), 0, I)
+                mm(p, R("tri"), ch("NEQ", k, I), True, False)
+                mm(p, R("cst"), R("oneb"), False, True)
+    mm(R("P7", 0, I), R("blkK"), R("meas", 2 * I, V), True, True)
+    class_rows(1)
+    class_rows(2)
+    for ph in range(PH):
+        for x in range(16):
+            mm(R("P2", 72 + 24 * ph, 96 + 24 * ph), sk("selz", x), R("meas", 3 * x + ph, V, 48), x == 0, x == 15)
+    for k in range(3):
+        tt(ch("W", k, I), R("P%d" % (4 + k), 0, I), ch("der_i", k, I), OP.add)
+    send(topo, core, asker[0], "qm0", MS, "rm0")
+    send(topo, core, asker[0], "qk0", R("KU"), "rk0")
+    send(topo, core, asker[0], "qw0", R("W"), "rw0")
+    for t in range(1, RO):
+        send(topo, core, asker[t], "qm%d" % t, MS, "rm%d" % t)
+
+    def rest1():
+        ts(R("blkn"), R("blk"), -1.0, None, OP.mult)
+        ts(R("blk2"), R("blk"), 2.0, None, OP.mult)
+        ts(R("blk2n"), R("blk"), -2.0, None, OP.mult)
+        ts(R("dg"), R("dgf"), col("pm"), None, OP.is_equal)
+        cp(R("Dv"), R("der_i"))
+
+    def rest2():
+        for y in range(2):
+            o = R("KLX", 2 * I + y, V, 2)
+            tt(o, R("P7", 1 - y, I, 2), o, OP.add)
+        classes([1], 1)
+        classes([2], 2)
+        for t in range(RO):
+            ts(ch("zi", t, 24), ch("P2", 3 + t % PH, 24), float(t), None, OP.add)
+        ts(R("zi"), R("zi"), 7, None, OP.bitwise_and)
+        tt(R("i8"), R("i8"), R("zi"), OP.add)
+        cp(R("zof"), R("i8"))
+
+    def ge(lo, hi, vec):
+        o, w = R("GE", 768 * lo, 768 * hi), at(MO, R("e16", 48 * lo, 48 * hi))
+        if vec:
+            cp(o, w)
+        else:
+            act(o, w)
+
+    def sd(k):
+        scan(ch("SD", k, 16 * CH), R("rmask", 0, 16 * CH), ch("GD", k, 16 * CH), OP.mult, OP.max)
+
+    def se(lo, hi):
+        scan(R("SE", 768 * lo, 768 * hi), R("rmask", 0, 768 * (hi - lo)), R("GE", 768 * lo, 768 * hi), OP.mult, OP.max)
+
+    def dist(t):
+        ph = t % PH
+        lm = lanes("meas", ph)
+        half = R("P4", 0, I)
+        if t:
+            gd(0)
+            change(t - 1)
+            for k in range(1, 4):
+                gd(k)
+        ea = R("Ea", 0, I)
+        tt(ea, at(R("W"), R("m16")), lanes("Bf", ph), OP.max)
+        ts(ea, ea, 4095, None, OP.bitwise_and)
+        cp(R("e16"), ea)
+        va = [(a, min(a + 2, EV[t])) for a in range(0, EV[t], 2)]
+        aa = [(a, min(a + 2, 8)) for a in range(EV[t], 8, 2)]
+        act(R("P6", 0, I), lm)
+        for a in aa:
+            ge(a[0], a[1], False)
+        for k, a in enumerate(va):
+            ge(a[0], a[1], True)
+            sd(k)
+        if t == 0:
+            rest1()
+        for k in range(len(va), 4):
+            sd(k)
+        for a in va:
+            se(a[0], a[1])
+        od, oe = R("SD", 15, W16, 16), R("SE", 15, W16, 16)
+        tt(R("MD"), od, R("P6", 0, I), OP.min)
+        mm(R("P0", 0, I), R("blk"), od, True, False)
+        mm(R("P0", 0, I), R("blk2n"), R("MD"), False, True)
+        mm(half, R("blkn"), od, True, False)
+        mm(half, R("blk2"), R("MD"), False, False)
+        for a in aa:
+            se(a[0], a[1])
+        if t == 0:
+            rest2()
+        kd, ku = R("P3", 0, I), R("KU", 37 * t, 37 * t + I)
+        act(R("KN"), at(R("KLX"), R("m16")))
+        act(kd, R("KN"))
+        tt(R("ME"), oe, R("P6", 0, I), OP.min)
+        mm(half, R("blk"), oe, False, False)
+        mm(half, R("blk2n"), R("ME"), False, True)
+        tt(kd, kd, ku, OP.subtract)
+        act(R("KQ", 0, I), at(R("qk%d" % t), cls(t)))
+        act(R("thr", 0, I), R("P0", 0, I), AF.Identity, bias=col("nm"))
+        if t + 1 < RO:
+            act(R("P6", 0, I), lanes("VR", (t + 1) % PH))
+        ts(R("non", 0, I), half, col("nm"), None, OP.is_ge)
+        scan(R("cum"), R("non"), R("c128"), OP.add, OP.min)
+        for n in range(6):
+            act(R("junk"), R("cum"), AF.Sign, bias=col("cb", n), accum=col("acc", n))
+        ts(R("got", 0, I), half, col("nm"), None, OP.is_lt)
+        tt(kd, kd, R("dg", t, t + I), OP.mult)
+        tt(kd, kd, R("got", 0, I), OP.mult)
+        tt(ku, kd, ku, OP.add)
+        if t + 1 < RO:
+            send(topo, core, asker[t + 1], "qk%d" % (t + 1), R("KU"), "rk%d" % (t + 1))
+
+    def ask(t):
+        ph = t % PH
+        s6, v6 = R("s16", 0, 6), R("sv16", 0, 6)
+        zs = R("Z", 0, 16 * CAP, 16)
+        ts(s6, R("acc", 0, 6), -0.5, IX / 2.0, OP.mult, OP.add)
+        ts(v6, R("acc", 0, 6), -1.5, PH * IX / 2.0 + ph, OP.mult, OP.add)
+        cp(R("KQs"), at(R("KQ"), s6))
+        ts(R("uq"), R("KQs"), 2047, None, OP.bitwise_and)
+        cp(R("uq16"), R("uq"))
+        act(zs, at(R("meas"), v6))
+        act(R("Bs"), at(R("Bf"), v6))
+        act(R("ths"), at(R("thr"), s6))
+        scan(R("RQ"), R("rmask", 0, 16 * CAP), R("Z", 0, 16 * CAP), OP.mult, OP.add)
+        yield
+        act(R("old"), at(MO, zof(t)))
+        act(R("P5", 0, I), lanes("Dv", ph))
+        for k in range(2):
+            tt(ch("GQ", k, 768), at(R("qm%d" % t), ch("uq16", k, 48)), ch("RQ", k, 768), OP.min)
+        for j in range(16):
+            mm(R("P1", 0, CAP), sk("selm", j), R("GQ", j, 16 * CAP, 16), j == 0, j == 15)
+        yield
+        tt(R("KEY2"), R("P1", 0, CAP), R("KQs"), OP.add)
+        winners(R("KEY2"), R("KT2"), R("KS2"), CAP, 32)
+        yield
+        numbers("n16", "ni", 32, 6)
+        tt(R("E2"), at(R("qw%d" % t), R("n16", 0, 6)), R("Bs"), OP.max)
+        ts(R("E2"), R("E2"), 4095, None, OP.bitwise_and)
+        cp(R("e216"), R("E2"))
+        for k in range(2):
+            act(ch("GQ", k, 768), at(MO, ch("e216", k, 48)))
+        mm(R("P7", 0, I), R("idb"), lanes("meas", ph), True, False)
+        mm(R("P7", 0, I), R("idn"), R("old"), False, True)
+        cp(at(R("Ea"), s6), R("E2"))
+        if t + 1 < RO:
+            cp(R("d16"), lanes("Dv", (t + 1) % PH))
+        yield
+        for k in range(2):
+            scan(ch("S2", k, 768), R("rmask", 0, 768), ch("GQ", k, 768), OP.mult, OP.max)
+        tt(R("MM2"), R("S2", 15, 16 * CAP, 16), zs, OP.min)
+        mm(R("P1", 0, CAP), R("blk"), R("S2", 15, 16 * CAP, 16), True, False)
+        mm(R("P1", 0, CAP), R("blk2n"), R("MM2"), False, True)
+        yield
+        tt(R("ad2"), R("P1", 0, CAP), R("ths"), OP.is_lt)
+        cp(at(R("got"), s6), R("ad2"))
+        tt(R("gx"), R("P7", 0, I), R("got", 0, I), OP.mult)
+        tt(at(MO, zof(t)), R("old"), R("gx"), OP.add)
+        yield
+
+    def change(t):
+        ph = t % PH
+        last = t + 1 == RO
+        d, e = lanes("Dv", ph), R("P5", 0, I)
+        if not last:
+            keys(t + 1)
+        tt(e, e, R("Ea", 0, I), OP.subtract)
+        tt(e, e, R("got", 0, I), OP.mult)
+        tt(d if last else e, d, e, OP.subtract)
+        if last:
+            return
+        tt(R("NEQ", 0, I), e, lanes("Bf", ph), OP.not_equal)
+        cp(d, e)
+        models()
+        act(R("junk", 0, I), R("got", 0, I), accum=col("cnt"))
+        mm(R("P4", 0, I), R("tri"), R("NEQ", 0, I), True, False)
+        mm(R("P4", 0, I), R("cst"), R("oneb"), False, True)
+        mm(R("P2", 40, 41), R("oall"), col("cnt"), True, True)
+        tt(lanes("W", ph), R("P4", 0, I), d, OP.add)
+        cp(R("nmi", 0, 1), R("P2", 40, 41))
+        ts(R("nmi", 0, 1), R("nmi", 0, 1), 127, None, OP.bitwise_and)
+        ts(R("nm", 0, 1), R("nmi", 0, 1), -1.0, None, OP.mult)
+        send(topo, core, asker[t + 1], "qw%d" % (t + 1), R("W"), "rw%d" % (t + 1))
+
+    for t in range(RO):
+        dist(t)
+        a = ask(t)
+        if t + 1 < RO:
+            s = search(t + 1)
+            for z in ORDER:
+                if z == "a":
+                    next(a)
+                else:
+                    s(z)
+    cp(R("use_i"), R("KU"))
+    ts(R("use_i"), R("use_i"), 2047, None, OP.bitwise_and)
+    cp(R("KU"), R("use_i"))
+    dma("s", T.yu[:], R("KU"))
+    for _ in a:
+        pass
+    dma("a", T.ym[:], MO)
+    change(RO - 1)
+    dma("s", T.yd[:], R("Dv"))
+    F["finish"]()

@@ -5,15 +5,21 @@ P, V, C, PH, I, CAP, RO = 3072, 1152, 512, 3, 384, 96, 4
 IX = I + CAP
 VX = V + PH * CAP
 W16 = 16 * I
-CH = 96
-SC = 128
-VC, NVC = 64, 4
-EV = [0, 3, 3, 3]
+PC = 64
 BIG = float(1 << 23)
-FIRST = "cvdewvfwvhwivwspq"
-ORDER = "bacadvawevfavwhviawaw"
+CFG = {
+    "sums": "aaaaaaaa",
+    "search": [[("m", 128), ("m", 128), ("m", 128)]] + [[("m", 192), ("p", 96), ("p", 96)]] * 3,
+    "old": [[("a", 96)] * 4] * 4,
+    "pair": [0, 1, 1, 1],
+    "new": [[("a", 48), ("v", 48)] * 4] + [[("a", 128), ("a", 128), ("v", 32), ("a", 48), ("a", 48)]] * 3,
+    "ask2": ["av", "av", "av", "av"],
+    "bulk": ("GD", "GE", "SD", "SE"),
+    "mu": 2.0, "passes": 3, "hop": 0.15, "gath": 1.56, "kf": "a", "x0": 256, "cut": 288, "stage": "aaa",
+}
 
 SCRATCH = {}
+SMALL = ["pm", "pw", "cb", "cn", "a2", "acc", "mg", "cnt"]
 
 
 def _sb(dtype, **kw):
@@ -21,29 +27,136 @@ def _sb(dtype, **kw):
         SCRATCH[n] = ("sbuf", [128, w], dtype)
 
 
-_sb("int32", bas_i=V, der_i=V, use_i=C, pi=8, clsi=96, zi=96, mi=24, ni=8, KUg=I, U=I, Ea=IX, nmi=8, KQs=CAP, uq=CAP, E2=CAP)
-_sb("uint16", cls=96, zof=96, use16=C, u16=I, d16=I, e16=I, m16=24, s16=8, sv16=8, n16=8, uq16=CAP, e216=CAP)
-_sb("float32", Bf=VX, Dv=V, W=V, KU=C, KLX=V, VR=V, onef=144, selr=144, swp=512, oall=128, pm=8, pw=8, cb=8, i8=96, dgf=400,
-    amask=I, acc=8, KEY=I, KT=I, KS=I, thr=IX, nm=8, cnt=8, KN=I, KQ=IX, KEY2=CAP, KT2=CAP, KS2=CAP, Bs=CAP, ths=CAP)
-_sb("bfloat16", meas=VX, morph=P, oneb=I, sel1=144, selm=144, selp=144, selq=144, selz=144, blk=128, blkn=128, blk2=128,
-    blk2n=128, tri=128, cst=128, idb=128, idn=128, idbig=128, blkK=128, dg=400, rmask=16 * SC, c128=IX, Z=16 * SC,
-    GM=16 * SC, RA=16 * SC, EQ=I, GD=W16, GE=W16, SD=W16, SE=W16, MD=I, ME=I, got=IX, non=IX, cum=IX, junk=IX, old=I, gx=I,
-    NEQ=V, GQ=16 * CAP, RQ=16 * CAP, S2=16 * CAP, MM2=CAP, ad2=CAP, x0=16 * VC * NVC, x1=16 * VC * NVC, x2=16 * VC * NVC)
+_sb("int32", bas_i=V, der_i=V, use_i=C, pi=8, clsi=96, zi=96, mi=24, ni=8, Ea=I, nmi=8, E2=CAP)
+_sb("uint16", cls=96, zof=96, u16=I, d16=V, use16=C, e16=I, m16=24, s16=8, sv16=8, n16=8, uq16=CAP, e216=CAP)
+_sb("float32", Bf=VX, Dv=VX, W=V, USE=C, LX=V, VR=V, onef=144, selr=144, swp=512, cum=IX, wlo=144, whi=144, oalln=128,
+    idf=128, idfn=128, idk=128, idkn=128, small=8 * len(SMALL), i8=96, dgf=400, amask=I, KT=I, KS=I, U=I, KF=I, LXg=I, UQ=IX,
+    UQs=CAP, U2=CAP, KT2=CAP, KS2=CAP, Bs=CAP, tD=IX, dE2=CAP, adf=CAP)
+_sb("bfloat16", meas=VX, morph=P, oneb=IX, sel1=144, selp=144, selm=144, selk=144, selz=144, blk=128, blkn=128, blk2n=128,
+    blkp=128, tri=128, cst=128, idb=128, idn=128, idbig=128, dg=400, rmask=2048, rmask8=1024, Z=2048, EQ=I, GD=W16, GE=W16,
+    SD=W16, SE=W16, AD=IX, AE=I, got=IX, junk=IX, old=IX, gx=IX, NEQ=V, GQ=16 * CAP, RQ=16 * CAP, SQ=16 * CAP, MM2=CAP,
+    AD2=CAP, dxs=CAP, adb=CAP, x0=W16, x1=W16)
+SCRATCH["b15i"] = ("sbuf", [8, V], "int32")
+SCRATCH["b15"] = ("sbuf", [8, I], "float32")
+SCRATCH["sel8"] = ("sbuf", [8, 144], "float32")
+SCRATCH["one8"] = ("sbuf", [8, 144], "float32")
 for _t in range(RO):
     _sb("bfloat16", **{"qm%d" % _t: V})
     _sb("float32", **{"qk%d" % _t: C, "qw%d" % _t: V})
 for _t in range(8):
     SCRATCH["P%d" % _t] = ("psum", [128, 512], "float32")
-SEMAPHORES = ["q_v", "q_a", "q_t", "q_g"] + ["d%d" % k for k in range(9)] + ["l%d" % k for k in range(12)] + ["r%s%d" % (a, k) for a in "mkw" for k in range(RO)]
+SEMAPHORES = (["q_v", "q_a", "q_t", "q_g"] + ["d%d" % k for k in range(12)] + ["l%d" % k for k in range(12)]
+              + ["r%s%d" % (a, k) for a in "mkw" for k in range(RO)])
+CYC = 0.83e-3
+WIDE = {"int32": 4, "float32": 4, "bfloat16": 2, "uint16": 2}
 
 
 def R(name, lo=0, hi=None, step=1):
+    if name in SMALL:
+        return ("small", 8 * SMALL.index(name) + lo, 8 * SMALL.index(name) + hi, step)
     return (name, lo, SCRATCH[name][1][1] if hi is None else hi, step)
+
+
+def size(r):
+    return 16 * size(r[2]) if r[0] == "@" else (r[2] - r[1] + r[3] - 1) // r[3]
+
+
+def accesses(reads, writes):
+    a = []
+    for w, rs in ((0, reads), (1, writes)):
+        for r in rs:
+            a += [(r[1], w), (r[2], 0)] if r[0] == "@" else [(r, w)]
+    return a
+
+
+def clash(q, a, p, b):
+    (n, lo, hi, st), w = a
+    (_, l2, h2, s2), w2 = b
+    if SCRATCH[n][0] == "psum" and (q != p or q == "t"):
+        return True
+    if st > 1 and st == s2 and (lo - l2) % st:
+        return False
+    return (w or w2) and lo < h2 and l2 < hi
+
+
+def plan(calls):
+    n = len(calls)
+    pred, succ, seen = [set() for _ in calls], [set() for _ in calls], {}
+    for i, c in enumerate(calls):
+        for a in c["acc"] + c["also"]:
+            keep = []
+            for j, b in seen.get(a[0][0], []):
+                if j != i and clash(c["q"], a, calls[j]["q"], b):
+                    pred[i].add(j)
+                    if (a[1] and a[0][3] == 1 and a[0][1] <= b[0][1] and b[0][2] <= a[0][2]) or (a[1] and a[0] == b[0]):
+                        continue
+                    if SCRATCH[a[0][0]][0] == "psum" and c["q"] == "t":
+                        continue
+                keep.append((j, b))
+            seen[a[0][0]] = keep + [(i, a)]
+        pred[i].update(c["after"])
+        for j in pred[i]:
+            succ[j].add(i)
+
+    def gap(i, j):
+        if i in calls[j]["after"]:
+            return calls[j]["after"][i]
+        return calls[i]["lat"] + (0.0 if calls[i]["q"] == calls[j]["q"] == "t" else CFG["hop"])
+
+    def run(before, after, rank, back):
+        left = [len(b) for b in before]
+        ready, start, free = [0.0] * n, [0.0] * n, {}
+        pool = {}
+        for i in range(n):
+            if not left[i]:
+                pool.setdefault(calls[i]["q"], []).append(i)
+        for _ in range(n):
+            best = None
+            for q, l in pool.items():
+                if not l:
+                    continue
+                now = max(free.get(q, 0.0), min(ready[i] for i in l))
+                a = max((i for i in l if ready[i] <= now), key=lambda i: rank[i])
+                pick, score = a, None
+                for b in l:
+                    if ready[b] > now and rank[b] > rank[a] and ready[b] < now + calls[a]["cost"]:
+                        go = max(rank[a] + now, rank[b] + now + calls[a]["cost"])
+                        hold = max(rank[b] + ready[b], rank[a] + ready[b] + calls[b]["cost"]) + CFG["mu"] * (ready[b] - now)
+                        if hold < go and (score is None or hold - go < score):
+                            pick, score = b, hold - go
+                at = max(now, ready[pick])
+                if best is None or now < best[0]:
+                    best = (now, at, q, pick)
+            _, at, q, i = best
+            pool[q].remove(i)
+            start[i] = at
+            free[q] = at + calls[i]["cost"]
+            for j in after[i]:
+                ready[j] = max(ready[j], free[q] + (gap(j, i) if back else gap(i, j)))
+                left[j] -= 1
+                if not left[j]:
+                    pool.setdefault(calls[j]["q"], []).append(j)
+        return start, max(start[i] + calls[i]["cost"] + calls[i]["lat"] for i in range(n))
+
+    rank = [0.0] * n
+    for i in reversed(range(n)):
+        rank[i] = calls[i]["cost"] + max([calls[i]["lat"]] + [gap(i, j) + rank[j] for j in succ[i]])
+    best = run(pred, succ, rank, False)
+    now = best
+    for _ in range(CFG["passes"]):
+        back = run(succ, pred, [s + c["cost"] for s, c in zip(now[0], calls)], True)
+        now = run(pred, succ, [s + c["cost"] for s, c in zip(back[0], calls)], False)
+        if now[1] < best[1]:
+            best = now
+    return sorted(range(n), key=lambda i: (best[0][i], i)), best[1]
+
+
+PLAN = {}
 
 
 def make(g, T):
     eng = {"v": g.vector, "a": g.scalar, "t": g.tensor, "g": g, "s": g.sync}
-    count, known, waited, hist, total = {}, {k: {} for k in eng}, {}, {}, {}
+    calls, total, lines = [], {}, {}
 
     def ap(r):
         if r[0] == "@":
@@ -51,84 +164,51 @@ def make(g, T):
         n, lo, hi, st = r
         return T[n][:, lo:hi] if st == 1 else T[n][:, lo:hi:st]
 
-    def acc(reads, writes):
-        a = []
-        for w, rs in ((0, reads), (1, writes)):
-            for r in rs:
-                if r[0] == "@":
-                    a += [(r[1], w), (r[2], 0)]
-                else:
-                    a.append((r, w))
-        return a
-
-    def sync(q, accs):
-        need = []
-        for (n, lo, hi, st), w in accs:
-            ps = SCRATCH[n][0] == "psum"
-            for e in hist.get(n, []):
-                if ps and q == "t" and e[3] == "t":
-                    continue
-                if (ps and e[3] != q) or ((w or e[2]) and lo < e[1] and e[0] < hi):
-                    need.append(e)
-        need.sort(key=lambda e: -e[5])
-        k = known[q]
-        for e in need:
-            if k.get(e[4], 0) >= e[5]:
-                continue
-            eng[q].wait_ge(T.sem[e[4]], e[5])
-            waited[e[4]] = max(waited.get(e[4], 0), e[5])
-            for s, v in e[6].items():
-                k[s] = max(k.get(s, 0), v)
-            k[e[4]] = max(k.get(e[4], 0), e[5])
-
-    def note(q, accs, sem, val):
-        clock = dict(known[q]) if q in known else {}
-        for (n, lo, hi, st), w in accs:
-            ps = SCRATCH[n][0] == "psum"
-            keep = []
-            for e in hist.get(n, []):
-                same = e[0] == lo and e[1] == hi and e[7] == st
-                if ps and e[3] != q:
-                    continue
-                if w and (same or (st == 1 and lo <= e[0] and e[1] <= hi)):
-                    continue
-                if not w and not e[2] and same and e[3] == q and e[4] == sem:
-                    continue
-                keep.append(e)
-            keep.append((lo, hi, w, q, sem, val, clock, st))
-            hist[n] = keep
-
-    def do(q, reads, writes, call):
-        a = acc(reads, writes)
-        sync(q, a)
-        s = "q_" + q
-        count[q] = total[s] = count.get(q, 0) + 1
-        call().then_inc(T.sem[s], 1)
-        note(q, a, s, count[q])
-
     def isr(x):
         return isinstance(x, tuple)
 
+    def psum(r):
+        return r[0] != "@" and SCRATCH[r[0]][0] == "psum"
+
+    def note(q, reads, writes, call, cost, lat=0.0, sem=None, also=(), line=None, busy=0.0):
+        if q in "va" and writes and writes[0][0] in CFG["bulk"]:
+            line = q + ("g" if reads[0][0] == "@" else "f")
+        after = {lines[line][0]: lines[line][1]} if line in lines else {}
+        if line:
+            lines[line] = (len(calls), busy)
+        calls.append({"q": q, "acc": accesses(reads, writes), "also": list(also), "call": call, "cost": cost, "lat": lat, "sem": sem, "after": after})
+
+    def price(out, ins, rate=None):
+        if out[0] == "@":
+            return 0.05 + 3.8 * CYC * size(out)
+        if ins and ins[0][0] == "@":
+            return 0.06 + CFG["gath"] * CYC * size(out)
+        if rate is None:
+            rate = 0.5 if all(WIDE[SCRATCH[r[0]][2]] == 2 for r in [out] + ins) else 1.0
+        return 0.03 + CYC * max(64, rate * size(out))
+
     def tt(out, a, b, op):
-        do("v", [a, b], [out], lambda: g.vector.tensor_tensor(out=ap(out), in0=ap(a), in1=ap(b), op=op))
+        note("v", [a, b], [out], lambda: g.vector.tensor_tensor(out=ap(out), in0=ap(a), in1=ap(b), op=op),
+             price(out, [a, b], 1.0 if psum(a) or psum(b) else 2.0))
 
     def ts(out, a, s1, s2, op0, op1=None):
-        rs = [a] + [s for s in (s1, s2) if isr(s)]
         v = [ap(s) if isr(s) else s for s in (s1, s2)]
         kw = {} if op1 is None else {"op1": op1}
-        do("v", rs, [out], lambda: g.vector.tensor_scalar(out=ap(out), in0=ap(a), scalar1=v[0], scalar2=v[1], op0=op0, **kw))
+        note("v", [a] + [s for s in (s1, s2) if isr(s)], [out],
+             lambda: g.vector.tensor_scalar(out=ap(out), in0=ap(a), scalar1=v[0], scalar2=v[1], op0=op0, **kw), price(out, [a]))
 
     def cp(out, a):
-        do("v", [a], [out], lambda: g.vector.tensor_copy(out=ap(out), in_=ap(a)))
+        note("v", [a], [out], lambda: g.vector.tensor_copy(out=ap(out), in_=ap(a)), price(out, [a]))
 
     def ms(out, c):
-        do("v", [], [out], lambda: g.vector.memset(ap(out), c))
+        note("v", [], [out], lambda: g.vector.memset(ap(out), c), price(out, []))
 
     def scan(out, a, b, op0, op1):
-        do("v", [a, b], [out], lambda: g.vector.tensor_tensor_scan(out=ap(out), data0=ap(a), data1=ap(b), initial=0.0, op0=op0, op1=op1))
+        note("v", [a, b], [out], lambda: g.vector.tensor_tensor_scan(out=ap(out), data0=ap(a), data1=ap(b), initial=0.0, op0=op0, op1=op1),
+             price(out, [a, b]))
 
     def tr(out, a):
-        do("v", [a], [out], lambda: g.vector.transpose(out=ap(out), in_=ap(a)))
+        note("v", [a], [out], lambda: g.vector.transpose(out=ap(out), in_=ap(a)), price(out, [a]))
 
     def act(out, a, func=AF.Copy, bias=None, accum=None):
         kw = {}
@@ -136,51 +216,80 @@ def make(g, T):
             kw["bias"] = ap(bias)
         if accum is not None:
             kw["accum_out"] = ap(accum)
-        do("a", [a] + [b for b in [bias] if b], [out] + [b for b in [accum] if b],
-           lambda: g.scalar.activation(out=ap(out), in_=ap(a), func=func, **kw))
+        note("a", [a] + [b for b in [bias] if b], [out] + [b for b in [accum] if b],
+             lambda: g.scalar.activation(out=ap(out), in_=ap(a), func=func, **kw), price(out, [a], 1.0))
 
     def mm(out, lhsT, rhs, start, stop):
-        do("t", [lhsT, rhs], [out], lambda: g.tensor.matmul(ap(out), ap(lhsT), ap(rhs), start, stop))
+        note("t", [lhsT, rhs], [out], lambda: g.tensor.matmul(ap(out), ap(lhsT), ap(rhs), start, stop),
+             0.03 + 0.5e-3 * max(64, size(rhs)) * (4 if SCRATCH[rhs[0]][2] == "float32" else 1))
 
     def iota(out, pattern, base, cm):
         kw = {} if SCRATCH[out[0]][2] == "int32" else {"allow_small_or_imprecise_dtypes": True}
-        do("g", [], [out], lambda: g.iota(ap(out), pattern, base, cm, **kw))
+        note("g", [], [out], lambda: g.iota(ap(out), pattern, base, cm, **kw), 0.13 + 2 * CYC * size(out))
 
     def aff(out, a, pattern, op, base, cm):
-        do("g", [a], [out], lambda: g.affine_select(ap(out), ap(a), pattern, op, 0.0, base, cm))
+        note("g", [a], [out], lambda: g.affine_select(ap(out), ap(a), pattern, op, 0.0, base, cm), 0.17 + 2 * CYC * size(out))
 
     nd, nl = [0], [0]
 
+    def nbytes(r):
+        return SCRATCH[r[0]][1][0] * size(r) * WIDE[SCRATCH[r[0]][2]]
+
     def dma(q, out, a):
-        accs = acc([a] if isr(a) else [], [out] if isr(out) else [])
-        sync(q, accs)
         s = "d%d" % nd[0]
         nd[0] += 1
         total[s] = 16
-        eng[q].dma_start(out=ap(out) if isr(out) else out, in_=ap(a) if isr(a) else a).then_inc(T.sem[s], 16)
-        note("dma" + s, accs, s, 16)
+        busy = nbytes(out if isr(out) else a) / 180e3
+        note(q, [a] if isr(a) else [], [out] if isr(out) else [],
+             lambda: eng[q].dma_start(out=ap(out) if isr(out) else out, in_=ap(a) if isr(a) else a).then_inc(T.sem[s], 16),
+             0.05, 2.0 + busy, s, (), "dma", busy)
 
     def send(topo, src, dst, land, a, rsem):
-        accs = acc([a], [])
-        sync("g", accs)
         s = "l%d" % nl[0]
         nl[0] += 1
         rid, pid, _ = topo.addr(dst)
         total[s] = len(topo.engines(src, dst))
-        g.remote_dma(out_ap=T[land][:], in_ap=ap(a), remote_sem=T.sem[rsem], local_sem=T.sem[s], pid=pid, routing_id=rid, dma_engine_mask=topo.mask(src, dst))
-        note("rem" + s, accs, s, total[s])
+        note("g", [a], [], lambda: g.remote_dma(out_ap=T[land][:], in_ap=ap(a), remote_sem=T.sem[rsem], local_sem=T.sem[s], pid=pid,
+                                                routing_id=rid, dma_engine_mask=topo.mask(src, dst)),
+             0.5 if nl[0] > 1 else 3.5, 3.0 + nbytes(a) / 40e3, s, [(R(land), 1)], "link", nbytes(a) / 40e3)
 
-    def arrive(land, rsem, n):
-        total[rsem] = n
-        note("arr" + rsem, acc([], [R(land)]), rsem, n)
-
-    def finish():
+    def issue(arrivals):
+        count, known, waited, hist = {}, {k: {} for k in eng}, {}, {}
+        for land, rsem, n in arrivals:
+            total[rsem] = n
+            hist[land] = [((R(land), 1), "remote", rsem, n, {})]
+        if "order" not in PLAN:
+            PLAN["order"], PLAN["end"] = plan(calls)
+        for i in PLAN["order"]:
+            c = calls[i]
+            q, k = c["q"], known[c["q"]]
+            need = [e for a in c["acc"] for e in hist.get(a[0][0], []) if clash(q, a, e[1], e[0]) and not (q == e[1] == "t" and psum(a[0]))]
+            for e in sorted(need, key=lambda e: -e[3]):
+                if k.get(e[2], 0) < e[3]:
+                    eng[q].wait_ge(T.sem[e[2]], e[3])
+                    waited[e[2]] = max(waited.get(e[2], 0), e[3])
+                    for s, v in list(e[4].items()) + [(e[2], e[3])]:
+                        k[s] = max(k.get(s, 0), v)
+            if c["sem"]:
+                c["call"]()
+                s, v, p = c["sem"], total[c["sem"]], "dma"
+            else:
+                s, p = "q_" + q, q
+                count[q] = total[s] = v = count.get(q, 0) + 1
+                c["call"]().then_inc(T.sem[s], 1)
+            clock = dict(k)
+            for a in c["acc"]:
+                keep = [e for e in hist.get(a[0][0], [])
+                        if not (psum(a[0]) and e[1] != q)
+                        and not (a[1] and (e[0][0] == a[0] or (a[0][3] == 1 and a[0][1] <= e[0][0][1] and e[0][0][2] <= a[0][2])))
+                        and not (e[0] == a and e[2] == s)]
+                hist[a[0][0]] = keep + [(a, p, s, v, clock)]
         for s, n in total.items():
             if waited.get(s, 0) < n:
                 g.wait_ge(T.sem[s], n)
 
     return {"tt": tt, "ts": ts, "cp": cp, "ms": ms, "scan": scan, "tr": tr, "act": act, "mm": mm, "iota": iota, "aff": aff,
-            "dma": dma, "send": send, "arrive": arrive, "finish": finish}
+            "dma": dma, "send": send, "issue": issue}
 
 
 def rank_program(g, core, T, topo):
@@ -189,12 +298,9 @@ def rank_program(g, core, T, topo):
         return
     F = make(g, T)
     tt, ts, cp, ms, scan, tr, act, mm = (F[k] for k in ("tt", "ts", "cp", "ms", "scan", "tr", "act", "mm"))
-    iota, aff, dma, send, arrive = (F[k] for k in ("iota", "aff", "dma", "send", "arrive"))
+    iota, aff, dma, send = (F[k] for k in ("iota", "aff", "dma", "send"))
     asker = [T.cores[(rank - 1 - t) % NR] for t in range(RO)]
     asked = [T.cores[(rank + 1 + t) % NR] for t in range(RO)]
-    for t in range(RO):
-        for a in "mkw":
-            arrive("q%s%d" % (a, t), "r%s%d" % (a, t), len(topo.engines(asked[t], core)))
 
     def at(win, off):
         return ("@", win, off)
@@ -202,8 +308,8 @@ def rank_program(g, core, T, topo):
     def col(n, k=0):
         return R(n, k, k + 1)
 
-    def lanes(n, ph):
-        return R(n, ph, V, PH)
+    def lanes(n, ph, lo=0, hi=I):
+        return R(n, PH * lo + ph, PH * hi, PH)
 
     def ch(n, k, w):
         return R(n, w * k, w * (k + 1))
@@ -214,17 +320,30 @@ def rank_program(g, core, T, topo):
     def cls(t):
         return ch("cls", t, 24)
 
-    def zof(t):
-        return ch("zof", t, 24)
+    def gather(who, out, a):
+        if who == "v":
+            cp(out, a)
+        else:
+            act(out, a)
+
+    def stage(out, a, who):
+        if who == "t":
+            mm(out, R("idf"), a, True, True)
+        else:
+            act(out, a)
 
     MO, MS = R("morph"), R("meas", 0, V)
+    DV = R("Dv", 0, V)
 
-    dma("s", R("bas_i"), T.bas[:])
-    dma("a", MS, T.mea[:])
+    dma("s", R("b15i"), T.bas[15:128:16, :])
     dma("s", R("use_i"), T.use[:])
+    dma("s", MS, T.mea[:])
     dma("s", R("der_i"), T.der[:])
+    dma("s", R("bas_i"), T.bas[:])
     dma("s", MO, T.mor[:])
 
+    ms(R("one8"), 1.0)
+    aff(R("sel8"), R("one8"), [[1, 144]], OP.is_equal, -15, -16)
     ms(R("onef"), 1.0)
     aff(R("selr"), R("onef"), [[1, 144]], OP.is_equal, 0, -1)
     aff(R("selr"), R("selr"), [[0, 9], [1, 16]], OP.is_equal, -15, 0)
@@ -235,7 +354,9 @@ def rank_program(g, core, T, topo):
     iota(R("pi", 0, 1), [[0, 1]], 0, 1)
     iota(R("i8"), [[0, 4], [128, 24]], 0, 0)
     iota(R("cb", 0, 6), [[-16, 6]], 0, 0)
+    iota(R("cn", 0, 6), [[32, 6]], 400, 0)
     aff(R("idb"), R("oneb", 0, 128), [[1, 128]], OP.is_equal, 0, -1)
+    aff(R("idf"), R("onef", 0, 128), [[1, 128]], OP.is_equal, 0, -1)
     aff(R("blk"), R("oneb", 0, 128), [[-16, 8], [0, 16]], OP.is_ge, 0, 1)
     aff(R("blk"), R("blk"), [[16, 8], [0, 16]], OP.is_ge, 15, -1)
     aff(R("tri"), R("blk"), [[1, 128]], OP.is_ge, 0, -1)
@@ -246,379 +367,331 @@ def rank_program(g, core, T, topo):
             aff(o, R("onef", 0, 128), [[1, 128]], OP.is_equal, -16 * (h - y), -1)
             aff(o, o, [[0, 4], [1, 2], [0, 16]], OP.is_equal, -h, 0)
     iota(R("dgf"), [[0, 25], [1, 16]], 0, 0)
-    iota(R("KLX"), [[2, V // 2], [-1, 2]], 1, 0)
+    iota(R("LX"), [[2, V // 2], [-1, 2]], 1, 0)
     ms(R("rmask"), 1.0)
-    ms(R("rmask", 0, 16 * SC, 16), 0.0)
+    ms(R("rmask", 0, 2048, 16), 0.0)
     ms(R("Z"), 0.0)
     ms(R("amask"), -2.0 * 2 ** 25)
     ms(R("amask", 0, I, 16), 2.0 * 2 ** 25)
-    ms(R("Bf", V, VX), 0.0)
-    ms(R("meas", V, VX), 0.0)
+    for n in ("Bf", "Dv", "meas"):
+        ms(R(n, V, VX), 0.0)
+    for n in ("UQ", "AD", "old", "got"):
+        ms(R(n, I, IX), 0.0)
     ms(R("cst"), -32.0)
     ms(R("cst", 15, 128, 16), 32.0)
-    ms(R("nm", 0, 1), 0.0)
-    ms(R("thr", I, IX), -1e9)
-    ms(R("non", I, IX), 1.0)
-    ms(R("c128"), 128.0)
-    ms(R("KQ", I, IX), 0.0)
-    ms(R("Ea", I, IX), 0)
-    ms(R("got", I, IX), 0.0)
-    ms(R("oall"), 0.0625)
+    ms(col("mg"), -0.5)
+    ms(R("oalln"), -0.0625)
+    ts(R("pi", 0, 1), R("pi", 0, 1), 15, None, OP.bitwise_and)
+    cp(col("pm"), R("pi", 0, 1))
+    ts(col("pw"), col("pm"), 1.0, None, OP.add)
+    ts(col("pw", 1), col("pm"), 8.0, None, OP.mult)
+    ts(R("cb", 0, 6), R("cb", 0, 6), col("pm"), 0.5, OP.subtract, OP.subtract)
+    aff(R("wlo"), R("onef"), [[1, 144]], OP.is_equal, -8, -1)
+    ts(col("pw", 2), col("pm"), 8.0, None, OP.is_ge)
+    ts(col("pw", 3), col("pm"), 8.0, None, OP.is_lt)
+    ts(R("whi"), R("wlo"), col("pw", 2), None, OP.mult)
+    ts(R("wlo"), R("wlo"), col("pw", 3), None, OP.mult)
+    ms(R("rmask8"), 1.0)
+    ms(R("rmask8", 0, 1024, 8), 0.0)
+    ts(R("selz"), R("sel1"), col("pw"), None, OP.mult)
+    ts(R("i8"), R("i8"), col("pw", 1), None, OP.add)
+    for n, src, f in (("selp", "sel1", 2.0 ** -13), ("selm", "sel1", -4096.0), ("selk", "sel1", 2048.0), ("idbig", "idb", BIG),
+                      ("idn", "idb", -1.0), ("idk", "idf", 2.0 ** 24), ("idkn", "idf", -2.0 ** 24), ("blkp", "blk", 2.0 ** -13),
+                      ("idfn", "idf", -1.0), ("blkn", "blk", -1.0), ("blk2n", "blk", -2.0), ("tri", "tri", 8192.0)):
+        ts(R(n), R(src), f, None, OP.mult)
+    ts(R("dg"), R("dgf"), col("pm"), None, OP.is_equal)
 
-    def classes(rounds, ph):
+    def classes(rounds, rows):
         for t in rounds:
             c = ch("clsi", t, 24)
-            ts(c, ch("P2", ph, 24), float(97 * t), None, OP.add)
+            ts(c, rows, float(97 * t), None, OP.add)
             ts(c, c, 511, None, OP.bitwise_and)
             cp(cls(t), c)
 
-    def class_rows(ph):
-        for x in range(16):
-            mm(ch("P2", ph, 24), sk("selr", x), R("Bf", 3 * x + ph, V, 48), x == 0, x == 15)
+    cp(R("b15"), lanes("b15i", 0))
+    for x in range(16):
+        mm(R("P4", 0, 24), sk("sel8", x), R("b15", x, I, 16), x == 0, x == 15)
+    classes([0, 3], R("P4", 0, 24))
+    cp(R("use16"), R("use_i"))
 
-    def spread(ph):
-        for k in range(VC * NVC // SC):
-            cp(R("Z", 0, 16 * SC, 16), R("meas", PH * SC * k + ph, PH * SC * (k + 1), PH))
-            scan(ch("x%d" % ph, k, 16 * SC), R("rmask"), R("Z"), OP.mult, OP.add)
+    def sums():
+        for k, who in enumerate(CFG["sums"]):
+            gather(who, ch("GD", k, 1024) if k < 6 else ch("SD", k - 6, 1024), at(MS, ch("use16", k, 64)))
+        for lo, hi, b in ((0, 192, R("GD", 0, 3072)), (192, 384, R("GD", 3072, W16)), (384, C, R("SD", 0, 2048))):
+            for j in range(16):
+                mm(R("P3", lo, hi), sk("selp", j), R(b[0], b[1] + j, b[2], 16), j == 0, j == 15)
+        tt(R("USE"), R("P3"), R("use_i"), OP.add)
 
-    def prelude(t):
-        if t:
-            cp(R("KUg"), at(R("KU"), cls(t)))
-            ts(R("U"), R("KUg"), 2047, None, OP.bitwise_and)
-            cp(R("u16"), R("U"))
-            tt(R("EQ"), R("U"), R("P6", 0, I), OP.is_equal)
-        else:
-            cp(R("U"), at(R("use_i"), cls(t)))
-            cp(R("u16"), R("U"))
-            tt(R("EQ"), R("U"), lanes("VR", t), OP.is_equal)
+    def partners():
+        for k in range(PH):
+            for y in range(2):
+                o = R("P2", y, I, 2)
+                mm(o, R("idf"), R("LX", I * k + y, I * k + I, 2), True, False)
+                mm(o, R("blkp"), R("meas", I * k + 1 - y, I * k + I, 2), False, True)
+            act(ch("LX", k, I), R("P2", 0, I))
 
-    def vpiece(t, k):
-        tt(ch("GE", k, 16 * VC), at(MS, ch("u16", k, VC)), ch("x%d" % (t % PH), k, 16 * VC), OP.min)
+    def spread(t):
+        ph, n = t % PH, I
+        m = CFG["x0"] if t == 0 else 0
+        for a in range(0, m, PC):
+            b = min(a + PC, m)
+            z = 16 * PC * (a // PC % 2)
+            cp(R("Z", z, z + 16 * (b - a), 16), lanes("meas", ph, a, b))
+            scan(R("x0", 16 * a, 16 * b), R("rmask", 0, 16 * (b - a)), R("Z", z, z + 16 * (b - a)), OP.mult, OP.add)
+        for j in range(16 if m < n else 0):
+            aff(R("x%d" % (t % 2), 16 * m + j, 16 * n, 16), lanes("meas", ph, m, n), [[0, n - m]], OP.is_ge, 0, 0)
 
-    def vsum(k):
-        mm(ch("P0", k, VC), R("idbig"), ch("EQ", k, VC), True, False)
-        for j in range(16):
-            mm(ch("P0", k, VC), sk("selm", j), R("GE", 16 * VC * k + j, 16 * VC * (k + 1), 16), False, j == 15)
+    def tables():
+        for k in range(PH):
+            cp(lanes("Dv", k), lanes("der_i", k))
+            cp(lanes("Bf", k), lanes("bas_i", k))
+        for k in range(PH):
+            p = R("P%d" % (5 + k), 0, I)
+            tt(ch("NEQ", k, I), ch("der_i", k, I), ch("bas_i", k, I), OP.not_equal)
+            mm(p, R("cst"), R("oneb", 0, I), True, False)
+            mm(p, R("tri"), ch("NEQ", k, I), False, True)
+            tt(ch("W", k, I), p, ch("der_i", k, I), OP.add)
 
-    def apiece(t, part):
-        n = VC * NVC
+    def later():
+        for ph in (1, 2):
+            for x in range(16):
+                mm(ch("P1", ph, 24), sk("selr", x), R("Bf", 3 * x + ph, V, 48), x == 0, x == 15)
+        for ph in range(PH):
+            for x in range(16):
+                mm(ch("P1", 3 + ph, 24), sk("selz", x), R("meas", 3 * x + ph, V, 48), x == 0, x == 15)
+        for ph in (1, 2):
+            classes([ph], ch("P1", ph, 24))
+        for t in range(RO):
+            ts(ch("zi", t, 24), ch("P1", 3 + t % PH, 24), float(t), None, OP.add)
+        ts(R("zi"), R("zi"), 7, None, OP.bitwise_and)
+        ts(R("i8", 84, 96), R("i8", 84, 96), -4.0 * I, None, OP.add)
+        tt(R("i8"), R("i8"), R("zi"), OP.add)
+        cp(R("zof"), R("i8"))
 
-        def sub(q):
-            b = "P3" if q % 2 else "P6"
-            for j in range(4):
-                mm(ch(b, j, SC), R("idb"), R("meas", PH * n + t % PH, V, PH), True, False)
-                mm(ch(b, j, SC), R("idn"), R("GM", 4 * q + j, 16 * SC, 16), False, True)
-            act(ch("RA", q, 4 * SC), R(b), AF.Relu)
-
-        def add(q):
-            for k in range(4 * q, 4 * q + 4):
-                mm(R("P4", n, I), sk("selq", k), ch("RA", k, SC), False, k == 15)
-
-        if part == 0:
-            act(R("GM"), at(MS, R("u16", n, I)))
-        elif part < 3:
-            sub(part - 1)
-        elif part == 3:
-            mm(R("P4", n, I), R("idbig"), R("EQ", n, I), True, False)
-            add(0)
-            sub(2)
-        elif part == 4:
-            add(1)
-            sub(3)
-        else:
-            add(2)
-            add(3)
-
-    def winners(keys, kt, ks, n, p2):
+    def winners(keys, kt, ks, n, out, li, lst):
         tr(kt, keys)
         scan(ks, R("amask", 0, n), kt, OP.max, OP.min)
         for y in range(2):
             for h in range(2):
-                mm(R("P2", p2 + y, p2 + n // 16, 2), ch("swp", 2 * h + y, 128), R(ks[0], 15 + 16 * h, n, 32), h == 0, h == 1)
+                mm(R(out[0], out[1] + y, out[2], 2), ch("swp", 2 * h + y, 128), R(ks[0], 15 + 16 * h, n, 32), h == 0, h == 1)
+        cp(li, out)
+        ts(li, li, 2047, None, OP.bitwise_and)
+        cp(lst, li)
 
-    def numbers(lst, li, p2, n):
-        cp(R(li, 0, n), R("P2", p2, p2 + n))
-        ts(R(li, 0, n), R(li, 0, n), 2047, None, OP.bitwise_and)
-        cp(R(lst, 0, n), R(li, 0, n))
-
-    def keys(t):
-        if t == 0:
-            cp(R("KUg"), at(R("KU"), cls(t)))
-        n = VC * NVC
-        tt(R("KEY", 0, n), R("P0", 0, n), R("KUg", 0, n), OP.add)
-        tt(R("KEY", n, I), R("P4", n, I), R("KUg", n, I), OP.add)
-        winners(R("KEY"), R("KT"), R("KS"), I, 0)
-
-    def models():
-        numbers("m16", "mi", 0, 24)
+    def entry(out, kf, u, stop):
+        mm(out, R("idk"), kf, True, False)
+        mm(out, R("idkn"), u, False, False)
+        mm(out, R("idf"), u, False, stop)
 
     def search(t):
-        n = {"v": 0, "w": 0}
-
-        def step(z):
-            if z == "b":
-                prelude(t)
-            elif z == "v":
-                vpiece(t, n["v"])
-            elif z == "w":
-                vsum(n["w"])
-            elif z in "cdefhi":
-                apiece(t, "cdefhi".index(z))
-            elif z == "s":
-                spread(1)
-                spread(2)
-            elif z == "p":
-                keys(t)
-            elif z == "q":
-                models()
-            if z in n:
-                n[z] += 1
-        return step
-
-    def gd(k):
-        act(ch("GD", k, 16 * CH), at(MO, ch("d16", k, CH)))
-
-    cp(lanes("Bf", 0), lanes("bas_i", 0))
-    cp(R("use16"), R("use_i"))
-    for ph in (1, 2):
-        cp(lanes("Bf", ph), lanes("bas_i", ph))
-    ts(R("selp"), R("sel1"), 2048.0, None, OP.mult)
-    for k in range(2):
-        act(R("SD" if k == 0 else "SE", 0, 4096), at(MS, ch("use16", k, 256)))
-    ts(R("pi", 0, 1), R("pi", 0, 1), 15, None, OP.bitwise_and)
-    cp(R("pm", 0, 1), R("pi", 0, 1))
-    ts(R("pw", 0, 1), R("pm", 0, 1), 1.0, None, OP.add)
-    ts(R("pw", 1, 2), R("pm", 0, 1), 8.0, None, OP.mult)
-    ts(R("cb", 0, 6), R("cb", 0, 6), col("pm"), 0.5, OP.subtract, OP.subtract)
-    ts(R("selz"), R("sel1"), col("pw"), None, OP.mult)
-    ts(R("i8"), R("i8"), col("pw", 1), None, OP.add)
-    spread(0)
-    class_rows(0)
-    classes([0, 3], 0)
-    ts(R("selm"), R("sel1"), -4096.0, None, OP.mult)
-    ts(R("idbig"), R("idb"), BIG, None, OP.mult)
-    ts(R("idn"), R("idb"), -1.0, None, OP.mult)
-    ts(R("selq"), R("sel1"), 4096.0, None, OP.mult)
-    ts(R("blkK"), R("blk"), 2048.0, None, OP.mult)
-    for k in range(2):
-        mm(R("P5" if k == 0 else "P7", 0, I), R("blkK"), ch("meas", k, I), True, True)
-    s0 = search(0)
-    s0("b")
-    cp(R("d16"), lanes("der_i", 0))
-    for k in range(2):
-        for j in range(16):
-            mm(ch("P1", k, 256), sk("selp", j), R("SD" if k == 0 else "SE", j, 4096, 16), j == 0, j == 15)
-    for z in FIRST:
-        if z == "p":
-            tt(R("NEQ"), R("bas_i"), R("der_i"), OP.not_equal)
-            for k in range(2):
-                for y in range(2):
-                    o = R("KLX", I * k + y, I * k + I, 2)
-                    tt(o, R("P5" if k == 0 else "P7", 1 - y, I, 2), o, OP.add)
-            tt(R("KU"), R("P1"), R("use_i"), OP.add)
-            ts(R("tri"), R("tri"), 8192.0, None, OP.mult)
-        s0(z)
-        for k in {"e": [0], "h": [1, 2, 3]}.get(z, []):
-            gd(k)
-        if z == "p":
-            for k in range(3):
-                p = R("P%d" % (4 + k), 0, I)
-                mm(p, R("tri"), ch("NEQ", k, I), True, False)
-                mm(p, R("cst"), R("oneb"), False, True)
-    mm(R("P7", 0, I), R("blkK"), R("meas", 2 * I, V), True, True)
-    class_rows(1)
-    class_rows(2)
-    for ph in range(PH):
-        for x in range(16):
-            mm(R("P2", 72 + 24 * ph, 96 + 24 * ph), sk("selz", x), R("meas", 3 * x + ph, V, 48), x == 0, x == 15)
-    for k in range(3):
-        tt(ch("W", k, I), R("P%d" % (4 + k), 0, I), ch("der_i", k, I), OP.add)
-    send(topo, core, asker[0], "qm0", MS, "rm0")
-    send(topo, core, asker[0], "qk0", R("KU"), "rk0")
-    send(topo, core, asker[0], "qw0", R("W"), "rw0")
-    for t in range(1, RO):
-        send(topo, core, asker[t], "qm%d" % t, MS, "rm%d" % t)
-
-    def rest1():
-        ts(R("blkn"), R("blk"), -1.0, None, OP.mult)
-        ts(R("blk2"), R("blk"), 2.0, None, OP.mult)
-        ts(R("blk2n"), R("blk"), -2.0, None, OP.mult)
-        ts(R("dg"), R("dgf"), col("pm"), None, OP.is_equal)
-        cp(R("Dv"), R("der_i"))
-
-    def rest2():
-        for y in range(2):
-            o = R("KLX", 2 * I + y, V, 2)
-            tt(o, R("P7", 1 - y, I, 2), o, OP.add)
-        classes([1], 1)
-        classes([2], 2)
-        for t in range(RO):
-            ts(ch("zi", t, 24), ch("P2", 3 + t % PH, 24), float(t), None, OP.add)
-        ts(R("zi"), R("zi"), 7, None, OP.bitwise_and)
-        tt(R("i8"), R("i8"), R("zi"), OP.add)
-        cp(R("zof"), R("i8"))
-
-    def ge(lo, hi, vec):
-        o, w = R("GE", 768 * lo, 768 * hi), at(MO, R("e16", 48 * lo, 48 * hi))
-        if vec:
-            cp(o, w)
+        ph = t % PH
+        if t and CFG["kf"] == "a":
+            cp(R("u16"), at(R("USE"), cls(t)))
+            act(R("KF"), at(R("USE"), cls(t)))
+            cp(R("U"), R("u16"))
+        elif t:
+            cp(R("KF"), at(R("USE"), cls(t)))
+            cp(R("u16"), R("KF"))
+            cp(R("U"), R("u16"))
         else:
-            act(o, w)
+            cp(R("u16"), at(R("use_i"), cls(t)))
+            cp(R("U"), R("u16"))
+            act(R("KF"), at(R("USE"), cls(t)))
+            entry(R("P1", 0, I), R("KF"), R("U"), True)
+            act(R("KF"), R("P1", 0, I))
+        stage(R("P1", 0, I), lanes("VR", ph), CFG["stage"][0])
+        tt(R("EQ"), R("U"), R("P1", 0, I), OP.is_equal)
+        lo, x = 0, "x%d" % (t % 2)
+        for who, n in CFG["search"][t]:
+            hi = lo + n
+            cuts = [(a, min(a + PC, hi)) for a in range(lo, hi, PC)]
+            if who == "p":
+                for a, b in cuts:
+                    act(R("GE", 16 * a, 16 * b), at(MS, R("u16", a, b)))
+                for a in range(16 * lo, 16 * hi, 512):
+                    bank = R("P%d" % (2 + a // 512 % 2))
+                    mm(bank, R("idb"), R(x, a, a + 512), True, False)
+                    mm(bank, R("idn"), R("GE", a, a + 512), False, True)
+                    act(R("SE", a, a + 512), bank, AF.Abs)
+                sums = [("selk", j, R("SE", 16 * lo + j, 16 * hi, 16)) for j in range(16)]
+            else:
+                for a, b in cuts:
+                    tt(R("GE", 16 * a, 16 * b), at(MS, R("u16", a, b)), R(x, 16 * a, 16 * b), OP.min)
+                sums = [("selm", j, R("GE", 16 * lo + j, 16 * hi, 16)) for j in range(16)]
+            key = R("P0", lo, hi)
+            first = who == "m" and t > 0
+            if first:
+                entry(key, R("KF", lo, hi), R("U", lo, hi), False)
+            for k, (s, j, r) in enumerate(sums):
+                mm(key, sk(s, j), r, k == 0 and not first, False)
+            if not first:
+                mm(key, R("idf"), R("U" if who == "p" else "KF", lo, hi), False, False)
+            mm(key, R("idbig"), R("EQ", lo, hi), False, True)
+            lo = hi
+        winners(R("P0", 0, I), R("KT"), R("KS"), I, R("P0", 400, 424), R("mi"), R("m16"))
 
-    def sd(k):
-        scan(ch("SD", k, 16 * CH), R("rmask", 0, 16 * CH), ch("GD", k, 16 * CH), OP.mult, OP.max)
+    def old_lists(t, bank):
+        ph, o = t % PH, ch("d16", t % PH, I)
+        if not CFG["pair"][t]:
+            cp(o, lanes("der_i" if t < PH else "Dv", ph))
+            return
+        for k, (a, b) in enumerate(((8, 8), (16, 0))):
+            p = ch(bank, k, I // 2)
+            mm(p, R("whi" if k else "wlo", a, a + 128), R("Dv", ph, V, 2 * PH), True, False)
+            mm(p, R("wlo" if k else "whi", b, b + 128), R("Dv", ph + PH, V, 2 * PH), False, True)
+        cp(o, R(bank, 0, I))
 
-    def se(lo, hi):
-        scan(R("SE", 768 * lo, 768 * hi), R("rmask", 0, 768 * (hi - lo)), R("GE", 768 * lo, 768 * hi), OP.mult, OP.max)
+    def tops(t, gat, top, lst, parts, pair, bank, out, cuts):
+        lo, w = 0, 8 if pair else 16
+        for who, n in parts:
+            hi = lo + n
+            a = R(gat, w * lo, w * hi)
+            gather(who, a, at(MO, R(lst[0], lst[1] + w * lo // 16, lst[1] + w * hi // 16)))
+            if pair:
+                b = R(gat, w * (I + lo), w * (I + hi))
+                tt(b, at(MO, R(lst[0], lst[1] + (I + lo) // 2, lst[1] + (I + hi) // 2)), a, OP.max)
+                a = b
+            scan(R(top, w * lo, w * hi), R("rmask8" if pair else "rmask", 0, w * n), a, OP.mult, OP.max)
+            lo = hi
+        for lo, hi in cuts:
+            mm(R(bank, lo, hi), R("idb"), R(top, w * lo + w - 1, w * hi, w), True, False)
+            mm(R(bank, lo, hi), R("idn"), lanes("meas", t % PH, lo, hi), False, True)
+            act(R(out, lo, hi), R(bank, lo, hi), AF.Abs)
+
+    def blocks(t):
+        return [(0, I)] if t + 1 < RO else [(0, I // 2), (I // 2, I)]
+
+    def rewritten(t, lo, hi):
+        return at(R("morph", 8 * lo, 8 * hi), R("zof", 24 * t + lo // 16, 24 * t + hi // 16))
 
     def dist(t):
         ph = t % PH
-        lm = lanes("meas", ph)
-        half = R("P4", 0, I)
-        if t:
-            gd(0)
-            change(t - 1)
-            for k in range(1, 4):
-                gd(k)
-        ea = R("Ea", 0, I)
-        tt(ea, at(R("W"), R("m16")), lanes("Bf", ph), OP.max)
-        ts(ea, ea, 4095, None, OP.bitwise_and)
-        cp(R("e16"), ea)
-        va = [(a, min(a + 2, EV[t])) for a in range(0, EV[t], 2)]
-        aa = [(a, min(a + 2, 8)) for a in range(EV[t], 8, 2)]
-        act(R("P6", 0, I), lm)
-        for a in aa:
-            ge(a[0], a[1], False)
-        for k, a in enumerate(va):
-            ge(a[0], a[1], True)
-            sd(k)
-        if t == 0:
-            rest1()
-        for k in range(len(va), 4):
-            sd(k)
-        for a in va:
-            se(a[0], a[1])
-        od, oe = R("SD", 15, W16, 16), R("SE", 15, W16, 16)
-        tt(R("MD"), od, R("P6", 0, I), OP.min)
-        mm(R("P0", 0, I), R("blk"), od, True, False)
-        mm(R("P0", 0, I), R("blk2n"), R("MD"), False, True)
-        mm(half, R("blkn"), od, True, False)
-        mm(half, R("blk2"), R("MD"), False, False)
-        for a in aa:
-            se(a[0], a[1])
-        if t == 0:
-            rest2()
-        kd, ku = R("P3", 0, I), R("KU", 37 * t, 37 * t + I)
-        act(R("KN"), at(R("KLX"), R("m16")))
-        act(kd, R("KN"))
-        tt(R("ME"), oe, R("P6", 0, I), OP.min)
-        mm(half, R("blk"), oe, False, False)
-        mm(half, R("blk2n"), R("ME"), False, True)
-        tt(kd, kd, ku, OP.subtract)
-        act(R("KQ", 0, I), at(R("qk%d" % t), cls(t)))
-        act(R("thr", 0, I), R("P0", 0, I), AF.Identity, bias=col("nm"))
-        if t + 1 < RO:
-            act(R("P6", 0, I), lanes("VR", (t + 1) % PH))
-        ts(R("non", 0, I), half, col("nm"), None, OP.is_ge)
-        scan(R("cum"), R("non"), R("c128"), OP.add, OP.min)
+        half, kd, us = R("P5", 0, I), R("P7", 0, I), R("USE", 37 * t, 37 * t + I)
+        tops(t, "GD", "SD", ch("d16", ph, I), CFG["old"][t], CFG["pair"][t], "P2", "AD", [(0, I)])
+        tt(R("Ea"), at(R("W"), R("m16")), lanes("Bf", ph), OP.max)
+        ts(R("Ea"), R("Ea"), 4095, None, OP.bitwise_and)
+        cp(R("e16"), R("Ea"))
+        cuts = [(0, CFG["cut"]), (CFG["cut"], I)]
+        tops(t, "GE", "SE", R("e16"), CFG["new"][t], 0, "P3", "AE", cuts)
+        for lo, hi in cuts:
+            mm(R("P5", lo, hi), R("blkn"), R("AD", lo, hi), True, False)
+            mm(R("P5", lo, hi), R("blk"), R("AE", lo, hi), False, True)
+        got = R("got", 0, I)
+        ts(got, half, col("mg"), None, OP.is_lt)
+        scan(R("cum"), R("oneb"), R("got"), OP.add, OP.subtract)
         for n in range(6):
-            act(R("junk"), R("cum"), AF.Sign, bias=col("cb", n), accum=col("acc", n))
-        ts(R("got", 0, I), half, col("nm"), None, OP.is_lt)
+            act(R("junk", 0, 400), R("cum", 16 * n, 16 * n + 400), AF.Sign, bias=col("cb", n), accum=col("acc", n))
+        act(R("LXg"), at(R("LX"), R("m16")))
+        mm(kd, R("idf"), R("LXg"), True, False)
+        mm(kd, R("idfn"), us, False, True)
         tt(kd, kd, R("dg", t, t + I), OP.mult)
-        tt(kd, kd, R("got", 0, I), OP.mult)
-        tt(ku, kd, ku, OP.add)
+        tt(kd, kd, got, OP.mult)
+        tt(us, kd, us, OP.add)
         if t + 1 < RO:
-            send(topo, core, asker[t + 1], "qk%d" % (t + 1), R("KU"), "rk%d" % (t + 1))
+            send(topo, core, asker[t + 1], "qk%d" % (t + 1), R("USE"), "rk%d" % (t + 1))
+        else:
+            cp(R("use_i"), R("USE"))
+            cp(R("USE"), R("use_i"))
+            dma("s", T.yu[:], R("USE"))
+        if t + 1 < RO:
+            old_lists(t + 1, "P6")
+        stage(R("P6", 0, I), lanes("Dv", ph), CFG["stage"][1])
+        tt(kd, R("Ea"), R("P6", 0, I), OP.subtract)
+        tt(R("tD", 0, I), kd, got, OP.mult)
+        for lo, hi in blocks(t):
+            act(R("old", lo, hi), rewritten(t, lo, hi))
+        mm(kd, R("idb"), lanes("meas", ph), True, False)
+        mm(kd, R("idn"), R("old", 0, I), False, True)
+        tt(R("gx", 0, I), kd, got, OP.mult)
 
     def ask(t):
         ph = t % PH
         s6, v6 = R("s16", 0, 6), R("sv16", 0, 6)
         zs = R("Z", 0, 16 * CAP, 16)
-        ts(s6, R("acc", 0, 6), -0.5, IX / 2.0, OP.mult, OP.add)
-        ts(v6, R("acc", 0, 6), -1.5, PH * IX / 2.0 + ph, OP.mult, OP.add)
-        cp(R("KQs"), at(R("KQ"), s6))
-        ts(R("uq"), R("KQs"), 2047, None, OP.bitwise_and)
-        cp(R("uq16"), R("uq"))
-        act(zs, at(R("meas"), v6))
+        act(R("UQ", 0, I), at(R("qk%d" % t), cls(t)))
+        tt(R("a2", 0, 6), R("cn", 0, 6), R("acc", 0, 6), OP.subtract)
+        ts(v6, R("a2", 0, 6), 1.5, float(ph), OP.mult, OP.add)
+        ts(s6, R("a2", 0, 6), 0.5, None, OP.mult)
+        cp(zs, at(R("meas"), v6))
+        cp(R("uq16"), at(R("UQ"), s6))
+        act(R("UQs"), at(R("UQ"), s6))
         act(R("Bs"), at(R("Bf"), v6))
-        act(R("ths"), at(R("thr"), s6))
-        scan(R("RQ"), R("rmask", 0, 16 * CAP), R("Z", 0, 16 * CAP), OP.mult, OP.add)
-        yield
-        act(R("old"), at(MO, zof(t)))
-        act(R("P5", 0, I), lanes("Dv", ph))
+        act(R("AD2"), at(R("AD"), s6))
         for k in range(2):
+            scan(ch("RQ", k, 768), R("rmask", 0, 768), ch("Z", k, 768), OP.mult, OP.add)
             tt(ch("GQ", k, 768), at(R("qm%d" % t), ch("uq16", k, 48)), ch("RQ", k, 768), OP.min)
+        key = R("P4", 0, CAP)
+        cp(R("U2"), R("uq16"))
+        entry(key, R("UQs"), R("U2"), False)
         for j in range(16):
-            mm(R("P1", 0, CAP), sk("selm", j), R("GQ", j, 16 * CAP, 16), j == 0, j == 15)
-        yield
-        tt(R("KEY2"), R("P1", 0, CAP), R("KQs"), OP.add)
-        winners(R("KEY2"), R("KT2"), R("KS2"), CAP, 32)
-        yield
-        numbers("n16", "ni", 32, 6)
+            mm(key, sk("selm", j), R("GQ", j, 16 * CAP, 16), False, j == 15)
+        winners(key, R("KT2"), R("KS2"), CAP, R("P4", 100, 106), R("ni", 0, 6), R("n16", 0, 6))
         tt(R("E2"), at(R("qw%d" % t), R("n16", 0, 6)), R("Bs"), OP.max)
         ts(R("E2"), R("E2"), 4095, None, OP.bitwise_and)
         cp(R("e216"), R("E2"))
         for k in range(2):
-            act(ch("GQ", k, 768), at(MO, ch("e216", k, 48)))
-        mm(R("P7", 0, I), R("idb"), lanes("meas", ph), True, False)
-        mm(R("P7", 0, I), R("idn"), R("old"), False, True)
-        cp(at(R("Ea"), s6), R("E2"))
-        if t + 1 < RO:
-            cp(R("d16"), lanes("Dv", (t + 1) % PH))
-        yield
-        for k in range(2):
-            scan(ch("S2", k, 768), R("rmask", 0, 768), ch("GQ", k, 768), OP.mult, OP.max)
-        tt(R("MM2"), R("S2", 15, 16 * CAP, 16), zs, OP.min)
-        mm(R("P1", 0, CAP), R("blk"), R("S2", 15, 16 * CAP, 16), True, False)
-        mm(R("P1", 0, CAP), R("blk2n"), R("MM2"), False, True)
-        yield
-        tt(R("ad2"), R("P1", 0, CAP), R("ths"), OP.is_lt)
-        cp(at(R("got"), s6), R("ad2"))
-        tt(R("gx"), R("P7", 0, I), R("got", 0, I), OP.mult)
-        tt(at(MO, zof(t)), R("old"), R("gx"), OP.add)
-        yield
+            gather(CFG["ask2"][t][k], ch("GQ", k, 768), at(MO, ch("e216", k, 48)))
+            scan(ch("SQ", k, 768), R("rmask", 0, 768), ch("GQ", k, 768), OP.mult, OP.max)
+        tt(R("dE2"), at(R("Dv"), v6), R("E2"), OP.subtract)
+        tt(R("dxs"), at(R("old"), s6), zs, OP.subtract)
+        top, g2 = R("SQ", 15, 16 * CAP, 16), R("P4", 128, 128 + CAP)
+        tt(R("MM2"), top, zs, OP.min)
+        mm(g2, R("blkn"), R("AD2"), True, False)
+        mm(g2, R("blk"), zs, False, False)
+        mm(g2, R("blk"), top, False, False)
+        mm(g2, R("blk2n"), R("MM2"), False, True)
+        for n in ("adb", "adf") if t + 1 < RO else ("adf", "adb"):
+            ts(R(n), g2, col("mg"), -1.0, OP.is_lt, OP.mult)
 
     def change(t):
         ph = t % PH
-        last = t + 1 == RO
-        d, e = lanes("Dv", ph), R("P5", 0, I)
-        if not last:
-            keys(t + 1)
-        tt(e, e, R("Ea", 0, I), OP.subtract)
-        tt(e, e, R("got", 0, I), OP.mult)
-        tt(d if last else e, d, e, OP.subtract)
-        if last:
-            return
-        tt(R("NEQ", 0, I), e, lanes("Bf", ph), OP.not_equal)
-        cp(d, e)
-        models()
-        act(R("junk", 0, I), R("got", 0, I), accum=col("cnt"))
-        mm(R("P4", 0, I), R("tri"), R("NEQ", 0, I), True, False)
-        mm(R("P4", 0, I), R("cst"), R("oneb"), False, True)
-        mm(R("P2", 40, 41), R("oall"), col("cnt"), True, True)
-        tt(lanes("W", ph), R("P4", 0, I), d, OP.add)
-        cp(R("nmi", 0, 1), R("P2", 40, 41))
-        ts(R("nmi", 0, 1), R("nmi", 0, 1), 127, None, OP.bitwise_and)
-        ts(R("nm", 0, 1), R("nmi", 0, 1), -1.0, None, OP.mult)
-        send(topo, core, asker[t + 1], "qw%d" % (t + 1), R("W"), "rw%d" % (t + 1))
+        s6, d = R("s16", 0, 6), lanes("Dv", ph)
 
+        def morphs():
+            tt(at(R("gx"), s6), R("adb"), R("dxs"), OP.mult)
+            for lo, hi in blocks(t):
+                tt(rewritten(t, lo, hi), R("old", lo, hi), R("gx", lo, hi), OP.add)
+                if t + 1 == RO:
+                    dma("a", T.ym[:, 8 * lo:8 * hi], R("morph", 8 * lo, 8 * hi))
+
+        if t + 1 < RO:
+            morphs()
+        tt(at(R("tD"), s6), R("adf"), R("dE2"), OP.mult)
+        tt(d, R("P6", 0, I), R("tD", 0, I), OP.add)
+        if t + 1 == RO:
+            dma("s", T.yd[:], DV)
+            morphs()
+            return
+        stage(R("P7", 0, I), lanes("Bf", ph), CFG["stage"][2])
+        tt(R("NEQ", 0, I), d, R("P7", 0, I), OP.not_equal)
+        mm(R("P5", 0, I), R("cst"), R("oneb", 0, I), True, False)
+        mm(R("P5", 0, I), R("tri"), R("NEQ", 0, I), False, True)
+        tt(lanes("W", ph), R("P5", 0, I), d, OP.add)
+        send(topo, core, asker[t + 1], "qw%d" % (t + 1), R("W"), "rw%d" % (t + 1))
+        act(R("junk", 0, CAP), R("adb"), accum=col("cnt", 1))
+        mm(R("P4", 300, 301), R("oalln"), col("cum", I - 1), True, False)
+        mm(R("P4", 300, 301), R("oalln"), col("cnt", 1), False, True)
+        ts(col("nmi"), R("P4", 300, 301), 8.0 * I, None, OP.add)
+        ts(col("nmi"), col("nmi"), 127, None, OP.bitwise_and)
+        ts(col("mg"), col("nmi"), -1.0, -0.5, OP.mult, OP.add)
+
+    spread(0)
+    send(topo, core, asker[0], "qm0", MS, "rm0")
+    sums()
+    send(topo, core, asker[0], "qk0", R("USE"), "rk0")
+    tables()
+    old_lists(0, "P2")
+    send(topo, core, asker[0], "qw0", R("W"), "rw0")
+    search(0)
+    partners()
+    later()
     for t in range(RO):
         dist(t)
-        a = ask(t)
         if t + 1 < RO:
-            s = search(t + 1)
-            for z in ORDER:
-                if z == "a":
-                    next(a)
-                else:
-                    s(z)
-    cp(R("use_i"), R("KU"))
-    ts(R("use_i"), R("use_i"), 2047, None, OP.bitwise_and)
-    cp(R("KU"), R("use_i"))
-    dma("s", T.yu[:], R("KU"))
-    for _ in a:
-        pass
-    dma("a", T.ym[:], MO)
-    change(RO - 1)
-    dma("s", T.yd[:], R("Dv"))
-    F["finish"]()
+            send(topo, core, asker[t + 1], "qm%d" % (t + 1), MS, "rm%d" % (t + 1))
+            spread(t + 1)
+        ask(t)
+        if t + 1 < RO:
+            search(t + 1)
+        change(t)
+    F["issue"]([("q%s%d" % (a, t), "r%s%d" % (a, t), len(topo.engines(asked[t], core))) for t in range(RO) for a in "mkw"])

@@ -1,4 +1,4 @@
-from concourse.mybir import AluOpType as OP, ActivationFunctionType as AF
+from concourse.mybir import AluOpType as OP, ActivationFunctionType as AF, AxisListType as AX
 
 NR = 6
 P, V, C, PH, I, CAP, RO = 3072, 1152, 512, 3, 384, 96, 4
@@ -7,19 +7,40 @@ VX = V + PH * CAP
 W16 = 16 * I
 PC = 64
 BIG = float(1 << 23)
+IN_ORDER = 1e6
 CFG = {
     "sums": "aaaaaaaa",
     "search": [[("m", 128), ("m", 128), ("m", 128)]] + [[("m", 192), ("p", 96), ("p", 96)]] * 3,
     "old": [[("a", 96)] * 4] * 4,
-    "pair": [0, 1, 1, 1],
+    "pair": [0, I, I, I], "chain": 0.0, "both": 0.0, "two": [1, 1, 1, 1], "hop2": 0.08, "look": 12, "depth": 20, "muy": [2.0, 2.0, 2.0, 0.0], "mix": (0.0, 0.3, 0.6), "neq": 3,
     "new": [[("a", 48), ("v", 48)] * 4] + [[("a", 128), ("a", 128), ("v", 32), ("a", 48), ("a", 48)]] * 3,
     "ask2": ["av", "av", "av", "av"],
     "bulk": ("GD", "GE", "SD", "SE"),
-    "mu": 2.0, "passes": 3, "hop": 0.15, "gath": 1.56, "kf": "a", "x0": 256, "cut": 288, "stage": "aaa",
+    "mu": 2.0, "passes": 3, "hop": 0.15, "gath": 1.56, "kf": "a", "x0": 256, "cut": 288, "stage": "aaa", "signs": [6, 6, 6, 5], "last": 1, "df": "P7", "early": 100.0, "d16": 10.0, "later": 5.0, "end": 2.0, "moves": 3, "deep": 2, "pc": (64, 64), "tries": 0, "jit": 1.0,
 }
 
+CFG.update(later=0, chain=1, end=3, depth=0, mu=2, hop=0.1, signs=[6, 6, 6, 6], tries=16000, jit=0.15, moves=4, two=[0, 0, 0, 1], both=0.8)
+CFG["search"] = [[("m", 256), ("m", 128)]] + [[("m", 192), ("p", 192)]] * 3
+CFG["new"] = [[("v", 48), ("a", 96), ("v", 48), ("a", 96), ("v", 48), ("a", 48)]] + [[("a", 128), ("a", 96), ("v", 96), ("a", 64)]] * 3
+CFG["relay"] = [("m", 1), ("m", 2), ("m", 3)]
+CFG.update(two=[0, 0, 0, 0], hop2=0.1, link=40e3, send=20.0)
+CFG.update(pe=0.47e-3, two=[1, 1, 1, 1], both=0.0, hop=0.2, hop2=0.18, gath=1.4, mu=1, muy=[1, 1, 1, 0])
+CFG.update(two=[0, 0, 0, 1], both=0.8, cut=224)
+CFG["search"] = [[("m", 256), ("m", 128)]] + [[("m", 128), ("p", 128), ("p", 128)]] * 3
+CFG["new"] = CFG["new"][:1] + [[("a", 128), ("a", 96), ("v", 64), ("a", 96)]] * 3
+CFG["relay"] = [("m", t) for t in range(RO)]
+CFG.update(w1=1, send0=3e6, x0=256, later=3, pc=(32, 64), end=6, tries=25000)
+CFG["old"] = CFG["old"][:1] + [[("a", 128)] * 3] * 3
+CFG["search"][0] = [("m", 192), ("m", 192)]
+CFG["new"][0] = [("v", 64), ("a", 96), ("v", 64), ("a", 96), ("a", 64)]
+CFG.update(w1=0, kf="v", cut=256, both=1.0)
+CFG["new"] = CFG["new"][:1] + [[("a", 128), ("a", 128), ("v", 80), ("a", 48)]] * 3
+CFG["new"][0] = [("v", 96), ("a", 128), ("v", 64), ("a", 96)]
+CFG.update(later=6, tries=25000)
 SCRATCH = {}
-SMALL = ["pm", "pw", "cb", "cn", "a2", "acc", "mg", "cnt"]
+VIEW = {"idb": ("idw", 16), "idf": ("idfw", 8), "blk": ("blkw", 0)}
+WHOLE = ["pi", "ni", "nmi", "nz"]
+SMALL = ["pm", "pw", "cb", "cn", "a2", "acc", "mg", "cnt", "a8"]
 
 
 def _sb(dtype, **kw):
@@ -27,33 +48,40 @@ def _sb(dtype, **kw):
         SCRATCH[n] = ("sbuf", [128, w], dtype)
 
 
-_sb("int32", bas_i=V, der_i=V, use_i=C, pi=8, clsi=96, zi=96, mi=24, ni=8, Ea=I, nmi=8, E2=CAP)
+_sb("int32", bas_i=V, der_i=V, use_i=C, whole=8 * len(WHOLE), clsi=96, zi=96, mi=24, Ea=IX, E2=CAP)
 _sb("uint16", cls=96, zof=96, u16=I, d16=V, use16=C, e16=I, m16=24, s16=8, sv16=8, n16=8, uq16=CAP, e216=CAP)
-_sb("float32", Bf=VX, Dv=VX, W=V, USE=C, LX=V, VR=V, onef=144, selr=144, swp=512, cum=IX, wlo=144, whi=144, oalln=128,
-    idf=128, idfn=128, idk=128, idkn=128, small=8 * len(SMALL), i8=96, dgf=400, amask=I, KT=I, KS=I, U=I, KF=I, LXg=I, UQ=IX,
-    UQs=CAP, U2=CAP, KT2=CAP, KS2=CAP, Bs=CAP, tD=IX, dE2=CAP, adf=CAP)
-_sb("bfloat16", meas=VX, morph=P, oneb=IX, sel1=144, selp=144, selm=144, selk=144, selz=144, blk=128, blkn=128, blk2n=128,
-    blkp=128, tri=128, cst=128, idb=128, idn=128, idbig=128, dg=400, rmask=2048, rmask8=1024, Z=2048, EQ=I, GD=W16, GE=W16,
-    SD=W16, SE=W16, AD=IX, AE=I, got=IX, junk=IX, old=IX, gx=IX, NEQ=V, GQ=16 * CAP, RQ=16 * CAP, SQ=16 * CAP, MM2=CAP,
-    AD2=CAP, dxs=CAP, adb=CAP, x0=W16, x1=W16)
+_sb("float32", Bf=VX, Dv=V, W=V, USE=C, LX=V, VR=I, onef=160, idfw=160, selr=144, wlo=144, whi=144, oalln=128,
+    idfn=128, idk=128, small=8 * len(SMALL), i8=96, amask=I, KT=I, KS=I, KF=I, SA=C, LXg=I, UQ=IX,
+    UQs=CAP, KT2=CAP, KS2=CAP, Bs=CAP, XD=I, W1=IX)
+_sb("float16", U=I, U2=CAP, mh=32)
+_sb("bfloat16", sw0=160, sw1=160, idw=160, blkw=144, idkn=128, idK=128, idKn=128)
+_sb("uint16", z16=8)
+_sb("bfloat16", morc=P, dxs=CAP, meas=VX, morph=8 * IX, oneb=IX, sel1=144, selp=144, selm=144, selk=144, selz=144, blkn=128, blk2n=128,
+    blkp=128, tri=128, cst=128, idn=128, idbig=128, dg=400, rmask=2048, rmask8=1024, Z=2048, EQ=I, GD=W16, GE=W16,
+    SD=W16, SE=W16, AD=IX, AE=I, non=IX, cum=IX, junk=800, old=IX, gx=I, NEQ=V, GQ=16 * CAP, RQ=16 * CAP, SQ=16 * CAP, MM2=CAP,
+    AD2=CAP, adb=CAP, x0=W16, x1=W16)
 SCRATCH["b15i"] = ("sbuf", [8, V], "int32")
-SCRATCH["b15"] = ("sbuf", [8, I], "float32")
-SCRATCH["sel8"] = ("sbuf", [8, 144], "float32")
-SCRATCH["one8"] = ("sbuf", [8, 144], "float32")
+SCRATCH["b15"] = ("sbuf", [8, I], "float16")
+SCRATCH["sel8"] = ("sbuf", [8, 144], "bfloat16")
+SCRATCH["one8"] = ("sbuf", [8, 144], "bfloat16")
 for _t in range(RO):
     _sb("bfloat16", **{"qm%d" % _t: V})
     _sb("float32", **{"qk%d" % _t: C, "qw%d" % _t: V})
 for _t in range(8):
     SCRATCH["P%d" % _t] = ("psum", [128, 512], "float32")
-SEMAPHORES = (["q_v", "q_a", "q_t", "q_g"] + ["d%d" % k for k in range(12)] + ["l%d" % k for k in range(12)]
-              + ["r%s%d" % (a, k) for a in "mkw" for k in range(RO)])
+SEMAPHORES = (["q_v", "q_a", "q_t", "q_g"] + ["d%d" % k for k in range(16)] + ["l%d" % k for k in range(16)]
+              + ["r%s%d" % (a, k) for a in "mkwp" for k in range(RO)])
 CYC = 0.83e-3
-WIDE = {"int32": 4, "float32": 4, "bfloat16": 2, "uint16": 2}
+WIDE = {"int32": 4, "float32": 4, "bfloat16": 2, "uint16": 2, "float16": 2}
 
 
 def R(name, lo=0, hi=None, step=1):
     if name in SMALL:
         return ("small", 8 * SMALL.index(name) + lo, 8 * SMALL.index(name) + hi, step)
+    if name in VIEW:
+        return (VIEW[name][0], VIEW[name][1], VIEW[name][1] + 128, 1)
+    if name in WHOLE:
+        return ("whole", 8 * WHOLE.index(name) + lo, 8 * WHOLE.index(name) + hi, step)
     return (name, lo, SCRATCH[name][1][1] if hi is None else hi, step)
 
 
@@ -104,39 +132,62 @@ def plan(calls):
         return calls[i]["lat"] + (0.0 if calls[i]["q"] == calls[j]["q"] == "t" else CFG["hop"])
 
     def run(before, after, rank, back):
+        if not back:
+            rank = [r + c["first"] for r, c in zip(rank, calls)]
         left = [len(b) for b in before]
         ready, start, free = [0.0] * n, [0.0] * n, {}
-        pool = {}
+        pool, cause, last = {}, [None] * n, {}
         for i in range(n):
             if not left[i]:
                 pool.setdefault(calls[i]["q"], []).append(i)
-        for _ in range(n):
-            best = None
-            for q, l in pool.items():
-                if not l:
-                    continue
-                now = max(free.get(q, 0.0), min(ready[i] for i in l))
-                a = max((i for i in l if ready[i] <= now), key=lambda i: rank[i])
-                pick, score = a, None
-                for b in l:
-                    if ready[b] > now and rank[b] > rank[a] and ready[b] < now + calls[a]["cost"]:
-                        go = max(rank[a] + now, rank[b] + now + calls[a]["cost"])
-                        hold = max(rank[b] + ready[b], rank[a] + ready[b] + calls[b]["cost"]) + CFG["mu"] * (ready[b] - now)
-                        if hold < go and (score is None or hold - go < score):
-                            pick, score = b, hold - go
-                at = max(now, ready[pick])
-                if best is None or now < best[0]:
-                    best = (now, at, q, pick)
-            _, at, q, i = best
+        done, ahead = [False] * n, {}
+        for i in sorted(range(n), key=lambda i: rank[i]):
+            ahead.setdefault(calls[i]["q"], []).append(i)
+
+        def soon(b, q, now, limit, depth):
+            r = ready[b]
+            for p in before[b]:
+                if not done[p]:
+                    if calls[p]["q"] == q or not depth:
+                        return limit
+                    r = max(r, max(soon(p, q, now, limit, depth - 1), free.get(calls[p]["q"], 0.0), now) + calls[p]["cost"]
+                            + (gap(b, p) if back else gap(p, b)))
+                    if r >= limit:
+                        return limit
+            return r
+
+        todo = n
+        while todo:
+            now, q = min((max(free.get(q, 0.0), min(ready[i] for i in l)), q) for q, l in pool.items() if l)
+            i = max((i for i in pool[q] if ready[i] <= now), key=lambda i: rank[i])
+            cost, wait = calls[i]["cost"], None
+            while done[ahead[q][-1]]:
+                ahead[q].pop()
+            for b in [b for b in ahead[q][-CFG["look"]:] if not done[b] and rank[b] > rank[i]]:
+                r = soon(b, q, now, now + cost, CFG["depth"])
+                if now < r < now + cost:
+                    go = max(rank[i] + now, rank[b] + now + cost)
+                    hold = max(rank[b] + r, rank[i] + r + calls[b]["cost"]) + calls[b]["mu"] * (r - now)
+                    if hold < go:
+                        wait = r if wait is None else min(wait, r)
+            if wait is not None:
+                free[q] = wait
+                continue
+            at, todo, done[i] = now, todo - 1, True
             pool[q].remove(i)
             start[i] = at
+            if at > ready[i]:
+                cause[i] = last.get(q)
+            last[q] = i
             free[q] = at + calls[i]["cost"]
             for j in after[i]:
-                ready[j] = max(ready[j], free[q] + (gap(j, i) if back else gap(i, j)))
+                r = free[q] + (gap(j, i) if back else gap(i, j))
+                if r > ready[j]:
+                    ready[j], cause[j] = r, i
                 left[j] -= 1
                 if not left[j]:
                     pool.setdefault(calls[j]["q"], []).append(j)
-        return start, max(start[i] + calls[i]["cost"] + calls[i]["lat"] for i in range(n))
+        return start, max(start[i] + calls[i]["cost"] + calls[i]["lat"] for i in range(n)), cause, [r - c["first"] for r, c in zip(rank, calls)]
 
     rank = [0.0] * n
     for i in reversed(range(n)):
@@ -145,10 +196,87 @@ def plan(calls):
     now = best
     for _ in range(CFG["passes"]):
         back = run(succ, pred, [s + c["cost"] for s, c in zip(now[0], calls)], True)
-        now = run(pred, succ, [s + c["cost"] for s, c in zip(back[0], calls)], False)
+        now = min((run(pred, succ, [a * r + (1 - a) * (s + c["cost"]) for r, s, c in zip(rank, back[0], calls)], False) for a in CFG["mix"]),
+                  key=lambda x: x[1])
         if now[1] < best[1]:
             best = now
-    return sorted(range(n), key=lambda i: (best[0][i], i)), best[1]
+    order = sorted(range(n), key=lambda i: (best[0][i], i))
+
+    CFG["hop"], hop = CFG["hop2"], CFG["hop"]
+    need = [[(p, gap(p, i)) for p in pred[i]] for i in range(n)]
+    CFG["hop"] = hop
+    cost, lat, que = [c["cost"] for c in calls], [c["lat"] for c in calls], [c["q"] for c in calls]
+
+    slow = [c["slow"] for c in calls]
+
+    def replay(order, lo=0, old=None):
+        a = replay1(order, cost, lo, old and old[2])
+        b = replay1(order, slow, lo, old and old[3]) if CFG["both"] else (0.0, [], None)
+        return a[0] + CFG["both"] * b[0], a[1] + b[1], a[2], b[2]
+
+    def replay1(order, cost, lo, old):
+        end, why = (list(old[0]), list(old[1])) if old else ([0.0] * n, [None] * n)
+        last, top, tip = {}, 0.0, None
+        for i in order[max(0, lo - 60):lo]:
+            last[que[i]] = i
+        for i in order[lo:]:
+            j = last.get(que[i])
+            s, w = (0.0, None) if j is None else (end[j], j)
+            for p, d in need[i]:
+                if end[p] + d > s:
+                    s, w = end[p] + d, p
+            end[i], why[i], last[que[i]] = s + cost[i], w, i
+            if end[i] + lat[i] > top:
+                top, tip = end[i] + lat[i], i
+        arcs = []
+        while tip is not None:
+            j = why[tip]
+            if j is not None and j not in pred[tip] and que[j] != "g":
+                arcs.append((j, tip))
+            tip = j
+        return top, arcs, (end, why)
+
+    now = replay(order)
+    keep, x = (now[0], order), 1
+    for k in range(CFG["tries"]):
+        x = (x * 1103515245 + 12345) % 2 ** 31
+        m = (x >> 8) % len(now[1])
+        a, b = now[1][m]
+        x = (x * 1103515245 + 12345) % 2 ** 31
+        for _ in range((x >> 8) % CFG["moves"]):
+            if x & 64 and m + 1 < len(now[1]) and now[1][m + 1][1] == a:
+                m += 1
+                a = now[1][m][0]
+            elif not x & 64 and m and now[1][m - 1][0] == b:
+                m -= 1
+                b = now[1][m][1]
+        lo, hi = order.index(a), order.index(b)
+        if x & 64:
+            part, seen = [b], {que[b]: 0}
+            for i in reversed(order[lo:hi]):
+                if (que[i] in seen and que[i] != que[b]) or any(j in succ[i] for j in part):
+                    part.append(i)
+                    seen[que[i]] = 0
+            if a in part or sum(que[i] == que[b] for i in part) > 1:
+                continue
+            part = set(part)
+            new = order[:lo] + [i for i in order[lo:hi + 1] if i in part] + [i for i in order[lo:hi + 1] if i not in part] + order[hi + 1:]
+        else:
+            part, seen = [a], {que[a]: 0}
+            for i in order[lo + 1:hi + 1]:
+                if (que[i] in seen and que[i] != que[a]) or any(j in pred[i] for j in part):
+                    part.append(i)
+                    seen[que[i]] = 0
+            if b in part or sum(que[i] == que[a] for i in part) > 1:
+                continue
+            part = set(part)
+            new = order[:lo] + [i for i in order[lo:hi + 1] if i not in part] + [i for i in order[lo:hi + 1] if i in part] + order[hi + 1:]
+        nxt = replay(new, lo, now)
+        if nxt[0] <= now[0] + CFG["jit"] * (1 - k / CFG["tries"]) * (x % 1024) / 1024:
+            now, order = nxt, new
+            if now[0] < keep[0]:
+                keep = (now[0], order)
+    return keep[1], keep[0]
 
 
 PLAN = {}
@@ -156,7 +284,7 @@ PLAN = {}
 
 def make(g, T):
     eng = {"v": g.vector, "a": g.scalar, "t": g.tensor, "g": g, "s": g.sync}
-    calls, total, lines = [], {}, {}
+    calls, total, lines, first = [], {}, {}, [0.0, CFG["mu"]]
 
     def ap(r):
         if r[0] == "@":
@@ -176,7 +304,9 @@ def make(g, T):
         after = {lines[line][0]: lines[line][1]} if line in lines else {}
         if line:
             lines[line] = (len(calls), busy)
-        calls.append({"q": q, "acc": accesses(reads, writes), "also": list(also), "call": call, "cost": cost, "lat": lat, "sem": sem, "after": after})
+        calls.append({"q": q, "acc": accesses(reads, writes), "also": list(also), "call": [call], "cost": cost, "lat": lat, "sem": sem, "after": after,
+                      "first": first[0] - (500.0 * len(calls) if first[0] >= IN_ORDER else 0.0), "mu": first[1],
+                      "slow": cost + CYC * sum(f * size(r) for f, rs in ((0.5, reads), (2.0, writes)) for r in rs if r[0] == "@")})
 
     def price(out, ins, rate=None):
         if out[0] == "@":
@@ -207,21 +337,31 @@ def make(g, T):
         note("v", [a, b], [out], lambda: g.vector.tensor_tensor_scan(out=ap(out), data0=ap(a), data1=ap(b), initial=0.0, op0=op0, op1=op1),
              price(out, [a, b]))
 
+    def red(out, a):
+        note("v", [a], [out], lambda: g.vector.tensor_reduce(out=ap(out), in_=ap(a), axis=AX.X, op=OP.add), price(a, [], 1.0))
+
     def tr(out, a):
         note("v", [a], [out], lambda: g.vector.transpose(out=ap(out), in_=ap(a)), price(out, [a]))
 
-    def act(out, a, func=AF.Copy, bias=None, accum=None):
+    def act(out, a, func=AF.Copy, bias=None, accum=None, scale=None):
         kw = {}
         if bias is not None:
-            kw["bias"] = ap(bias)
+            kw["bias"] = ap(bias) if isr(bias) else bias
+        if scale is not None:
+            kw["scale"] = ap(scale) if isr(scale) else scale
         if accum is not None:
             kw["accum_out"] = ap(accum)
-        note("a", [a] + [b for b in [bias] if b], [out] + [b for b in [accum] if b],
+        note("a", [a] + [b for b in [bias, scale] if isr(b)], [out] + [b for b in [accum] if b],
              lambda: g.scalar.activation(out=ap(out), in_=ap(a), func=func, **kw), price(out, [a], 1.0))
 
     def mm(out, lhsT, rhs, start, stop):
         note("t", [lhsT, rhs], [out], lambda: g.tensor.matmul(ap(out), ap(lhsT), ap(rhs), start, stop),
-             0.03 + 0.5e-3 * max(64, size(rhs)) * (4 if SCRATCH[rhs[0]][2] == "float32" else 1))
+             0.03 + CFG["pe"] * max(64, size(rhs)) * (4 if SCRATCH[rhs[0]][2] == "float32" else 1))
+        a, b = calls[-2:]
+        if a["q"] == "t" and len(a["call"]) < 4 and [x[0][0] for x in a["acc"][-3:]] == [lhsT[0], rhs[0], out[0]] and a["acc"][-1][0] == out:
+            calls.pop()
+            for k in ("acc", "call", "cost", "slow"):
+                a[k] += b[k]
 
     def iota(out, pattern, base, cm):
         kw = {} if SCRATCH[out[0]][2] == "int32" else {"allow_small_or_imprecise_dtypes": True}
@@ -244,20 +384,24 @@ def make(g, T):
              lambda: eng[q].dma_start(out=ap(out) if isr(out) else out, in_=ap(a) if isr(a) else a).then_inc(T.sem[s], 16),
              0.05, 2.0 + busy, s, (), "dma", busy)
 
-    def send(topo, src, dst, land, a, rsem):
+    def send(topo, dst, mask, out, land, a, rsem, near):
         s = "l%d" % nl[0]
         nl[0] += 1
         rid, pid, _ = topo.addr(dst)
-        total[s] = len(topo.engines(src, dst))
-        note("g", [a], [], lambda: g.remote_dma(out_ap=T[land][:], in_ap=ap(a), remote_sem=T.sem[rsem], local_sem=T.sem[s], pid=pid,
-                                                routing_id=rid, dma_engine_mask=topo.mask(src, dst)),
-             0.5 if nl[0] > 1 else 3.5, 3.0 + nbytes(a) / 40e3, s, [(R(land), 1)], "link", nbytes(a) / 40e3)
+        total[s] = bin(mask).count("1")
+        far = 3.0 + nbytes(a) / CFG["link"]
+        first[0] = CFG["send0"] if nl[0] == 1 else CFG["send"]
+        note("g", [a], [], lambda: g.remote_dma(out_ap=ap(out), in_ap=ap(a), remote_sem=T.sem[rsem], local_sem=T.sem[s], pid=pid,
+                                                routing_id=rid, dma_engine_mask=mask),
+             0.5 if nl[0] > 1 else 3.5, far + (3.0 + nbytes(a) / 80e3 if near else 0.0), s, [(r, 1) for r in land],
+             "chip" if near else "link", nbytes(a) / (80e3 if near else CFG["link"]))
+        first[0] = 0.0
 
     def issue(arrivals):
         count, known, waited, hist = {}, {k: {} for k in eng}, {}, {}
         for land, rsem, n in arrivals:
             total[rsem] = n
-            hist[land] = [((R(land), 1), "remote", rsem, n, {})]
+            hist.setdefault(land[0], []).append(((land, 1), "remote", rsem, n, {}))
         if "order" not in PLAN:
             PLAN["order"], PLAN["end"] = plan(calls)
         for i in PLAN["order"]:
@@ -271,12 +415,13 @@ def make(g, T):
                     for s, v in list(e[4].items()) + [(e[2], e[3])]:
                         k[s] = max(k.get(s, 0), v)
             if c["sem"]:
-                c["call"]()
+                c["call"][0]()
                 s, v, p = c["sem"], total[c["sem"]], "dma"
             else:
                 s, p = "q_" + q, q
-                count[q] = total[s] = v = count.get(q, 0) + 1
-                c["call"]().then_inc(T.sem[s], 1)
+                count[q] = total[s] = v = count.get(q, 0) + len(c["call"])
+                for call in c["call"]:
+                    call().then_inc(T.sem[s], 1)
             clock = dict(k)
             for a in c["acc"]:
                 keep = [e for e in hist.get(a[0][0], [])
@@ -289,17 +434,49 @@ def make(g, T):
                 g.wait_ge(T.sem[s], n)
 
     return {"tt": tt, "ts": ts, "cp": cp, "ms": ms, "scan": scan, "tr": tr, "act": act, "mm": mm, "iota": iota, "aff": aff,
-            "dma": dma, "send": send, "issue": issue}
+            "red": red, "first": first, "dma": dma, "send": send, "issue": issue}
+
+
+HAND_ON = [("rm0", "qm0", "m", 0, 0), (None, "qm0", "m", 1, 0), (None, "qm0", "m", 2, 0), (None, "qm0", "m", 3, 0)]
+
+
+def helper(topo, cores, core):
+    return [c for c in topo.cores_of(core) if topo.die(c) != topo.die(core) and all(topo.may_write(c, d) for d in cores)][0]
+
+
+def hand_on(g, core, T, topo, rank):
+    home = T.cores[rank]
+    n = 0
+    for wait, src, kind, t, lo in HAND_ON:
+        dst = T.cores[(rank - 1 - t) % NR]
+        if wait:
+            g.wait_ge(T.sem[wait], bin(topo.mask(home, core) & ~topo.mask(home, dst)).count("1"))
+        rid, pid, _ = topo.addr(dst)
+        g.remote_dma(out_ap=T["q%s%d" % (kind, t)][:, lo:V], in_ap=T[src][:, lo:V], remote_sem=T.sem["r%s%d" % (kind, t)],
+                     local_sem=T.sem["l0"], pid=pid, routing_id=rid, dma_engine_mask=topo.mask(core, dst))
+        n += len(topo.engines(core, dst))
+    g.wait_ge(T.sem["l0"], n)
 
 
 def rank_program(g, core, T, topo):
     rank = T.rank_of(core)
     if rank is None:
+        for r in range(NR):
+            if helper(topo, T.cores, T.cores[r]) == core:
+                hand_on(g, core, T, topo, r)
         return
     F = make(g, T)
+    aide = helper(topo, T.cores, core)
+
+    def offer(t, out, a, sem):
+        dst = T.cores[(rank - 1 - t) % NR]
+        F["send"](topo, dst, topo.mask(core, dst), out, [out], a, sem, False)
+
+    def hand(out, lands, a, sem):
+        F["send"](topo, aide, topo.mask(core, aide) & ~topo.mask(core, T.cores[rank - 1]), out, lands, a, sem, True)
+
     tt, ts, cp, ms, scan, tr, act, mm = (F[k] for k in ("tt", "ts", "cp", "ms", "scan", "tr", "act", "mm"))
-    iota, aff, dma, send = (F[k] for k in ("iota", "aff", "dma", "send"))
-    asker = [T.cores[(rank - 1 - t) % NR] for t in range(RO)]
+    iota, aff, dma, red = (F[k] for k in ("iota", "aff", "dma", "red"))
     asked = [T.cores[(rank + 1 + t) % NR] for t in range(RO)]
 
     def at(win, off):
@@ -332,7 +509,8 @@ def rank_program(g, core, T, topo):
         else:
             act(out, a)
 
-    MO, MS = R("morph"), R("meas", 0, V)
+    first = F["first"]
+    MO, MS = R("morph", 0, P), R("meas", 0, V)
     DV = R("Dv", 0, V)
 
     dma("s", R("b15i"), T.bas[15:128:16, :])
@@ -342,84 +520,88 @@ def rank_program(g, core, T, topo):
     dma("s", R("bas_i"), T.bas[:])
     dma("s", MO, T.mor[:])
 
+    first[0] = IN_ORDER
     ms(R("one8"), 1.0)
-    aff(R("sel8"), R("one8"), [[1, 144]], OP.is_equal, -15, -16)
-    ms(R("onef"), 1.0)
-    aff(R("selr"), R("onef"), [[1, 144]], OP.is_equal, 0, -1)
-    aff(R("selr"), R("selr"), [[0, 9], [1, 16]], OP.is_equal, -15, 0)
     ms(R("oneb"), 1.0)
-    aff(R("sel1"), R("oneb", 0, 144), [[0, 9], [1, 16]], OP.is_equal, -15, 0)
-    aff(R("sel1"), R("sel1"), [[-16, 9], [0, 16]], OP.is_ge, 0, 1)
-    aff(R("sel1"), R("sel1"), [[16, 9], [0, 16]], OP.is_ge, 15, -1)
+    ms(R("onef"), 1.0)
     iota(R("pi", 0, 1), [[0, 1]], 0, 1)
-    iota(R("i8"), [[0, 4], [128, 24]], 0, 0)
-    iota(R("cb", 0, 6), [[-16, 6]], 0, 0)
-    iota(R("cn", 0, 6), [[32, 6]], 400, 0)
-    aff(R("idb"), R("oneb", 0, 128), [[1, 128]], OP.is_equal, 0, -1)
-    aff(R("idf"), R("onef", 0, 128), [[1, 128]], OP.is_equal, 0, -1)
-    aff(R("blk"), R("oneb", 0, 128), [[-16, 8], [0, 16]], OP.is_ge, 0, 1)
-    aff(R("blk"), R("blk"), [[16, 8], [0, 16]], OP.is_ge, 15, -1)
+    aff(R("sel8"), R("one8"), [[1, 144]], OP.is_equal, -15, -16)
+    aff(R("blkw"), R("oneb", 0, 144), [[-16, 9], [0, 16]], OP.is_ge, 0, 1)
+    aff(R("blkw"), R("blkw"), [[16, 9], [0, 16]], OP.is_ge, 15, -1)
+    aff(R("sel1"), R("blkw"), [[0, 9], [1, 16]], OP.is_equal, -15, 0)
+    aff(R("idw"), R("oneb", 0, 160), [[1, 160]], OP.is_equal, -16, -1)
+    aff(R("idfw"), R("onef"), [[1, 160]], OP.is_equal, -8, -1)
     aff(R("tri"), R("blk"), [[1, 128]], OP.is_ge, 0, -1)
-    iota(R("VR"), [[1, V]], 0, 0)
-    for h in range(2):
-        for y in range(2):
-            o = ch("swp", 2 * h + y, 128)
-            aff(o, R("onef", 0, 128), [[1, 128]], OP.is_equal, -16 * (h - y), -1)
-            aff(o, o, [[0, 4], [1, 2], [0, 16]], OP.is_equal, -h, 0)
-    iota(R("dgf"), [[0, 25], [1, 16]], 0, 0)
-    iota(R("LX"), [[2, V // 2], [-1, 2]], 1, 0)
+    for n, pat, base in ((R("cb", 0, 6), [[-16, 6]], 0), (R("cn", 0, 6), [[32, 6]], 400), (R("i8"), [[0, 4], [128, 24]], 0),
+                         (R("W1", 0, 400), [[0, 25], [1, 16]], 0)):
+        iota(n, pat, base, 0)
+
+    def fill(out, c):
+        act(out, R("oneb", 0, size(out)), scale=c)
+
     ms(R("rmask"), 1.0)
-    ms(R("rmask", 0, 2048, 16), 0.0)
     ms(R("Z"), 0.0)
-    ms(R("amask"), -2.0 * 2 ** 25)
+    ms(R("rmask", 0, 2048, 16), 0.0)
+    fill(R("amask"), -2.0 * 2 ** 25)
+    for n in ("Bf", "meas"):
+        fill(R(n, V, VX), 0.0)
+    for n in ("UQ", "AD", "old"):
+        fill(R(n, I, IX), 0.0)
+    fill(R("non", I, IX), 1.0)
+    fill(R("cst"), -32.0)
+    fill(R("oalln"), -0.0625)
     ms(R("amask", 0, I, 16), 2.0 * 2 ** 25)
-    for n in ("Bf", "Dv", "meas"):
-        ms(R(n, V, VX), 0.0)
-    for n in ("UQ", "AD", "old", "got"):
-        ms(R(n, I, IX), 0.0)
-    ms(R("cst"), -32.0)
     ms(R("cst", 15, 128, 16), 32.0)
     ms(col("mg"), -0.5)
-    ms(R("oalln"), -0.0625)
+    ts(R("pi", 1, 2), R("pi", 0, 1), 16, None, OP.bitwise_and)
     ts(R("pi", 0, 1), R("pi", 0, 1), 15, None, OP.bitwise_and)
     cp(col("pm"), R("pi", 0, 1))
     ts(col("pw"), col("pm"), 1.0, None, OP.add)
     ts(col("pw", 1), col("pm"), 8.0, None, OP.mult)
     ts(R("cb", 0, 6), R("cb", 0, 6), col("pm"), 0.5, OP.subtract, OP.subtract)
-    aff(R("wlo"), R("onef"), [[1, 144]], OP.is_equal, -8, -1)
     ts(col("pw", 2), col("pm"), 8.0, None, OP.is_ge)
     ts(col("pw", 3), col("pm"), 8.0, None, OP.is_lt)
-    ts(R("whi"), R("wlo"), col("pw", 2), None, OP.mult)
-    ts(R("wlo"), R("wlo"), col("pw", 3), None, OP.mult)
+    ts(col("pw", 4), col("pm"), 15.0, None, OP.is_equal)
+    ts(col("pw", 5), col("pi", 1), 0.0, None, OP.is_equal)
+    ts(col("pw", 6), col("pi", 1), 0.0, None, OP.is_gt)
     ms(R("rmask8"), 1.0)
     ms(R("rmask8", 0, 1024, 8), 0.0)
     ts(R("selz"), R("sel1"), col("pw"), None, OP.mult)
     ts(R("i8"), R("i8"), col("pw", 1), None, OP.add)
     for n, src, f in (("selp", "sel1", 2.0 ** -13), ("selm", "sel1", -4096.0), ("selk", "sel1", 2048.0), ("idbig", "idb", BIG),
-                      ("idn", "idb", -1.0), ("idk", "idf", 2.0 ** 24), ("idkn", "idf", -2.0 ** 24), ("blkp", "blk", 2.0 ** -13),
-                      ("idfn", "idf", -1.0), ("blkn", "blk", -1.0), ("blk2n", "blk", -2.0), ("tri", "tri", 8192.0)):
-        ts(R(n), R(src), f, None, OP.mult)
-    ts(R("dg"), R("dgf"), col("pm"), None, OP.is_equal)
+                      ("idn", "idb", -1.0), ("idk", "idf", 2.0 ** 24), ("idkn", "idb", -2.0 ** 24), ("blkp", "blk", 2.0 ** -13),
+                      ("idfn", "idf", -1.0), ("idK", "idb", 4096.0), ("idKn", "idb", -4096.0), ("blkn", "blk", -1.0), ("blk2n", "blk", -2.0), ("tri", "tri", 8192.0)):
+        act(R(n), R(src), scale=f)
+    for n, src, k in (("whi", R("idfw", 0, 144), 2), ("wlo", R("idfw", 0, 144), 3), ("selr", R("idfw", 8, 152), 4),
+                      ("sw0", R("idw"), 5), ("sw1", R("idw"), 6)):
+        act(R(n), src, AF.Identity, scale=col("pw", k))
+    ts(R("dg"), R("W1", 0, 400), col("pm"), None, OP.not_equal)
+    iota(R("VR"), [[PH, I]], 0, 0)
+    first[0] = 0.0
+    iota(R("LX"), [[2, V // 2], [-1, 2]], 1, 0)
 
     def classes(rounds, rows):
         for t in rounds:
             c = ch("clsi", t, 24)
-            ts(c, rows, float(97 * t), None, OP.add)
+            ts(c, rows, 97.0 * t + P / 2.0, None, OP.add)
             ts(c, c, 511, None, OP.bitwise_and)
             cp(cls(t), c)
 
-    cp(R("b15"), lanes("b15i", 0))
+    first[0] = 2 * IN_ORDER
+    ts(R("b15"), lanes("b15i", 0), -P / 2.0, None, OP.add)
     for x in range(16):
         mm(R("P4", 0, 24), sk("sel8", x), R("b15", x, I, 16), x == 0, x == 15)
-    classes([0, 3], R("P4", 0, 24))
     cp(R("use16"), R("use_i"))
+    classes([0, 3], R("P4", 0, 24))
+    first[0] = 0.0
 
     def sums():
         for k, who in enumerate(CFG["sums"]):
             gather(who, ch("GD", k, 1024) if k < 6 else ch("SD", k - 6, 1024), at(MS, ch("use16", k, 64)))
-        for lo, hi, b in ((0, 192, R("GD", 0, 3072)), (192, 384, R("GD", 3072, W16)), (384, C, R("SD", 0, 2048))):
+        for lo, hi, b in ((0, 192, R("GD", 0, 3072)), (192, 384, R("GD", 3072, W16)), (384, 448, R("SD", 0, 1024)), (448, C, R("SD", 1024, 2048))):
             for j in range(16):
                 mm(R("P3", lo, hi), sk("selp", j), R(b[0], b[1] + j, b[2], 16), j == 0, j == 15)
+        act(R("SA"), R("P3"), scale=2.0 ** 24)
         tt(R("USE"), R("P3"), R("use_i"), OP.add)
 
     def partners():
@@ -438,8 +620,10 @@ def rank_program(g, core, T, topo):
             z = 16 * PC * (a // PC % 2)
             cp(R("Z", z, z + 16 * (b - a), 16), lanes("meas", ph, a, b))
             scan(R("x0", 16 * a, 16 * b), R("rmask", 0, 16 * (b - a)), R("Z", z, z + 16 * (b - a)), OP.mult, OP.add)
+        first[0] = 0.0 if t else IN_ORDER
         for j in range(16 if m < n else 0):
             aff(R("x%d" % (t % 2), 16 * m + j, 16 * n, 16), lanes("meas", ph, m, n), [[0, n - m]], OP.is_ge, 0, 0)
+        first[0] = 0.0
 
     def tables():
         for k in range(PH):
@@ -447,7 +631,12 @@ def rank_program(g, core, T, topo):
             cp(lanes("Bf", k), lanes("bas_i", k))
         for k in range(PH):
             p = R("P%d" % (5 + k), 0, I)
-            tt(ch("NEQ", k, I), ch("der_i", k, I), ch("bas_i", k, I), OP.not_equal)
+            if k < CFG["neq"]:
+                tt(ch("NEQ", k, I), ch("der_i", k, I), ch("bas_i", k, I), OP.not_equal)
+            else:
+                mm(p, R("idf"), ch("Dv", k, I), True, False)
+                mm(p, R("idfn"), ch("Bf", k, I), False, True)
+                ts(ch("NEQ", k, I), p, 0.0, None, OP.not_equal)
             mm(p, R("cst"), R("oneb", 0, I), True, False)
             mm(p, R("tri"), ch("NEQ", k, I), False, True)
             tt(ch("W", k, I), p, ch("der_i", k, I), OP.add)
@@ -456,32 +645,34 @@ def rank_program(g, core, T, topo):
         for ph in (1, 2):
             for x in range(16):
                 mm(ch("P1", ph, 24), sk("selr", x), R("Bf", 3 * x + ph, V, 48), x == 0, x == 15)
+            classes([ph], ch("P1", ph, 24))
+
+    def targets():
         for ph in range(PH):
             for x in range(16):
-                mm(ch("P1", 3 + ph, 24), sk("selz", x), R("meas", 3 * x + ph, V, 48), x == 0, x == 15)
-        for ph in (1, 2):
-            classes([ph], ch("P1", ph, 24))
+                mm(ch("P4", 3 + ph, 24), sk("selz", x), R("meas", 3 * x + ph, V, 48), x == 0, x == 15)
         for t in range(RO):
-            ts(ch("zi", t, 24), ch("P1", 3 + t % PH, 24), float(t), None, OP.add)
+            ts(ch("zi", t, 24), ch("P4", 3 + t % PH, 24), float(t), None, OP.add)
         ts(R("zi"), R("zi"), 7, None, OP.bitwise_and)
         ts(R("i8", 84, 96), R("i8", 84, 96), -4.0 * I, None, OP.add)
         tt(R("i8"), R("i8"), R("zi"), OP.add)
         cp(R("zof"), R("i8"))
 
-    def winners(keys, kt, ks, n, out, li, lst):
+    def winners(keys, kt, ks, n, out, li, lh, lst):
         tr(kt, keys)
         scan(ks, R("amask", 0, n), kt, OP.max, OP.min)
+        cp(li, R(ks[0], 15, n, 16))
+        ts(li, li, 2047, None, OP.bitwise_and)
+        cp(lh, li)
         for y in range(2):
             for h in range(2):
-                mm(R(out[0], out[1] + y, out[2], 2), ch("swp", 2 * h + y, 128), R(ks[0], 15 + 16 * h, n, 32), h == 0, h == 1)
-        cp(li, out)
-        ts(li, li, 2047, None, OP.bitwise_and)
-        cp(lst, li)
+                mm(R(out[0], out[1] + y, out[2], 2), R("sw%d" % y, 16 - 16 * (h - y), 144 - 16 * (h - y)), R(lh[0], lh[1] + h, lh[2], 2), h == 0, h == 1)
+        cp(lst, out)
 
     def entry(out, kf, u, stop):
         mm(out, R("idk"), kf, True, False)
         mm(out, R("idkn"), u, False, False)
-        mm(out, R("idf"), u, False, stop)
+        mm(out, R("idb"), u, False, stop)
 
     def search(t):
         ph = t % PH
@@ -496,15 +687,14 @@ def rank_program(g, core, T, topo):
         else:
             cp(R("u16"), at(R("use_i"), cls(t)))
             cp(R("U"), R("u16"))
-            act(R("KF"), at(R("USE"), cls(t)))
-            entry(R("P1", 0, I), R("KF"), R("U"), True)
-            act(R("KF"), R("P1", 0, I))
-        stage(R("P1", 0, I), lanes("VR", ph), CFG["stage"][0])
+            act(R("KF"), at(R("SA"), cls(t)))
+        act(R("P1", 0, I), R("VR"), AF.Identity, bias=float(ph))
         tt(R("EQ"), R("U"), R("P1", 0, I), OP.is_equal)
         lo, x = 0, "x%d" % (t % 2)
         for who, n in CFG["search"][t]:
             hi = lo + n
-            cuts = [(a, min(a + PC, hi)) for a in range(lo, hi, PC)]
+            pc = CFG["pc"][who == "p"] if t else PC
+            cuts = [(a, min(a + pc, hi)) for a in range(lo, hi, pc)]
             if who == "p":
                 for a, b in cuts:
                     act(R("GE", 16 * a, 16 * b), at(MS, R("u16", a, b)))
@@ -525,41 +715,54 @@ def rank_program(g, core, T, topo):
             for k, (s, j, r) in enumerate(sums):
                 mm(key, sk(s, j), r, k == 0 and not first, False)
             if not first:
-                mm(key, R("idf"), R("U" if who == "p" else "KF", lo, hi), False, False)
-            mm(key, R("idbig"), R("EQ", lo, hi), False, True)
+                mm(key, R("idb"), R("U", lo, hi), False, False)
+            late = who == "m" and t == 0
+            mm(key, R("idbig"), R("EQ", lo, hi), False, not late)
+            if late:
+                mm(key, R("idf"), R("KF", lo, hi), False, True)
             lo = hi
-        winners(R("P0", 0, I), R("KT"), R("KS"), I, R("P0", 400, 424), R("mi"), R("m16"))
+        winners(R("P0", 0, I), R("KT"), R("KS"), I, R("P0", 400, 424), R("mi"), R("mh", 0, 24), R("m16"))
 
     def old_lists(t, bank):
-        ph, o = t % PH, ch("d16", t % PH, I)
-        if not CFG["pair"][t]:
-            cp(o, lanes("der_i" if t < PH else "Dv", ph))
-            return
-        for k, (a, b) in enumerate(((8, 8), (16, 0))):
-            p = ch(bank, k, I // 2)
-            mm(p, R("whi" if k else "wlo", a, a + 128), R("Dv", ph, V, 2 * PH), True, False)
-            mm(p, R("wlo" if k else "whi", b, b + 128), R("Dv", ph + PH, V, 2 * PH), False, True)
-        cp(o, R(bank, 0, I))
+        ph, n = t % PH, CFG["pair"][t]
+        if n < I:
+            cp(R("d16", I * ph + n, I * ph + I), lanes("der_i" if t < PH else "Dv", ph, n, I))
+        if n:
+            for k, (a, b) in enumerate(((8, 8), (16, 0))):
+                p = ch(bank, k, n // 2)
+                mm(p, R("whi" if k else "wlo", a, a + 128), R("Dv", ph, PH * n, 2 * PH), True, False)
+                mm(p, R("wlo" if k else "whi", b, b + 128), R("Dv", ph + PH, PH * n, 2 * PH), False, True)
+            cp(R("d16", I * ph, I * ph + n), R(bank, 0, n))
 
     def tops(t, gat, top, lst, parts, pair, bank, out, cuts):
-        lo, w = 0, 8 if pair else 16
+        lo = 0
         for who, n in parts:
             hi = lo + n
+            w = 8 if lo < pair else 16
             a = R(gat, w * lo, w * hi)
             gather(who, a, at(MO, R(lst[0], lst[1] + w * lo // 16, lst[1] + w * hi // 16)))
-            if pair:
-                b = R(gat, w * (I + lo), w * (I + hi))
-                tt(b, at(MO, R(lst[0], lst[1] + (I + lo) // 2, lst[1] + (I + hi) // 2)), a, OP.max)
+            if lo < pair:
+                b = R(gat, w * (pair + lo), w * (pair + hi))
+                tt(b, at(MO, R(lst[0], lst[1] + (pair + lo) // 2, lst[1] + (pair + hi) // 2)), a, OP.max)
                 a = b
-            scan(R(top, w * lo, w * hi), R("rmask8" if pair else "rmask", 0, w * n), a, OP.mult, OP.max)
+            scan(R(top, w * lo, w * hi), R("rmask8" if lo < pair else "rmask", 0, w * n), a, OP.mult, OP.max)
             lo = hi
         for lo, hi in cuts:
-            mm(R(bank, lo, hi), R("idb"), R(top, w * lo + w - 1, w * hi, w), True, False)
-            mm(R(bank, lo, hi), R("idn"), lanes("meas", t % PH, lo, hi), False, True)
+            for a, b, w in ((lo, min(hi, pair), 8), (max(lo, pair), hi, 16)):
+                if a < b:
+                    mm(R(bank, a, b), R("idb"), R(top, w * a + w - 1, w * b, w), True, False)
+                    mm(R(bank, a, b), R("idn"), lanes("meas", t % PH, a, b), False, True)
             act(R(out, lo, hi), R(bank, lo, hi), AF.Abs)
 
     def blocks(t):
         return [(0, I)] if t + 1 < RO else [(0, I // 2), (I // 2, I)]
+
+    def morphs(t):
+        tt(R("gx"), R("P7", 0, I), R("non", 0, I), OP.mult)
+        for lo, hi in blocks(t):
+            tt(rewritten(t, lo, hi), lanes("meas", t % PH, lo, hi), R("gx", lo, hi), OP.add)
+            if t + 1 == RO and not CFG["two"][t]:
+                dma("a", T.ym[:, 8 * lo:8 * hi], R("morph", 8 * lo, 8 * hi))
 
     def rewritten(t, lo, hi):
         return at(R("morph", 8 * lo, 8 * hi), R("zof", 24 * t + lo // 16, 24 * t + hi // 16))
@@ -567,48 +770,76 @@ def rank_program(g, core, T, topo):
     def dist(t):
         ph = t % PH
         half, kd, us = R("P5", 0, I), R("P7", 0, I), R("USE", 37 * t, 37 * t + I)
+        first[1] = CFG["mu"]
+        if CFG["two"][t]:
+            dma("s", R("morc"), MO)
         tops(t, "GD", "SD", ch("d16", ph, I), CFG["old"][t], CFG["pair"][t], "P2", "AD", [(0, I)])
-        tt(R("Ea"), at(R("W"), R("m16")), lanes("Bf", ph), OP.max)
-        ts(R("Ea"), R("Ea"), 4095, None, OP.bitwise_and)
-        cp(R("e16"), R("Ea"))
-        cuts = [(0, CFG["cut"]), (CFG["cut"], I)]
+        ea = R("Ea", 0, I)
+        tt(ea, at(R("W"), R("m16")), lanes("Bf", ph), OP.max)
+        ts(ea, ea, 4095, None, OP.bitwise_and)
+        cp(R("e16"), ea)
+        cut = CFG["cut"]
+        cuts = [(0, cut), (cut, I)][:2 - CFG["last"]]
         tops(t, "GE", "SE", R("e16"), CFG["new"][t], 0, "P3", "AE", cuts)
         for lo, hi in cuts:
             mm(R("P5", lo, hi), R("blkn"), R("AD", lo, hi), True, False)
             mm(R("P5", lo, hi), R("blk"), R("AE", lo, hi), False, True)
-        got = R("got", 0, I)
-        ts(got, half, col("mg"), None, OP.is_lt)
-        scan(R("cum"), R("oneb"), R("got"), OP.add, OP.subtract)
+        if CFG["last"]:
+            o, top, x, me = R("P5", cut, I), R("SE", 16 * cut + 15, W16, 16), lanes("meas", ph, cut, I), R("SQ", 0, I - cut)
+            tt(me, top, x, OP.min)
+            for k, (s, r) in enumerate((("blkn", R("AD", cut, I)), ("blk", x), ("blk", top), ("blk2n", me))):
+                mm(o, R(s), r, k == 0, k == 3)
+        non = R("non", 0, I)
+        first[0], first[1] = CFG["chain"], CFG["muy"][t]
+        ts(non, half, col("mg"), None, OP.is_gt)
+        scan(R("cum"), R("non"), R("oneb"), OP.add, OP.mult)
         for n in range(6):
-            act(R("junk", 0, 400), R("cum", 16 * n, 16 * n + 400), AF.Sign, bias=col("cb", n), accum=col("acc", n))
-        act(R("LXg"), at(R("LX"), R("m16")))
-        mm(kd, R("idf"), R("LXg"), True, False)
-        mm(kd, R("idfn"), us, False, True)
-        tt(kd, kd, R("dg", t, t + I), OP.mult)
-        tt(kd, kd, got, OP.mult)
-        tt(us, kd, us, OP.add)
+            if n < CFG["signs"][t]:
+                act(ch("junk", n % 2, 400), R("cum", 16 * n, 16 * n + 400), AF.Sign, bias=col("cb", n), accum=col("acc", n))
+            else:
+                o = ch("RQ", n % 2, 400)
+                ts(o, R("cum", 16 * n, 16 * n + 400), col("cb", n), 0.0, OP.add, OP.is_gt)
+                red(col("acc", n), o)
+        if CFG["signs"][t] < 6:
+            o = R("acc", CFG["signs"][t], 6)
+            ts(o, o, 2.0, -400.0, OP.mult, OP.add)
+        first[0] = 0.0
         if t + 1 < RO:
-            send(topo, core, asker[t + 1], "qk%d" % (t + 1), R("USE"), "rk%d" % (t + 1))
+            old_lists(t + 1, "P6")
+        act(R("LXg"), at(R("LX"), R("m16")))
+        for p, s in ((kd, "idK"), (R("P6", 0, I), "idKn")):
+            mm(p, R("idf"), R("LXg"), True, False)
+            mm(p, R(s), R("dg", t, t + I), False, False)
+            mm(p, R(s), non, False, True)
+        tt(R("LXg"), kd, us, OP.min)
+        tt(us, R("P6", 0, I), R("LXg"), OP.max)
+        if t + 1 < RO:
+            offer(t + 1, R("qk%d" % (t + 1)), R("USE"), "rk%d" % (t + 1))
         else:
             cp(R("use_i"), R("USE"))
             cp(R("USE"), R("use_i"))
             dma("s", T.yu[:], R("USE"))
-        if t + 1 < RO:
-            old_lists(t + 1, "P6")
-        stage(R("P6", 0, I), lanes("Dv", ph), CFG["stage"][1])
-        tt(kd, R("Ea"), R("P6", 0, I), OP.subtract)
-        tt(R("tD", 0, I), kd, got, OP.mult)
+        if t + 1 < RO and CFG["w1"]:
+            stage(half, lanes("Bf", ph), CFG["stage"][1])
+            tt(R("NEQ", 0, I), ea, half, OP.not_equal)
+            mm(half, R("cst"), R("oneb", 0, I), True, False)
+            mm(half, R("tri"), R("NEQ", 0, I), False, True)
+            tt(R("W1", 0, I), half, ea, OP.add)
         for lo, hi in blocks(t):
             act(R("old", lo, hi), rewritten(t, lo, hi))
-        mm(kd, R("idb"), lanes("meas", ph), True, False)
-        mm(kd, R("idn"), R("old", 0, I), False, True)
-        tt(R("gx", 0, I), kd, got, OP.mult)
+        mm(kd, R("idn"), lanes("meas", ph), True, False)
+        mm(kd, R("idb"), R("old", 0, I), False, True)
+        if CFG["two"][t]:
+            morphs(t)
+        mm(R("P6", 0, I), R("idf"), lanes("Dv", ph), True, False)
+        mm(R("P6", 0, I), R("idKn"), R("oneb", 0, I), False, False)
 
     def ask(t):
         ph = t % PH
         s6, v6 = R("s16", 0, 6), R("sv16", 0, 6)
         zs = R("Z", 0, 16 * CAP, 16)
         act(R("UQ", 0, I), at(R("qk%d" % t), cls(t)))
+        first[0] = CFG["chain"]
         tt(R("a2", 0, 6), R("cn", 0, 6), R("acc", 0, 6), OP.subtract)
         ts(v6, R("a2", 0, 6), 1.5, float(ph), OP.mult, OP.add)
         ts(s6, R("a2", 0, 6), 0.5, None, OP.mult)
@@ -625,73 +856,110 @@ def rank_program(g, core, T, topo):
         entry(key, R("UQs"), R("U2"), False)
         for j in range(16):
             mm(key, sk("selm", j), R("GQ", j, 16 * CAP, 16), False, j == 15)
-        winners(key, R("KT2"), R("KS2"), CAP, R("P4", 100, 106), R("ni", 0, 6), R("n16", 0, 6))
+        winners(key, R("KT2"), R("KS2"), CAP, R("P4", 100, 106), R("ni", 0, 6), R("mh", 24, 30), R("n16", 0, 6))
         tt(R("E2"), at(R("qw%d" % t), R("n16", 0, 6)), R("Bs"), OP.max)
         ts(R("E2"), R("E2"), 4095, None, OP.bitwise_and)
         cp(R("e216"), R("E2"))
         for k in range(2):
-            gather(CFG["ask2"][t][k], ch("GQ", k, 768), at(MO, ch("e216", k, 48)))
+            gather(CFG["ask2"][t][k], ch("GQ", k, 768), at(R("morc") if CFG["two"][t] else MO, ch("e216", k, 48)))
             scan(ch("SQ", k, 768), R("rmask", 0, 768), ch("GQ", k, 768), OP.mult, OP.max)
-        tt(R("dE2"), at(R("Dv"), v6), R("E2"), OP.subtract)
-        tt(R("dxs"), at(R("old"), s6), zs, OP.subtract)
+        first[0] = 0.0
+        if t + 1 < RO and CFG["w1"]:
+            w2 = R("P4", 300, 300 + CAP)
+            tt(R("NEQ", I, IX), R("E2"), R("Bs"), OP.not_equal)
+            mm(w2, R("cst"), R("oneb", 0, CAP), True, False)
+            mm(w2, R("tri"), R("NEQ", I, IX), False, True)
+            tt(R("Bs"), w2, R("E2"), OP.add)
+            cp(at(R("W1"), s6), R("Bs"))
+            mm(R("P5", 0, I), R("idf"), lanes("W", ph), True, False)
+            mm(R("P5", 0, I), R("idfn"), R("W1", 0, I), False, True)
+        cp(at(R("Ea"), s6), R("E2"))
+        if CFG["two"][t]:
+            tt(R("dxs"), at(R("old"), s6), zs, OP.subtract)
+            z6 = R("P4", 240, 246)
+            for x in range(16):
+                mm(z6, sk("selz", x), R("Z", 16 * x, 16 * CAP, 256), x == 0, x == 15)
+            ts(R("nz", 0, 6), z6, float(t), None, OP.add)
+            ts(R("nz", 0, 6), R("nz", 0, 6), 7, None, OP.bitwise_and)
+            ts(R("a8", 0, 6), R("a2", 0, 6), 4.0, None, OP.mult)
+            tt(R("a8", 0, 6), R("a8", 0, 6), R("nz", 0, 6), OP.add)
+            cp(R("z16", 0, 6), R("a8", 0, 6))
+        first[0] = CFG["chain"]
         top, g2 = R("SQ", 15, 16 * CAP, 16), R("P4", 128, 128 + CAP)
         tt(R("MM2"), top, zs, OP.min)
         mm(g2, R("blkn"), R("AD2"), True, False)
         mm(g2, R("blk"), zs, False, False)
         mm(g2, R("blk"), top, False, False)
         mm(g2, R("blk2n"), R("MM2"), False, True)
-        for n in ("adb", "adf") if t + 1 < RO else ("adf", "adb"):
-            ts(R(n), g2, col("mg"), -1.0, OP.is_lt, OP.mult)
+        ts(R("adb"), g2, col("mg"), None, OP.is_gt)
+        if not CFG["two"][t]:
+            cp(at(R("non"), s6), R("adb"))
+        first[0] = 0.0
 
     def change(t):
         ph = t % PH
-        s6, d = R("s16", 0, 6), lanes("Dv", ph)
-
-        def morphs():
-            tt(at(R("gx"), s6), R("adb"), R("dxs"), OP.mult)
-            for lo, hi in blocks(t):
-                tt(rewritten(t, lo, hi), R("old", lo, hi), R("gx", lo, hi), OP.add)
-                if t + 1 == RO:
-                    dma("a", T.ym[:, 8 * lo:8 * hi], R("morph", 8 * lo, 8 * hi))
-
-        if t + 1 < RO:
-            morphs()
-        tt(at(R("tD"), s6), R("adf"), R("dE2"), OP.mult)
-        tt(d, R("P6", 0, I), R("tD", 0, I), OP.add)
+        non, d, x, dn = R("non", 0, I), lanes("Dv", ph), R("XD"), R("P1", 0, I)
+        first[0] = CFG["end"]
+        if CFG["two"][t]:
+            tt(R("dxs"), R("adb"), R("dxs"), OP.mult)
+            tt(at(R("morph"), R("z16", 0, 6)), R("Z", 0, 16 * CAP, 16), R("dxs"), OP.add)
+            if t + 1 == RO:
+                dma("a", T.ym[:], MO)
+        else:
+            morphs(t)
+        cp(at(R("non"), R("s16", 0, 6)), R("adb")) if CFG["two"][t] else None
+        first[0] = 0.0
+        for k in range(2):
+            mm(R("P6", 0, I), R("idK"), non, False, k == 1)
+        tt(x, R("P6", 0, I), R("Ea", 0, I), OP.max)
+        mm(dn, R("idKn"), non, True, False)
+        mm(dn, R("idf"), x, False, True)
+        w = R("P5", 0, I)
+        if t + 1 < RO and not CFG["w1"]:
+            tt(R("NEQ", 0, I), dn, lanes("Bf", ph), OP.not_equal)
+        act(d, dn)
         if t + 1 == RO:
             dma("s", T.yd[:], DV)
-            morphs()
             return
-        stage(R("P7", 0, I), lanes("Bf", ph), CFG["stage"][2])
-        tt(R("NEQ", 0, I), d, R("P7", 0, I), OP.not_equal)
-        mm(R("P5", 0, I), R("cst"), R("oneb", 0, I), True, False)
-        mm(R("P5", 0, I), R("tri"), R("NEQ", 0, I), False, True)
-        tt(lanes("W", ph), R("P5", 0, I), d, OP.add)
-        send(topo, core, asker[t + 1], "qw%d" % (t + 1), R("W"), "rw%d" % (t + 1))
-        act(R("junk", 0, CAP), R("adb"), accum=col("cnt", 1))
-        mm(R("P4", 300, 301), R("oalln"), col("cum", I - 1), True, False)
-        mm(R("P4", 300, 301), R("oalln"), col("cnt", 1), False, True)
-        ts(col("nmi"), R("P4", 300, 301), 8.0 * I, None, OP.add)
+        if CFG["w1"]:
+            tt(w, w, non, OP.mult)
+            tt(lanes("W", ph), w, R("W1", 0, I), OP.add)
+        else:
+            for k, (s, r) in enumerate((("cst", R("oneb", 0, I)), ("idKn", non), ("idf", x), ("tri", R("NEQ", 0, I)))):
+                mm(w, R(s), r, k == 0, k == 3)
+            act(lanes("W", ph), w)
+        offer(t + 1, R("qw%d" % (t + 1)), R("W"), "rw%d" % (t + 1))
+        act(R("junk", 0, I), non, accum=col("cnt"))
+        mm(R("P4", 400, 401), R("oalln"), col("cnt"), True, True)
+        ts(col("nmi"), R("P4", 400, 401), 8.0 * I, None, OP.add)
         ts(col("nmi"), col("nmi"), 127, None, OP.bitwise_and)
         ts(col("mg"), col("nmi"), -1.0, -0.5, OP.mult, OP.add)
 
     spread(0)
-    send(topo, core, asker[0], "qm0", MS, "rm0")
+    hand(R("qm0"), [R("qm%d" % t) for t in range(RO)], MS, "rm0")
     sums()
-    send(topo, core, asker[0], "qk0", R("USE"), "rk0")
+    offer(0, R("qk0"), R("USE"), "rk0")
     tables()
+    first[0] = CFG["d16"]
     old_lists(0, "P2")
-    send(topo, core, asker[0], "qw0", R("W"), "rw0")
+    first[0] = 0.0
+    offer(0, R("qw0"), R("W"), "rw0")
     search(0)
+    first[0] = CFG["later"]
+    targets()
     partners()
     later()
+    first[0] = 0.0
     for t in range(RO):
         dist(t)
         if t + 1 < RO:
-            send(topo, core, asker[t + 1], "qm%d" % (t + 1), MS, "rm%d" % (t + 1))
             spread(t + 1)
         ask(t)
         if t + 1 < RO:
             search(t + 1)
         change(t)
-    F["issue"]([("q%s%d" % (a, t), "r%s%d" % (a, t), len(topo.engines(asked[t], core))) for t in range(RO) for a in "mkw"])
+    come = []
+    for t in range(RO):
+        a, b = len(topo.engines(asked[t], core)), len(topo.engines(helper(topo, T.cores, asked[t]), core))
+        come += [(R("qm%d" % t), "rm%d" % t, b), (R("qk%d" % t), "rk%d" % t, a), (R("qw%d" % t), "rw%d" % t, a)]
+    F["issue"](come)

@@ -5,40 +5,27 @@ P, V, C, PH, I, CAP, RO = 3072, 1152, 512, 3, 384, 96, 4
 IX = I + CAP
 VX = V + PH * CAP
 W16 = 16 * I
-PC = 64
+PC = 32
+FAR = 4096
+DW = 388
 BIG = float(1 << 23)
+ROUND = 1.5 * 2.0 ** 34
 IN_ORDER = 1e6
 CFG = {
-    "sums": "aaaaaaaa",
-    "search": [[("m", 128), ("m", 128), ("m", 128)]] + [[("m", 192), ("p", 96), ("p", 96)]] * 3,
-    "old": [[("a", 96)] * 4] * 4,
-    "pair": [0, I, I, I], "chain": 0.0, "both": 0.0, "two": [1, 1, 1, 1], "hop2": 0.08, "look": 12, "depth": 20, "muy": [2.0, 2.0, 2.0, 0.0], "mix": (0.0, 0.3, 0.6), "neq": 3,
-    "new": [[("a", 48), ("v", 48)] * 4] + [[("a", 128), ("a", 128), ("v", 32), ("a", 48), ("a", 48)]] * 3,
-    "ask2": ["av", "av", "av", "av"],
-    "bulk": ("GD", "GE", "SD", "SE"),
-    "mu": 2.0, "passes": 3, "hop": 0.15, "gath": 1.56, "kf": "a", "x0": 256, "cut": 288, "stage": "aaa", "signs": [6, 6, 6, 5], "last": 1, "df": "P7", "early": 100.0, "d16": 10.0, "later": 5.0, "end": 2.0, "moves": 3, "deep": 2, "pc": (64, 64), "tries": 0, "jit": 1.0,
+    "search": [[("s", 128), ("r", 128), ("p", 128)]] + [[("r", 128), ("r", 128), ("p", 128)]] * 3, "loads": "dmb",
+    "ask1": [[("s", 96)]] * 3 + [[("s", 32), ("p", 32), ("t", 32)]],
+    "old": [[("a", 96)] * 4] + [[("2", 128)] * 3] * 3,
+    "new": [[("v", 64), ("a", 128), ("v", 64), ("a", 128)]] + [[("a", 128), ("a", 128), ("v", 64), ("a", 64)]] * 3,
+    "ask2": [[("a", 48), ("v", 48)]] * 4,
+    "two": [1, 1, 1, 1], "x0": 256, "cut": 256, "pc": {"s": 32, "r": 64, "p": 64, "t": 32}, "non": "vv", "zs": "v", "late": 1, "wev": "a", "neq": 0, "rest": 50.0, "dbw": 220e3, "dma0": 1.6, "peo": 0.015, "peo2": 0.0, "dear": 0.5, "dtwo": 1, "m1": 20.0, "use": [5.0, 5.0, 5.0, 0.0], "olds": 20.0, "abank": ("P2", "P3", "P1"), "obank": "P0", "signs": [6, 6, 6, 3], "cnt": "a",
+    "bulk": ("GA", "GD", "GE", "SD", "SE"),
+    "hop": 0.2, "hop2": 0.18, "gath": 1.4, "pe": 0.47e-3, "link": 40e3,
+    "chain": 1, "end": 6, "later": 6, "d16": 10.0, "send": 20.0, "send0": 3e6, "mu": 1, "muy": [1, 1, 1, 0],
+    "look": 12, "depth": 0, "passes": 3, "mix": (0.0, 0.3, 0.6), "tries": 200000, "moves": 12, "jit": 1.5, "both": 1.0,
+    "seed": 1, "near": (0.05, 0.05), "pull": 0.001, "fixed": "", "steps": 400, "span": 200,
 }
-
-CFG.update(later=0, chain=1, end=3, depth=0, mu=2, hop=0.1, signs=[6, 6, 6, 6], tries=16000, jit=0.15, moves=4, two=[0, 0, 0, 1], both=0.8)
-CFG["search"] = [[("m", 256), ("m", 128)]] + [[("m", 192), ("p", 192)]] * 3
-CFG["new"] = [[("v", 48), ("a", 96), ("v", 48), ("a", 96), ("v", 48), ("a", 48)]] + [[("a", 128), ("a", 96), ("v", 96), ("a", 64)]] * 3
-CFG["relay"] = [("m", 1), ("m", 2), ("m", 3)]
-CFG.update(two=[0, 0, 0, 0], hop2=0.1, link=40e3, send=20.0)
-CFG.update(pe=0.47e-3, two=[1, 1, 1, 1], both=0.0, hop=0.2, hop2=0.18, gath=1.4, mu=1, muy=[1, 1, 1, 0])
-CFG.update(two=[0, 0, 0, 1], both=0.8, cut=224)
-CFG["search"] = [[("m", 256), ("m", 128)]] + [[("m", 128), ("p", 128), ("p", 128)]] * 3
-CFG["new"] = CFG["new"][:1] + [[("a", 128), ("a", 96), ("v", 64), ("a", 96)]] * 3
-CFG["relay"] = [("m", t) for t in range(RO)]
-CFG.update(w1=1, send0=3e6, x0=256, later=3, pc=(32, 64), end=6, tries=25000)
-CFG["old"] = CFG["old"][:1] + [[("a", 128)] * 3] * 3
-CFG["search"][0] = [("m", 192), ("m", 192)]
-CFG["new"][0] = [("v", 64), ("a", 96), ("v", 64), ("a", 96), ("a", 64)]
-CFG.update(w1=0, kf="v", cut=256, both=1.0)
-CFG["new"] = CFG["new"][:1] + [[("a", 128), ("a", 128), ("v", 80), ("a", 48)]] * 3
-CFG["new"][0] = [("v", 96), ("a", 128), ("v", 64), ("a", 96)]
-CFG.update(later=6, tries=25000)
 SCRATCH = {}
-VIEW = {"idb": ("idw", 16), "idf": ("idfw", 8), "blk": ("blkw", 0)}
+VIEW = {"idb": ("idw", 16), "blk": ("blkw", 0)}
 WHOLE = ["pi", "ni", "nmi", "nz"]
 SMALL = ["pm", "pw", "cb", "cn", "a2", "acc", "mg", "cnt", "a8"]
 
@@ -48,18 +35,17 @@ def _sb(dtype, **kw):
         SCRATCH[n] = ("sbuf", [128, w], dtype)
 
 
-_sb("int32", bas_i=V, der_i=V, use_i=C, whole=8 * len(WHOLE), clsi=96, zi=96, mi=24, Ea=IX, E2=CAP)
-_sb("uint16", cls=96, zof=96, u16=I, d16=V, use16=C, e16=I, m16=24, s16=8, sv16=8, n16=8, uq16=CAP, e216=CAP)
-_sb("float32", Bf=VX, Dv=V, W=V, USE=C, LX=V, VR=I, onef=160, idfw=160, selr=144, wlo=144, whi=144, oalln=128,
-    idfn=128, idk=128, small=8 * len(SMALL), i8=96, amask=I, KT=I, KS=I, KF=I, SA=C, LXg=I, UQ=IX,
-    UQs=CAP, KT2=CAP, KS2=CAP, Bs=CAP, XD=I, W1=IX)
-_sb("float16", U=I, U2=CAP, mh=32)
-_sb("bfloat16", sw0=160, sw1=160, idw=160, blkw=144, idkn=128, idK=128, idKn=128)
-_sb("uint16", z16=8)
-_sb("bfloat16", morc=P, dxs=CAP, meas=VX, morph=8 * IX, oneb=IX, sel1=144, selp=144, selm=144, selk=144, selz=144, blkn=128, blk2n=128,
-    blkp=128, tri=128, cst=128, idn=128, idbig=128, dg=400, rmask=2048, rmask8=1024, Z=2048, EQ=I, GD=W16, GE=W16,
-    SD=W16, SE=W16, AD=IX, AE=I, non=IX, cum=IX, junk=800, old=IX, gx=I, NEQ=V, GQ=16 * CAP, RQ=16 * CAP, SQ=16 * CAP, MM2=CAP,
-    AD2=CAP, adb=CAP, x0=W16, x1=W16)
+_sb("int32", bas_i=V, der_i=V, use_i=C, whole=8 * len(WHOLE), clsi=96, zi=96, Ea=IX, E2=CAP)
+_sb("float32", mi=32)
+_sb("uint16", cls=96, u16=I, d16=RO * DW, e16=I, m16=24, s16=8, sv16=8, n16=8, uq16=CAP, e216=CAP, z16=8, zw=24)
+_sb("float32", Bf=VX, Dv=VX, W=V, USE=C, onef=144, idf=128, selr=144, wlo=128, whi=128, oalln=128,
+    small=8 * len(SMALL), i8=96, amask=I, KT=I, KS=I, LXg=I, UQ=IX, KT2=CAP, KS2=CAP, Bs=CAP, XD=I, W1=400)
+_sb("float16", U=I, U2=CAP, mh=32, CN=1200, m1=72)
+_sb("bfloat16", sw0=160, sw1=160, idw=160, blkw=144, idK=128, idKn=128, zer=128, idK2=128, tlo=128, thi=128, cyc=384, VR=2 * I)
+_sb("bfloat16", morc=P, dxs=CAP, meas=VX, morph=P + FAR, oneb=IX, sel1=144, selm=144, selk=144, selp=144, seln=144, selz=144,
+    selo=144, blkn=128, blk2n=128, tri=128, trin=128, cst=128, cs2=128, idn=128, idbig=128, dg=400, rmask=2048, rmask8=1040,
+    Z=16 * CAP, EQ=I, GA=W16 + 16, GD=8 * I + 16, SD=W16 + 16, GE=W16, SE=W16, AD=IX, AE=I, non=IX, cum=IX, junk=2 * IX, NEQ=V,
+    GQ=16 * CAP, RQ=16 * CAP, SQ=16 * CAP, MM2=CAP, AD2=CAP, adb=CAP, x0=W16, x1=W16)
 SCRATCH["b15i"] = ("sbuf", [8, V], "int32")
 SCRATCH["b15"] = ("sbuf", [8, I], "float16")
 SCRATCH["sel8"] = ("sbuf", [8, 144], "bfloat16")
@@ -70,7 +56,7 @@ for _t in range(RO):
 for _t in range(8):
     SCRATCH["P%d" % _t] = ("psum", [128, 512], "float32")
 SEMAPHORES = (["q_v", "q_a", "q_t", "q_g"] + ["d%d" % k for k in range(16)] + ["l%d" % k for k in range(16)]
-              + ["r%s%d" % (a, k) for a in "mkwp" for k in range(RO)])
+              + ["r%s%d" % (a, k) for a in "mkw" for k in range(RO)])
 CYC = 0.83e-3
 WIDE = {"int32": 4, "float32": 4, "bfloat16": 2, "uint16": 2, "float16": 2}
 
@@ -107,6 +93,312 @@ def clash(q, a, p, b):
     return (w or w2) and lo < h2 and l2 < hi
 
 
+def improve(order, need, pred, succ, c0, c1, lat, que):
+    n, both = len(order), CFG["both"]
+    give = [[] for _ in order]
+    for i in range(n):
+        for p, d in need[i]:
+            give[p].append((i, d))
+    pos, up, down = [0] * n + [n], [n] * (n + 1), [n] * (n + 1)
+    e0, e1, t0, t1 = ([0.0] * (n + 1) for _ in range(4))
+
+    def ahead(k, hi, stop, log):
+        while k <= hi and k < stop:
+            i = order[k]
+            k += 1
+            a, b = e0[up[i]], e1[up[i]]
+            for p, d in need[i]:
+                if e0[p] + d > a:
+                    a = e0[p] + d
+                if e1[p] + d > b:
+                    b = e1[p] + d
+            a += c0[i]
+            b += c1[i]
+            if a != e0[i] or b != e1[i]:
+                log.append((i, e0[i], e1[i]))
+                e0[i], e1[i] = a, b
+                if hi < stop:
+                    if pos[down[i]] > hi:
+                        hi = pos[down[i]]
+                    for s, d in give[i]:
+                        if pos[s] > hi:
+                            hi = pos[s]
+
+    def back(lo, k, stop):
+        while k >= lo and k >= stop:
+            i = order[k]
+            k -= 1
+            a, b = t0[down[i]], t1[down[i]]
+            for s, d in give[i] or ((n, lat[i]),):
+                if t0[s] + d > a:
+                    a = t0[s] + d
+                if t1[s] + d > b:
+                    b = t1[s] + d
+            a += c0[i]
+            b += c1[i]
+            if a != t0[i] or b != t1[i]:
+                t0[i], t1[i] = a, b
+                if lo > stop:
+                    if up[i] < n and pos[up[i]] < lo:
+                        lo = pos[up[i]]
+                    for p, d in need[i]:
+                        if pos[p] < lo:
+                            lo = pos[p]
+
+    def place(lo, part, before, behind):
+        last = dict(before)
+        for k, i in enumerate(part):
+            order[lo + k], pos[i], up[i] = i, lo + k, last[que[i]]
+            down[up[i]] = i
+            last[que[i]] = i
+        for q, i in last.items():
+            down[i] = behind[q]
+            up[behind[q]] = i
+        down[n] = up[n] = n
+
+    ends = {q: n for q in que}
+    keep, x, steps = (1e9, None), CFG["seed"], CFG["steps"]
+    for step in range(steps + 1):
+        place(0, list(order), ends, ends)
+        ahead(0, n, n, [])
+        order.sort(key=lambda i: e0[i] - c0[i] + e1[i] - c1[i])
+        place(0, list(order), ends, ends)
+        back(0, n - 1, 0)
+        top = [max(t0), max(t1)]
+        if top[0] + both * top[1] < keep[0]:
+            keep = (top[0] + both * top[1], list(order))
+        if step == steps:
+            return keep[1], keep[0]
+        x = (x * 1103515245 + 12345) % 2 ** 31
+        first = max(0, (x >> 8) % (n + CFG["span"] // 2) - CFG["span"] // 2)
+        stop = min(n, first + CFG["span"])
+        out, by = [], [0.0, 0.0]
+        for i in order[:stop]:
+            far = [(s, d) for s, d in give[i] or ((n, lat[i]),) if pos[s] >= stop]
+            if pos[i] < first and pos[down[i]] >= stop:
+                far.append((down[i], 0.0))
+            if far:
+                u, v = max(d + t0[s] for s, d in far), max(d + t1[s] for s, d in far)
+                if pos[i] < first:
+                    by = [max(by[0], e0[i] + u), max(by[1], e1[i] + v)]
+                else:
+                    out.append((i, u, v))
+        nxt = {que[i]: i for i in reversed(order[stop:])}
+        heat, k, misses = CFG["jit"] * (1 - step / steps), 0, 0
+        while k < CFG["tries"] // steps and misses < 20000:
+            x = (x * 1103515245 + 12345) % 2 ** 31
+            b = order[first + (x >> 8) % (stop - first)]
+            a = up[b]
+            e, t, c, m = (e0, t0, c0, 0) if x & 128 else (e1, t1, c1, 1)
+            if a == n or pos[a] < first or a in pred[b] or e[a] + c[b] < e[b] - 1e-9 or e[b] - c[b] + t[b] < top[m] - CFG["near"][x >> 5 & 1]:
+                misses += 1
+                continue
+            k += 1
+            x = (x * 1103515245 + 12345) % 2 ** 31
+            for _ in range((x >> 8) % CFG["moves"]):
+                if x & 64 and first <= pos[up[a]] < n:
+                    a = up[a]
+                elif not x & 64 and pos[down[b]] < stop:
+                    b = down[b]
+            lo, hi = pos[a], pos[b]
+            old = order[lo:hi + 1]
+            part, seen, link = ({b}, set(), succ) if x & 64 else ({a}, set(), pred)
+            for i in old[-2::-1] if x & 64 else old[1:]:
+                if que[i] in seen or not part.isdisjoint(link[i]):
+                    if que[i] == que[a]:
+                        break
+                    part.add(i)
+                    seen.add(que[i])
+            else:
+                i = n
+            if i < n:
+                continue
+            new = [j for j in old if (j in part) == bool(x & 64)] + [j for j in old if (j in part) != bool(x & 64)]
+            before, behind = {}, {}
+            for i in old:
+                if que[i] not in before:
+                    before[que[i]] = up[i]
+                behind[que[i]] = down[i]
+            place(lo, new, before, behind)
+            log, room = [], top[0] + both * top[1] + heat * (x % 1024) / 1024
+            ahead(lo, hi, hi + 1, log)
+            u = v = 0.0
+            far, near = hi, lo
+            for i in new:
+                for s, d in give[i] + [(down[i], 0.0)]:
+                    if pos[s] > hi:
+                        if e0[i] + d + t0[s] > u:
+                            u = e0[i] + d + t0[s]
+                        if e1[i] + d + t1[s] > v:
+                            v = e1[i] + d + t1[s]
+                        if pos[s] > far:
+                            far = pos[s]
+            if u + both * v <= room:
+                ahead(hi + 1, far, stop, log)
+                u = max([by[0]] + [e0[i] + a for i, a, b in out] + [e0[up[i]] + t0[i] for i in nxt.values()])
+                v = max([by[1]] + [e1[i] + b for i, a, b in out] + [e1[up[i]] + t1[i] for i in nxt.values()])
+                if u + both * v + CFG["pull"] * sum(e0[i] - a + e1[i] - b for i, a, b in log) <= room:
+                    top = [u, v]
+                    back(min([pos[p] for i in new for p, d in need[i]] + [pos[j] for j in before.values()] + [lo]), hi, first)
+                    continue
+            for i, a, b in reversed(log):
+                e0[i], e1[i] = a, b
+            place(lo, old, before, behind)
+
+
+def improve_old(order, need, pred, succ, c0, c1, lat, que):
+    n, both = len(order), CFG["both"]
+    give = [[] for _ in order]
+    for i in range(n):
+        for p, d in need[i]:
+            give[p].append((i, d))
+    pos, up, down, last = [0] * n, [n] * (n + 1), [n] * (n + 1), {}
+    for k, i in enumerate(order):
+        pos[i], up[i] = k, last.get(que[i], n)
+        down[up[i]] = i
+        last[que[i]] = i
+    e0, e1, t0, t1 = ([0.0] * (n + 1) for _ in range(4))
+    tips = [i for i in range(n) if not give[i]]
+
+    def ahead(lo, hi, log):
+        for k in range(lo, n):
+            if k > hi:
+                break
+            i = order[k]
+            a, b = e0[up[i]], e1[up[i]]
+            for p, d in need[i]:
+                if e0[p] + d > a:
+                    a = e0[p] + d
+                if e1[p] + d > b:
+                    b = e1[p] + d
+            a, b = a + c0[i], b + c1[i]
+            if a != e0[i] or b != e1[i]:
+                log.append((i, e0[i], e1[i]))
+                e0[i], e1[i] = a, b
+                if hi < n:
+                    if down[i] < n and pos[down[i]] > hi:
+                        hi = pos[down[i]]
+                    for s, d in give[i]:
+                        if pos[s] > hi:
+                            hi = pos[s]
+        return max(e0[i] + lat[i] for i in tips), max(e1[i] + lat[i] for i in tips)
+
+    def back(lo, hi):
+        for k in range(hi, -1, -1):
+            if k < lo:
+                break
+            i = order[k]
+            a, b = max(lat[i], t0[down[i]]), max(lat[i], t1[down[i]])
+            for s, d in give[i]:
+                if t0[s] + d > a:
+                    a = t0[s] + d
+                if t1[s] + d > b:
+                    b = t1[s] + d
+            a, b = a + c0[i], b + c1[i]
+            if a != t0[i] or b != t1[i]:
+                t0[i], t1[i] = a, b
+                if lo > 0:
+                    if up[i] < n and pos[up[i]] < lo:
+                        lo = pos[up[i]]
+                    for p, d in need[i]:
+                        if pos[p] < lo:
+                            lo = pos[p]
+
+    def place(lo, part, before, behind):
+        last = dict(before)
+        for k, i in enumerate(part):
+            order[lo + k], pos[i], up[i] = i, lo + k, last[que[i]]
+            down[up[i]] = i
+            last[que[i]] = i
+        for q, i in last.items():
+            down[i] = behind[q]
+            up[behind[q]] = i
+        down[n] = up[n] = n
+
+    top = ahead(0, n, [])
+    down[n] = n
+    back(0, n - 1)
+    keep, x, k, tries = (top[0] + both * top[1], list(order)), CFG["seed"], 0, CFG["tries"]
+    while k < tries:
+        x = (x * 1103515245 + 12345) % 2 ** 31
+        b = (x >> 8) % n
+        a = up[b]
+        e, t, c, m = (e0, t0, c0, 0) if x & 128 else (e1, t1, c1, 1)
+        if a == n or que[b] in CFG["fixed"] or a in pred[b] or e[a] + c[b] < e[b] - 1e-9 or e[b] - c[b] + t[b] < top[m] - CFG["near"][x >> 5 & 1]:
+            continue
+        k += 1
+        x = (x * 1103515245 + 12345) % 2 ** 31
+        for _ in range((x >> 8) % CFG["moves"]):
+            if x & 64 and up[a] < n:
+                a = up[a]
+            elif not x & 64 and down[b] < n:
+                b = down[b]
+        lo, hi = pos[a], pos[b]
+        old = order[lo:hi + 1]
+        q = que[a]
+        if x & 64:
+            part, seen = {b}, set()
+            for i in reversed(old[:-1]):
+                if que[i] in seen or not part.isdisjoint(succ[i]):
+                    if que[i] == q:
+                        break
+                    part.add(i)
+                    seen.add(que[i])
+            else:
+                i = n
+            new = [j for j in old if j in part] + [j for j in old if j not in part]
+        else:
+            part, seen = {a}, set()
+            for i in old[1:]:
+                if que[i] in seen or not part.isdisjoint(pred[i]):
+                    if que[i] == q:
+                        break
+                    part.add(i)
+                    seen.add(que[i])
+            else:
+                i = n
+            new = [j for j in old if j not in part] + [j for j in old if j in part]
+        if i < n:
+            continue
+        before, behind = {}, {}
+        for i in old:
+            if que[i] not in before:
+                before[que[i]] = up[i]
+            behind[que[i]] = down[i]
+        place(lo, new, before, behind)
+        log, room = [], top[0] + both * top[1] + CFG["jit"] * (1 - k / tries) * (x % 1024) / 1024
+        u = v = 0.0
+        for i in new:
+            a, b = e0[up[i]], e1[up[i]]
+            for p, d in need[i]:
+                if e0[p] + d > a:
+                    a = e0[p] + d
+                if e1[p] + d > b:
+                    b = e1[p] + d
+            log.append((i, e0[i], e1[i]))
+            a, b = a + c0[i], b + c1[i]
+            e0[i], e1[i] = a, b
+            for s, d in give[i] + [(down[i], 0.0)]:
+                if s < n and pos[s] > hi:
+                    if a + d + t0[s] > u:
+                        u = a + d + t0[s]
+                    if b + d + t1[s] > v:
+                        v = b + d + t1[s]
+        if u + both * v <= room:
+            far = max([pos[s] for i in new for s, d in give[i]] + [pos[j] for j in behind.values() if j < n] + [hi])
+            nxt = ahead(hi + 1, far, log)
+            if nxt[0] + both * nxt[1] + CFG["pull"] * sum(e0[i] - a + e1[i] - b for i, a, b in log) <= room:
+                top = nxt
+                back(min([pos[p] for i in new for p, d in need[i]] + [pos[j] for j in before.values() if j < n] + [lo]), hi)
+                if top[0] + both * top[1] < keep[0]:
+                    keep = (top[0] + both * top[1], list(order))
+                continue
+        for i, a, b in reversed(log):
+            e0[i], e1[i] = a, b
+        place(lo, old, before, behind)
+    return keep[1], keep[0]
+
+
 def plan(calls):
     n = len(calls)
     pred, succ, seen = [set() for _ in calls], [set() for _ in calls], {}
@@ -136,7 +428,7 @@ def plan(calls):
             rank = [r + c["first"] for r, c in zip(rank, calls)]
         left = [len(b) for b in before]
         ready, start, free = [0.0] * n, [0.0] * n, {}
-        pool, cause, last = {}, [None] * n, {}
+        pool = {}
         for i in range(n):
             if not left[i]:
                 pool.setdefault(calls[i]["q"], []).append(i)
@@ -144,17 +436,8 @@ def plan(calls):
         for i in sorted(range(n), key=lambda i: rank[i]):
             ahead.setdefault(calls[i]["q"], []).append(i)
 
-        def soon(b, q, now, limit, depth):
-            r = ready[b]
-            for p in before[b]:
-                if not done[p]:
-                    if calls[p]["q"] == q or not depth:
-                        return limit
-                    r = max(r, max(soon(p, q, now, limit, depth - 1), free.get(calls[p]["q"], 0.0), now) + calls[p]["cost"]
-                            + (gap(b, p) if back else gap(p, b)))
-                    if r >= limit:
-                        return limit
-            return r
+        def soon(b, limit):
+            return ready[b] if all(done[p] for p in before[b]) else limit
 
         todo = n
         while todo:
@@ -164,7 +447,7 @@ def plan(calls):
             while done[ahead[q][-1]]:
                 ahead[q].pop()
             for b in [b for b in ahead[q][-CFG["look"]:] if not done[b] and rank[b] > rank[i]]:
-                r = soon(b, q, now, now + cost, CFG["depth"])
+                r = soon(b, now + cost)
                 if now < r < now + cost:
                     go = max(rank[i] + now, rank[b] + now + cost)
                     hold = max(rank[b] + r, rank[i] + r + calls[b]["cost"]) + calls[b]["mu"] * (r - now)
@@ -176,18 +459,13 @@ def plan(calls):
             at, todo, done[i] = now, todo - 1, True
             pool[q].remove(i)
             start[i] = at
-            if at > ready[i]:
-                cause[i] = last.get(q)
-            last[q] = i
             free[q] = at + calls[i]["cost"]
             for j in after[i]:
-                r = free[q] + (gap(j, i) if back else gap(i, j))
-                if r > ready[j]:
-                    ready[j], cause[j] = r, i
+                ready[j] = max(ready[j], free[q] + (gap(j, i) if back else gap(i, j)))
                 left[j] -= 1
                 if not left[j]:
                     pool.setdefault(calls[j]["q"], []).append(j)
-        return start, max(start[i] + calls[i]["cost"] + calls[i]["lat"] for i in range(n)), cause, [r - c["first"] for r, c in zip(rank, calls)]
+        return start, max(start[i] + calls[i]["cost"] + calls[i]["lat"] for i in range(n))
 
     rank = [0.0] * n
     for i in reversed(range(n)):
@@ -206,12 +484,13 @@ def plan(calls):
     need = [[(p, gap(p, i)) for p in pred[i]] for i in range(n)]
     CFG["hop"] = hop
     cost, lat, que = [c["cost"] for c in calls], [c["lat"] for c in calls], [c["q"] for c in calls]
-
     slow = [c["slow"] for c in calls]
+    PLAN["all"] = (order, need, pred, succ, cost, slow, lat, que, calls)
+    return improve(order, need, pred, succ, cost, slow, lat, que)
 
     def replay(order, lo=0, old=None):
         a = replay1(order, cost, lo, old and old[2])
-        b = replay1(order, slow, lo, old and old[3]) if CFG["both"] else (0.0, [], None)
+        b = replay1(order, slow, lo, old and old[3])
         return a[0] + CFG["both"] * b[0], a[1] + b[1], a[2], b[2]
 
     def replay1(order, cost, lo, old):
@@ -300,13 +579,15 @@ def make(g, T):
 
     def note(q, reads, writes, call, cost, lat=0.0, sem=None, also=(), line=None, busy=0.0):
         if q in "va" and writes and writes[0][0] in CFG["bulk"]:
-            line = q + ("g" if reads[0][0] == "@" else "f")
+            line = q + ("g" if reads and reads[0][0] == "@" else "f")
         after = {lines[line][0]: lines[line][1]} if line in lines else {}
+        if lines.pop("behind", None):
+            after[len(calls) - 1] = 0.0
         if line:
             lines[line] = (len(calls), busy)
         calls.append({"q": q, "acc": accesses(reads, writes), "also": list(also), "call": [call], "cost": cost, "lat": lat, "sem": sem, "after": after,
                       "first": first[0] - (500.0 * len(calls) if first[0] >= IN_ORDER else 0.0), "mu": first[1],
-                      "slow": cost + CYC * sum(f * size(r) for f, rs in ((0.5, reads), (2.0, writes)) for r in rs if r[0] == "@")})
+                      "slow": cost + CYC * sum(f * size(r) for f, rs in ((CFG["dear"], reads), (2.0, writes)) for r in rs if r[0] == "@")})
 
     def price(out, ins, rate=None):
         if out[0] == "@":
@@ -333,8 +614,8 @@ def make(g, T):
     def ms(out, c):
         note("v", [], [out], lambda: g.vector.memset(ap(out), c), price(out, []))
 
-    def scan(out, a, b, op0, op1):
-        note("v", [a, b], [out], lambda: g.vector.tensor_tensor_scan(out=ap(out), data0=ap(a), data1=ap(b), initial=0.0, op0=op0, op1=op1),
+    def scan(out, a, b, op0, op1, initial=0.0):
+        note("v", [a, b], [out], lambda: g.vector.tensor_tensor_scan(out=ap(out), data0=ap(a), data1=ap(b), initial=initial, op0=op0, op1=op1),
              price(out, [a, b]))
 
     def red(out, a):
@@ -356,9 +637,10 @@ def make(g, T):
 
     def mm(out, lhsT, rhs, start, stop):
         note("t", [lhsT, rhs], [out], lambda: g.tensor.matmul(ap(out), ap(lhsT), ap(rhs), start, stop),
-             0.03 + CFG["pe"] * max(64, size(rhs)) * (4 if SCRATCH[rhs[0]][2] == "float32" else 1))
+             CFG["peo"] + CFG["pe"] * max(64, size(rhs)) * (4 if SCRATCH[rhs[0]][2] == "float32" else 1))
+        calls[-1]["slow"] += CFG["peo2"]
         a, b = calls[-2:]
-        if a["q"] == "t" and len(a["call"]) < 4 and [x[0][0] for x in a["acc"][-3:]] == [lhsT[0], rhs[0], out[0]] and a["acc"][-1][0] == out:
+        if a["q"] == "t" and len(a["call"]) < 4 and not start and [x[0][0] for x in a["acc"][-3:]] == [lhsT[0], rhs[0], out[0]]:
             calls.pop()
             for k in ("acc", "call", "cost", "slow"):
                 a[k] += b[k]
@@ -375,14 +657,15 @@ def make(g, T):
     def nbytes(r):
         return SCRATCH[r[0]][1][0] * size(r) * WIDE[SCRATCH[r[0]][2]]
 
-    def dma(q, out, a):
+    def dma(q, out, a, parts=None):
         s = "d%d" % nd[0]
         nd[0] += 1
-        total[s] = 16
-        busy = nbytes(out if isr(out) else a) / 180e3
+        busy = nbytes(out if isr(out) else a) / CFG["dbw"]
+        pairs = parts or [(ap(out) if isr(out) else out, ap(a) if isr(a) else a)]
+        total[s] = 16 * len(pairs)
         note(q, [a] if isr(a) else [], [out] if isr(out) else [],
-             lambda: eng[q].dma_start(out=ap(out) if isr(out) else out, in_=ap(a) if isr(a) else a).then_inc(T.sem[s], 16),
-             0.05, 2.0 + busy, s, (), "dma", busy)
+             lambda: [eng[q].dma_start(out=o, in_=i).then_inc(T.sem[s], 16) for o, i in pairs],
+             0.05 * len(pairs), CFG["dma0"] + busy, s, (), "dma", busy)
 
     def send(topo, dst, mask, out, land, a, rsem, near):
         s = "l%d" % nl[0]
@@ -434,10 +717,7 @@ def make(g, T):
                 g.wait_ge(T.sem[s], n)
 
     return {"tt": tt, "ts": ts, "cp": cp, "ms": ms, "scan": scan, "tr": tr, "act": act, "mm": mm, "iota": iota, "aff": aff,
-            "red": red, "first": first, "dma": dma, "send": send, "issue": issue}
-
-
-HAND_ON = [("rm0", "qm0", "m", 0, 0), (None, "qm0", "m", 1, 0), (None, "qm0", "m", 2, 0), (None, "qm0", "m", 3, 0)]
+            "red": red, "first": first, "behind": lambda: lines.update(behind=1), "dma": dma, "send": send, "issue": issue}
 
 
 def helper(topo, cores, core):
@@ -447,12 +727,11 @@ def helper(topo, cores, core):
 def hand_on(g, core, T, topo, rank):
     home = T.cores[rank]
     n = 0
-    for wait, src, kind, t, lo in HAND_ON:
+    g.wait_ge(T.sem["rm0"], bin(topo.mask(home, core) & ~topo.mask(home, T.cores[rank - 1])).count("1"))
+    for t in range(RO):
         dst = T.cores[(rank - 1 - t) % NR]
-        if wait:
-            g.wait_ge(T.sem[wait], bin(topo.mask(home, core) & ~topo.mask(home, dst)).count("1"))
         rid, pid, _ = topo.addr(dst)
-        g.remote_dma(out_ap=T["q%s%d" % (kind, t)][:, lo:V], in_ap=T[src][:, lo:V], remote_sem=T.sem["r%s%d" % (kind, t)],
+        g.remote_dma(out_ap=T["qm%d" % t][:], in_ap=T["qm0"][:], remote_sem=T.sem["rm%d" % t],
                      local_sem=T.sem["l0"], pid=pid, routing_id=rid, dma_engine_mask=topo.mask(core, dst))
         n += len(topo.engines(core, dst))
     g.wait_ge(T.sem["l0"], n)
@@ -497,28 +776,32 @@ def rank_program(g, core, T, topo):
     def cls(t):
         return ch("cls", t, 24)
 
+    def paired(t):
+        return sum(w for who, w in CFG["old"][t] if who == "2")
+
+    def fold(out, a, mask="rmask"):
+        scan(out, R(mask, 0, size(a)), a, OP.min, OP.max)
+
     def gather(who, out, a):
         if who == "v":
             cp(out, a)
         else:
             act(out, a)
 
-    def stage(out, a, who):
-        if who == "t":
-            mm(out, R("idf"), a, True, True)
-        else:
-            act(out, a)
-
-    first = F["first"]
+    first, late = F["first"], []
     MO, MS = R("morph", 0, P), R("meas", 0, V)
     DV = R("Dv", 0, V)
 
     dma("s", R("b15i"), T.bas[15:128:16, :])
     dma("s", R("use_i"), T.use[:])
     dma("s", MS, T.mea[:])
-    dma("s", R("der_i"), T.der[:])
-    dma("s", R("bas_i"), T.bas[:])
-    dma("s", MO, T.mor[:])
+    for k in CFG["loads"]:
+        if k == "m":
+            dma("s", MO, T.mor[:])
+        if k == "d":
+            dma("s", R("der_i"), T.der[:])
+        if k == "b":
+            dma("s", R("bas_i"), T.bas[:])
 
     first[0] = IN_ORDER
     ms(R("one8"), 1.0)
@@ -530,7 +813,12 @@ def rank_program(g, core, T, topo):
     aff(R("blkw"), R("blkw"), [[16, 9], [0, 16]], OP.is_ge, 15, -1)
     aff(R("sel1"), R("blkw"), [[0, 9], [1, 16]], OP.is_equal, -15, 0)
     aff(R("idw"), R("oneb", 0, 160), [[1, 160]], OP.is_equal, -16, -1)
-    aff(R("idfw"), R("onef"), [[1, 160]], OP.is_equal, -8, -1)
+    first[0] = CFG["rest"]
+    iota(ch("VR", 0, I), [[16 * PH, 24], [0, 16]], 0, 0)
+    iota(ch("VR", 1, I), [[0, 24], [PH, 16]], 0, 0)
+    iota(R("rmask", 1024, 2048), [[0, 64], [256, 16]], 0, 0)
+    aff(R("idf"), R("onef", 0, 128), [[1, 128]], OP.is_equal, 0, -1)
+    aff(R("selr"), R("onef"), [[1, 144]], OP.is_equal, 0, -1)
     aff(R("tri"), R("blk"), [[1, 128]], OP.is_ge, 0, -1)
     for n, pat, base in ((R("cb", 0, 6), [[-16, 6]], 0), (R("cn", 0, 6), [[32, 6]], 400), (R("i8"), [[0, 4], [128, 24]], 0),
                          (R("W1", 0, 400), [[0, 25], [1, 16]], 0)):
@@ -539,20 +827,36 @@ def rank_program(g, core, T, topo):
     def fill(out, c):
         act(out, R("oneb", 0, size(out)), scale=c)
 
-    ms(R("rmask"), 1.0)
-    ms(R("Z"), 0.0)
-    ms(R("rmask", 0, 2048, 16), 0.0)
+    first[0] = IN_ORDER
+    ms(R("rmask", 0, 1024), 256.0)
+    ms(R("Z", 0, 1024), 0.0)
+    ms(R("rmask", 0, 1024, 16), 0.0)
+    fill(R("zer"), 0.0)
+    first[0] = CFG["rest"]
+    for k in range(2):
+        fill(R("Z", 1024 + 256 * k, 1280 + 256 * k), 0.0)
     fill(R("amask"), -2.0 * 2 ** 25)
-    for n in ("Bf", "meas"):
+    for n in ("Bf", "meas", "Dv"):
         fill(R(n, V, VX), 0.0)
-    for n in ("UQ", "AD", "old"):
+    for n in ("UQ", "AD"):
         fill(R(n, I, IX), 0.0)
+    if any(CFG["two"]):
+        for k in range(2):
+            fill(R("morph", P + I * k, P + I * (k + 1)), 0.0)
+    fill(R("GA", 0, 8), 0.0)
+    for m in sorted({paired(t) for t in range(RO)} - {0}):
+        fill(R("GA", 8 * m + 8, 8 * m + 16), 0.0)
     fill(R("non", I, IX), 1.0)
     fill(R("cst"), -32.0)
+    fill(R("cs2"), 0.0)
     fill(R("oalln"), -0.0625)
     ms(R("amask", 0, I, 16), 2.0 * 2 ** 25)
     ms(R("cst", 15, 128, 16), 32.0)
+    ms(R("cs2", 15, 128, 16), -64.0)
     ms(col("mg"), -0.5)
+    ms(col("mg", 1), 128.0)
+    if "a" in CFG["non"]:
+        act(R("adb"), R("oneb", 0, CAP), AF.Sigmoid)
     ts(R("pi", 1, 2), R("pi", 0, 1), 16, None, OP.bitwise_and)
     ts(R("pi", 0, 1), R("pi", 0, 1), 15, None, OP.bitwise_and)
     cp(col("pm"), R("pi", 0, 1))
@@ -564,21 +868,31 @@ def rank_program(g, core, T, topo):
     ts(col("pw", 4), col("pm"), 15.0, None, OP.is_equal)
     ts(col("pw", 5), col("pi", 1), 0.0, None, OP.is_equal)
     ts(col("pw", 6), col("pi", 1), 0.0, None, OP.is_gt)
-    ms(R("rmask8"), 1.0)
-    ms(R("rmask8", 0, 1024, 8), 0.0)
+    ts(col("pm", 1), col("pm"), -1.0, None, OP.mult)
     ts(R("selz"), R("sel1"), col("pw"), None, OP.mult)
     ts(R("i8"), R("i8"), col("pw", 1), None, OP.add)
-    for n, src, f in (("selp", "sel1", 2.0 ** -13), ("selm", "sel1", -4096.0), ("selk", "sel1", 2048.0), ("idbig", "idb", BIG),
-                      ("idn", "idb", -1.0), ("idk", "idf", 2.0 ** 24), ("idkn", "idb", -2.0 ** 24), ("blkp", "blk", 2.0 ** -13),
-                      ("idfn", "idf", -1.0), ("idK", "idb", 4096.0), ("idKn", "idb", -4096.0), ("blkn", "blk", -1.0), ("blk2n", "blk", -2.0), ("tri", "tri", 8192.0)):
+    for n, src, f in (("selm", "sel1", -4096.0), ("selk", "sel1", 2048.0), ("selp", "sel1", 4096.0), ("seln", "sel1", -2048.0),
+                      ("idbig", "idb", BIG), ("idn", "idb", -1.0), ("selo", "sel1", FAR / 16.0),
+                      ("idK", "idb", 4096.0), ("idK2", "idb", 8192.0), ("idKn", "idb", -4096.0), ("blkn", "blk", -1.0),
+                      ("blk2n", "blk", -2.0), ("trin", "tri", -8192.0), ("tri", "tri", 8192.0)):
+        first[0] = IN_ORDER if n in ("selm", "selk", "selp", "seln", "idbig", "idn") else CFG["rest"]
         act(R(n), R(src), scale=f)
-    for n, src, k in (("whi", R("idfw", 0, 144), 2), ("wlo", R("idfw", 0, 144), 3), ("selr", R("idfw", 8, 152), 4),
+    ts(col("pw", 7), col("pw", 4), -8192.0, 4096.0, OP.mult, OP.add)
+    aff(R("thi"), R("trin"), [[0, 8], [1, 16]], OP.is_ge, -8, 0)
+    aff(R("tlo"), R("trin"), [[0, 8], [-1, 16]], OP.is_ge, 7, 0)
+    for n, src, k in (("whi", R("idf"), 2), ("wlo", R("idf"), 3), ("selr", R("selr"), 4),
                       ("sw0", R("idw"), 5), ("sw1", R("idw"), 6)):
         act(R(n), src, AF.Identity, scale=col("pw", k))
-    ts(R("dg"), R("W1", 0, 400), col("pm"), None, OP.not_equal)
-    iota(R("VR"), [[PH, I]], 0, 0)
+    act(R("dg"), R("W1", 0, 400), AF.Abs, bias=col("pm", 1))
     first[0] = 0.0
-    iota(R("LX"), [[2, V // 2], [-1, 2]], 1, 0)
+
+    def turns(t):
+        F["behind"]()
+        aff(ch("cyc", t - 1, 128), R("blk"), [[-16, 8], [-1, 16]], OP.is_equal, t, 1)
+        for k in range(t):
+            aff(R("cyc", 128 * (t - 1) + k, 128 * t, 16), R("oneb", 0, 8), [[-16, 8]], OP.is_equal, t - 16 - k, 1)
+        if t == 1:
+            iota(R("rmask8"), [[0, 130], [256, 8]], 0, 0)
 
     def classes(rounds, rows):
         for t in rounds:
@@ -591,26 +905,8 @@ def rank_program(g, core, T, topo):
     ts(R("b15"), lanes("b15i", 0), -P / 2.0, None, OP.add)
     for x in range(16):
         mm(R("P4", 0, 24), sk("sel8", x), R("b15", x, I, 16), x == 0, x == 15)
-    cp(R("use16"), R("use_i"))
     classes([0, 3], R("P4", 0, 24))
     first[0] = 0.0
-
-    def sums():
-        for k, who in enumerate(CFG["sums"]):
-            gather(who, ch("GD", k, 1024) if k < 6 else ch("SD", k - 6, 1024), at(MS, ch("use16", k, 64)))
-        for lo, hi, b in ((0, 192, R("GD", 0, 3072)), (192, 384, R("GD", 3072, W16)), (384, 448, R("SD", 0, 1024)), (448, C, R("SD", 1024, 2048))):
-            for j in range(16):
-                mm(R("P3", lo, hi), sk("selp", j), R(b[0], b[1] + j, b[2], 16), j == 0, j == 15)
-        act(R("SA"), R("P3"), scale=2.0 ** 24)
-        tt(R("USE"), R("P3"), R("use_i"), OP.add)
-
-    def partners():
-        for k in range(PH):
-            for y in range(2):
-                o = R("P2", y, I, 2)
-                mm(o, R("idf"), R("LX", I * k + y, I * k + I, 2), True, False)
-                mm(o, R("blkp"), R("meas", I * k + 1 - y, I * k + I, 2), False, True)
-            act(ch("LX", k, I), R("P2", 0, I))
 
     def spread(t):
         ph, n = t % PH, I
@@ -619,33 +915,32 @@ def rank_program(g, core, T, topo):
             b = min(a + PC, m)
             z = 16 * PC * (a // PC % 2)
             cp(R("Z", z, z + 16 * (b - a), 16), lanes("meas", ph, a, b))
-            scan(R("x0", 16 * a, 16 * b), R("rmask", 0, 16 * (b - a)), R("Z", z, z + 16 * (b - a)), OP.mult, OP.add)
+            fold(R("x0", 16 * a, 16 * b), R("Z", z, z + 16 * (b - a)))
         first[0] = 0.0 if t else IN_ORDER
+        if t == 0:
+            n = sum(w for who, w in CFG["search"][0] if who != "p")
         for j in range(16 if m < n else 0):
             aff(R("x%d" % (t % 2), 16 * m + j, 16 * n, 16), lanes("meas", ph, m, n), [[0, n - m]], OP.is_ge, 0, 0)
         first[0] = 0.0
 
     def tables():
         for k in range(PH):
-            cp(lanes("Dv", k), lanes("der_i", k))
-            cp(lanes("Bf", k), lanes("bas_i", k))
+            cp(ch("Bf", k, I), ch("bas_i", k, I))
         for k in range(PH):
-            p = R("P%d" % (5 + k), 0, I)
+            p = R("P%d" % (5, 6, 3)[k], 0, I)
             if k < CFG["neq"]:
-                tt(ch("NEQ", k, I), ch("der_i", k, I), ch("bas_i", k, I), OP.not_equal)
+                mm(p, R("idf"), ch("Bf", k, I), True, True)
+                tt(ch("NEQ", k, I), p, ch("der_i", k, I), OP.not_equal)
             else:
-                mm(p, R("idf"), ch("Dv", k, I), True, False)
-                mm(p, R("idfn"), ch("Bf", k, I), False, True)
-                ts(ch("NEQ", k, I), p, 0.0, None, OP.not_equal)
+                tt(ch("NEQ", k, I), ch("der_i", k, I), ch("bas_i", k, I), OP.not_equal)
             mm(p, R("cst"), R("oneb", 0, I), True, False)
             mm(p, R("tri"), ch("NEQ", k, I), False, True)
             tt(ch("W", k, I), p, ch("der_i", k, I), OP.add)
 
-    def later():
-        for ph in (1, 2):
-            for x in range(16):
-                mm(ch("P1", ph, 24), sk("selr", x), R("Bf", 3 * x + ph, V, 48), x == 0, x == 15)
-            classes([ph], ch("P1", ph, 24))
+    def later(ph):
+        for x in range(16):
+            mm(ch("P4", 18 + ph, 24), sk("selr", x), R("Bf", 3 * x + ph, V, 48), x == 0, x == 15)
+        classes([ph], ch("P4", 18 + ph, 24))
 
     def targets():
         for ph in range(PH):
@@ -654,236 +949,315 @@ def rank_program(g, core, T, topo):
         for t in range(RO):
             ts(ch("zi", t, 24), ch("P4", 3 + t % PH, 24), float(t), None, OP.add)
         ts(R("zi"), R("zi"), 7, None, OP.bitwise_and)
-        ts(R("i8", 84, 96), R("i8", 84, 96), -4.0 * I, None, OP.add)
         tt(R("i8"), R("i8"), R("zi"), OP.add)
-        cp(R("zof"), R("i8"))
 
     def winners(keys, kt, ks, n, out, li, lh, lst):
-        tr(kt, keys)
-        scan(ks, R("amask", 0, n), kt, OP.max, OP.min)
-        cp(li, R(ks[0], 15, n, 16))
-        ts(li, li, 2047, None, OP.bitwise_and)
-        cp(lh, li)
+        for key, lo, hi in keys:
+            tr(R(kt, lo, hi), key)
+        scan(R(ks), R("amask", 0, n), R(kt), OP.max, OP.min)
+        ts(li, R(ks, 15, n, 16), ROUND, ROUND, OP.add, OP.subtract)
+        tt(lh, R(ks, 15, n, 16), li, OP.subtract)
         for y in range(2):
             for h in range(2):
                 mm(R(out[0], out[1] + y, out[2], 2), R("sw%d" % y, 16 - 16 * (h - y), 144 - 16 * (h - y)), R(lh[0], lh[1] + h, lh[2], 2), h == 0, h == 1)
-        cp(lst, out)
+        ts(lst, out, V / 2.0, None, OP.add)
 
-    def entry(out, kf, u, stop):
-        mm(out, R("idk"), kf, True, False)
-        mm(out, R("idkn"), u, False, False)
-        mm(out, R("idb"), u, False, stop)
+    def sums(key, lo, hi, terms, stop):
+        for k, (s, buf) in enumerate(terms):
+            for j in range(16):
+                mm(key, sk(s, j), R(buf, 16 * lo + j, 16 * hi, 16), False, stop and j == 15 and k + 1 == len(terms))
 
     def search(t):
         ph = t % PH
-        if t and CFG["kf"] == "a":
-            cp(R("u16"), at(R("USE"), cls(t)))
-            act(R("KF"), at(R("USE"), cls(t)))
-            cp(R("U"), R("u16"))
-        elif t:
-            cp(R("KF"), at(R("USE"), cls(t)))
-            cp(R("u16"), R("KF"))
-            cp(R("U"), R("u16"))
-        else:
-            cp(R("u16"), at(R("use_i"), cls(t)))
-            cp(R("U"), R("u16"))
-            act(R("KF"), at(R("SA"), cls(t)))
-        act(R("P1", 0, I), R("VR"), AF.Identity, bias=float(ph))
-        tt(R("EQ"), R("U"), R("P1", 0, I), OP.is_equal)
-        lo, x = 0, "x%d" % (t % 2)
-        for who, n in CFG["search"][t]:
+        first[0] = CFG["use"][t - 1] if t else 0.0
+        cp(R("u16"), at(R("USE" if t else "use_i"), cls(t)))
+        first[0] = 0.0
+        ts(R("U"), R("u16"), -V / 2.0, None, OP.add)
+        d = R("P5", 0, I)
+        mm(d, R("idb"), R("U"), True, False)
+        for k in range(2):
+            mm(d, R("idn"), ch("VR", k, I), False, k == 1)
+        ts(R("EQ"), d, ph - V / 2.0, None, OP.is_equal)
+        lo, x, keys = 0, "x%d" % (t % 2), []
+        for k, (who, n) in enumerate(CFG["search"][t]):
             hi = lo + n
-            pc = CFG["pc"][who == "p"] if t else PC
+            pc = CFG["pc"][who]
             cuts = [(a, min(a + pc, hi)) for a in range(lo, hi, pc)]
+            key = R(("P0", "P7", "P1")[k % 3], lo, hi)
+            keys.append((key, lo, hi))
+            mm(key, R("idb"), R("U", lo, hi), True, False)
             if who == "p":
                 for a, b in cuts:
                     act(R("GE", 16 * a, 16 * b), at(MS, R("u16", a, b)))
                 for a in range(16 * lo, 16 * hi, 512):
-                    bank = R("P%d" % (2 + a // 512 % 2))
-                    mm(bank, R("idb"), R(x, a, a + 512), True, False)
+                    bank = R("P%d" % ((2 if t else 3) + a // 512 % 2 * (1 if t else 3)))
+                    if t:
+                        mm(bank, R("idb"), R(x, a, a + 512), True, False)
+                    else:
+                        mm(bank, R("zer"), R("rmask", 0, 512), True, False)
+                        for j in range(16):
+                            mm(R(bank[0], j, 512, 16), R("idb"), lanes("meas", ph, a // 16, a // 16 + 32), False, False)
                     mm(bank, R("idn"), R("GE", a, a + 512), False, True)
                     act(R("SE", a, a + 512), bank, AF.Abs)
-                sums = [("selk", j, R("SE", 16 * lo + j, 16 * hi, 16)) for j in range(16)]
+                terms = [("selk", "SE")]
+            elif who == "r":
+                for a, b in cuts:
+                    act(R("GE", 16 * a, 16 * b), at(MS, R("u16", a, b)))
+                sums(key, lo, hi, [("selk", "GE")], False)
+                head = R("GE", 16 * lo, 16 * hi, 16)
+                tt(head, head, lanes("meas", ph, lo, hi), OP.min)
+                for a, b in cuts:
+                    scan(R("SE", 16 * a, 16 * b), R(x, 16 * a, 16 * b), R("GE", 16 * a, 16 * b), OP.max, OP.min)
+                terms = [("selm", "SE")]
+            elif who == "t":
+                for a, b in cuts:
+                    tt(R("GE", 16 * a, 16 * b), at(MS, R("u16", a, b)), R(x, 16 * a, 16 * b), OP.subtract)
+                    act(R("SE", 16 * a, 16 * b), R("GE", 16 * a, 16 * b), AF.Abs)
+                terms = [("selk", "SE")]
             else:
                 for a, b in cuts:
-                    tt(R("GE", 16 * a, 16 * b), at(MS, R("u16", a, b)), R(x, 16 * a, 16 * b), OP.min)
-                sums = [("selm", j, R("GE", 16 * lo + j, 16 * hi, 16)) for j in range(16)]
-            key = R("P0", lo, hi)
-            first = who == "m" and t > 0
-            if first:
-                entry(key, R("KF", lo, hi), R("U", lo, hi), False)
-            for k, (s, j, r) in enumerate(sums):
-                mm(key, sk(s, j), r, k == 0 and not first, False)
-            if not first:
-                mm(key, R("idb"), R("U", lo, hi), False, False)
-            late = who == "m" and t == 0
-            mm(key, R("idbig"), R("EQ", lo, hi), False, not late)
-            if late:
-                mm(key, R("idf"), R("KF", lo, hi), False, True)
+                    tt(R("GE", 16 * a, 16 * b), at(MS, R("u16", a, b)), R(x, 16 * a, 16 * b), OP.subtract)
+                sums(key, lo, hi, [("seln", "GE")], False)
+                for a in range(lo, hi, 64):
+                    b = min(a + 64, hi)
+                    ts(R("SE", 16 * a, 16 * b), R("GE", 16 * a, 16 * b), 0.0, None, OP.max)
+                terms = [("selp", "SE")]
+            mm(key, R("idbig"), R("EQ", lo, hi), False, False)
+            sums(key, lo, hi, terms, True)
             lo = hi
-        winners(R("P0", 0, I), R("KT"), R("KS"), I, R("P0", 400, 424), R("mi"), R("mh", 0, 24), R("m16"))
+        winners(keys, "KT", "KS", I, R("P0", 400, 424), R("mi", 0, 24), R("mh", 0, 24), R("m16"))
+        first[0] = CFG["m1"]
+        ts(R("m1", 24, 48), R("P0", 400, 424), 0.5, V / 4.0 + 1099.75, OP.mult, OP.add)
+        ts(R("m1", 48, 72), R("m1", 24, 48), 4.0, 1.0 - 4400.0 - V / 2.0, OP.mult, OP.add)
+        tt(R("m1", 0, 24), R("m1", 48, 72), R("P0", 400, 424), OP.subtract)
+        first[0] = 0.0
 
-    def old_lists(t, bank):
-        ph, n = t % PH, CFG["pair"][t]
-        if n < I:
-            cp(R("d16", I * ph + n, I * ph + I), lanes("der_i" if t < PH else "Dv", ph, n, I))
-        if n:
-            for k, (a, b) in enumerate(((8, 8), (16, 0))):
-                p = ch(bank, k, n // 2)
-                mm(p, R("whi" if k else "wlo", a, a + 128), R("Dv", ph, PH * n, 2 * PH), True, False)
-                mm(p, R("wlo" if k else "whi", b, b + 128), R("Dv", ph + PH, PH * n, 2 * PH), False, True)
-            cp(R("d16", I * ph, I * ph + n), R(bank, 0, n))
+    def old_lists(t):
+        ph, n, o = t % PH, paired(t) // 2, DW * t
+        if t == 0 and n == 0:
+            cp(R("d16", 2, I + 2), lanes("der_i", 0))
+            return
+        terms = [("wlo", "whi", "idf", "W"), ("tlo", "thi", "trin", "NEQ")]
+        if t in (0, PH):
+            terms = [("wlo", "whi", "idf", "Dv")]
+        if t == 0:
+            cp(lanes("Dv", 0), lanes("der_i", 0))
+        bank = CFG["obank"] if t else "P2"
+        mm(R(bank, 0, I + 2), R("zer"), R("oneb", 0, I + 2), True, False)
+        for k, (lo, hi, both, src) in enumerate(terms):
+            even, odd = R(src, ph, 2 * PH * n, 2 * PH), R(src, ph + PH, 2 * PH * n, 2 * PH)
+            steps = [(1, lo, odd), (0, hi, even), (n + 2, lo, even), (n + 2, hi, odd)] if n else []
+            steps += [(2 * n + 2, both, lanes(src, ph, 2 * n, I))] if 2 * n < I else []
+            for j, (a, s, r) in enumerate(steps):
+                mm(R(bank, a, a + size(r)), R(s), r, False, k + 1 == len(terms) and j + 1 == len(steps))
+        if len(terms) == 1:
+            cp(R("d16", o, o + I + 2), R(bank, 0, I + 2))
+        else:
+            ts(R("d16", o, o + I + 2), R(bank, 0, I + 2), col("pw", 7), P - 1.0, OP.add, OP.min)
 
-    def tops(t, gat, top, lst, parts, pair, bank, out, cuts):
+    def old_tops(t):
+        m, o = paired(t), DW * t
+        n, lo, one = m // 2, 0, m
+        for who, w in CFG["old"][t]:
+            if who == "2":
+                hi = lo + w // 2
+                act(R("GA", 8 + 16 * lo, 8 + 16 * hi), at(MO, R("d16", o + n + 2 + lo, o + n + 2 + hi)))
+                end = hi + (hi == n)
+                b = R("GD", 16 * lo, 16 * end)
+                tt(b, at(MO, R("d16", o + lo, o + end)), R("GA", 16 * lo, 16 * end), OP.max)
+                fold(R("SD", 16 * lo, 16 * end), b, "rmask8")
+                lo = hi
+            else:
+                a = 16 * (one + 1) - 8 * m
+                gather(who, R("GA", a, a + 16 * w), at(MO, R("d16", o + one + 2, o + one + w + 2)))
+                fold(R("SD", a, a + 16 * w), R("GA", a, a + 16 * w))
+                one += w
+        for a, b, top in ((0, m, R("SD", 15, 8 * m + 8, 8)), (m, I, R("SD", 8 * m + 31, 16 * (I + 1) - 8 * m, 16))):
+            if a < b:
+                mm(R("P2", a, b), R("idb"), top, True, False)
+                mm(R("P2", a, b), R("idn"), lanes("meas", t % PH, a, b), False, True)
+        act(R("AD", 0, I), R("P2", 0, I), AF.Abs)
+
+    def new_tops(t, cut):
         lo = 0
-        for who, n in parts:
+        for who, n in CFG["new"][t]:
             hi = lo + n
-            w = 8 if lo < pair else 16
-            a = R(gat, w * lo, w * hi)
-            gather(who, a, at(MO, R(lst[0], lst[1] + w * lo // 16, lst[1] + w * hi // 16)))
-            if lo < pair:
-                b = R(gat, w * (pair + lo), w * (pair + hi))
-                tt(b, at(MO, R(lst[0], lst[1] + (pair + lo) // 2, lst[1] + (pair + hi) // 2)), a, OP.max)
-                a = b
-            scan(R(top, w * lo, w * hi), R("rmask8" if lo < pair else "rmask", 0, w * n), a, OP.mult, OP.max)
+            a = R("GE", 16 * lo, 16 * hi)
+            gather(who, a, at(MO, R("e16", lo, hi)))
+            fold(R("SE", 16 * lo, 16 * hi), a)
             lo = hi
-        for lo, hi in cuts:
-            for a, b, w in ((lo, min(hi, pair), 8), (max(lo, pair), hi, 16)):
-                if a < b:
-                    mm(R(bank, a, b), R("idb"), R(top, w * a + w - 1, w * b, w), True, False)
-                    mm(R(bank, a, b), R("idn"), lanes("meas", t % PH, a, b), False, True)
-            act(R(out, lo, hi), R(bank, lo, hi), AF.Abs)
+        mm(R("P3", 0, cut), R("idb"), R("SE", 15, 16 * cut, 16), True, False)
+        mm(R("P3", 0, cut), R("idn"), lanes("meas", t % PH, 0, cut), False, True)
+        act(R("AE", 0, cut), R("P3", 0, cut), AF.Abs)
+        late.append(lambda: act(R("UQ", 0, I), at(R("qk%d" % t), cls(t))))
+        while late:
+            if CFG["late"]:
+                F["behind"]()
+            late.pop()()
 
-    def blocks(t):
-        return [(0, I)] if t + 1 < RO else [(0, I // 2), (I // 2, I)]
+    def decide(who, out, gain):
+        if who == "v":
+            ts(out, gain, col("mg"), None, OP.is_gt)
+        else:
+            act(out, gain, AF.Sigmoid, bias=col("mg", 1), scale=256.0)
 
     def morphs(t):
-        tt(R("gx"), R("P7", 0, I), R("non", 0, I), OP.mult)
-        for lo, hi in blocks(t):
-            tt(rewritten(t, lo, hi), lanes("meas", t % PH, lo, hi), R("gx", lo, hi), OP.add)
-            if t + 1 == RO and not CFG["two"][t]:
-                dma("a", T.ym[:, 8 * lo:8 * hi], R("morph", 8 * lo, 8 * hi))
-
-    def rewritten(t, lo, hi):
-        return at(R("morph", 8 * lo, 8 * hi), R("zof", 24 * t + lo // 16, 24 * t + hi // 16))
+        o = R("P4", 300, 324)
+        mm(o, R("idf"), ch("i8", t, 24), True, False)
+        for x in range(16):
+            mm(o, sk("selo", x), R("non", x, I, 16), False, x == 15)
+        cp(R("zw"), o)
+        cp(at(R("morph"), R("zw")), lanes("meas", t % PH))
 
     def dist(t):
         ph = t % PH
         half, kd, us = R("P5", 0, I), R("P7", 0, I), R("USE", 37 * t, 37 * t + I)
         first[1] = CFG["mu"]
-        if CFG["two"][t]:
+        if CFG["two"][t] == 1 and t:
             dma("s", R("morc"), MO)
-        tops(t, "GD", "SD", ch("d16", ph, I), CFG["old"][t], CFG["pair"][t], "P2", "AD", [(0, I)])
+        old_tops(t)
+        if CFG["two"][t] == 1 and not t:
+            dma("s", R("morc"), MO)
         ea = R("Ea", 0, I)
         tt(ea, at(R("W"), R("m16")), lanes("Bf", ph), OP.max)
         ts(ea, ea, 4095, None, OP.bitwise_and)
         cp(R("e16"), ea)
+        if t == 1:
+            F["behind"]()
+            later(2)
+        if t + 1 < RO and CFG["obank"] != "P6":
+            first[0] = CFG["olds"]
+            old_lists(t + 1)
+            first[0] = 0.0
         cut = CFG["cut"]
-        cuts = [(0, cut), (cut, I)][:2 - CFG["last"]]
-        tops(t, "GE", "SE", R("e16"), CFG["new"][t], 0, "P3", "AE", cuts)
-        for lo, hi in cuts:
-            mm(R("P5", lo, hi), R("blkn"), R("AD", lo, hi), True, False)
-            mm(R("P5", lo, hi), R("blk"), R("AE", lo, hi), False, True)
-        if CFG["last"]:
+        new_tops(t, cut)
+        mm(R("P5", 0, cut), R("blkn"), R("AD", 0, cut), True, False)
+        mm(R("P5", 0, cut), R("blk"), R("AE", 0, cut), False, True)
+        if cut < I:
             o, top, x, me = R("P5", cut, I), R("SE", 16 * cut + 15, W16, 16), lanes("meas", ph, cut, I), R("SQ", 0, I - cut)
             tt(me, top, x, OP.min)
             for k, (s, r) in enumerate((("blkn", R("AD", cut, I)), ("blk", x), ("blk", top), ("blk2n", me))):
                 mm(o, R(s), r, k == 0, k == 3)
         non = R("non", 0, I)
         first[0], first[1] = CFG["chain"], CFG["muy"][t]
-        ts(non, half, col("mg"), None, OP.is_gt)
+        decide(CFG["non"][0], non, half)
         scan(R("cum"), R("non"), R("oneb"), OP.add, OP.mult)
+        na = CFG["signs"][t]
+        w = I + 16 * na
         for n in range(6):
-            if n < CFG["signs"][t]:
+            if na == 6:
                 act(ch("junk", n % 2, 400), R("cum", 16 * n, 16 * n + 400), AF.Sign, bias=col("cb", n), accum=col("acc", n))
+            elif n < na:
+                act(R("junk", IX * (n % 2), IX * (n % 2) + w), R("cum", 0, w), AF.Sign, bias=col("cb", n), accum=col("acc", n))
             else:
-                o = ch("RQ", n % 2, 400)
-                ts(o, R("cum", 16 * n, 16 * n + 400), col("cb", n), 0.0, OP.add, OP.is_gt)
-                red(col("acc", n), o)
-        if CFG["signs"][t] < 6:
-            o = R("acc", CFG["signs"][t], 6)
-            ts(o, o, 2.0, -400.0, OP.mult, OP.add)
+                o = ch("RQ", n - na, 400)
+                ts(o, R("cum", 16 * n, 16 * n + 400), col("cb", n), 0.0, OP.add, OP.is_lt)
+                scan(ch("CN", n - na, 400), o, R("oneb", 0, 400), OP.add, OP.mult, 16.0 * n)
         first[0] = 0.0
-        if t + 1 < RO:
-            old_lists(t + 1, "P6")
-        act(R("LXg"), at(R("LX"), R("m16")))
         for p, s in ((kd, "idK"), (R("P6", 0, I), "idKn")):
-            mm(p, R("idf"), R("LXg"), True, False)
-            mm(p, R(s), R("dg", t, t + I), False, False)
+            first[0] = CFG["m1"]
+            mm(p, R(s), R("dg", t, t + I), True, False)
+            for x in range(16):
+                mm(R(p[0], x, I, 16), ch("cyc", t - 1, 128) if t else R("idb"), R("m1", 0, 24), False, False)
+            first[0] = CFG["use"][t]
             mm(p, R(s), non, False, True)
         tt(R("LXg"), kd, us, OP.min)
         tt(us, R("P6", 0, I), R("LXg"), OP.max)
+        first[0] = 0.0
         if t + 1 < RO:
             offer(t + 1, R("qk%d" % (t + 1)), R("USE"), "rk%d" % (t + 1))
         else:
-            cp(R("use_i"), R("USE"))
-            cp(R("USE"), R("use_i"))
             dma("s", T.yu[:], R("USE"))
-        if t + 1 < RO and CFG["w1"]:
-            stage(half, lanes("Bf", ph), CFG["stage"][1])
-            tt(R("NEQ", 0, I), ea, half, OP.not_equal)
-            mm(half, R("cst"), R("oneb", 0, I), True, False)
-            mm(half, R("tri"), R("NEQ", 0, I), False, True)
-            tt(R("W1", 0, I), half, ea, OP.add)
-        for lo, hi in blocks(t):
-            act(R("old", lo, hi), rewritten(t, lo, hi))
-        mm(kd, R("idn"), lanes("meas", ph), True, False)
-        mm(kd, R("idb"), R("old", 0, I), False, True)
-        if CFG["two"][t]:
+        if t + 1 < RO and CFG["obank"] == "P6":
+            old_lists(t + 1)
+        if CFG["two"][t] == 1:
             morphs(t)
-        mm(R("P6", 0, I), R("idf"), lanes("Dv", ph), True, False)
-        mm(R("P6", 0, I), R("idKn"), R("oneb", 0, I), False, False)
+        for k, (s, r) in enumerate((("idf", lanes("W", ph)), ("trin", lanes("NEQ", ph)), ("cs2", R("oneb", 0, I)))):
+            mm(R("P6", 0, I), R(s), r, k == 0, False)
+        if t + 1 == RO and CFG["dtwo"]:
+            mm(R("P6", 0, I), R("idK2"), non, False, True)
+            tt(R("XD"), R("P6", 0, I), ea, OP.max)
+            mm(R("P1", 0, I), R("idKn"), non, True, False)
+            mm(R("P1", 0, I), R("idf"), R("XD"), False, True)
+            act(lanes("Dv", ph), R("P1", 0, I))
 
     def ask(t):
         ph = t % PH
         s6, v6 = R("s16", 0, 6), R("sv16", 0, 6)
         zs = R("Z", 0, 16 * CAP, 16)
-        act(R("UQ", 0, I), at(R("qk%d" % t), cls(t)))
         first[0] = CFG["chain"]
-        tt(R("a2", 0, 6), R("cn", 0, 6), R("acc", 0, 6), OP.subtract)
-        ts(v6, R("a2", 0, 6), 1.5, float(ph), OP.mult, OP.add)
-        ts(s6, R("a2", 0, 6), 0.5, None, OP.mult)
-        cp(zs, at(R("meas"), v6))
+        na = CFG["signs"][t]
+        spots = [(0, na, R("acc", 0, na), -0.5, I / 2.0 + 8 * na), (na, 6, R("CN", 399, 400 * (6 - na), 400), 1.0, 0.0)]
+        if na == 6:
+            tt(R("a2", 0, 6), R("cn", 0, 6), R("acc", 0, 6), OP.subtract)
+            spots[0] = (0, 6, R("a2", 0, 6), 0.5, 0.0)
+        for out, f, c in (("sv16", 3.0, ph), ("s16", 1.0, 0), ("a8", 8.0, 0))[:3 if CFG["two"][t] else 2]:
+            for lo, hi, src, a, b in spots[:2 - (na == 6)]:
+                ts(R(out, lo, hi), src, a * f, b * f + c, OP.mult, OP.add)
+        gather(CFG["zs"], zs, at(R("meas"), v6))
         cp(R("uq16"), at(R("UQ"), s6))
-        act(R("UQs"), at(R("UQ"), s6))
         act(R("Bs"), at(R("Bf"), v6))
         act(R("AD2"), at(R("AD"), s6))
-        for k in range(2):
-            scan(ch("RQ", k, 768), R("rmask", 0, 768), ch("Z", k, 768), OP.mult, OP.add)
-            tt(ch("GQ", k, 768), at(R("qm%d" % t), ch("uq16", k, 48)), ch("RQ", k, 768), OP.min)
-        key = R("P4", 0, CAP)
-        cp(R("U2"), R("uq16"))
-        entry(key, R("UQs"), R("U2"), False)
-        for j in range(16):
-            mm(key, sk("selm", j), R("GQ", j, 16 * CAP, 16), False, j == 15)
-        winners(key, R("KT2"), R("KS2"), CAP, R("P4", 100, 106), R("ni", 0, 6), R("mh", 24, 30), R("n16", 0, 6))
+        ts(R("U2"), R("uq16"), -V / 2.0, None, OP.add)
+        mm(R("P4", 0, CAP), R("idb"), R("U2"), True, False)
+        lo, qm, nb = 0, R("qm%d" % t), 0
+        for k, (who, n) in enumerate(CFG["ask1"][t]):
+            hi = lo + n
+            key, gq = R("P4", lo, hi), R("GQ", 16 * lo, 16 * hi)
+            if who == "p":
+                for a in range(lo, hi, 32):
+                    b, bank = min(a + 32, hi), CFG["abank"][nb]
+                    nb += 1
+                    w = 16 * (b - a)
+                    act(R("GQ", 16 * a, 16 * b), at(qm, R("uq16", a, b)))
+                    mm(R(bank, 0, w), R("zer"), R("rmask", 0, w), True, False)
+                    for j in range(16):
+                        mm(R(bank, j, w, 16), R("idb"), R("Z", 16 * a, 16 * b, 16), False, False)
+                    mm(R(bank, 0, w), R("idn"), R("GQ", 16 * a, 16 * b), False, True)
+                    act(R("SQ", 16 * a, 16 * b), R(bank, 0, w), AF.Abs)
+                terms = [("selk", "SQ")]
+            else:
+                fold(R("RQ", 16 * lo, 16 * hi), R("Z", 16 * lo, 16 * hi))
+                tt(gq, at(qm, R("uq16", lo, hi)), R("RQ", 16 * lo, 16 * hi), OP.subtract)
+                if who == "t":
+                    act(R("SQ", 16 * lo, 16 * hi), gq, AF.Abs)
+                    terms = [("selk", "SQ")]
+                else:
+                    ts(R("SQ", 16 * lo, 16 * hi), gq, 0.0, None, OP.max)
+                    terms = [("seln", "GQ"), ("selp", "SQ")]
+            if [w for w, _ in CFG["ask1"][t][k + 1:k + 2]] == [who]:
+                lo = hi
+                continue
+            lo = sum(m for w, m in CFG["ask1"][t][:min(j for j in range(k + 1) if all(w == who for w, _ in CFG["ask1"][t][j:k + 1]))])
+            key = R("P4", lo, hi)
+            sums(key, lo, hi, terms, hi == CAP)
+            lo = hi
+        winners([(R("P4", 0, CAP), 0, CAP)], "KT2", "KS2", CAP, R("P4", 100, 106), R("mi", 24, 30), R("mh", 24, 30), R("n16", 0, 6))
         tt(R("E2"), at(R("qw%d" % t), R("n16", 0, 6)), R("Bs"), OP.max)
         ts(R("E2"), R("E2"), 4095, None, OP.bitwise_and)
         cp(R("e216"), R("E2"))
-        for k in range(2):
-            gather(CFG["ask2"][t][k], ch("GQ", k, 768), at(R("morc") if CFG["two"][t] else MO, ch("e216", k, 48)))
-            scan(ch("SQ", k, 768), R("rmask", 0, 768), ch("GQ", k, 768), OP.mult, OP.max)
+        lo = 0
+        for who, n in CFG["ask2"][t]:
+            gather(who, R("GQ", 16 * lo, 16 * (lo + n)), at(R("morc") if CFG["two"][t] == 1 else MO, R("e216", lo, lo + n)))
+            fold(R("SQ", 16 * lo, 16 * (lo + n)), R("GQ", 16 * lo, 16 * (lo + n)))
+            lo += n
         first[0] = 0.0
-        if t + 1 < RO and CFG["w1"]:
-            w2 = R("P4", 300, 300 + CAP)
-            tt(R("NEQ", I, IX), R("E2"), R("Bs"), OP.not_equal)
-            mm(w2, R("cst"), R("oneb", 0, CAP), True, False)
-            mm(w2, R("tri"), R("NEQ", I, IX), False, True)
-            tt(R("Bs"), w2, R("E2"), OP.add)
-            cp(at(R("W1"), s6), R("Bs"))
-            mm(R("P5", 0, I), R("idf"), lanes("W", ph), True, False)
-            mm(R("P5", 0, I), R("idfn"), R("W1", 0, I), False, True)
-        cp(at(R("Ea"), s6), R("E2"))
+        if t + 1 == RO and CFG["dtwo"]:
+            cp(R("KT2"), R("E2"))
+            tt(R("Bs"), at(R("Dv"), v6), R("KT2"), OP.subtract)
+        else:
+            cp(at(R("Ea"), s6), R("E2"))
         if CFG["two"][t]:
-            tt(R("dxs"), at(R("old"), s6), zs, OP.subtract)
             z6 = R("P4", 240, 246)
             for x in range(16):
                 mm(z6, sk("selz", x), R("Z", 16 * x, 16 * CAP, 256), x == 0, x == 15)
             ts(R("nz", 0, 6), z6, float(t), None, OP.add)
             ts(R("nz", 0, 6), R("nz", 0, 6), 7, None, OP.bitwise_and)
-            ts(R("a8", 0, 6), R("a2", 0, 6), 4.0, None, OP.mult)
             tt(R("a8", 0, 6), R("a8", 0, 6), R("nz", 0, 6), OP.add)
             cp(R("z16", 0, 6), R("a8", 0, 6))
+            tt(R("dxs"), at(R("morph", 0, 8 * IX), R("z16", 0, 6)), zs, OP.subtract)
+        if CFG["two"][t] == 2:
+            morphs(t)
         first[0] = CFG["chain"]
         top, g2 = R("SQ", 15, 16 * CAP, 16), R("P4", 128, 128 + CAP)
         tt(R("MM2"), top, zs, OP.min)
@@ -891,69 +1265,87 @@ def rank_program(g, core, T, topo):
         mm(g2, R("blk"), zs, False, False)
         mm(g2, R("blk"), top, False, False)
         mm(g2, R("blk2n"), R("MM2"), False, True)
-        ts(R("adb"), g2, col("mg"), None, OP.is_gt)
-        if not CFG["two"][t]:
-            cp(at(R("non"), s6), R("adb"))
+        decide(CFG["non"][1], R("adb"), g2)
         first[0] = 0.0
 
     def change(t):
         ph = t % PH
         non, d, x, dn = R("non", 0, I), lanes("Dv", ph), R("XD"), R("P1", 0, I)
         first[0] = CFG["end"]
+        if t + 1 == RO and CFG["dtwo"]:
+            tt(R("Bs"), R("adb"), R("Bs"), OP.mult)
+            tt(at(R("Dv"), R("sv16", 0, 6)), R("KT2"), R("Bs"), OP.add)
+            dma("s", T.yd[:], DV)
+            tt(R("dxs"), R("adb"), R("dxs"), OP.mult)
+            tt(at(R("morph", 0, 8 * IX), R("z16", 0, 6)), R("Z", 0, 16 * CAP, 16), R("dxs"), OP.add)
+            dma("a", T.ym[:], MO)
+            return
         if CFG["two"][t]:
             tt(R("dxs"), R("adb"), R("dxs"), OP.mult)
-            tt(at(R("morph"), R("z16", 0, 6)), R("Z", 0, 16 * CAP, 16), R("dxs"), OP.add)
-            if t + 1 == RO:
-                dma("a", T.ym[:], MO)
-        else:
+            tt(at(R("morph", 0, 8 * IX), R("z16", 0, 6)), R("Z", 0, 16 * CAP, 16), R("dxs"), OP.add)
+        cp(at(R("non"), R("s16", 0, 6)), R("adb"))
+        if not CFG["two"][t]:
             morphs(t)
-        cp(at(R("non"), R("s16", 0, 6)), R("adb")) if CFG["two"][t] else None
+        if t + 1 == RO:
+            dma("a", T.ym[:], MO)
         first[0] = 0.0
-        for k in range(2):
-            mm(R("P6", 0, I), R("idK"), non, False, k == 1)
+        mm(R("P6", 0, I), R("idK2"), non, False, True)
+        if t + 1 < RO:
+            first[0] = CFG["olds"]
+            mm(R("P5", 0, I), R("idf"), lanes("Bf", ph), True, False)
+            first[0] = 0.0
+            mm(R("P5", 0, I), R("idK"), non, False, True)
         tt(x, R("P6", 0, I), R("Ea", 0, I), OP.max)
+        w = R("P6", 0, I)
+        if t + 1 < RO:
+            tt(lanes("NEQ", ph), R("P5", 0, I), x, OP.not_equal)
         mm(dn, R("idKn"), non, True, False)
         mm(dn, R("idf"), x, False, True)
-        w = R("P5", 0, I)
-        if t + 1 < RO and not CFG["w1"]:
-            tt(R("NEQ", 0, I), dn, lanes("Bf", ph), OP.not_equal)
-        act(d, dn)
+        if t + 1 < RO and CFG["late"]:
+            late.append(lambda: act(d, dn))
+        else:
+            act(d, dn)
         if t + 1 == RO:
             dma("s", T.yd[:], DV)
             return
-        if CFG["w1"]:
-            tt(w, w, non, OP.mult)
-            tt(lanes("W", ph), w, R("W1", 0, I), OP.add)
-        else:
-            for k, (s, r) in enumerate((("cst", R("oneb", 0, I)), ("idKn", non), ("idf", x), ("tri", R("NEQ", 0, I)))):
-                mm(w, R(s), r, k == 0, k == 3)
-            act(lanes("W", ph), w)
+        for k, (s, r) in enumerate((("idf", x), ("cst", R("oneb", 0, I)), ("idKn", non), ("tri", lanes("NEQ", ph)))):
+            mm(w, R(s), r, k == 0, k == 3)
+        gather(CFG["wev"], lanes("W", ph), w)
         offer(t + 1, R("qw%d" % (t + 1)), R("W"), "rw%d" % (t + 1))
-        act(R("junk", 0, I), non, accum=col("cnt"))
+        o = R("P4", 330, 354)
+        for x in range(16):
+            mm(o, sk("sel1", x), R("non", x, I, 16), x == 0, x == 15)
+        if CFG["cnt"] == "a":
+            act(R("junk", 0, 24), o, accum=col("cnt"))
+        else:
+            red(col("cnt"), o)
         mm(R("P4", 400, 401), R("oalln"), col("cnt"), True, True)
         ts(col("nmi"), R("P4", 400, 401), 8.0 * I, None, OP.add)
         ts(col("nmi"), col("nmi"), 127, None, OP.bitwise_and)
-        ts(col("mg"), col("nmi"), -1.0, -0.5, OP.mult, OP.add)
+        if "v" in CFG["non"]:
+            ts(col("mg"), col("nmi"), -1.0, -0.5, OP.mult, OP.add)
+        if "a" in CFG["non"]:
+            ts(col("mg", 1), col("nmi"), 256.0, 128.0, OP.mult, OP.add)
 
     spread(0)
     hand(R("qm0"), [R("qm%d" % t) for t in range(RO)], MS, "rm0")
-    sums()
-    offer(0, R("qk0"), R("USE"), "rk0")
-    tables()
-    first[0] = CFG["d16"]
-    old_lists(0, "P2")
-    first[0] = 0.0
-    offer(0, R("qw0"), R("W"), "rw0")
     search(0)
+    cp(R("USE"), R("use_i"))
+    offer(0, R("qk0"), R("USE"), "rk0")
+    first[0] = CFG["d16"]
+    old_lists(0)
+    first[0] = 0.0
+    tables()
+    offer(0, R("qw0"), R("W"), "rw0")
     first[0] = CFG["later"]
     targets()
-    partners()
-    later()
+    later(1)
     first[0] = 0.0
     for t in range(RO):
         dist(t)
         if t + 1 < RO:
             spread(t + 1)
+            turns(t + 1)
         ask(t)
         if t + 1 < RO:
             search(t + 1)

@@ -1,4 +1,4 @@
-from concourse.mybir import AluOpType as OP, ActivationFunctionType as AF, AxisListType as AX
+from concourse.mybir import AluOpType as OP, ActivationFunctionType as AF
 
 NR = 6
 P, V, C, PH, I, CAP, RO = 3072, 1152, 512, 3, 384, 96, 4
@@ -6,28 +6,33 @@ IX = I + CAP
 VX = V + PH * CAP
 W16 = 16 * I
 PC = 32
-FAR = 4096
+FAR = 3072
 DW = 388
 BIG = float(1 << 23)
-ROUND = 1.5 * 2.0 ** 34
+ROUND = 1.5 * 2.0 ** 23
 IN_ORDER = 1e6
 CFG = {
-    "search": [[("s", 128), ("r", 128), ("p", 128)]] + [[("r", 128), ("r", 128), ("p", 128)]] * 3, "loads": "dmb",
+    "search": [[("s", 128), ("r", 128), ("p", 128)]] + [[("r", 128), ("r", 128), ("p", 128)]] * 3, "loads": "mdb",
     "ask1": [[("s", 96)]] * 3 + [[("s", 32), ("p", 32), ("t", 32)]],
     "old": [[("a", 96)] * 4] + [[("2", 128)] * 3] * 3,
-    "new": [[("v", 64), ("a", 128), ("v", 64), ("a", 128)]] + [[("a", 128), ("a", 128), ("v", 64), ("a", 64)]] * 3,
-    "ask2": [[("a", 48), ("v", 48)]] * 4,
-    "two": [1, 1, 1, 1], "x0": 256, "cut": 256, "pc": {"s": 32, "r": 64, "p": 64, "t": 32}, "non": "vv", "zs": "v", "late": 1, "wev": "a", "neq": 0, "rest": 50.0, "dbw": 220e3, "dma0": 1.6, "peo": 0.015, "peo2": 0.0, "dear": 0.5, "dtwo": 1, "m1": 20.0, "use": [5.0, 5.0, 5.0, 0.0], "olds": 20.0, "abank": ("P2", "P3", "P1"), "obank": "P0", "signs": [6, 6, 6, 3], "cnt": "a",
-    "bulk": ("GA", "GD", "GE", "SD", "SE"),
-    "hop": 0.2, "hop2": 0.18, "gath": 1.4, "pe": 0.47e-3, "link": 40e3,
+    "new": [[("v", 64), ("a", 128), ("v", 64), ("a", 128)]] + [[("a", 96), ("2", 160), ("a", 128)]] * 3,
+    "ask2": [[("a", 26), ("v", 44), ("a", 26)]] * 4,
+    "x0": 256, "cut": 256, "pc": {"s": 32, "r": 64, "p": 64, "t": 32}, "non": "vv", "zs": "v", "late": 1, "wev": "a", "neq": 0,
+    "patch": [0, 0, 0, 2], "bf": "g", "dv": "", "use0": 1, "heads": 1, "xcut": 1, "wlate": 1, "mor": [0, 0, 0, 0],
+    "turned": 1, "kbank": ("P0", "P0", "P7"), "mz": [1, 1, 1, 0], "again": 1, "join": [1, 1, 1, 1], "straight": [704, 704, 704, 704], "rs": 64, "ms": [1, 1, 1, 1], "fs": {}, "wbank": "P5", "ybank": "P3",
+    "rest": 50.0, "dbw": 220e3, "dma0": 1.6, "peo": 0.015, "dear": 0.7, "scat": 4.2, "dsc": -1.7, "m1": 20.0, "use": [5.0, 5.0, 5.0, 0.0], "olds": 20.0,
+    "abank": ("P2", "P3", "P5"), "obank": "P0", "bulk": ("GA", "GD", "GE", "SD", "SE"),
+    "hop": 0.2, "hop2": 0.18, "gath": 1.35, "pe": 0.47e-3, "link": 30e3,
     "chain": 1, "end": 6, "later": 6, "d16": 10.0, "send": 20.0, "send0": 3e6, "mu": 1, "muy": [1, 1, 1, 0],
-    "look": 12, "depth": 0, "passes": 3, "mix": (0.0, 0.3, 0.6), "tries": 200000, "moves": 12, "jit": 1.5, "both": 1.0,
-    "seed": 1, "near": (0.05, 0.05), "pull": 0.001, "fixed": "", "steps": 400, "span": 200,
+    "look": 12, "passes": 3, "mix": (0.0, 0.3, 0.6), "tries": 400000, "moves": 12, "jit": 1.5, "both": 1.0,
+    "seed": 4, "near": (0.05, 0.05), "pull": 0.001, "steps": 800, "span": 100,
 }
 SCRATCH = {}
-VIEW = {"idb": ("idw", 16), "blk": ("blkw", 0)}
-WHOLE = ["pi", "ni", "nmi", "nz"]
-SMALL = ["pm", "pw", "cb", "cn", "a2", "acc", "mg", "cnt", "a8"]
+VIEW = {"idb": ("idw", 16), "blk": ("blkw", 0), "blkn": ("blks", 0), "blk2n": ("blks", 128), "tri": ("tris", 0), "trin": ("tris", 128),
+        "id16n": ("ids", 0), "id12n": ("ids", 128), "wlo": ("ids", 256), "whi": ("ids", 384), "oalln": ("ids", 512), "idf": ("ids", 640)}
+VIEW.update({n: ("idm", 128 * k) for k, n in enumerate(["idK", "idKn", "idK2", "zer", "idn", "idbig", "tlo", "thi", "cst", "cs2", "cstn", "blo", "bhi", "idH"])})
+WHOLE = ["pi"]
+SMALL = ["pm", "pw", "cb", "acc", "mg", "cnt", "r2"]
 
 
 def _sb(dtype, **kw):
@@ -35,28 +40,32 @@ def _sb(dtype, **kw):
         SCRATCH[n] = ("sbuf", [128, w], dtype)
 
 
-_sb("int32", bas_i=V, der_i=V, use_i=C, whole=8 * len(WHOLE), clsi=96, zi=96, Ea=IX, E2=CAP)
-_sb("float32", mi=32)
-_sb("uint16", cls=96, u16=I, d16=RO * DW, e16=I, m16=24, s16=8, sv16=8, n16=8, uq16=CAP, e216=CAP, z16=8, zw=24)
-_sb("float32", Bf=VX, Dv=VX, W=V, USE=C, onef=144, idf=128, selr=144, wlo=128, whi=128, oalln=128,
-    small=8 * len(SMALL), i8=96, amask=I, KT=I, KS=I, LXg=I, UQ=IX, KT2=CAP, KS2=CAP, Bs=CAP, XD=I, W1=400)
-_sb("float16", U=I, U2=CAP, mh=32, CN=1200, m1=72)
-_sb("bfloat16", sw0=160, sw1=160, idw=160, blkw=144, idK=128, idKn=128, zer=128, idK2=128, tlo=128, thi=128, cyc=384, VR=2 * I)
-_sb("bfloat16", morc=P, dxs=CAP, meas=VX, morph=P + FAR, oneb=IX, sel1=144, selm=144, selk=144, selp=144, seln=144, selz=144,
-    selo=144, blkn=128, blk2n=128, tri=128, trin=128, cst=128, cs2=128, idn=128, idbig=128, dg=400, rmask=2048, rmask8=1040,
-    Z=16 * CAP, EQ=I, GA=W16 + 16, GD=8 * I + 16, SD=W16 + 16, GE=W16, SE=W16, AD=IX, AE=I, non=IX, cum=IX, junk=2 * IX, NEQ=V,
-    GQ=16 * CAP, RQ=16 * CAP, SQ=16 * CAP, MM2=CAP, AD2=CAP, adb=CAP, x0=W16, x1=W16)
+_sb("int32", bas_i=VX, der_i=V, use_i=C, whole=8 * len(WHOLE), clsi=96, zi=96, Ea=IX, E2=CAP, qk0=C)
+_sb("float32", mi=64, mix=128)
+_sb("bfloat16", swb=400, dxs=CAP)
+_sb("uint16", cls=96, u16=I, d16=RO * DW, e16=I + 2, m16=24, s16=8, sv16=8, n16=8, uq16=CAP, e216=CAP, z16=16, zw=24)
+_sb("float32", Bf=V, Dv=VX + FAR // 2 * (CFG["patch"] != [0, 0, 0, 2]), W=VX + FAR // 2 if any(CFG["patch"][:3]) else V, USE=C, onef=144, ids=768, selr=144,
+    small=8 * len(SMALL), i8=96, amask=I, KT=I, KS=512, LXg=I, UQ=IX, KT2=CAP, KS2=128, Bs=CAP, W2=CAP, Wd=CAP, XD=I, W1=400)
+_sb("float16", U=I, U2=CAP, mh=64, m1=72, Eh=256)
+_sb("bfloat16", sw0=160, sw1=160, idw=160, blkw=144, idm=1792, cyc=384)
+_sb("float32", VR=I)
+_sb("bfloat16", morc=P, meas=VX, morph=8 * IX + FAR, oneb=IX, sel1=144, selm=144, selk=144, selp=144, seln=144, selz=144,
+    selo=144, blks=256, tris=256, dg=400, rmask=2048, rmask8=1296, tz=24, z2=8,
+    Z=16 * CAP, EQ=I, GA=8 * I + 16, GD=8 * I + 16, SD=8 * I + 16, GE=W16 + 32, SE=W16, AD=IX, AE=I, non=IX, cum=IX, junk=IX, NEQ=V,
+    GQ=16 * CAP, RQ=16 * CAP, SQ=16 * CAP, MM2=CAP, AD2=CAP, NE2=CAP, adb=2 * CAP, x0=W16, x1=W16)
 SCRATCH["b15i"] = ("sbuf", [8, V], "int32")
 SCRATCH["b15"] = ("sbuf", [8, I], "float16")
 SCRATCH["sel8"] = ("sbuf", [8, 144], "bfloat16")
 SCRATCH["one8"] = ("sbuf", [8, 144], "bfloat16")
 for _t in range(RO):
     _sb("bfloat16", **{"qm%d" % _t: V})
-    _sb("float32", **{"qk%d" % _t: C, "qw%d" % _t: V})
+    _sb("float32", **{"qw%d" % _t: V})
+    if _t or not CFG["use0"]:
+        _sb("float32", **{"qk%d" % _t: C})
 for _t in range(8):
     SCRATCH["P%d" % _t] = ("psum", [128, 512], "float32")
-SEMAPHORES = (["q_v", "q_a", "q_t", "q_g"] + ["d%d" % k for k in range(16)] + ["l%d" % k for k in range(16)]
-              + ["r%s%d" % (a, k) for a in "mkw" for k in range(RO)])
+SEMAPHORES = (["q_v", "q_a", "q_t", "q_g"] + ["d%d" % k for k in range(20)] + ["l%d" % k for k in range(16)]
+              + ["r%s%d" % (a, k) for a in "mkwh" for k in range(RO)])
 CYC = 0.83e-3
 WIDE = {"int32": 4, "float32": 4, "bfloat16": 2, "uint16": 2, "float16": 2}
 
@@ -65,7 +74,7 @@ def R(name, lo=0, hi=None, step=1):
     if name in SMALL:
         return ("small", 8 * SMALL.index(name) + lo, 8 * SMALL.index(name) + hi, step)
     if name in VIEW:
-        return (VIEW[name][0], VIEW[name][1], VIEW[name][1] + 128, 1)
+        return (VIEW[name][0], VIEW[name][1] + lo, VIEW[name][1] + 128, step)
     if name in WHOLE:
         return ("whole", 8 * WHOLE.index(name) + lo, 8 * WHOLE.index(name) + hi, step)
     return (name, lo, SCRATCH[name][1][1] if hi is None else hi, step)
@@ -84,8 +93,8 @@ def accesses(reads, writes):
 
 
 def clash(q, a, p, b):
-    (n, lo, hi, st), w = a
-    (_, l2, h2, s2), w2 = b
+    (n, lo, hi, st), w = a[0][:4], a[1]
+    (l2, h2, s2), w2 = b[0][1:4], b[1]
     if SCRATCH[n][0] == "psum" and (q != p or q == "t"):
         return True
     if st > 1 and st == s2 and (lo - l2) % st:
@@ -93,7 +102,7 @@ def clash(q, a, p, b):
     return (w or w2) and lo < h2 and l2 < hi
 
 
-def improve(order, need, pred, succ, c0, c1, lat, que):
+def improve(order, need, pred, succ, c0, c1, lat, que, steps, fixed):
     n, both = len(order), CFG["both"]
     give = [[] for _ in order]
     for i in range(n):
@@ -157,7 +166,7 @@ def improve(order, need, pred, succ, c0, c1, lat, que):
         down[n] = up[n] = n
 
     ends = {q: n for q in que}
-    keep, x, steps = (1e9, None), CFG["seed"], CFG["steps"]
+    keep, x = (1e9, None), CFG["seed"]
     for step in range(steps + 1):
         place(0, list(order), ends, ends)
         ahead(0, n, n, [])
@@ -185,7 +194,7 @@ def improve(order, need, pred, succ, c0, c1, lat, que):
                     out.append((i, u, v))
         nxt = {que[i]: i for i in reversed(order[stop:])}
         heat, k, misses = CFG["jit"] * (1 - step / steps), 0, 0
-        while k < CFG["tries"] // steps and misses < 20000:
+        while k < CFG["tries"] // CFG["steps"] and misses < 20000:
             x = (x * 1103515245 + 12345) % 2 ** 31
             b = order[first + (x >> 8) % (stop - first)]
             a = up[b]
@@ -202,6 +211,8 @@ def improve(order, need, pred, succ, c0, c1, lat, que):
                     b = down[b]
             lo, hi = pos[a], pos[b]
             old = order[lo:hi + 1]
+            if que[a] == "g" and not fixed.isdisjoint(old):
+                continue
             part, seen, link = ({b}, set(), succ) if x & 64 else ({a}, set(), pred)
             for i in old[-2::-1] if x & 64 else old[1:]:
                 if que[i] in seen or not part.isdisjoint(link[i]):
@@ -223,7 +234,7 @@ def improve(order, need, pred, succ, c0, c1, lat, que):
             log, room = [], top[0] + both * top[1] + heat * (x % 1024) / 1024
             ahead(lo, hi, hi + 1, log)
             u = v = 0.0
-            far, near = hi, lo
+            far = hi
             for i in new:
                 for s, d in give[i] + [(down[i], 0.0)]:
                     if pos[s] > hi:
@@ -244,159 +255,6 @@ def improve(order, need, pred, succ, c0, c1, lat, que):
             for i, a, b in reversed(log):
                 e0[i], e1[i] = a, b
             place(lo, old, before, behind)
-
-
-def improve_old(order, need, pred, succ, c0, c1, lat, que):
-    n, both = len(order), CFG["both"]
-    give = [[] for _ in order]
-    for i in range(n):
-        for p, d in need[i]:
-            give[p].append((i, d))
-    pos, up, down, last = [0] * n, [n] * (n + 1), [n] * (n + 1), {}
-    for k, i in enumerate(order):
-        pos[i], up[i] = k, last.get(que[i], n)
-        down[up[i]] = i
-        last[que[i]] = i
-    e0, e1, t0, t1 = ([0.0] * (n + 1) for _ in range(4))
-    tips = [i for i in range(n) if not give[i]]
-
-    def ahead(lo, hi, log):
-        for k in range(lo, n):
-            if k > hi:
-                break
-            i = order[k]
-            a, b = e0[up[i]], e1[up[i]]
-            for p, d in need[i]:
-                if e0[p] + d > a:
-                    a = e0[p] + d
-                if e1[p] + d > b:
-                    b = e1[p] + d
-            a, b = a + c0[i], b + c1[i]
-            if a != e0[i] or b != e1[i]:
-                log.append((i, e0[i], e1[i]))
-                e0[i], e1[i] = a, b
-                if hi < n:
-                    if down[i] < n and pos[down[i]] > hi:
-                        hi = pos[down[i]]
-                    for s, d in give[i]:
-                        if pos[s] > hi:
-                            hi = pos[s]
-        return max(e0[i] + lat[i] for i in tips), max(e1[i] + lat[i] for i in tips)
-
-    def back(lo, hi):
-        for k in range(hi, -1, -1):
-            if k < lo:
-                break
-            i = order[k]
-            a, b = max(lat[i], t0[down[i]]), max(lat[i], t1[down[i]])
-            for s, d in give[i]:
-                if t0[s] + d > a:
-                    a = t0[s] + d
-                if t1[s] + d > b:
-                    b = t1[s] + d
-            a, b = a + c0[i], b + c1[i]
-            if a != t0[i] or b != t1[i]:
-                t0[i], t1[i] = a, b
-                if lo > 0:
-                    if up[i] < n and pos[up[i]] < lo:
-                        lo = pos[up[i]]
-                    for p, d in need[i]:
-                        if pos[p] < lo:
-                            lo = pos[p]
-
-    def place(lo, part, before, behind):
-        last = dict(before)
-        for k, i in enumerate(part):
-            order[lo + k], pos[i], up[i] = i, lo + k, last[que[i]]
-            down[up[i]] = i
-            last[que[i]] = i
-        for q, i in last.items():
-            down[i] = behind[q]
-            up[behind[q]] = i
-        down[n] = up[n] = n
-
-    top = ahead(0, n, [])
-    down[n] = n
-    back(0, n - 1)
-    keep, x, k, tries = (top[0] + both * top[1], list(order)), CFG["seed"], 0, CFG["tries"]
-    while k < tries:
-        x = (x * 1103515245 + 12345) % 2 ** 31
-        b = (x >> 8) % n
-        a = up[b]
-        e, t, c, m = (e0, t0, c0, 0) if x & 128 else (e1, t1, c1, 1)
-        if a == n or que[b] in CFG["fixed"] or a in pred[b] or e[a] + c[b] < e[b] - 1e-9 or e[b] - c[b] + t[b] < top[m] - CFG["near"][x >> 5 & 1]:
-            continue
-        k += 1
-        x = (x * 1103515245 + 12345) % 2 ** 31
-        for _ in range((x >> 8) % CFG["moves"]):
-            if x & 64 and up[a] < n:
-                a = up[a]
-            elif not x & 64 and down[b] < n:
-                b = down[b]
-        lo, hi = pos[a], pos[b]
-        old = order[lo:hi + 1]
-        q = que[a]
-        if x & 64:
-            part, seen = {b}, set()
-            for i in reversed(old[:-1]):
-                if que[i] in seen or not part.isdisjoint(succ[i]):
-                    if que[i] == q:
-                        break
-                    part.add(i)
-                    seen.add(que[i])
-            else:
-                i = n
-            new = [j for j in old if j in part] + [j for j in old if j not in part]
-        else:
-            part, seen = {a}, set()
-            for i in old[1:]:
-                if que[i] in seen or not part.isdisjoint(pred[i]):
-                    if que[i] == q:
-                        break
-                    part.add(i)
-                    seen.add(que[i])
-            else:
-                i = n
-            new = [j for j in old if j not in part] + [j for j in old if j in part]
-        if i < n:
-            continue
-        before, behind = {}, {}
-        for i in old:
-            if que[i] not in before:
-                before[que[i]] = up[i]
-            behind[que[i]] = down[i]
-        place(lo, new, before, behind)
-        log, room = [], top[0] + both * top[1] + CFG["jit"] * (1 - k / tries) * (x % 1024) / 1024
-        u = v = 0.0
-        for i in new:
-            a, b = e0[up[i]], e1[up[i]]
-            for p, d in need[i]:
-                if e0[p] + d > a:
-                    a = e0[p] + d
-                if e1[p] + d > b:
-                    b = e1[p] + d
-            log.append((i, e0[i], e1[i]))
-            a, b = a + c0[i], b + c1[i]
-            e0[i], e1[i] = a, b
-            for s, d in give[i] + [(down[i], 0.0)]:
-                if s < n and pos[s] > hi:
-                    if a + d + t0[s] > u:
-                        u = a + d + t0[s]
-                    if b + d + t1[s] > v:
-                        v = b + d + t1[s]
-        if u + both * v <= room:
-            far = max([pos[s] for i in new for s, d in give[i]] + [pos[j] for j in behind.values() if j < n] + [hi])
-            nxt = ahead(hi + 1, far, log)
-            if nxt[0] + both * nxt[1] + CFG["pull"] * sum(e0[i] - a + e1[i] - b for i, a, b in log) <= room:
-                top = nxt
-                back(min([pos[p] for i in new for p, d in need[i]] + [pos[j] for j in before.values() if j < n] + [lo]), hi)
-                if top[0] + both * top[1] < keep[0]:
-                    keep = (top[0] + both * top[1], list(order))
-                continue
-        for i, a, b in reversed(log):
-            e0[i], e1[i] = a, b
-        place(lo, old, before, behind)
-    return keep[1], keep[0]
 
 
 def plan(calls):
@@ -486,76 +344,24 @@ def plan(calls):
     cost, lat, que = [c["cost"] for c in calls], [c["lat"] for c in calls], [c["q"] for c in calls]
     slow = [c["slow"] for c in calls]
     PLAN["all"] = (order, need, pred, succ, cost, slow, lat, que, calls)
-    return improve(order, need, pred, succ, cost, slow, lat, que)
+    order, top = improve(order, need, pred, succ, cost, slow, lat, que, CFG["steps"] // 3, set())
 
-    def replay(order, lo=0, old=None):
-        a = replay1(order, cost, lo, old and old[2])
-        b = replay1(order, slow, lo, old and old[3])
-        return a[0] + CFG["both"] * b[0], a[1] + b[1], a[2], b[2]
-
-    def replay1(order, cost, lo, old):
-        end, why = (list(old[0]), list(old[1])) if old else ([0.0] * n, [None] * n)
-        last, top, tip = {}, 0.0, None
-        for i in order[max(0, lo - 60):lo]:
-            last[que[i]] = i
-        for i in order[lo:]:
-            j = last.get(que[i])
-            s, w = (0.0, None) if j is None else (end[j], j)
-            for p, d in need[i]:
-                if end[p] + d > s:
-                    s, w = end[p] + d, p
-            end[i], why[i], last[que[i]] = s + cost[i], w, i
-            if end[i] + lat[i] > top:
-                top, tip = end[i] + lat[i], i
-        arcs = []
-        while tip is not None:
-            j = why[tip]
-            if j is not None and j not in pred[tip] and que[j] != "g":
-                arcs.append((j, tip))
-            tip = j
-        return top, arcs, (end, why)
-
-    now = replay(order)
-    keep, x = (now[0], order), 1
-    for k in range(CFG["tries"]):
-        x = (x * 1103515245 + 12345) % 2 ** 31
-        m = (x >> 8) % len(now[1])
-        a, b = now[1][m]
-        x = (x * 1103515245 + 12345) % 2 ** 31
-        for _ in range((x >> 8) % CFG["moves"]):
-            if x & 64 and m + 1 < len(now[1]) and now[1][m + 1][1] == a:
-                m += 1
-                a = now[1][m][0]
-            elif not x & 64 and m and now[1][m - 1][0] == b:
-                m -= 1
-                b = now[1][m][1]
-        lo, hi = order.index(a), order.index(b)
-        if x & 64:
-            part, seen = [b], {que[b]: 0}
-            for i in reversed(order[lo:hi]):
-                if (que[i] in seen and que[i] != que[b]) or any(j in succ[i] for j in part):
-                    part.append(i)
-                    seen[que[i]] = 0
-            if a in part or sum(que[i] == que[b] for i in part) > 1:
-                continue
-            part = set(part)
-            new = order[:lo] + [i for i in order[lo:hi + 1] if i in part] + [i for i in order[lo:hi + 1] if i not in part] + order[hi + 1:]
-        else:
-            part, seen = [a], {que[a]: 0}
-            for i in order[lo + 1:hi + 1]:
-                if (que[i] in seen and que[i] != que[a]) or any(j in pred[i] for j in part):
-                    part.append(i)
-                    seen[que[i]] = 0
-            if b in part or sum(que[i] == que[a] for i in part) > 1:
-                continue
-            part = set(part)
-            new = order[:lo] + [i for i in order[lo:hi + 1] if i not in part] + [i for i in order[lo:hi + 1] if i in part] + order[hi + 1:]
-        nxt = replay(new, lo, now)
-        if nxt[0] <= now[0] + CFG["jit"] * (1 - k / CFG["tries"]) * (x % 1024) / 1024:
-            now, order = nxt, new
-            if now[0] < keep[0]:
-                keep = (now[0], order)
-    return keep[1], keep[0]
+    sends = [i for i in order if que[i] == "g" and calls[i]["sem"]]
+    for i in sends:
+        end, last = {}, {}
+        for j in order:
+            end[j] = last[que[j]] = max([last.get(que[j], 0.0)] + [end[p] + d for p, d in need[j]]) + cost[j]
+        ready, k = max(end[p] + d for p, d in need[i]), order.index(i)
+        to = k
+        while order[k - 1] not in pred[i]:
+            k -= 1
+            if que[order[k]] == "g":
+                if end[order[k]] - cost[order[k]] / 2 < ready:
+                    break
+                to = k
+        order.remove(i)
+        order.insert(to, i)
+    return improve(order, need, pred, succ, cost, slow, lat, que, CFG["steps"] - CFG["steps"] // 3, set(sends))
 
 
 PLAN = {}
@@ -568,8 +374,9 @@ def make(g, T):
     def ap(r):
         if r[0] == "@":
             return ap(r[1]).indirect(ap(r[2]))
-        n, lo, hi, st = r
-        return T[n][:, lo:hi] if st == 1 else T[n][:, lo:hi:st]
+        n, lo, hi, st = r[:4]
+        rows = slice(*r[4:]) if r[4:] else slice(None)
+        return T[n][rows, lo:hi] if st == 1 else T[n][rows, lo:hi:st]
 
     def isr(x):
         return isinstance(x, tuple)
@@ -587,11 +394,11 @@ def make(g, T):
             lines[line] = (len(calls), busy)
         calls.append({"q": q, "acc": accesses(reads, writes), "also": list(also), "call": [call], "cost": cost, "lat": lat, "sem": sem, "after": after,
                       "first": first[0] - (500.0 * len(calls) if first[0] >= IN_ORDER else 0.0), "mu": first[1],
-                      "slow": cost + CYC * sum(f * size(r) for f, rs in ((CFG["dear"], reads), (2.0, writes)) for r in rs if r[0] == "@")})
+                      "slow": cost + CYC * sum(f * size(r) for f, rs in ((CFG["dear"], reads), (CFG["dsc"], writes)) for r in rs if r[0] == "@")})
 
     def price(out, ins, rate=None):
         if out[0] == "@":
-            return 0.05 + 3.8 * CYC * size(out)
+            return 0.05 + CFG["scat"] * CYC * size(out)
         if ins and ins[0][0] == "@":
             return 0.06 + CFG["gath"] * CYC * size(out)
         if rate is None:
@@ -615,16 +422,14 @@ def make(g, T):
         note("v", [], [out], lambda: g.vector.memset(ap(out), c), price(out, []))
 
     def scan(out, a, b, op0, op1, initial=0.0):
-        note("v", [a, b], [out], lambda: g.vector.tensor_tensor_scan(out=ap(out), data0=ap(a), data1=ap(b), initial=initial, op0=op0, op1=op1),
-             price(out, [a, b]))
-
-    def red(out, a):
-        note("v", [a], [out], lambda: g.vector.tensor_reduce(out=ap(out), in_=ap(a), axis=AX.X, op=OP.add), price(a, [], 1.0))
+        s = ap(initial) if isr(initial) else initial
+        note("v", [a, b] + [initial] * isr(initial), [out],
+             lambda: g.vector.tensor_tensor_scan(out=ap(out), data0=ap(a), data1=ap(b), initial=s, op0=op0, op1=op1), price(out, [a, b]))
 
     def tr(out, a):
         note("v", [a], [out], lambda: g.vector.transpose(out=ap(out), in_=ap(a)), price(out, [a]))
 
-    def act(out, a, func=AF.Copy, bias=None, accum=None, scale=None):
+    def act(out, a, func=AF.Copy, bias=None, accum=None, scale=None, more=0.0):
         kw = {}
         if bias is not None:
             kw["bias"] = ap(bias) if isr(bias) else bias
@@ -632,15 +437,16 @@ def make(g, T):
             kw["scale"] = ap(scale) if isr(scale) else scale
         if accum is not None:
             kw["accum_out"] = ap(accum)
+            more += 0.02
         note("a", [a] + [b for b in [bias, scale] if isr(b)], [out] + [b for b in [accum] if b],
-             lambda: g.scalar.activation(out=ap(out), in_=ap(a), func=func, **kw), price(out, [a], 1.0))
+             lambda: g.scalar.activation(out=ap(out), in_=ap(a), func=func, **kw), price(out, [a], 1.0) + more)
 
     def mm(out, lhsT, rhs, start, stop):
         note("t", [lhsT, rhs], [out], lambda: g.tensor.matmul(ap(out), ap(lhsT), ap(rhs), start, stop),
-             CFG["peo"] + CFG["pe"] * max(64, size(rhs)) * (4 if SCRATCH[rhs[0]][2] == "float32" else 1))
-        calls[-1]["slow"] += CFG["peo2"]
+             CFG["peo"] + CFG["pe"] * max(min(64, size(lhsT)), size(rhs)) * (4 if SCRATCH[rhs[0]][2] == "float32" else 1))
         a, b = calls[-2:]
-        if a["q"] == "t" and len(a["call"]) < 4 and not start and [x[0][0] for x in a["acc"][-3:]] == [lhsT[0], rhs[0], out[0]]:
+        same = [x[0][0] for x in a["acc"][-3:]] == [lhsT[0], rhs[0], out[0]] and abs(a["acc"][-3][0][1] - lhsT[1]) < 128
+        if a["q"] == "t" and len(a["call"]) < 4 and not start and same:
             calls.pop()
             for k in ("acc", "call", "cost", "slow"):
                 a[k] += b[k]
@@ -657,15 +463,14 @@ def make(g, T):
     def nbytes(r):
         return SCRATCH[r[0]][1][0] * size(r) * WIDE[SCRATCH[r[0]][2]]
 
-    def dma(q, out, a, parts=None):
+    def dma(q, out, a):
         s = "d%d" % nd[0]
         nd[0] += 1
         busy = nbytes(out if isr(out) else a) / CFG["dbw"]
-        pairs = parts or [(ap(out) if isr(out) else out, ap(a) if isr(a) else a)]
-        total[s] = 16 * len(pairs)
+        total[s] = 16
         note(q, [a] if isr(a) else [], [out] if isr(out) else [],
-             lambda: [eng[q].dma_start(out=o, in_=i).then_inc(T.sem[s], 16) for o, i in pairs],
-             0.05 * len(pairs), CFG["dma0"] + busy, s, (), "dma", busy)
+             lambda: eng[q].dma_start(out=ap(out) if isr(out) else out, in_=ap(a) if isr(a) else a).then_inc(T.sem[s], 16),
+             0.05, CFG["dma0"] + busy, s, (), "dma", busy)
 
     def send(topo, dst, mask, out, land, a, rsem, near):
         s = "l%d" % nl[0]
@@ -676,8 +481,7 @@ def make(g, T):
         first[0] = CFG["send0"] if nl[0] == 1 else CFG["send"]
         note("g", [a], [], lambda: g.remote_dma(out_ap=ap(out), in_ap=ap(a), remote_sem=T.sem[rsem], local_sem=T.sem[s], pid=pid,
                                                 routing_id=rid, dma_engine_mask=mask),
-             0.5 if nl[0] > 1 else 3.5, far + (3.0 + nbytes(a) / 80e3 if near else 0.0), s, [(r, 1) for r in land],
-             "chip" if near else "link", nbytes(a) / (80e3 if near else CFG["link"]))
+             0.5 if nl[0] > 1 else 3.5, far + (3.0 + nbytes(a) / 80e3 if near else 0.0), s, [(r, 1) for r in land])
         first[0] = 0.0
 
     def issue(arrivals):
@@ -717,7 +521,7 @@ def make(g, T):
                 g.wait_ge(T.sem[s], n)
 
     return {"tt": tt, "ts": ts, "cp": cp, "ms": ms, "scan": scan, "tr": tr, "act": act, "mm": mm, "iota": iota, "aff": aff,
-            "red": red, "first": first, "behind": lambda: lines.update(behind=1), "dma": dma, "send": send, "issue": issue}
+            "first": first, "behind": lambda: lines.update(behind=1), "dma": dma, "send": send, "issue": issue}
 
 
 def helper(topo, cores, core):
@@ -726,14 +530,20 @@ def helper(topo, cores, core):
 
 def hand_on(g, core, T, topo, rank):
     home = T.cores[rank]
-    n = 0
-    g.wait_ge(T.sem["rm0"], bin(topo.mask(home, core) & ~topo.mask(home, T.cores[rank - 1])).count("1"))
+    n, near = 0, bin(topo.mask(home, core) & ~topo.mask(home, T.cores[rank - 1])).count("1")
+    g.wait_ge(T.sem["rm0"], near)
     for t in range(RO):
         dst = T.cores[(rank - 1 - t) % NR]
         rid, pid, _ = topo.addr(dst)
         g.remote_dma(out_ap=T["qm%d" % t][:], in_ap=T["qm0"][:], remote_sem=T.sem["rm%d" % t],
                      local_sem=T.sem["l0"], pid=pid, routing_id=rid, dma_engine_mask=topo.mask(core, dst))
         n += len(topo.engines(core, dst))
+        lo = CFG["straight"][t]
+        if lo < V:
+            g.wait_ge(T.sem["rh%d" % t], near)
+            g.remote_dma(out_ap=T["qw%d" % t][:, lo:V], in_ap=T["qw%d" % t][:, lo:V], remote_sem=T.sem["rh%d" % t],
+                         local_sem=T.sem["l0"], pid=pid, routing_id=rid, dma_engine_mask=topo.mask(core, dst))
+            n += len(topo.engines(core, dst))
     g.wait_ge(T.sem["l0"], n)
 
 
@@ -754,8 +564,14 @@ def rank_program(g, core, T, topo):
     def hand(out, lands, a, sem):
         F["send"](topo, aide, topo.mask(core, aide) & ~topo.mask(core, T.cores[rank - 1]), out, lands, a, sem, True)
 
+    def offer_lists(t):
+        lo, out = CFG["straight"][t], "qw%d" % t
+        if lo < V:
+            hand(R(out, lo, V), [R(out, lo, V)], R("W", lo, V), "rh%d" % t)
+        offer(t, R(out, 0, lo), R("W", 0, lo), "rw%d" % t)
+
     tt, ts, cp, ms, scan, tr, act, mm = (F[k] for k in ("tt", "ts", "cp", "ms", "scan", "tr", "act", "mm"))
-    iota, aff, dma, red = (F[k] for k in ("iota", "aff", "dma", "red"))
+    iota, aff, dma = (F[k] for k in ("iota", "aff", "dma"))
     asked = [T.cores[(rank + 1 + t) % NR] for t in range(RO)]
 
     def at(win, off):
@@ -780,17 +596,22 @@ def rank_program(g, core, T, topo):
         return sum(w for who, w in CFG["old"][t] if who == "2")
 
     def fold(out, a, mask="rmask"):
-        scan(out, R(mask, 0, size(a)), a, OP.min, OP.max)
+        n, most = size(a), CFG["fs"].get(out[0], W16)
+        cuts = list(range(0, n - most // 2, most)) + [n] if n > most else [0, n]
+        for lo, hi in zip(cuts, cuts[1:]):
+            scan(R(out[0], out[1] + lo, out[1] + hi), R(mask, 0, hi - lo), R(a[0], a[1] + lo, a[1] + hi), OP.min, OP.max)
 
-    def gather(who, out, a):
+    def copy(who, out, a):
         if who == "v":
             cp(out, a)
-        else:
+        elif who == "a":
             act(out, a)
+        else:
+            aff(out, a, [[0, size(out)]], OP.is_ge, 0, 0)
 
     first, late = F["first"], []
     MO, MS = R("morph", 0, P), R("meas", 0, V)
-    DV = R("Dv", 0, V)
+    DV, WV = R("Dv", 0, V), R("W", 0, V)
 
     dma("s", R("b15i"), T.bas[15:128:16, :])
     dma("s", R("use_i"), T.use[:])
@@ -801,7 +622,7 @@ def rank_program(g, core, T, topo):
         if k == "d":
             dma("s", R("der_i"), T.der[:])
         if k == "b":
-            dma("s", R("bas_i"), T.bas[:])
+            dma("s", R("bas_i", 0, V), T.bas[:])
 
     first[0] = IN_ORDER
     ms(R("one8"), 1.0)
@@ -813,14 +634,18 @@ def rank_program(g, core, T, topo):
     aff(R("blkw"), R("blkw"), [[16, 9], [0, 16]], OP.is_ge, 15, -1)
     aff(R("sel1"), R("blkw"), [[0, 9], [1, 16]], OP.is_equal, -15, 0)
     aff(R("idw"), R("oneb", 0, 160), [[1, 160]], OP.is_equal, -16, -1)
+    iota(R("VR"), [[PH, I]], -V // 2, 0)
     first[0] = CFG["rest"]
-    iota(ch("VR", 0, I), [[16 * PH, 24], [0, 16]], 0, 0)
-    iota(ch("VR", 1, I), [[0, 24], [PH, 16]], 0, 0)
-    iota(R("rmask", 1024, 2048), [[0, 64], [256, 16]], 0, 0)
     aff(R("idf"), R("onef", 0, 128), [[1, 128]], OP.is_equal, 0, -1)
     aff(R("selr"), R("onef"), [[1, 144]], OP.is_equal, 0, -1)
     aff(R("tri"), R("blk"), [[1, 128]], OP.is_ge, 0, -1)
-    for n, pat, base in ((R("cb", 0, 6), [[-16, 6]], 0), (R("cn", 0, 6), [[32, 6]], 400), (R("i8"), [[0, 4], [128, 24]], 0),
+    if CFG["turned"]:
+        aff(R("mix"), R("onef", 0, 128), [[4, 4], [1, 4], [16, 8]], OP.is_equal, 0, -1)
+        aff(R("swb"), R("oneb", 0, 400), [[1, 25], [32, 4], [1000, 4]], OP.is_equal, -1, -1)
+        ms(R("KS", I, 512), 0.0)
+    if any(who == "2" for who, w in CFG["new"][0]):
+        iota(R("rmask8"), [[0, 162], [256, 8]], 0, 0)
+    for n, pat, base in ((R("cb", 0, 6), [[-32, 6]], -1), (R("i8"), [[0, 4], [256, 24]], 0), (R("tz"), [[2, 4], [0, 6]], -7),
                          (R("W1", 0, 400), [[0, 25], [1, 16]], 0)):
         iota(n, pat, base, 0)
 
@@ -831,58 +656,73 @@ def rank_program(g, core, T, topo):
     ms(R("rmask", 0, 1024), 256.0)
     ms(R("Z", 0, 1024), 0.0)
     ms(R("rmask", 0, 1024, 16), 0.0)
+    dma("s", R("rmask", 1024, 2048), R("rmask", 0, 1024))
     fill(R("zer"), 0.0)
     first[0] = CFG["rest"]
     for k in range(2):
         fill(R("Z", 1024 + 256 * k, 1280 + 256 * k), 0.0)
     fill(R("amask"), -2.0 * 2 ** 25)
-    for n in ("Bf", "meas", "Dv"):
+    for n in ["Dv"] + ["W"] * (2 in CFG["patch"][:RO - 1]):
         fill(R(n, V, VX), 0.0)
     for n in ("UQ", "AD"):
         fill(R(n, I, IX), 0.0)
-    if any(CFG["two"]):
-        for k in range(2):
-            fill(R("morph", P + I * k, P + I * (k + 1)), 0.0)
     fill(R("GA", 0, 8), 0.0)
     for m in sorted({paired(t) for t in range(RO)} - {0}):
         fill(R("GA", 8 * m + 8, 8 * m + 16), 0.0)
-    fill(R("non", I, IX), 1.0)
+    if "a" in CFG["non"]:
+        act(R("non", I, IX), R("oneb", 0, CAP), AF.Sigmoid, scale=128.0, more=1.3)
+    else:
+        fill(R("non", I, IX), 1.0)
     fill(R("cst"), -32.0)
-    fill(R("cs2"), 0.0)
     fill(R("oalln"), -0.0625)
     ms(R("amask", 0, I, 16), 2.0 * 2 ** 25)
     ms(R("cst", 15, 128, 16), 32.0)
-    ms(R("cs2", 15, 128, 16), -64.0)
-    ms(col("mg"), -0.5)
-    ms(col("mg", 1), 128.0)
+    if not CFG["dv"]:
+        fill(R("cs2"), 0.0)
+        ms(R("cs2", 15, 128, 16), -64.0)
+    if "v" in CFG["non"]:
+        ms(col("mg"), -0.5)
     if "a" in CFG["non"]:
-        act(R("adb"), R("oneb", 0, CAP), AF.Sigmoid)
-    ts(R("pi", 1, 2), R("pi", 0, 1), 16, None, OP.bitwise_and)
+        ms(col("mg", 1), 128.0)
+    ms(col("cnt", 2), 63.5 / 8)
+    if CFG["turned"] < 2:
+        ts(R("pi", 1, 2), R("pi", 0, 1), 16, None, OP.bitwise_and)
     ts(R("pi", 0, 1), R("pi", 0, 1), 15, None, OP.bitwise_and)
     cp(col("pm"), R("pi", 0, 1))
-    ts(col("pw"), col("pm"), 1.0, None, OP.add)
-    ts(col("pw", 1), col("pm"), 8.0, None, OP.mult)
-    ts(R("cb", 0, 6), R("cb", 0, 6), col("pm"), 0.5, OP.subtract, OP.subtract)
+    ts(col("pw"), col("pm"), 2.0, 2.0, OP.mult, OP.add)
+    ts(col("pw", 1), col("pm"), 16.0, None, OP.mult)
+    ts(col("pm", 2), col("pm"), 2.0, None, OP.mult)
+    ts(R("cb", 0, 6), R("cb", 0, 6), col("pm", 2), None, OP.subtract)
     ts(col("pw", 2), col("pm"), 8.0, None, OP.is_ge)
     ts(col("pw", 3), col("pm"), 8.0, None, OP.is_lt)
     ts(col("pw", 4), col("pm"), 15.0, None, OP.is_equal)
-    ts(col("pw", 5), col("pi", 1), 0.0, None, OP.is_equal)
-    ts(col("pw", 6), col("pi", 1), 0.0, None, OP.is_gt)
+    if CFG["turned"] < 2:
+        ts(col("pw", 5), col("pi", 1), 0.0, None, OP.is_equal)
+        ts(col("pw", 6), col("pi", 1), 0.0, None, OP.is_gt)
     ts(col("pm", 1), col("pm"), -1.0, None, OP.mult)
     ts(R("selz"), R("sel1"), col("pw"), None, OP.mult)
     ts(R("i8"), R("i8"), col("pw", 1), None, OP.add)
     for n, src, f in (("selm", "sel1", -4096.0), ("selk", "sel1", 2048.0), ("selp", "sel1", 4096.0), ("seln", "sel1", -2048.0),
-                      ("idbig", "idb", BIG), ("idn", "idb", -1.0), ("selo", "sel1", FAR / 16.0),
-                      ("idK", "idb", 4096.0), ("idK2", "idb", 8192.0), ("idKn", "idb", -4096.0), ("blkn", "blk", -1.0),
-                      ("blk2n", "blk", -2.0), ("trin", "tri", -8192.0), ("tri", "tri", 8192.0)):
+                      ("idbig", "idb", BIG), ("idn", "idb", -1.0), ("selo", "sel1", FAR / 8.0),
+                      ("idK", "idb", 4096.0), ("idK2", "idb", 8192.0), ("idH", "idb", 2048.0), ("idKn", "idb", -4096.0), ("blkn", "blk", -1.0),
+                      ("blk2n", "blk", -2.0), ("trin", "tri", -8192.0), ("tri", "tri", 8192.0), ("id16n", "idb", -16.0), ("id12n", "idb", -12.0),
+                      ("cstn", "cst", -1.0)):
         first[0] = IN_ORDER if n in ("selm", "selk", "selp", "seln", "idbig", "idn") else CFG["rest"]
+        if n == "id12n" and not (any(CFG["patch"][:RO - 1]) or CFG["patch"][RO - 1] == 1):
+            continue
+        if n == "cstn" and (all(CFG["patch"]) or not CFG["again"]):
+            continue
         act(R(n), R(src), scale=f)
-    ts(col("pw", 7), col("pw", 4), -8192.0, 4096.0, OP.mult, OP.add)
-    aff(R("thi"), R("trin"), [[0, 8], [1, 16]], OP.is_ge, -8, 0)
-    aff(R("tlo"), R("trin"), [[0, 8], [-1, 16]], OP.is_ge, 7, 0)
+    if not CFG["dv"]:
+        ts(col("pw", 7), col("pw", 4), -8192.0, 4096.0, OP.mult, OP.add)
+        aff(R("thi"), R("trin"), [[0, 8], [1, 16]], OP.is_ge, -8, 0)
+        aff(R("tlo"), R("trin"), [[0, 8], [-1, 16]], OP.is_ge, 7, 0)
     for n, src, k in (("whi", R("idf"), 2), ("wlo", R("idf"), 3), ("selr", R("selr"), 4),
-                      ("sw0", R("idw"), 5), ("sw1", R("idw"), 6)):
+                      ("sw0", R("idw"), 5), ("sw1", R("idw"), 6))[:3 if CFG["turned"] > 1 else 5]:
         act(R(n), src, AF.Identity, scale=col("pw", k))
+    if any(who == "2" for r in CFG["new"] for who, w in r):
+        aff(R("bhi"), R("idb"), [[0, 8], [1, 16]], OP.is_ge, -8, 0)
+        aff(R("blo"), R("idb"), [[0, 8], [-1, 16]], OP.is_ge, 7, 0)
     act(R("dg"), R("W1", 0, 400), AF.Abs, bias=col("pm", 1))
     first[0] = 0.0
 
@@ -891,8 +731,8 @@ def rank_program(g, core, T, topo):
         aff(ch("cyc", t - 1, 128), R("blk"), [[-16, 8], [-1, 16]], OP.is_equal, t, 1)
         for k in range(t):
             aff(R("cyc", 128 * (t - 1) + k, 128 * t, 16), R("oneb", 0, 8), [[-16, 8]], OP.is_equal, t - 16 - k, 1)
-        if t == 1:
-            iota(R("rmask8"), [[0, 130], [256, 8]], 0, 0)
+        if t == 1 and all(who != "2" for who, w in CFG["new"][0]):
+            iota(R("rmask8"), [[0, 162], [256, 8]], 0, 0)
 
     def classes(rounds, rows):
         for t in rounds:
@@ -925,7 +765,9 @@ def rank_program(g, core, T, topo):
 
     def tables():
         for k in range(PH):
-            cp(ch("Bf", k, I), ch("bas_i", k, I))
+            copy(CFG["bf"], lanes("Bf", k), lanes("bas_i", k))
+            if CFG["dv"]:
+                copy(CFG["dv"][0], ch("Dv", k, I), ch("der_i", k, I))
         for k in range(PH):
             p = R("P%d" % (5, 6, 3)[k], 0, I)
             if k < CFG["neq"]:
@@ -934,8 +776,13 @@ def rank_program(g, core, T, topo):
             else:
                 tt(ch("NEQ", k, I), ch("der_i", k, I), ch("bas_i", k, I), OP.not_equal)
             mm(p, R("cst"), R("oneb", 0, I), True, False)
+            if CFG["dv"][1:] == "a":
+                mm(p, R("idf"), ch("Dv", k, I), False, False)
             mm(p, R("tri"), ch("NEQ", k, I), False, True)
-            tt(ch("W", k, I), p, ch("der_i", k, I), OP.add)
+            if CFG["dv"][1:] == "a":
+                act(ch("W", k, I), p)
+            else:
+                tt(ch("W", k, I), p, ch("der_i", k, I), OP.add)
 
     def later(ph):
         for x in range(16):
@@ -947,45 +794,87 @@ def rank_program(g, core, T, topo):
             for x in range(16):
                 mm(ch("P4", 3 + ph, 24), sk("selz", x), R("meas", 3 * x + ph, V, 48), x == 0, x == 15)
         for t in range(RO):
-            ts(ch("zi", t, 24), ch("P4", 3 + t % PH, 24), float(t), None, OP.add)
-        ts(R("zi"), R("zi"), 7, None, OP.bitwise_and)
+            ts(ch("zi", t, 24), ch("P4", 3 + t % PH, 24), 2.0 * t, None, OP.add)
+        ts(R("zi"), R("zi"), 14, None, OP.bitwise_and)
         tt(R("i8"), R("i8"), R("zi"), OP.add)
 
-    def winners(keys, kt, ks, n, out, li, lh, lst):
+    def winners(keys, kt, ks, n, out, li, lh, lst, mid=V / 2.0):
         for key, lo, hi in keys:
             tr(R(kt, lo, hi), key)
-        scan(R(ks), R("amask", 0, n), R(kt), OP.max, OP.min)
-        ts(li, R(ks, 15, n, 16), ROUND, ROUND, OP.add, OP.subtract)
+        scan(R(ks, 0, n), R("amask", 0, n), R(kt), OP.max, OP.min)
+        ts(li, R(ks, 15, n, 16), 2048 * ROUND, 2048 * ROUND, OP.add, OP.subtract)
         tt(lh, R(ks, 15, n, 16), li, OP.subtract)
         for y in range(2):
             for h in range(2):
                 mm(R(out[0], out[1] + y, out[2], 2), R("sw%d" % y, 16 - 16 * (h - y), 144 - 16 * (h - y)), R(lh[0], lh[1] + h, lh[2], 2), h == 0, h == 1)
-        ts(lst, out, V / 2.0, None, OP.add)
+        ts(lst, out, mid, None, OP.add)
 
-    def sums(key, lo, hi, terms, stop):
+    def sums(key, lo, hi, terms, stop, turned=False):
         for k, (s, buf) in enumerate(terms):
             for j in range(16):
-                mm(key, sk(s, j), R(buf, 16 * lo + j, 16 * hi, 16), False, stop and j == 15 and k + 1 == len(terms))
+                a, last = R(buf, 16 * lo + j, 16 * hi, 16), stop and j == 15 and k + 1 == len(terms)
+                if turned:
+                    mm(R(key[0], key[1] + j, key[2], 16) + key[4:], a, R(s, 15, 128, 16), False, last)
+                else:
+                    mm(key, sk(s, j), a, False, last)
+
+    def leaders(keys, out, lst, mid):
+        for key, lo, hi in keys:
+            scan(R("KS", lo, hi), R("amask", 0, hi - lo), key, OP.max, OP.min)
+        q, kt, li, lh = R(out[0], out[2], out[2] + 32), R("KT", 0, 32), R("mi", 32, 64), R("mh", 32, 64)
+        mm(q, R("mix"), R("KS", 15, 512, 16), True, True)
+        tr(kt, q)
+        ts(li, kt, 2048 * ROUND, 2048 * ROUND, OP.add, OP.subtract)
+        tt(lh, kt, li, OP.subtract)
+        for b in range(PH):
+            for j in range(4):
+                mm(R(out[0], out[1] + 8 * b, out[1] + 8 * b + 8), R("swb", 16 + 128 * b - j, 144 + 128 * b - j), R("mh", 32 + 8 * j, 40 + 8 * j),
+                   b + j == 0, b + j == 5)
+        ts(lst, out, mid, None, OP.add)
+
+    def answers():
+        rows = (0, CAP)
+        scan(R("KS2") + rows, R("amask", 0, 128) + rows, R("P4", 0, 128) + rows, OP.max, OP.min)
+        kt, li, lh, out = R("KT2", 0, 32), R("mi", 0, 32), R("mh", 0, 32), R("P4", 100, 106)
+        mm(R("P4", 112, 120), R("mix") + rows, R("KS2", 15, 128, 16) + rows, True, True)
+        tr(kt, R("P4", 112, 144))
+        ts(li, kt, 2048 * ROUND, 2048 * ROUND, OP.add, OP.subtract)
+        tt(lh, kt, li, OP.subtract)
+        for j in range(4):
+            mm(out, R("swb", 16 - j, 144 - j), R("mh", 8 * j, 8 * j + 6), j == 0, j == 3)
+        ts(R("n16", 0, 6), out, V / 2.0, None, OP.add)
 
     def search(t):
         ph = t % PH
         first[0] = CFG["use"][t - 1] if t else 0.0
         cp(R("u16"), at(R("USE" if t else "use_i"), cls(t)))
         first[0] = 0.0
-        ts(R("U"), R("u16"), -V / 2.0, None, OP.add)
+        mid = V / 2.0 + ph
+        ts(R("U"), R("u16"), -mid, None, OP.add)
         d = R("P5", 0, I)
-        mm(d, R("idb"), R("U"), True, False)
-        for k in range(2):
-            mm(d, R("idn"), ch("VR", k, I), False, k == 1)
-        ts(R("EQ"), d, ph - V / 2.0, None, OP.is_equal)
-        lo, x, keys = 0, "x%d" % (t % 2), []
+        mm(d, R("idb"), R("U"), True, True)
+        tt(R("EQ"), d, R("VR"), OP.is_equal)
+        if CFG["heads"]:
+            mm(d, R("idb"), lanes("meas", ph), True, True)
+        lo, x, keys, turned = 0, "x%d" % (t % 2), [], CFG["turned"]
         for k, (who, n) in enumerate(CFG["search"][t]):
             hi = lo + n
             pc = CFG["pc"][who]
             cuts = [(a, min(a + pc, hi)) for a in range(lo, hi, pc)]
-            key = R(("P0", "P7", "P1")[k % 3], lo, hi)
-            keys.append((key, lo, hi))
-            mm(key, R("idb"), R("U", lo, hi), True, False)
+            banks, k = CFG["kbank"], lo // 128
+            b0, b1 = 128 * k, 128 * k + 128
+            whole = R(banks[k], b0, b1)
+            key = whole + (lo - b0, hi - b0) * (n < 128)
+            opens, ends = banks[k] not in banks[:k], banks[k] not in banks[k + 1:] and hi == b1
+            if lo == b0:
+                if opens:
+                    keys.append((whole, b0, b1))
+                else:
+                    keys[-1] = (R(banks[k], keys[-1][1], b1), keys[-1][1], b1)
+                if turned:
+                    mm(whole, R("U", b0, b1), R("idb"), opens, False)
+                else:
+                    mm(whole, R("idb"), R("U", b0, b1), opens, False)
             if who == "p":
                 for a, b in cuts:
                     act(R("GE", 16 * a, 16 * b), at(MS, R("u16", a, b)))
@@ -994,19 +883,18 @@ def rank_program(g, core, T, topo):
                     if t:
                         mm(bank, R("idb"), R(x, a, a + 512), True, False)
                     else:
-                        mm(bank, R("zer"), R("rmask", 0, 512), True, False)
                         for j in range(16):
-                            mm(R(bank[0], j, 512, 16), R("idb"), lanes("meas", ph, a // 16, a // 16 + 32), False, False)
+                            mm(R(bank[0], j, 512, 16), R("idb"), lanes("meas", ph, a // 16, a // 16 + 32), j == 0, False)
                     mm(bank, R("idn"), R("GE", a, a + 512), False, True)
                     act(R("SE", a, a + 512), bank, AF.Abs)
                 terms = [("selk", "SE")]
             elif who == "r":
                 for a, b in cuts:
                     act(R("GE", 16 * a, 16 * b), at(MS, R("u16", a, b)))
-                sums(key, lo, hi, [("selk", "GE")], False)
+                sums(key, lo, hi, [("selk", "GE")], False, turned)
                 head = R("GE", 16 * lo, 16 * hi, 16)
-                tt(head, head, lanes("meas", ph, lo, hi), OP.min)
-                for a, b in cuts:
+                tt(head, head, R("P5", lo, hi) if CFG["heads"] else lanes("meas", ph, lo, hi), OP.min)
+                for a, b in [(a, min(hi, a + CFG["rs"])) for a in range(lo, hi, CFG["rs"])]:
                     scan(R("SE", 16 * a, 16 * b), R(x, 16 * a, 16 * b), R("GE", 16 * a, 16 * b), OP.max, OP.min)
                 terms = [("selm", "SE")]
             elif who == "t":
@@ -1017,18 +905,24 @@ def rank_program(g, core, T, topo):
             else:
                 for a, b in cuts:
                     tt(R("GE", 16 * a, 16 * b), at(MS, R("u16", a, b)), R(x, 16 * a, 16 * b), OP.subtract)
-                sums(key, lo, hi, [("seln", "GE")], False)
+                sums(key, lo, hi, [("seln", "GE")], False, turned)
                 for a in range(lo, hi, 64):
                     b = min(a + 64, hi)
                     ts(R("SE", 16 * a, 16 * b), R("GE", 16 * a, 16 * b), 0.0, None, OP.max)
                 terms = [("selp", "SE")]
-            mm(key, R("idbig"), R("EQ", lo, hi), False, False)
-            sums(key, lo, hi, terms, True)
+            if hi == b1 and turned:
+                mm(whole, R("EQ", b0, b1), R("idbig"), False, False)
+            elif hi == b1:
+                mm(whole, R("idbig"), R("EQ", b0, b1), False, False)
+            sums(key, lo, hi, terms, ends, turned)
             lo = hi
-        winners(keys, "KT", "KS", I, R("P0", 400, 424), R("mi", 0, 24), R("mh", 0, 24), R("m16"))
+        if turned:
+            leaders(keys, R("P0", 400, 424), R("m16"), mid)
+        else:
+            winners(keys, "KT", "KS", I, R("P0", 400, 424), R("mi", 0, 24), R("mh", 0, 24), R("m16"), mid)
         first[0] = CFG["m1"]
-        ts(R("m1", 24, 48), R("P0", 400, 424), 0.5, V / 4.0 + 1099.75, OP.mult, OP.add)
-        ts(R("m1", 48, 72), R("m1", 24, 48), 4.0, 1.0 - 4400.0 - V / 2.0, OP.mult, OP.add)
+        ts(R("m1", 24, 48), R("P0", 400, 424), 0.5, mid / 2.0 + 1099.75, OP.mult, OP.add)
+        ts(R("m1", 48, 72), R("m1", 24, 48), 4.0, 1.0 - 4400.0 - mid, OP.mult, OP.add)
         tt(R("m1", 0, 24), R("m1", 48, 72), R("P0", 400, 424), OP.subtract)
         first[0] = 0.0
 
@@ -1038,10 +932,8 @@ def rank_program(g, core, T, topo):
             cp(R("d16", 2, I + 2), lanes("der_i", 0))
             return
         terms = [("wlo", "whi", "idf", "W"), ("tlo", "thi", "trin", "NEQ")]
-        if t in (0, PH):
+        if CFG["dv"] or (t == PH and not CFG["again"]):
             terms = [("wlo", "whi", "idf", "Dv")]
-        if t == 0:
-            cp(lanes("Dv", 0), lanes("der_i", 0))
         bank = CFG["obank"] if t else "P2"
         mm(R(bank, 0, I + 2), R("zer"), R("oneb", 0, I + 2), True, False)
         for k, (lo, hi, both, src) in enumerate(terms):
@@ -1068,25 +960,58 @@ def rank_program(g, core, T, topo):
                 fold(R("SD", 16 * lo, 16 * end), b, "rmask8")
                 lo = hi
             else:
-                a = 16 * (one + 1) - 8 * m
-                gather(who, R("GA", a, a + 16 * w), at(MO, R("d16", o + one + 2, o + one + w + 2)))
+                a = 16 + 16 * w * (one // w % 2)
+                copy(who, R("GA", a, a + 16 * w), at(MO, R("d16", o + one + 2, o + one + w + 2)))
                 fold(R("SD", a, a + 16 * w), R("GA", a, a + 16 * w))
+                mm(R("P2", one, one + w), R("idb"), R("SD", a + 15, a + 16 * w, 16), True, False)
+                mm(R("P2", one, one + w), R("idn"), lanes("meas", t % PH, one, one + w), False, True)
                 one += w
-        for a, b, top in ((0, m, R("SD", 15, 8 * m + 8, 8)), (m, I, R("SD", 8 * m + 31, 16 * (I + 1) - 8 * m, 16))):
-            if a < b:
-                mm(R("P2", a, b), R("idb"), top, True, False)
-                mm(R("P2", a, b), R("idn"), lanes("meas", t % PH, a, b), False, True)
+        if m:
+            mm(R("P2", 0, m), R("idb"), R("SD", 15, 8 * m + 8, 8), True, False)
+            mm(R("P2", 0, m), R("idn"), lanes("meas", t % PH, 0, m), False, True)
         act(R("AD", 0, I), R("P2", 0, I), AF.Abs)
 
+    def single(t):
+        return sum(w for who, w in CFG["new"][t] if who == "2")
+
+    def tops(t, a, b):
+        if a >= single(t):
+            return R("SE", 16 * a + 15, 16 * b, 16)
+        return R("SE", 8 * a + 15, 8 * b + 8, 8)
+
+    def new_lists(t):
+        one = single(t)
+        cp(R("e16", one + 2, I + 2), R("Ea", one, I))
+        if one:
+            n = one // 2
+            ts(R("Eh", 0, one), R("Ea", 0, one), -P / 2.0, None, OP.add)
+            even, odd = R("Eh", 0, one, 2), R("Eh", 1, one, 2)
+            mm(R("P3", 0, one + 2), R("zer"), R("oneb", 0, one + 2), True, False)
+            for j, (a, s, r) in enumerate(((1, "blo", odd), (0, "bhi", even), (n + 2, "blo", even), (n + 2, "bhi", odd))):
+                mm(R("P3", a, a + n), R(s), r, False, j == 3)
+            ts(R("e16", 0, one + 2), R("P3", 0, one + 2), P / 2.0, None, OP.add)
+
     def new_tops(t, cut):
-        lo = 0
-        for who, n in CFG["new"][t]:
-            hi = lo + n
-            a = R("GE", 16 * lo, 16 * hi)
-            gather(who, a, at(MO, R("e16", lo, hi)))
-            fold(R("SE", 16 * lo, 16 * hi), a)
-            lo = hi
-        mm(R("P3", 0, cut), R("idb"), R("SE", 15, 16 * cut, 16), True, False)
+        a, lo = 0, single(t)
+        one, n = lo, lo // 2
+        for who, w in CFG["new"][t]:
+            if who == "2":
+                b = a + w // 2
+                act(R("GE", 8 + 16 * a, 8 + 16 * b), at(MO, R("e16", n + 2 + a, n + 2 + b)))
+                end = b + (b == n)
+                both = R("GE", 16 * (n + 1 + a), 16 * (n + 1 + end))
+                tt(both, at(MO, R("e16", a, end)), R("GE", 16 * a, 16 * end), OP.max)
+                fold(R("SE", 16 * a, 16 * end), both, "rmask8")
+                a = b
+            else:
+                hi = lo + w
+                got = R("GE", 16 * lo + 32, 16 * hi + 32)
+                copy(who, got, at(MO, R("e16", lo + 2, hi + 2)))
+                fold(R("SE", 16 * lo, 16 * hi), got)
+                lo = hi
+        for a, b in ((0, min(one, cut)), (one, cut)):
+            if a < b:
+                mm(R("P3", a, b), R("idb"), tops(t, a, b), a == 0, False)
         mm(R("P3", 0, cut), R("idn"), lanes("meas", t % PH, 0, cut), False, True)
         act(R("AE", 0, cut), R("P3", 0, cut), AF.Abs)
         late.append(lambda: act(R("UQ", 0, I), at(R("qk%d" % t), cls(t))))
@@ -1095,248 +1020,347 @@ def rank_program(g, core, T, topo):
                 F["behind"]()
             late.pop()()
 
-    def decide(who, out, gain):
+    def decide(who, out, gain, count=None):
         if who == "v":
             ts(out, gain, col("mg"), None, OP.is_gt)
         else:
-            act(out, gain, AF.Sigmoid, bias=col("mg", 1), scale=256.0)
+            act(out, gain, AF.Sigmoid, bias=col("mg", 1), scale=256.0, accum=count)
 
     def morphs(t):
-        o = R("P4", 300, 324)
+        o = R("P4", 320, 344)
         mm(o, R("idf"), ch("i8", t, 24), True, False)
         for x in range(16):
             mm(o, sk("selo", x), R("non", x, I, 16), False, x == 15)
-        cp(R("zw"), o)
-        cp(at(R("morph"), R("zw")), lanes("meas", t % PH))
+        ts(R("zw"), o, 0.5, None, OP.mult)
+        n = 24 // CFG["ms"][t]
+        for a in range(0, 24, n):
+            cp(at(R("morph"), R("zw", a, a + n)), lanes("meas", t % PH, 16 * a, 16 * (a + n)))
+
+    def lists(t, banks):
+        ph, non, x = t % PH, R("non", 0, I), R("XD")
+        old, base, dn = (R(b, 0, I) for b in banks)
+        mm(old, R("idK2"), non, False, True)
+        if CFG["patch"][t]:
+            tt(x, old, R("Ea", 0, I), OP.max)
+            mm(base, R("idKn"), non, True, False)
+            mm(base, R("idf"), x, False, True)
+            if t + 1 < RO:
+                tt(lanes("NEQ", ph), base, lanes("Bf", ph), OP.not_equal)
+            act(lanes("Dv", ph), base)
+            if t + 1 < RO:
+                for k, (s, r) in enumerate((("cst", R("oneb", 0, I)), ("idKn", non), ("idf", x), ("tri", lanes("NEQ", ph)))):
+                    mm(dn, R(s), r, k == 0, k == 3)
+                if not CFG["wlate"]:
+                    copy(CFG["wev"], lanes("W", ph), dn)
+            return
+        mm(base, R("idK"), non, False, True)
+        tt(x, old, R("Ea", 0, I), OP.max)
+        tt(lanes("NEQ", ph), base, x, OP.not_equal)
+        for k, (s, r) in enumerate((("cst", R("oneb", 0, I)), ("idKn", non), ("idf", x), ("tri", lanes("NEQ", ph)))):
+            mm(dn, R(s), r, k == 0, k == 3)
+        copy(CFG["wev"], lanes("W", ph), dn)
+        if not CFG["again"]:
+            mm(base, R("idKn"), non, True, False)
+            mm(base, R("idf"), x, False, True)
+            act(lanes("Dv", ph), base)
+
+    def settled():
+        for ph, bank in ((1, "P0"), (2, "P7")):
+            p = R(bank, 0, I)
+            for k, (s, r) in enumerate((("idf", lanes("W", ph)), ("trin", lanes("NEQ", ph)), ("cstn", R("oneb", 0, I)))):
+                mm(p, R(s), r, k == 0, k == 2)
+            act(lanes("Dv", ph), p)
+
+    def counts():
+        o = R("P4", 344, 345)
+        for k in range(PH):
+            mm(o, ch("non", k, 128), col("oneb"), k == 0, k == PH - 1)
+        act(col("cnt"), o)
 
     def dist(t):
         ph = t % PH
-        half, kd, us = R("P5", 0, I), R("P7", 0, I), R("USE", 37 * t, 37 * t + I)
+        half, kd, non = R("P5", 0, I), R("P7", 0, I), R("non", 0, I)
+        us = R("USE", 37 * t, 37 * t + I)
         first[1] = CFG["mu"]
-        if CFG["two"][t] == 1 and t:
+        if t:
             dma("s", R("morc"), MO)
         old_tops(t)
-        if CFG["two"][t] == 1 and not t:
+        if not t:
             dma("s", R("morc"), MO)
+            dma("s", R("meas", V, VX), T.mea[:, 0:VX - V])
+            dma("s", R("bas_i", V, VX), T.bas[:, 0:VX - V])
+            if any(CFG["mz"]):
+                dma("s", R("morph", P, 8 * IX), T.mor[:, 0:8 * CAP])
         ea = R("Ea", 0, I)
-        tt(ea, at(R("W"), R("m16")), lanes("Bf", ph), OP.max)
+        tt(ea, at(WV, R("m16")), lanes("bas_i", ph), OP.max)
         ts(ea, ea, 4095, None, OP.bitwise_and)
-        cp(R("e16"), ea)
+        new_lists(t)
         if t == 1:
             F["behind"]()
             later(2)
-        if t + 1 < RO and CFG["obank"] != "P6":
+        if t + 1 < RO:
             first[0] = CFG["olds"]
             old_lists(t + 1)
             first[0] = 0.0
         cut = CFG["cut"]
+        xc = R("P7", I, 2 * I - cut) if CFG["xcut"] else lanes("meas", ph, cut, I)
+        if CFG["xcut"]:
+            mm(xc, R("idb"), lanes("meas", ph, cut, I), True, True)
+        first[0] = CFG["m1"]
+        mm(kd, R("idK"), R("dg", t, t + I), True, False)
+        for x in range(16):
+            mm(R("P7", x, I, 16), ch("cyc", t - 1, 128) if t else R("idb"), R("m1", 0, 24), False, False)
+        mm(R("P6", 0, I), R("idKn"), R("dg", t, t + I), True, False)
+        mm(R("P6", 0, I), R("idH"), R("oneb", 0, I), False, False)
+        terms = (("idf", lanes("W", ph)), ("trin", lanes("NEQ", ph)), ("cs2", R("oneb", 0, I)))
+        if CFG["dv"] or (t == PH and not CFG["again"]):
+            terms = (("idf", lanes("Dv", ph)), ("idKn", R("oneb", 0, I)))
+        for k, (s, r) in enumerate(terms):
+            mm(R("P1", 0, I), R(s), r, k == 0, False)
+        first[0] = 0.0
         new_tops(t, cut)
         mm(R("P5", 0, cut), R("blkn"), R("AD", 0, cut), True, False)
         mm(R("P5", 0, cut), R("blk"), R("AE", 0, cut), False, True)
         if cut < I:
-            o, top, x, me = R("P5", cut, I), R("SE", 16 * cut + 15, W16, 16), lanes("meas", ph, cut, I), R("SQ", 0, I - cut)
-            tt(me, top, x, OP.min)
+            o, top, x, me = R("P5", cut, I), tops(t, cut, I), lanes("meas", ph, cut, I), R("SQ", 0, I - cut)
+            tt(me, top, xc, OP.min)
             for k, (s, r) in enumerate((("blkn", R("AD", cut, I)), ("blk", x), ("blk", top), ("blk2n", me))):
                 mm(o, R(s), r, k == 0, k == 3)
-        non = R("non", 0, I)
         first[0], first[1] = CFG["chain"], CFG["muy"][t]
-        decide(CFG["non"][0], non, half)
-        scan(R("cum"), R("non"), R("oneb"), OP.add, OP.mult)
-        na = CFG["signs"][t]
-        w = I + 16 * na
+        summed = CFG["non"][0] == "a" and CFG["patch"][t] and t + 1 < RO
+        decide(CFG["non"][0], non, half, col("cnt") if summed else None)
+        scan(R("cum", 1, IX), R("non", 1, IX), R("non", 0, IX - 1), OP.add, OP.add, col("non"))
         for n in range(6):
-            if na == 6:
-                act(ch("junk", n % 2, 400), R("cum", 16 * n, 16 * n + 400), AF.Sign, bias=col("cb", n), accum=col("acc", n))
-            elif n < na:
-                act(R("junk", IX * (n % 2), IX * (n % 2) + w), R("cum", 0, w), AF.Sign, bias=col("cb", n), accum=col("acc", n))
-            else:
-                o = ch("RQ", n - na, 400)
-                ts(o, R("cum", 16 * n, 16 * n + 400), col("cb", n), 0.0, OP.add, OP.is_lt)
-                scan(ch("CN", n - na, 400), o, R("oneb", 0, 400), OP.add, OP.mult, 16.0 * n)
-        first[0] = 0.0
-        for p, s in ((kd, "idK"), (R("P6", 0, I), "idKn")):
-            first[0] = CFG["m1"]
-            mm(p, R(s), R("dg", t, t + I), True, False)
-            for x in range(16):
-                mm(R(p[0], x, I, 16), ch("cyc", t - 1, 128) if t else R("idb"), R("m1", 0, 24), False, False)
-            first[0] = CFG["use"][t]
-            mm(p, R(s), non, False, True)
-        tt(R("LXg"), kd, us, OP.min)
-        tt(us, R("P6", 0, I), R("LXg"), OP.max)
+            act(ch("junk", n % 2, IX // 2), R("cum", 1, IX, 2), AF.Sign, bias=col("cb", n), accum=col("acc", n))
+        first[0] = CFG["use"][t]
+        mm(R("P6", 0, I), R("idKn"), non, False, True)
+        mm(kd, R("idK"), non, False, True)
+        tt(R("LXg"), R("P6", 0, I), R("use_i", 0, I) if CFG["use0"] and not t else us, OP.max)
+        tt(us, kd, R("LXg"), OP.min)
         first[0] = 0.0
         if t + 1 < RO:
             offer(t + 1, R("qk%d" % (t + 1)), R("USE"), "rk%d" % (t + 1))
         else:
             dma("s", T.yu[:], R("USE"))
-        if t + 1 < RO and CFG["obank"] == "P6":
-            old_lists(t + 1)
-        if CFG["two"][t] == 1:
+        if not CFG["mor"][t]:
             morphs(t)
-        for k, (s, r) in enumerate((("idf", lanes("W", ph)), ("trin", lanes("NEQ", ph)), ("cs2", R("oneb", 0, I)))):
-            mm(R("P6", 0, I), R(s), r, k == 0, False)
-        if t + 1 == RO and CFG["dtwo"]:
-            mm(R("P6", 0, I), R("idK2"), non, False, True)
-            tt(R("XD"), R("P6", 0, I), ea, OP.max)
-            mm(R("P1", 0, I), R("idKn"), non, True, False)
-            mm(R("P1", 0, I), R("idf"), R("XD"), False, True)
-            act(lanes("Dv", ph), R("P1", 0, I))
+        if CFG["patch"][t]:
+            lists(t, ("P1", "P6", "P1"))
+            if CFG["again"]:
+                settled()
+        else:
+            first[0] = CFG["olds"]
+            mm(R("P6", 0, I), R("idf"), lanes("Bf", ph), True, False)
+            first[0] = 0.0
 
     def ask(t):
-        ph = t % PH
-        s6, v6 = R("s16", 0, 6), R("sv16", 0, 6)
+        ph, patch = t % PH, CFG["patch"][t]
+        s6, v6, acc = R("s16", 0, 6), R("sv16", 0, 6), R("acc", 0, 6)
         zs = R("Z", 0, 16 * CAP, 16)
         first[0] = CFG["chain"]
-        na = CFG["signs"][t]
-        spots = [(0, na, R("acc", 0, na), -0.5, I / 2.0 + 8 * na), (na, 6, R("CN", 399, 400 * (6 - na), 400), 1.0, 0.0)]
-        if na == 6:
-            tt(R("a2", 0, 6), R("cn", 0, 6), R("acc", 0, 6), OP.subtract)
-            spots[0] = (0, 6, R("a2", 0, 6), 0.5, 0.0)
-        for out, f, c in (("sv16", 3.0, ph), ("s16", 1.0, 0), ("a8", 8.0, 0))[:3 if CFG["two"][t] else 2]:
-            for lo, hi, src, a, b in spots[:2 - (na == 6)]:
-                ts(R(out, lo, hi), src, a * f, b * f + c, OP.mult, OP.add)
-        gather(CFG["zs"], zs, at(R("meas"), v6))
+        ts(v6, acc, -3.0, 3.0 * IX / 2 + ph, OP.mult, OP.add)
+        ts(s6, acc, -1.0, IX / 2.0, OP.mult, OP.add)
+        copy(CFG["zs"], zs, at(R("meas"), v6))
         cp(R("uq16"), at(R("UQ"), s6))
-        act(R("Bs"), at(R("Bf"), v6))
+        act(R("Bs"), at(R("bas_i"), v6))
         act(R("AD2"), at(R("AD"), s6))
+        first[0] = 0.0
+        spots(t)
+        first[0] = CFG["chain"]
         ts(R("U2"), R("uq16"), -V / 2.0, None, OP.add)
-        mm(R("P4", 0, CAP), R("idb"), R("U2"), True, False)
+        turned = CFG["turned"] > 1
+        if turned:
+            mm(R("P4", 0, 128) + (0, CAP), R("U2"), R("idb"), True, False)
+        else:
+            mm(R("P4", 0, CAP), R("idb"), R("U2"), True, False)
         lo, qm, nb = 0, R("qm%d" % t), 0
         for k, (who, n) in enumerate(CFG["ask1"][t]):
             hi = lo + n
-            key, gq = R("P4", lo, hi), R("GQ", 16 * lo, 16 * hi)
+            key, gq = R("P4", 0, 128) + (lo, hi) if turned else R("P4", lo, hi), R("GQ", 16 * lo, 16 * hi)
             if who == "p":
                 for a in range(lo, hi, 32):
                     b, bank = min(a + 32, hi), CFG["abank"][nb]
                     nb += 1
                     w = 16 * (b - a)
                     act(R("GQ", 16 * a, 16 * b), at(qm, R("uq16", a, b)))
-                    mm(R(bank, 0, w), R("zer"), R("rmask", 0, w), True, False)
                     for j in range(16):
-                        mm(R(bank, j, w, 16), R("idb"), R("Z", 16 * a, 16 * b, 16), False, False)
+                        mm(R(bank, j, w, 16), R("idb"), R("Z", 16 * a, 16 * b, 16), j == 0, False)
                     mm(R(bank, 0, w), R("idn"), R("GQ", 16 * a, 16 * b), False, True)
                     act(R("SQ", 16 * a, 16 * b), R(bank, 0, w), AF.Abs)
                 terms = [("selk", "SQ")]
             else:
                 fold(R("RQ", 16 * lo, 16 * hi), R("Z", 16 * lo, 16 * hi))
-                tt(gq, at(qm, R("uq16", lo, hi)), R("RQ", 16 * lo, 16 * hi), OP.subtract)
-                if who == "t":
-                    act(R("SQ", 16 * lo, 16 * hi), gq, AF.Abs)
+                if who == "q":
+                    for a in range(lo, hi, 32):
+                        b, bank = min(a + 32, hi), CFG["abank"][nb]
+                        nb += 1
+                        w = 16 * (b - a)
+                        act(R("GQ", 16 * a, 16 * b), at(qm, R("uq16", a, b)))
+                        mm(R(bank, 0, w), R("idb"), R("RQ", 16 * a, 16 * b), True, False)
+                        mm(R(bank, 0, w), R("idn"), R("GQ", 16 * a, 16 * b), False, True)
+                        act(R("SQ", 16 * a, 16 * b), R(bank, 0, w), AF.Abs)
                     terms = [("selk", "SQ")]
+                elif who == "r":
+                    act(gq, at(qm, R("uq16", lo, hi)))
+                    sums(key, lo, hi, [("selk", "GQ")], False, turned)
+                    head = R("GQ", 16 * lo, 16 * hi, 16)
+                    tt(head, head, R("Z", 16 * lo, 16 * hi, 16), OP.min)
+                    scan(R("SQ", 16 * lo, 16 * hi), R("RQ", 16 * lo, 16 * hi), gq, OP.max, OP.min)
+                    terms = [("selm", "SQ")]
                 else:
-                    ts(R("SQ", 16 * lo, 16 * hi), gq, 0.0, None, OP.max)
-                    terms = [("seln", "GQ"), ("selp", "SQ")]
-            if [w for w, _ in CFG["ask1"][t][k + 1:k + 2]] == [who]:
-                lo = hi
-                continue
-            lo = sum(m for w, m in CFG["ask1"][t][:min(j for j in range(k + 1) if all(w == who for w, _ in CFG["ask1"][t][j:k + 1]))])
-            key = R("P4", lo, hi)
-            sums(key, lo, hi, terms, hi == CAP)
+                    tt(gq, at(qm, R("uq16", lo, hi)), R("RQ", 16 * lo, 16 * hi), OP.subtract)
+                    if who == "t":
+                        act(R("SQ", 16 * lo, 16 * hi), gq, AF.Abs)
+                        terms = [("selk", "SQ")]
+                    else:
+                        ts(R("SQ", 16 * lo, 16 * hi), gq, 0.0, None, OP.max)
+                        terms = [("seln", "GQ"), ("selp", "SQ")]
+            kinds = [w if w in "sr" else "" for w, _ in CFG["ask1"][t]]
+            if CFG["join"][t]:
+                if kinds[k + 1:k + 2] == [kinds[k]]:
+                    lo = hi
+                    continue
+                lo = sum(m for w, m in CFG["ask1"][t][:min(j for j in range(k + 1) if len(set(kinds[j:k + 1])) == 1)])
+            key = R("P4", 0, 128) + (lo, hi) if turned else R("P4", lo, hi)
+            sums(key, lo, hi, terms, hi == CAP, turned)
             lo = hi
-        winners([(R("P4", 0, CAP), 0, CAP)], "KT2", "KS2", CAP, R("P4", 100, 106), R("mi", 24, 30), R("mh", 24, 30), R("n16", 0, 6))
+        if turned:
+            answers()
+        else:
+            winners([(R("P4", 0, CAP), 0, CAP)], "KT2", "KS2", CAP, R("P4", 100, 106), R("mi", 24, 30), R("mh", 24, 30), R("n16", 0, 6))
+        if CFG["mor"][t]:
+            first[0] = 0.0
+            morphs(t)
+            first[0] = CFG["chain"]
         tt(R("E2"), at(R("qw%d" % t), R("n16", 0, 6)), R("Bs"), OP.max)
         ts(R("E2"), R("E2"), 4095, None, OP.bitwise_and)
         cp(R("e216"), R("E2"))
+        if patch and t + 1 < RO and CFG["wlate"]:
+            F["behind"]()
+            copy(CFG["wev"], lanes("W", ph), R("P1", 0, I))
         lo = 0
         for who, n in CFG["ask2"][t]:
-            gather(who, R("GQ", 16 * lo, 16 * (lo + n)), at(R("morc") if CFG["two"][t] == 1 else MO, R("e216", lo, lo + n)))
+            copy(who, R("GQ", 16 * lo, 16 * (lo + n)), at(R("morc"), R("e216", lo, lo + n)))
             fold(R("SQ", 16 * lo, 16 * (lo + n)), R("GQ", 16 * lo, 16 * (lo + n)))
             lo += n
         first[0] = 0.0
-        if t + 1 == RO and CFG["dtwo"]:
-            cp(R("KT2"), R("E2"))
-            tt(R("Bs"), at(R("Dv"), v6), R("KT2"), OP.subtract)
-        else:
+        if not patch:
             cp(at(R("Ea"), s6), R("E2"))
-        if CFG["two"][t]:
-            z6 = R("P4", 240, 246)
-            for x in range(16):
-                mm(z6, sk("selz", x), R("Z", 16 * x, 16 * CAP, 256), x == 0, x == 15)
-            ts(R("nz", 0, 6), z6, float(t), None, OP.add)
-            ts(R("nz", 0, 6), R("nz", 0, 6), 7, None, OP.bitwise_and)
-            tt(R("a8", 0, 6), R("a8", 0, 6), R("nz", 0, 6), OP.add)
-            cp(R("z16", 0, 6), R("a8", 0, 6))
+        elif t + 1 < RO:
+            tt(R("NE2"), R("E2"), R("Bs"), OP.not_equal)
+            w2 = R("P4", 410, 410 + CAP)
+            mm(w2, R("cst"), R("oneb", 0, CAP), True, False)
+            mm(w2, R("tri"), R("NE2"), False, True)
+            tt(R("W2"), w2, R("E2"), OP.add)
+            if patch == 2:
+                tt(R("Wd"), at(R("W", 0, VX), v6), R("W2"), OP.subtract)
+        elif patch == 2:
+            cp(R("W2"), R("E2"))
+            tt(R("Wd"), at(R("Dv", 0, VX), v6), R("W2"), OP.subtract)
+        if CFG["mz"][t]:
             tt(R("dxs"), at(R("morph", 0, 8 * IX), R("z16", 0, 6)), zs, OP.subtract)
-        if CFG["two"][t] == 2:
-            morphs(t)
         first[0] = CFG["chain"]
-        top, g2 = R("SQ", 15, 16 * CAP, 16), R("P4", 128, 128 + CAP)
+        top, two = R("SQ", 15, 16 * CAP, 16), twice(t)
         tt(R("MM2"), top, zs, OP.min)
-        mm(g2, R("blkn"), R("AD2"), True, False)
-        mm(g2, R("blk"), zs, False, False)
-        mm(g2, R("blk"), top, False, False)
-        mm(g2, R("blk2n"), R("MM2"), False, True)
-        decide(CFG["non"][1], R("adb"), g2)
+        terms = (("blkn", R("AD2")), ("blk", zs), ("blk", top), ("blk2n", R("MM2")))
+        for k, (s, r) in enumerate(terms):
+            for h in range(two):
+                mm(R("P4", 128 + CAP * h, 128 + CAP * (h + 1)), R(s), r, k + h == 0, k == 3 and h + 1 == two)
+        summed = CFG["non"][1] == "a" and patch and t + 1 < RO and two == 1
+        decide(CFG["non"][1], R("adb", 0, two * CAP), R("P4", 128, 128 + two * CAP), col("cnt", 1) if summed else None)
+        if patch and t + 1 < RO and not summed:
+            first[0] = 0.0
+            act(R("junk", 0, CAP), R("adb", 0, CAP), accum=col("cnt", 1))
         first[0] = 0.0
 
-    def change(t):
-        ph = t % PH
-        non, d, x, dn = R("non", 0, I), lanes("Dv", ph), R("XD"), R("P1", 0, I)
-        first[0] = CFG["end"]
-        if t + 1 == RO and CFG["dtwo"]:
-            tt(R("Bs"), R("adb"), R("Bs"), OP.mult)
-            tt(at(R("Dv"), R("sv16", 0, 6)), R("KT2"), R("Bs"), OP.add)
-            dma("s", T.yd[:], DV)
-            tt(R("dxs"), R("adb"), R("dxs"), OP.mult)
-            tt(at(R("morph", 0, 8 * IX), R("z16", 0, 6)), R("Z", 0, 16 * CAP, 16), R("dxs"), OP.add)
-            dma("a", T.ym[:], MO)
-            return
-        if CFG["two"][t]:
-            tt(R("dxs"), R("adb"), R("dxs"), OP.mult)
-            tt(at(R("morph", 0, 8 * IX), R("z16", 0, 6)), R("Z", 0, 16 * CAP, 16), R("dxs"), OP.add)
-        cp(at(R("non"), R("s16", 0, 6)), R("adb"))
-        if not CFG["two"][t]:
-            morphs(t)
-        if t + 1 == RO:
-            dma("a", T.ym[:], MO)
-        first[0] = 0.0
-        mm(R("P6", 0, I), R("idK2"), non, False, True)
-        if t + 1 < RO:
-            first[0] = CFG["olds"]
-            mm(R("P5", 0, I), R("idf"), lanes("Bf", ph), True, False)
-            first[0] = 0.0
-            mm(R("P5", 0, I), R("idK"), non, False, True)
-        tt(x, R("P6", 0, I), R("Ea", 0, I), OP.max)
-        w = R("P6", 0, I)
-        if t + 1 < RO:
-            tt(lanes("NEQ", ph), R("P5", 0, I), x, OP.not_equal)
-        mm(dn, R("idKn"), non, True, False)
-        mm(dn, R("idf"), x, False, True)
-        if t + 1 < RO and CFG["late"]:
-            late.append(lambda: act(d, dn))
-        else:
-            act(d, dn)
-        if t + 1 == RO:
-            dma("s", T.yd[:], DV)
-            return
-        for k, (s, r) in enumerate((("idf", x), ("cst", R("oneb", 0, I)), ("idKn", non), ("tri", lanes("NEQ", ph)))):
-            mm(w, R(s), r, k == 0, k == 3)
-        gather(CFG["wev"], lanes("W", ph), w)
-        offer(t + 1, R("qw%d" % (t + 1)), R("W"), "rw%d" % (t + 1))
-        o = R("P4", 330, 354)
+    def far(t):
+        return not CFG["mz"][t], CFG["patch"][t] == 1 or (CFG["patch"][t] == 2 and t + 1 < RO)
+
+    def twice(t):
+        return 2 if all(far(t)) else 1
+
+    def spots(t):
+        y = R(CFG["ybank"], 0, 6)
+        mm(y, R("idb"), ch("tz", t, 6), True, False)
         for x in range(16):
-            mm(o, sk("sel1", x), R("non", x, I, 16), x == 0, x == 15)
-        if CFG["cnt"] == "a":
-            act(R("junk", 0, 24), o, accum=col("cnt"))
+            mm(y, sk("selz", x), R("Z", 16 * x, 16 * CAP, 256), False, x == 15)
+        ts(R("r2", 0, 6), y, 16 * ROUND, 16 * ROUND, OP.add, OP.subtract)
+        tt(R("z2", 0, 6), y, R("r2", 0, 6), OP.subtract)
+        if CFG["mz"][t]:
+            mm(y, R("id16n"), R("acc", 0, 6), True, False)
+            mm(y, R("idb"), R("z2", 0, 6), False, True)
+            ts(R("z16", 0, 6), y, 0.5, 4.0 * IX + 3.5, OP.mult, OP.add)
+
+    def close(t):
+        ph, patch, two = t % PH, CFG["patch"][t], twice(t)
+        s6, v6, acc, zs, adb = R("s16", 0, 6), R("sv16", 0, 6), R("acc", 0, 6), R("Z", 0, 16 * CAP, 16), R("adb", 0, CAP)
+        bank, (fz, fw) = "P6" if patch else "P5", far(t)
+        zo, wo = R(bank, 0, 6), R(bank, 6 * (two - 1), 6 * two)
+        if fz:
+            mm(zo, R("id16n"), acc, True, False)
+            mm(zo, R("idb"), R("z2", 0, 6), False, False)
+        if fw:
+            mm(wo, R("id12n"), acc, not fz, False)
+        first[0] = CFG["end"]
+        if patch == 2:
+            tt(R("Wd"), adb, R("Wd"), OP.mult)
+            tt(at(R("W" if t + 1 < RO else "Dv", 0, VX), v6), R("W2"), R("Wd"), OP.add)
+        if not fz:
+            tt(R("dxs"), adb, R("dxs"), OP.mult)
+            tt(at(R("morph", 0, 8 * IX), R("z16", 0, 6)), zs, R("dxs"), OP.add)
+        if not patch:
+            cp(at(R("non"), s6), adb)
+        for x in range(16 * (fz or fw)):
+            mm(R(bank, 0, 6 * two), sk("selo", x), R("adb", x, two * CAP, 16), False, x == 15)
+        if fw:
+            ts(R("z16", 8, 14), wo, 0.25, 3.0 * IX / 2 + ph, OP.mult, OP.add)
+            if patch == 1 and t + 1 < RO:
+                cp(at(R("W"), R("z16", 8, 14)), R("W2"))
+        if fz:
+            ts(R("z16", 0, 6), zo, 0.5, 4.0 * IX + 3.5, OP.mult, OP.add)
+        if fw and t + 1 == RO:
+            cp(at(R("Dv"), R("z16", 8, 14)), R("E2"))
+        if t + 1 == RO:
+            dma("s", T.yd[:], DV)
+        if fz:
+            cp(at(R("morph"), R("z16", 0, 6)), zs)
+        first[0] = 0.0
+        if t + 1 == RO:
+            dma("a", T.ym[:], MO)
+            return
+        if patch:
+            offer_lists(t + 1)
+            cp(at(R("Dv"), R("z16", 8, 14)), R("E2"))
         else:
-            red(col("cnt"), o)
-        mm(R("P4", 400, 401), R("oalln"), col("cnt"), True, True)
-        ts(col("nmi"), R("P4", 400, 401), 8.0 * I, None, OP.add)
-        ts(col("nmi"), col("nmi"), 127, None, OP.bitwise_and)
-        if "v" in CFG["non"]:
-            ts(col("mg"), col("nmi"), -1.0, -0.5, OP.mult, OP.add)
+            lists(t, ("P1", "P6", CFG["wbank"]))
+            offer_lists(t + 1)
+        if CFG["non"][0] == "v" or not CFG["patch"][t]:
+            counts()
+        a = R("P4", 400, 401)
+        terms = (2, 0, 1) if CFG["patch"][t] else (2, 0)
+        for k in terms:
+            mm(a, R("oalln"), col("cnt", k), k == terms[0], k == terms[-1])
+        ts(col("mg", 2), a, 128 * ROUND, 128 * ROUND, OP.add, OP.subtract)
+        ts(col("mg"), col("mg", 2), a, -64.0, OP.subtract, OP.add)
         if "a" in CFG["non"]:
-            ts(col("mg", 1), col("nmi"), 256.0, 128.0, OP.mult, OP.add)
+            act(col("mg", 1), col("mg"), scale=-256.0)
 
     spread(0)
     hand(R("qm0"), [R("qm%d" % t) for t in range(RO)], MS, "rm0")
+    if CFG["use0"]:
+        F["behind"]()
+        offer(0, R("qk0"), R("use_i"), "rk0")
     search(0)
-    cp(R("USE"), R("use_i"))
-    offer(0, R("qk0"), R("USE"), "rk0")
+    if CFG["use0"]:
+        cp(R("USE", I, C), R("use_i", I, C))
+    else:
+        cp(R("USE"), R("use_i"))
+        offer(0, R("qk0"), R("USE"), "rk0")
     first[0] = CFG["d16"]
     old_lists(0)
     first[0] = 0.0
     tables()
-    offer(0, R("qw0"), R("W"), "rw0")
+    offer_lists(0)
     first[0] = CFG["later"]
     targets()
     later(1)
@@ -1349,9 +1373,10 @@ def rank_program(g, core, T, topo):
         ask(t)
         if t + 1 < RO:
             search(t + 1)
-        change(t)
+        close(t)
     come = []
     for t in range(RO):
         a, b = len(topo.engines(asked[t], core)), len(topo.engines(helper(topo, T.cores, asked[t]), core))
-        come += [(R("qm%d" % t), "rm%d" % t, b), (R("qk%d" % t), "rk%d" % t, a), (R("qw%d" % t), "rw%d" % t, a)]
+        come += [(R("qm%d" % t), "rm%d" % t, b), (R("qk%d" % t), "rk%d" % t, a), (R("qw%d" % t, 0, CFG["straight"][t]), "rw%d" % t, a)]
+        come += [(R("qw%d" % t, CFG["straight"][t], V), "rh%d" % t, b)] * (CFG["straight"][t] < V)
     F["issue"](come)

from concourse.mybir import AluOpType as OP, ActivationFunctionType as AF

NR = 6
P, V, C, PH, I, CAP, RO = 3072, 1152, 512, 3, 384, 96, 4
IX = I + CAP
VX = V + PH * CAP
W16 = 16 * I
PC = 32
FAR = 3072
DW = 388
BIG = float(1 << 23)
ROUND = 1.5 * 2.0 ** 23
IN_ORDER = 1e6
CFG = {
    "search": [[("s", 128), ("r", 128), ("p", 128)]] + [[("r", 128), ("r", 128), ("p", 128)]] * 3, "loads": "mdb",
    "ask1": [[("s", 96)]] * 3 + [[("s", 32), ("p", 32), ("t", 32)]],
    "old": [[("a", 96)] * 4] + [[("2", 128)] * 3] * 3,
    "new": [[("v", 64), ("a", 128), ("v", 64), ("a", 128)]] + [[("a", 96), ("2", 160), ("a", 128)]] * 3,
    "ask2": [[("a", 26), ("v", 44), ("a", 26)]] * 4,
    "x0": 256, "cut": 256, "pc": {"s": 32, "r": 64, "p": 64, "t": 32}, "non": "vv", "zs": "v", "late": 1, "wev": "a", "neq": 0,
    "patch": [0, 0, 0, 2], "bf": "g", "dv": "", "use0": 1, "heads": 1, "xcut": 1, "wlate": 1, "mor": [0, 0, 0, 0],
    "turned": 1, "kbank": ("P0", "P0", "P7"), "mz": [1, 1, 1, 0], "again": 1, "join": [1, 1, 1, 1], "straight": [704, 704, 704, 704], "rs": 64, "ms": [1, 1, 1, 1], "fs": {}, "wbank": "P5", "ybank": "P3",
    "rest": 50.0, "dbw": 220e3, "dma0": 1.6, "peo": 0.015, "dear": 0.7, "scat": 4.2, "dsc": -1.7, "m1": 20.0, "use": [5.0, 5.0, 5.0, 0.0], "olds": 20.0,
    "abank": ("P2", "P3", "P5"), "obank": "P0", "bulk": ("GA", "GD", "GE", "SD", "SE"),
    "hop": 0.2, "hop2": 0.18, "gath": 1.35, "pe": 0.47e-3, "link": 30e3,
    "chain": 1, "end": 6, "later": 6, "d16": 10.0, "send": 20.0, "send0": 3e6, "mu": 1, "muy": [1, 1, 1, 0],
    "look": 12, "passes": 3, "mix": (0.0, 0.3, 0.6), "tries": 400000, "moves": 12, "jit": 1.5, "both": 1.0,
    "seed": 4, "near": (0.05, 0.05), "pull": 0.001, "steps": 800, "span": 100,
}
SCRATCH = {}
VIEW = {"idb": ("idw", 16), "blk": ("blkw", 0), "blkn": ("blks", 0), "blk2n": ("blks", 128), "tri": ("tris", 0), "trin": ("tris", 128),
        "id16n": ("ids", 0), "id12n": ("ids", 128), "wlo": ("ids", 256), "whi": ("ids", 384), "oalln": ("ids", 512), "idf": ("ids", 640)}
VIEW.update({n: ("idm", 128 * k) for k, n in enumerate(["idK", "idKn", "idK2", "zer", "idn", "idbig", "tlo", "thi", "cst", "cs2", "cstn", "blo", "bhi", "idH"])})
WHOLE = ["pi"]
SMALL = ["pm", "pw", "cb", "acc", "mg", "cnt", "r2"]


def _sb(dtype, **kw):
    for n, w in kw.items():
        SCRATCH[n] = ("sbuf", [128, w], dtype)


_sb("int32", bas_i=VX, der_i=V, use_i=C, whole=8 * len(WHOLE), clsi=96, zi=96, Ea=IX, E2=CAP, qk0=C)
_sb("float32", mi=64, mix=128)
_sb("bfloat16", swb=400, dxs=CAP)
_sb("uint16", cls=96, u16=I, d16=RO * DW, e16=I + 2, m16=24, s16=8, sv16=8, n16=8, uq16=CAP, e216=CAP, z16=16, zw=24)
_sb("float32", Bf=V, Dv=VX + FAR // 2 * (CFG["patch"] != [0, 0, 0, 2]), W=VX + FAR // 2 if any(CFG["patch"][:3]) else V, USE=C, onef=144, ids=768, selr=144,
    small=8 * len(SMALL), i8=96, amask=I, KT=I, KS=512, LXg=I, UQ=IX, KT2=CAP, KS2=128, Bs=CAP, W2=CAP, Wd=CAP, XD=I, W1=400)
_sb("float16", U=I, U2=CAP, mh=64, m1=72, Eh=256)
_sb("bfloat16", sw0=160, sw1=160, idw=160, blkw=144, idm=1792, cyc=384)
_sb("float32", VR=I)
_sb("bfloat16", morc=P, meas=VX, morph=8 * IX + FAR, oneb=IX, sel1=144, selm=144, selk=144, selp=144, seln=144, selz=144,
    selo=144, blks=256, tris=256, dg=400, rmask=2048, rmask8=1296, tz=24, z2=8,
    Z=16 * CAP, EQ=I, GA=8 * I + 16, GD=8 * I + 16, SD=8 * I + 16, GE=W16 + 32, SE=W16, AD=IX, AE=I, non=IX, cum=IX, junk=IX, NEQ=V,
    GQ=16 * CAP, RQ=16 * CAP, SQ=16 * CAP, MM2=CAP, AD2=CAP, NE2=CAP, adb=2 * CAP, x0=W16, x1=W16)
SCRATCH["b15i"] = ("sbuf", [8, V], "int32")
SCRATCH["b15"] = ("sbuf", [8, I], "float16")
SCRATCH["sel8"] = ("sbuf", [8, 144], "bfloat16")
SCRATCH["one8"] = ("sbuf", [8, 144], "bfloat16")
for _t in range(RO):
    _sb("bfloat16", **{"qm%d" % _t: V})
    _sb("float32", **{"qw%d" % _t: V})
    if _t or not CFG["use0"]:
        _sb("float32", **{"qk%d" % _t: C})
for _t in range(8):
    SCRATCH["P%d" % _t] = ("psum", [128, 512], "float32")
SEMAPHORES = (["q_v", "q_a", "q_t", "q_g"] + ["d%d" % k for k in range(20)] + ["l%d" % k for k in range(16)]
              + ["r%s%d" % (a, k) for a in "mkwh" for k in range(RO)])
CYC = 0.83e-3
WIDE = {"int32": 4, "float32": 4, "bfloat16": 2, "uint16": 2, "float16": 2}


def R(name, lo=0, hi=None, step=1):
    if name in SMALL:
        return ("small", 8 * SMALL.index(name) + lo, 8 * SMALL.index(name) + hi, step)
    if name in VIEW:
        return (VIEW[name][0], VIEW[name][1] + lo, VIEW[name][1] + 128, step)
    if name in WHOLE:
        return ("whole", 8 * WHOLE.index(name) + lo, 8 * WHOLE.index(name) + hi, step)
    return (name, lo, SCRATCH[name][1][1] if hi is None else hi, step)


def size(r):
    return 16 * size(r[2]) if r[0] == "@" else (r[2] - r[1] + r[3] - 1) // r[3]


def accesses(reads, writes):
    a = []
    for w, rs in ((0, reads), (1, writes)):
        for r in rs:
            a += [(r[1], w), (r[2], 0)] if r[0] == "@" else [(r, w)]
    return a


def clash(q, a, p, b):
    (n, lo, hi, st), w = a[0][:4], a[1]
    (l2, h2, s2), w2 = b[0][1:4], b[1]
    if SCRATCH[n][0] == "psum" and (q != p or q == "t"):
        return True
    if st > 1 and st == s2 and (lo - l2) % st:
        return False
    return (w or w2) and lo < h2 and l2 < hi


def improve(order, need, pred, succ, c0, c1, lat, que, steps, fixed):
    n, both = len(order), CFG["both"]
    give = [[] for _ in order]
    for i in range(n):
        for p, d in need[i]:
            give[p].append((i, d))
    pos, up, down = [0] * n + [n], [n] * (n + 1), [n] * (n + 1)
    e0, e1, t0, t1 = ([0.0] * (n + 1) for _ in range(4))

    def ahead(k, hi, stop, log):
        while k <= hi and k < stop:
            i = order[k]
            k += 1
            a, b = e0[up[i]], e1[up[i]]
            for p, d in need[i]:
                if e0[p] + d > a:
                    a = e0[p] + d
                if e1[p] + d > b:
                    b = e1[p] + d
            a += c0[i]
            b += c1[i]
            if a != e0[i] or b != e1[i]:
                log.append((i, e0[i], e1[i]))
                e0[i], e1[i] = a, b
                if hi < stop:
                    if pos[down[i]] > hi:
                        hi = pos[down[i]]
                    for s, d in give[i]:
                        if pos[s] > hi:
                            hi = pos[s]

    def back(lo, k, stop):
        while k >= lo and k >= stop:
            i = order[k]
            k -= 1
            a, b = t0[down[i]], t1[down[i]]
            for s, d in give[i] or ((n, lat[i]),):
                if t0[s] + d > a:
                    a = t0[s] + d
                if t1[s] + d > b:
                    b = t1[s] + d
            a += c0[i]
            b += c1[i]
            if a != t0[i] or b != t1[i]:
                t0[i], t1[i] = a, b
                if lo > stop:
                    if up[i] < n and pos[up[i]] < lo:
                        lo = pos[up[i]]
                    for p, d in need[i]:
                        if pos[p] < lo:
                            lo = pos[p]

    def place(lo, part, before, behind):
        last = dict(before)
        for k, i in enumerate(part):
            order[lo + k], pos[i], up[i] = i, lo + k, last[que[i]]
            down[up[i]] = i
            last[que[i]] = i
        for q, i in last.items():
            down[i] = behind[q]
            up[behind[q]] = i
        down[n] = up[n] = n

    ends = {q: n for q in que}
    keep, x = (1e9, None), CFG["seed"]
    for step in range(steps + 1):
        place(0, list(order), ends, ends)
        ahead(0, n, n, [])
        order.sort(key=lambda i: e0[i] - c0[i] + e1[i] - c1[i])
        place(0, list(order), ends, ends)
        back(0, n - 1, 0)
        top = [max(t0), max(t1)]
        if top[0] + both * top[1] < keep[0]:
            keep = (top[0] + both * top[1], list(order))
        if step == steps:
            return keep[1], keep[0]
        x = (x * 1103515245 + 12345) % 2 ** 31
        first = max(0, (x >> 8) % (n + CFG["span"] // 2) - CFG["span"] // 2)
        stop = min(n, first + CFG["span"])
        out, by = [], [0.0, 0.0]
        for i in order[:stop]:
            far = [(s, d) for s, d in give[i] or ((n, lat[i]),) if pos[s] >= stop]
            if pos[i] < first and pos[down[i]] >= stop:
                far.append((down[i], 0.0))
            if far:
                u, v = max(d + t0[s] for s, d in far), max(d + t1[s] for s, d in far)
                if pos[i] < first:
                    by = [max(by[0], e0[i] + u), max(by[1], e1[i] + v)]
                else:
                    out.append((i, u, v))
        nxt = {que[i]: i for i in reversed(order[stop:])}
        heat, k, misses = CFG["jit"] * (1 - step / steps), 0, 0
        while k < CFG["tries"] // CFG["steps"] and misses < 20000:
            x = (x * 1103515245 + 12345) % 2 ** 31
            b = order[first + (x >> 8) % (stop - first)]
            a = up[b]
            e, t, c, m = (e0, t0, c0, 0) if x & 128 else (e1, t1, c1, 1)
            if a == n or pos[a] < first or a in pred[b] or e[a] + c[b] < e[b] - 1e-9 or e[b] - c[b] + t[b] < top[m] - CFG["near"][x >> 5 & 1]:
                misses += 1
                continue
            k += 1
            x = (x * 1103515245 + 12345) % 2 ** 31
            for _ in range((x >> 8) % CFG["moves"]):
                if x & 64 and first <= pos[up[a]] < n:
                    a = up[a]
                elif not x & 64 and pos[down[b]] < stop:
                    b = down[b]
            lo, hi = pos[a], pos[b]
            old = order[lo:hi + 1]
            if que[a] == "g" and not fixed.isdisjoint(old):
                continue
            part, seen, link = ({b}, set(), succ) if x & 64 else ({a}, set(), pred)
            for i in old[-2::-1] if x & 64 else old[1:]:
                if que[i] in seen or not part.isdisjoint(link[i]):
                    if que[i] == que[a]:
                        break
                    part.add(i)
                    seen.add(que[i])
            else:
                i = n
            if i < n:
                continue
            new = [j for j in old if (j in part) == bool(x & 64)] + [j for j in old if (j in part) != bool(x & 64)]
            before, behind = {}, {}
            for i in old:
                if que[i] not in before:
                    before[que[i]] = up[i]
                behind[que[i]] = down[i]
            place(lo, new, before, behind)
            log, room = [], top[0] + both * top[1] + heat * (x % 1024) / 1024
            ahead(lo, hi, hi + 1, log)
            u = v = 0.0
            far = hi
            for i in new:
                for s, d in give[i] + [(down[i], 0.0)]:
                    if pos[s] > hi:
                        if e0[i] + d + t0[s] > u:
                            u = e0[i] + d + t0[s]
                        if e1[i] + d + t1[s] > v:
                            v = e1[i] + d + t1[s]
                        if pos[s] > far:
                            far = pos[s]
            if u + both * v <= room:
                ahead(hi + 1, far, stop, log)
                u = max([by[0]] + [e0[i] + a for i, a, b in out] + [e0[up[i]] + t0[i] for i in nxt.values()])
                v = max([by[1]] + [e1[i] + b for i, a, b in out] + [e1[up[i]] + t1[i] for i in nxt.values()])
                if u + both * v + CFG["pull"] * sum(e0[i] - a + e1[i] - b for i, a, b in log) <= room:
                    top = [u, v]
                    back(min([pos[p] for i in new for p, d in need[i]] + [pos[j] for j in before.values()] + [lo]), hi, first)
                    continue
            for i, a, b in reversed(log):
                e0[i], e1[i] = a, b
            place(lo, old, before, behind)


def plan(calls):
    n = len(calls)
    pred, succ, seen = [set() for _ in calls], [set() for _ in calls], {}
    for i, c in enumerate(calls):
        for a in c["acc"] + c["also"]:
            keep = []
            for j, b in seen.get(a[0][0], []):
                if j != i and clash(c["q"], a, calls[j]["q"], b):
                    pred[i].add(j)
                    if (a[1] and a[0][3] == 1 and a[0][1] <= b[0][1] and b[0][2] <= a[0][2]) or (a[1] and a[0] == b[0]):
                        continue
                    if SCRATCH[a[0][0]][0] == "psum" and c["q"] == "t":
                        continue
                keep.append((j, b))
            seen[a[0][0]] = keep + [(i, a)]
        pred[i].update(c["after"])
        for j in pred[i]:
            succ[j].add(i)

    def gap(i, j):
        if i in calls[j]["after"]:
            return calls[j]["after"][i]
        return calls[i]["lat"] + (0.0 if calls[i]["q"] == calls[j]["q"] == "t" else CFG["hop"])

    def run(before, after, rank, back):
        if not back:
            rank = [r + c["first"] for r, c in zip(rank, calls)]
        left = [len(b) for b in before]
        ready, start, free = [0.0] * n, [0.0] * n, {}
        pool = {}
        for i in range(n):
            if not left[i]:
                pool.setdefault(calls[i]["q"], []).append(i)
        done, ahead = [False] * n, {}
        for i in sorted(range(n), key=lambda i: rank[i]):
            ahead.setdefault(calls[i]["q"], []).append(i)

        def soon(b, limit):
            return ready[b] if all(done[p] for p in before[b]) else limit

        todo = n
        while todo:
            now, q = min((max(free.get(q, 0.0), min(ready[i] for i in l)), q) for q, l in pool.items() if l)
            i = max((i for i in pool[q] if ready[i] <= now), key=lambda i: rank[i])
            cost, wait = calls[i]["cost"], None
            while done[ahead[q][-1]]:
                ahead[q].pop()
            for b in [b for b in ahead[q][-CFG["look"]:] if not done[b] and rank[b] > rank[i]]:
                r = soon(b, now + cost)
                if now < r < now + cost:
                    go = max(rank[i] + now, rank[b] + now + cost)
                    hold = max(rank[b] + r, rank[i] + r + calls[b]["cost"]) + calls[b]["mu"] * (r - now)
                    if hold < go:
                        wait = r if wait is None else min(wait, r)
            if wait is not None:
                free[q] = wait
                continue
            at, todo, done[i] = now, todo - 1, True
            pool[q].remove(i)
            start[i] = at
            free[q] = at + calls[i]["cost"]
            for j in after[i]:
                ready[j] = max(ready[j], free[q] + (gap(j, i) if back else gap(i, j)))
                left[j] -= 1
                if not left[j]:
                    pool.setdefault(calls[j]["q"], []).append(j)
        return start, max(start[i] + calls[i]["cost"] + calls[i]["lat"] for i in range(n))

    rank = [0.0] * n
    for i in reversed(range(n)):
        rank[i] = calls[i]["cost"] + max([calls[i]["lat"]] + [gap(i, j) + rank[j] for j in succ[i]])
    best = run(pred, succ, rank, False)
    now = best
    for _ in range(CFG["passes"]):
        back = run(succ, pred, [s + c["cost"] for s, c in zip(now[0], calls)], True)
        now = min((run(pred, succ, [a * r + (1 - a) * (s + c["cost"]) for r, s, c in zip(rank, back[0], calls)], False) for a in CFG["mix"]),
                  key=lambda x: x[1])
        if now[1] < best[1]:
            best = now
    order = sorted(range(n), key=lambda i: (best[0][i], i))

    CFG["hop"], hop = CFG["hop2"], CFG["hop"]
    need = [[(p, gap(p, i)) for p in pred[i]] for i in range(n)]
    CFG["hop"] = hop
    cost, lat, que = [c["cost"] for c in calls], [c["lat"] for c in calls], [c["q"] for c in calls]
    slow = [c["slow"] for c in calls]
    PLAN["all"] = (order, need, pred, succ, cost, slow, lat, que, calls)
    order, top = improve(order, need, pred, succ, cost, slow, lat, que, CFG["steps"] // 3, set())

    sends = [i for i in order if que[i] == "g" and calls[i]["sem"]]
    for i in sends:
        end, last = {}, {}
        for j in order:
            end[j] = last[que[j]] = max([last.get(que[j], 0.0)] + [end[p] + d for p, d in need[j]]) + cost[j]
        ready, k = max(end[p] + d for p, d in need[i]), order.index(i)
        to = k
        while order[k - 1] not in pred[i]:
            k -= 1
            if que[order[k]] == "g":
                if end[order[k]] - cost[order[k]] / 2 < ready:
                    break
                to = k
        order.remove(i)
        order.insert(to, i)
    return improve(order, need, pred, succ, cost, slow, lat, que, CFG["steps"] - CFG["steps"] // 3, set(sends))


PLAN = {}


def make(g, T):
    eng = {"v": g.vector, "a": g.scalar, "t": g.tensor, "g": g, "s": g.sync}
    calls, total, lines, first = [], {}, {}, [0.0, CFG["mu"]]

    def ap(r):
        if r[0] == "@":
            return ap(r[1]).indirect(ap(r[2]))
        n, lo, hi, st = r[:4]
        rows = slice(*r[4:]) if r[4:] else slice(None)
        return T[n][rows, lo:hi] if st == 1 else T[n][rows, lo:hi:st]

    def isr(x):
        return isinstance(x, tuple)

    def psum(r):
        return r[0] != "@" and SCRATCH[r[0]][0] == "psum"

    def note(q, reads, writes, call, cost, lat=0.0, sem=None, also=(), line=None, busy=0.0):
        if q in "va" and writes and writes[0][0] in CFG["bulk"]:
            line = q + ("g" if reads and reads[0][0] == "@" else "f")
        after = {lines[line][0]: lines[line][1]} if line in lines else {}
        if lines.pop("behind", None):
            after[len(calls) - 1] = 0.0
        if line:
            lines[line] = (len(calls), busy)
        calls.append({"q": q, "acc": accesses(reads, writes), "also": list(also), "call": [call], "cost": cost, "lat": lat, "sem": sem, "after": after,
                      "first": first[0] - (500.0 * len(calls) if first[0] >= IN_ORDER else 0.0), "mu": first[1],
                      "slow": cost + CYC * sum(f * size(r) for f, rs in ((CFG["dear"], reads), (CFG["dsc"], writes)) for r in rs if r[0] == "@")})

    def price(out, ins, rate=None):
        if out[0] == "@":
            return 0.05 + CFG["scat"] * CYC * size(out)
        if ins and ins[0][0] == "@":
            return 0.06 + CFG["gath"] * CYC * size(out)
        if rate is None:
            rate = 0.5 if all(WIDE[SCRATCH[r[0]][2]] == 2 for r in [out] + ins) else 1.0
        return 0.03 + CYC * max(64, rate * size(out))

    def tt(out, a, b, op):
        note("v", [a, b], [out], lambda: g.vector.tensor_tensor(out=ap(out), in0=ap(a), in1=ap(b), op=op),
             price(out, [a, b], 1.0 if psum(a) or psum(b) else 2.0))

    def ts(out, a, s1, s2, op0, op1=None):
        v = [ap(s) if isr(s) else s for s in (s1, s2)]
        kw = {} if op1 is None else {"op1": op1}
        note("v", [a] + [s for s in (s1, s2) if isr(s)], [out],
             lambda: g.vector.tensor_scalar(out=ap(out), in0=ap(a), scalar1=v[0], scalar2=v[1], op0=op0, **kw), price(out, [a]))

    def cp(out, a):
        note("v", [a], [out], lambda: g.vector.tensor_copy(out=ap(out), in_=ap(a)), price(out, [a]))

    def ms(out, c):
        note("v", [], [out], lambda: g.vector.memset(ap(out), c), price(out, []))

    def scan(out, a, b, op0, op1, initial=0.0):
        s = ap(initial) if isr(initial) else initial
        note("v", [a, b] + [initial] * isr(initial), [out],
             lambda: g.vector.tensor_tensor_scan(out=ap(out), data0=ap(a), data1=ap(b), initial=s, op0=op0, op1=op1), price(out, [a, b]))

    def tr(out, a):
        note("v", [a], [out], lambda: g.vector.transpose(out=ap(out), in_=ap(a)), price(out, [a]))

    def act(out, a, func=AF.Copy, bias=None, accum=None, scale=None, more=0.0):
        kw = {}
        if bias is not None:
            kw["bias"] = ap(bias) if isr(bias) else bias
        if scale is not None:
            kw["scale"] = ap(scale) if isr(scale) else scale
        if accum is not None:
            kw["accum_out"] = ap(accum)
            more += 0.02
        note("a", [a] + [b for b in [bias, scale] if isr(b)], [out] + [b for b in [accum] if b],
             lambda: g.scalar.activation(out=ap(out), in_=ap(a), func=func, **kw), price(out, [a], 1.0) + more)

    def mm(out, lhsT, rhs, start, stop):
        note("t", [lhsT, rhs], [out], lambda: g.tensor.matmul(ap(out), ap(lhsT), ap(rhs), start, stop),
             CFG["peo"] + CFG["pe"] * max(min(64, size(lhsT)), size(rhs)) * (4 if SCRATCH[rhs[0]][2] == "float32" else 1))
        a, b = calls[-2:]
        same = [x[0][0] for x in a["acc"][-3:]] == [lhsT[0], rhs[0], out[0]] and abs(a["acc"][-3][0][1] - lhsT[1]) < 128
        if a["q"] == "t" and len(a["call"]) < 4 and not start and same:
            calls.pop()
            for k in ("acc", "call", "cost", "slow"):
                a[k] += b[k]

    def iota(out, pattern, base, cm):
        kw = {} if SCRATCH[out[0]][2] == "int32" else {"allow_small_or_imprecise_dtypes": True}
        note("g", [], [out], lambda: g.iota(ap(out), pattern, base, cm, **kw), 0.13 + 2 * CYC * size(out))

    def aff(out, a, pattern, op, base, cm):
        note("g", [a], [out], lambda: g.affine_select(ap(out), ap(a), pattern, op, 0.0, base, cm), 0.17 + 2 * CYC * size(out))

    nd, nl = [0], [0]

    def nbytes(r):
        return SCRATCH[r[0]][1][0] * size(r) * WIDE[SCRATCH[r[0]][2]]

    def dma(q, out, a):
        s = "d%d" % nd[0]
        nd[0] += 1
        busy = nbytes(out if isr(out) else a) / CFG["dbw"]
        total[s] = 16
        note(q, [a] if isr(a) else [], [out] if isr(out) else [],
             lambda: eng[q].dma_start(out=ap(out) if isr(out) else out, in_=ap(a) if isr(a) else a).then_inc(T.sem[s], 16),
             0.05, CFG["dma0"] + busy, s, (), "dma", busy)

    def send(topo, dst, mask, out, land, a, rsem, near):
        s = "l%d" % nl[0]
        nl[0] += 1
        rid, pid, _ = topo.addr(dst)
        total[s] = bin(mask).count("1")
        far = 3.0 + nbytes(a) / CFG["link"]
        first[0] = CFG["send0"] if nl[0] == 1 else CFG["send"]
        note("g", [a], [], lambda: g.remote_dma(out_ap=ap(out), in_ap=ap(a), remote_sem=T.sem[rsem], local_sem=T.sem[s], pid=pid,
                                                routing_id=rid, dma_engine_mask=mask),
             0.5 if nl[0] > 1 else 3.5, far + (3.0 + nbytes(a) / 80e3 if near else 0.0), s, [(r, 1) for r in land])
        first[0] = 0.0

    def issue(arrivals):
        count, known, waited, hist = {}, {k: {} for k in eng}, {}, {}
        for land, rsem, n in arrivals:
            total[rsem] = n
            hist.setdefault(land[0], []).append(((land, 1), "remote", rsem, n, {}))
        if "order" not in PLAN:
            PLAN["order"], PLAN["end"] = plan(calls)
        for i in PLAN["order"]:
            c = calls[i]
            q, k = c["q"], known[c["q"]]
            need = [e for a in c["acc"] for e in hist.get(a[0][0], []) if clash(q, a, e[1], e[0]) and not (q == e[1] == "t" and psum(a[0]))]
            for e in sorted(need, key=lambda e: -e[3]):
                if k.get(e[2], 0) < e[3]:
                    eng[q].wait_ge(T.sem[e[2]], e[3])
                    waited[e[2]] = max(waited.get(e[2], 0), e[3])
                    for s, v in list(e[4].items()) + [(e[2], e[3])]:
                        k[s] = max(k.get(s, 0), v)
            if c["sem"]:
                c["call"][0]()
                s, v, p = c["sem"], total[c["sem"]], "dma"
            else:
                s, p = "q_" + q, q
                count[q] = total[s] = v = count.get(q, 0) + len(c["call"])
                for call in c["call"]:
                    call().then_inc(T.sem[s], 1)
            clock = dict(k)
            for a in c["acc"]:
                keep = [e for e in hist.get(a[0][0], [])
                        if not (psum(a[0]) and e[1] != q)
                        and not (a[1] and (e[0][0] == a[0] or (a[0][3] == 1 and a[0][1] <= e[0][0][1] and e[0][0][2] <= a[0][2])))
                        and not (e[0] == a and e[2] == s)]
                hist[a[0][0]] = keep + [(a, p, s, v, clock)]
        for s, n in total.items():
            if waited.get(s, 0) < n:
                g.wait_ge(T.sem[s], n)

    return {"tt": tt, "ts": ts, "cp": cp, "ms": ms, "scan": scan, "tr": tr, "act": act, "mm": mm, "iota": iota, "aff": aff,
            "first": first, "behind": lambda: lines.update(behind=1), "dma": dma, "send": send, "issue": issue}


def helper(topo, cores, core):
    return [c for c in topo.cores_of(core) if topo.die(c) != topo.die(core) and all(topo.may_write(c, d) for d in cores)][0]


def hand_on(g, core, T, topo, rank):
    home = T.cores[rank]
    n, near = 0, bin(topo.mask(home, core) & ~topo.mask(home, T.cores[rank - 1])).count("1")
    g.wait_ge(T.sem["rm0"], near)
    for t in range(RO):
        dst = T.cores[(rank - 1 - t) % NR]
        rid, pid, _ = topo.addr(dst)
        g.remote_dma(out_ap=T["qm%d" % t][:], in_ap=T["qm0"][:], remote_sem=T.sem["rm%d" % t],
                     local_sem=T.sem["l0"], pid=pid, routing_id=rid, dma_engine_mask=topo.mask(core, dst))
        n += len(topo.engines(core, dst))
        lo = CFG["straight"][t]
        if lo < V:
            g.wait_ge(T.sem["rh%d" % t], near)
            g.remote_dma(out_ap=T["qw%d" % t][:, lo:V], in_ap=T["qw%d" % t][:, lo:V], remote_sem=T.sem["rh%d" % t],
                         local_sem=T.sem["l0"], pid=pid, routing_id=rid, dma_engine_mask=topo.mask(core, dst))
            n += len(topo.engines(core, dst))
    g.wait_ge(T.sem["l0"], n)


def rank_program(g, core, T, topo):
    rank = T.rank_of(core)
    if rank is None:
        for r in range(NR):
            if helper(topo, T.cores, T.cores[r]) == core:
                hand_on(g, core, T, topo, r)
        return
    F = make(g, T)
    aide = helper(topo, T.cores, core)

    def offer(t, out, a, sem):
        dst = T.cores[(rank - 1 - t) % NR]
        F["send"](topo, dst, topo.mask(core, dst), out, [out], a, sem, False)

    def hand(out, lands, a, sem):
        F["send"](topo, aide, topo.mask(core, aide) & ~topo.mask(core, T.cores[rank - 1]), out, lands, a, sem, True)

    def offer_lists(t):
        lo, out = CFG["straight"][t], "qw%d" % t
        if lo < V:
            hand(R(out, lo, V), [R(out, lo, V)], R("W", lo, V), "rh%d" % t)
        offer(t, R(out, 0, lo), R("W", 0, lo), "rw%d" % t)

    tt, ts, cp, ms, scan, tr, act, mm = (F[k] for k in ("tt", "ts", "cp", "ms", "scan", "tr", "act", "mm"))
    iota, aff, dma = (F[k] for k in ("iota", "aff", "dma"))
    asked = [T.cores[(rank + 1 + t) % NR] for t in range(RO)]

    def at(win, off):
        return ("@", win, off)

    def col(n, k=0):
        return R(n, k, k + 1)

    def lanes(n, ph, lo=0, hi=I):
        return R(n, PH * lo + ph, PH * hi, PH)

    def ch(n, k, w):
        return R(n, w * k, w * (k + 1))

    def sk(name, k):
        return R(name, 15 - k, 15 - k + 128)

    def cls(t):
        return ch("cls", t, 24)

    def paired(t):
        return sum(w for who, w in CFG["old"][t] if who == "2")

    def fold(out, a, mask="rmask"):
        n, most = size(a), CFG["fs"].get(out[0], W16)
        cuts = list(range(0, n - most // 2, most)) + [n] if n > most else [0, n]
        for lo, hi in zip(cuts, cuts[1:]):
            scan(R(out[0], out[1] + lo, out[1] + hi), R(mask, 0, hi - lo), R(a[0], a[1] + lo, a[1] + hi), OP.min, OP.max)

    def copy(who, out, a):
        if who == "v":
            cp(out, a)
        elif who == "a":
            act(out, a)
        else:
            aff(out, a, [[0, size(out)]], OP.is_ge, 0, 0)

    first, late = F["first"], []
    MO, MS = R("morph", 0, P), R("meas", 0, V)
    DV, WV = R("Dv", 0, V), R("W", 0, V)

    dma("s", R("b15i"), T.bas[15:128:16, :])
    dma("s", R("use_i"), T.use[:])
    dma("s", MS, T.mea[:])
    for k in CFG["loads"]:
        if k == "m":
            dma("s", MO, T.mor[:])
        if k == "d":
            dma("s", R("der_i"), T.der[:])
        if k == "b":
            dma("s", R("bas_i", 0, V), T.bas[:])

    first[0] = IN_ORDER
    ms(R("one8"), 1.0)
    ms(R("oneb"), 1.0)
    ms(R("onef"), 1.0)
    iota(R("pi", 0, 1), [[0, 1]], 0, 1)
    aff(R("sel8"), R("one8"), [[1, 144]], OP.is_equal, -15, -16)
    aff(R("blkw"), R("oneb", 0, 144), [[-16, 9], [0, 16]], OP.is_ge, 0, 1)
    aff(R("blkw"), R("blkw"), [[16, 9], [0, 16]], OP.is_ge, 15, -1)
    aff(R("sel1"), R("blkw"), [[0, 9], [1, 16]], OP.is_equal, -15, 0)
    aff(R("idw"), R("oneb", 0, 160), [[1, 160]], OP.is_equal, -16, -1)
    iota(R("VR"), [[PH, I]], -V // 2, 0)
    first[0] = CFG["rest"]
    aff(R("idf"), R("onef", 0, 128), [[1, 128]], OP.is_equal, 0, -1)
    aff(R("selr"), R("onef"), [[1, 144]], OP.is_equal, 0, -1)
    aff(R("tri"), R("blk"), [[1, 128]], OP.is_ge, 0, -1)
    if CFG["turned"]:
        aff(R("mix"), R("onef", 0, 128), [[4, 4], [1, 4], [16, 8]], OP.is_equal, 0, -1)
        aff(R("swb"), R("oneb", 0, 400), [[1, 25], [32, 4], [1000, 4]], OP.is_equal, -1, -1)
        ms(R("KS", I, 512), 0.0)
    if any(who == "2" for who, w in CFG["new"][0]):
        iota(R("rmask8"), [[0, 162], [256, 8]], 0, 0)
    for n, pat, base in ((R("cb", 0, 6), [[-32, 6]], -1), (R("i8"), [[0, 4], [256, 24]], 0), (R("tz"), [[2, 4], [0, 6]], -7),
                         (R("W1", 0, 400), [[0, 25], [1, 16]], 0)):
        iota(n, pat, base, 0)

    def fill(out, c):
        act(out, R("oneb", 0, size(out)), scale=c)

    first[0] = IN_ORDER
    ms(R("rmask", 0, 1024), 256.0)
    ms(R("Z", 0, 1024), 0.0)
    ms(R("rmask", 0, 1024, 16), 0.0)
    dma("s", R("rmask", 1024, 2048), R("rmask", 0, 1024))
    fill(R("zer"), 0.0)
    first[0] = CFG["rest"]
    for k in range(2):
        fill(R("Z", 1024 + 256 * k, 1280 + 256 * k), 0.0)
    fill(R("amask"), -2.0 * 2 ** 25)
    for n in ["Dv"] + ["W"] * (2 in CFG["patch"][:RO - 1]):
        fill(R(n, V, VX), 0.0)
    for n in ("UQ", "AD"):
        fill(R(n, I, IX), 0.0)
    fill(R("GA", 0, 8), 0.0)
    for m in sorted({paired(t) for t in range(RO)} - {0}):
        fill(R("GA", 8 * m + 8, 8 * m + 16), 0.0)
    if "a" in CFG["non"]:
        act(R("non", I, IX), R("oneb", 0, CAP), AF.Sigmoid, scale=128.0, more=1.3)
    else:
        fill(R("non", I, IX), 1.0)
    fill(R("cst"), -32.0)
    fill(R("oalln"), -0.0625)
    ms(R("amask", 0, I, 16), 2.0 * 2 ** 25)
    ms(R("cst", 15, 128, 16), 32.0)
    if not CFG["dv"]:
        fill(R("cs2"), 0.0)
        ms(R("cs2", 15, 128, 16), -64.0)
    if "v" in CFG["non"]:
        ms(col("mg"), -0.5)
    if "a" in CFG["non"]:
        ms(col("mg", 1), 128.0)
    ms(col("cnt", 2), 63.5 / 8)
    if CFG["turned"] < 2:
        ts(R("pi", 1, 2), R("pi", 0, 1), 16, None, OP.bitwise_and)
    ts(R("pi", 0, 1), R("pi", 0, 1), 15, None, OP.bitwise_and)
    cp(col("pm"), R("pi", 0, 1))
    ts(col("pw"), col("pm"), 2.0, 2.0, OP.mult, OP.add)
    ts(col("pw", 1), col("pm"), 16.0, None, OP.mult)
    ts(col("pm", 2), col("pm"), 2.0, None, OP.mult)
    ts(R("cb", 0, 6), R("cb", 0, 6), col("pm", 2), None, OP.subtract)
    ts(col("pw", 2), col("pm"), 8.0, None, OP.is_ge)
    ts(col("pw", 3), col("pm"), 8.0, None, OP.is_lt)
    ts(col("pw", 4), col("pm"), 15.0, None, OP.is_equal)
    if CFG["turned"] < 2:
        ts(col("pw", 5), col("pi", 1), 0.0, None, OP.is_equal)
        ts(col("pw", 6), col("pi", 1), 0.0, None, OP.is_gt)
    ts(col("pm", 1), col("pm"), -1.0, None, OP.mult)
    ts(R("selz"), R("sel1"), col("pw"), None, OP.mult)
    ts(R("i8"), R("i8"), col("pw", 1), None, OP.add)
    for n, src, f in (("selm", "sel1", -4096.0), ("selk", "sel1", 2048.0), ("selp", "sel1", 4096.0), ("seln", "sel1", -2048.0),
                      ("idbig", "idb", BIG), ("idn", "idb", -1.0), ("selo", "sel1", FAR / 8.0),
                      ("idK", "idb", 4096.0), ("idK2", "idb", 8192.0), ("idH", "idb", 2048.0), ("idKn", "idb", -4096.0), ("blkn", "blk", -1.0),
                      ("blk2n", "blk", -2.0), ("trin", "tri", -8192.0), ("tri", "tri", 8192.0), ("id16n", "idb", -16.0), ("id12n", "idb", -12.0),
                      ("cstn", "cst", -1.0)):
        first[0] = IN_ORDER if n in ("selm", "selk", "selp", "seln", "idbig", "idn") else CFG["rest"]
        if n == "id12n" and not (any(CFG["patch"][:RO - 1]) or CFG["patch"][RO - 1] == 1):
            continue
        if n == "cstn" and (all(CFG["patch"]) or not CFG["again"]):
            continue
        act(R(n), R(src), scale=f)
    if not CFG["dv"]:
        ts(col("pw", 7), col("pw", 4), -8192.0, 4096.0, OP.mult, OP.add)
        aff(R("thi"), R("trin"), [[0, 8], [1, 16]], OP.is_ge, -8, 0)
        aff(R("tlo"), R("trin"), [[0, 8], [-1, 16]], OP.is_ge, 7, 0)
    for n, src, k in (("whi", R("idf"), 2), ("wlo", R("idf"), 3), ("selr", R("selr"), 4),
                      ("sw0", R("idw"), 5), ("sw1", R("idw"), 6))[:3 if CFG["turned"] > 1 else 5]:
        act(R(n), src, AF.Identity, scale=col("pw", k))
    if any(who == "2" for r in CFG["new"] for who, w in r):
        aff(R("bhi"), R("idb"), [[0, 8], [1, 16]], OP.is_ge, -8, 0)
        aff(R("blo"), R("idb"), [[0, 8], [-1, 16]], OP.is_ge, 7, 0)
    act(R("dg"), R("W1", 0, 400), AF.Abs, bias=col("pm", 1))
    first[0] = 0.0

    def turns(t):
        F["behind"]()
        aff(ch("cyc", t - 1, 128), R("blk"), [[-16, 8], [-1, 16]], OP.is_equal, t, 1)
        for k in range(t):
            aff(R("cyc", 128 * (t - 1) + k, 128 * t, 16), R("oneb", 0, 8), [[-16, 8]], OP.is_equal, t - 16 - k, 1)
        if t == 1 and all(who != "2" for who, w in CFG["new"][0]):
            iota(R("rmask8"), [[0, 162], [256, 8]], 0, 0)

    def classes(rounds, rows):
        for t in rounds:
            c = ch("clsi", t, 24)
            ts(c, rows, 97.0 * t + P / 2.0, None, OP.add)
            ts(c, c, 511, None, OP.bitwise_and)
            cp(cls(t), c)

    first[0] = 2 * IN_ORDER
    ts(R("b15"), lanes("b15i", 0), -P / 2.0, None, OP.add)
    for x in range(16):
        mm(R("P4", 0, 24), sk("sel8", x), R("b15", x, I, 16), x == 0, x == 15)
    classes([0, 3], R("P4", 0, 24))
    first[0] = 0.0

    def spread(t):
        ph, n = t % PH, I
        m = CFG["x0"] if t == 0 else 0
        for a in range(0, m, PC):
            b = min(a + PC, m)
            z = 16 * PC * (a // PC % 2)
            cp(R("Z", z, z + 16 * (b - a), 16), lanes("meas", ph, a, b))
            fold(R("x0", 16 * a, 16 * b), R("Z", z, z + 16 * (b - a)))
        first[0] = 0.0 if t else IN_ORDER
        if t == 0:
            n = sum(w for who, w in CFG["search"][0] if who != "p")
        for j in range(16 if m < n else 0):
            aff(R("x%d" % (t % 2), 16 * m + j, 16 * n, 16), lanes("meas", ph, m, n), [[0, n - m]], OP.is_ge, 0, 0)
        first[0] = 0.0

    def tables():
        for k in range(PH):
            copy(CFG["bf"], lanes("Bf", k), lanes("bas_i", k))
            if CFG["dv"]:
                copy(CFG["dv"][0], ch("Dv", k, I), ch("der_i", k, I))
        for k in range(PH):
            p = R("P%d" % (5, 6, 3)[k], 0, I)
            if k < CFG["neq"]:
                mm(p, R("idf"), ch("Bf", k, I), True, True)
                tt(ch("NEQ", k, I), p, ch("der_i", k, I), OP.not_equal)
            else:
                tt(ch("NEQ", k, I), ch("der_i", k, I), ch("bas_i", k, I), OP.not_equal)
            mm(p, R("cst"), R("oneb", 0, I), True, False)
            if CFG["dv"][1:] == "a":
                mm(p, R("idf"), ch("Dv", k, I), False, False)
            mm(p, R("tri"), ch("NEQ", k, I), False, True)
            if CFG["dv"][1:] == "a":
                act(ch("W", k, I), p)
            else:
                tt(ch("W", k, I), p, ch("der_i", k, I), OP.add)

    def later(ph):
        for x in range(16):
            mm(ch("P4", 18 + ph, 24), sk("selr", x), R("Bf", 3 * x + ph, V, 48), x == 0, x == 15)
        classes([ph], ch("P4", 18 + ph, 24))

    def targets():
        for ph in range(PH):
            for x in range(16):
                mm(ch("P4", 3 + ph, 24), sk("selz", x), R("meas", 3 * x + ph, V, 48), x == 0, x == 15)
        for t in range(RO):
            ts(ch("zi", t, 24), ch("P4", 3 + t % PH, 24), 2.0 * t, None, OP.add)
        ts(R("zi"), R("zi"), 14, None, OP.bitwise_and)
        tt(R("i8"), R("i8"), R("zi"), OP.add)

    def winners(keys, kt, ks, n, out, li, lh, lst, mid=V / 2.0):
        for key, lo, hi in keys:
            tr(R(kt, lo, hi), key)
        scan(R(ks, 0, n), R("amask", 0, n), R(kt), OP.max, OP.min)
        ts(li, R(ks, 15, n, 16), 2048 * ROUND, 2048 * ROUND, OP.add, OP.subtract)
        tt(lh, R(ks, 15, n, 16), li, OP.subtract)
        for y in range(2):
            for h in range(2):
                mm(R(out[0], out[1] + y, out[2], 2), R("sw%d" % y, 16 - 16 * (h - y), 144 - 16 * (h - y)), R(lh[0], lh[1] + h, lh[2], 2), h == 0, h == 1)
        ts(lst, out, mid, None, OP.add)

    def sums(key, lo, hi, terms, stop, turned=False):
        for k, (s, buf) in enumerate(terms):
            for j in range(16):
                a, last = R(buf, 16 * lo + j, 16 * hi, 16), stop and j == 15 and k + 1 == len(terms)
                if turned:
                    mm(R(key[0], key[1] + j, key[2], 16) + key[4:], a, R(s, 15, 128, 16), False, last)
                else:
                    mm(key, sk(s, j), a, False, last)

    def leaders(keys, out, lst, mid):
        for key, lo, hi in keys:
            scan(R("KS", lo, hi), R("amask", 0, hi - lo), key, OP.max, OP.min)
        q, kt, li, lh = R(out[0], out[2], out[2] + 32), R("KT", 0, 32), R("mi", 32, 64), R("mh", 32, 64)
        mm(q, R("mix"), R("KS", 15, 512, 16), True, True)
        tr(kt, q)
        ts(li, kt, 2048 * ROUND, 2048 * ROUND, OP.add, OP.subtract)
        tt(lh, kt, li, OP.subtract)
        for b in range(PH):
            for j in range(4):
                mm(R(out[0], out[1] + 8 * b, out[1] + 8 * b + 8), R("swb", 16 + 128 * b - j, 144 + 128 * b - j), R("mh", 32 + 8 * j, 40 + 8 * j),
                   b + j == 0, b + j == 5)
        ts(lst, out, mid, None, OP.add)

    def answers():
        rows = (0, CAP)
        scan(R("KS2") + rows, R("amask", 0, 128) + rows, R("P4", 0, 128) + rows, OP.max, OP.min)
        kt, li, lh, out = R("KT2", 0, 32), R("mi", 0, 32), R("mh", 0, 32), R("P4", 100, 106)
        mm(R("P4", 112, 120), R("mix") + rows, R("KS2", 15, 128, 16) + rows, True, True)
        tr(kt, R("P4", 112, 144))
        ts(li, kt, 2048 * ROUND, 2048 * ROUND, OP.add, OP.subtract)
        tt(lh, kt, li, OP.subtract)
        for j in range(4):
            mm(out, R("swb", 16 - j, 144 - j), R("mh", 8 * j, 8 * j + 6), j == 0, j == 3)
        ts(R("n16", 0, 6), out, V / 2.0, None, OP.add)

    def search(t):
        ph = t % PH
        first[0] = CFG["use"][t - 1] if t else 0.0
        cp(R("u16"), at(R("USE" if t else "use_i"), cls(t)))
        first[0] = 0.0
        mid = V / 2.0 + ph
        ts(R("U"), R("u16"), -mid, None, OP.add)
        d = R("P5", 0, I)
        mm(d, R("idb"), R("U"), True, True)
        tt(R("EQ"), d, R("VR"), OP.is_equal)
        if CFG["heads"]:
            mm(d, R("idb"), lanes("meas", ph), True, True)
        lo, x, keys, turned = 0, "x%d" % (t % 2), [], CFG["turned"]
        for k, (who, n) in enumerate(CFG["search"][t]):
            hi = lo + n
            pc = CFG["pc"][who]
            cuts = [(a, min(a + pc, hi)) for a in range(lo, hi, pc)]
            banks, k = CFG["kbank"], lo // 128
            b0, b1 = 128 * k, 128 * k + 128
            whole = R(banks[k], b0, b1)
            key = whole + (lo - b0, hi - b0) * (n < 128)
            opens, ends = banks[k] not in banks[:k], banks[k] not in banks[k + 1:] and hi == b1
            if lo == b0:
                if opens:
                    keys.append((whole, b0, b1))
                else:
                    keys[-1] = (R(banks[k], keys[-1][1], b1), keys[-1][1], b1)
                if turned:
                    mm(whole, R("U", b0, b1), R("idb"), opens, False)
                else:
                    mm(whole, R("idb"), R("U", b0, b1), opens, False)
            if who == "p":
                for a, b in cuts:
                    act(R("GE", 16 * a, 16 * b), at(MS, R("u16", a, b)))
                for a in range(16 * lo, 16 * hi, 512):
                    bank = R("P%d" % ((2 if t else 3) + a // 512 % 2 * (1 if t else 3)))
                    if t:
                        mm(bank, R("idb"), R(x, a, a + 512), True, False)
                    else:
                        for j in range(16):
                            mm(R(bank[0], j, 512, 16), R("idb"), lanes("meas", ph, a // 16, a // 16 + 32), j == 0, False)
                    mm(bank, R("idn"), R("GE", a, a + 512), False, True)
                    act(R("SE", a, a + 512), bank, AF.Abs)
                terms = [("selk", "SE")]
            elif who == "r":
                for a, b in cuts:
                    act(R("GE", 16 * a, 16 * b), at(MS, R("u16", a, b)))
                sums(key, lo, hi, [("selk", "GE")], False, turned)
                head = R("GE", 16 * lo, 16 * hi, 16)
                tt(head, head, R("P5", lo, hi) if CFG["heads"] else lanes("meas", ph, lo, hi), OP.min)
                for a, b in [(a, min(hi, a + CFG["rs"])) for a in range(lo, hi, CFG["rs"])]:
                    scan(R("SE", 16 * a, 16 * b), R(x, 16 * a, 16 * b), R("GE", 16 * a, 16 * b), OP.max, OP.min)
                terms = [("selm", "SE")]
            elif who == "t":
                for a, b in cuts:
                    tt(R("GE", 16 * a, 16 * b), at(MS, R("u16", a, b)), R(x, 16 * a, 16 * b), OP.subtract)
                    act(R("SE", 16 * a, 16 * b), R("GE", 16 * a, 16 * b), AF.Abs)
                terms = [("selk", "SE")]
            else:
                for a, b in cuts:
                    tt(R("GE", 16 * a, 16 * b), at(MS, R("u16", a, b)), R(x, 16 * a, 16 * b), OP.subtract)
                sums(key, lo, hi, [("seln", "GE")], False, turned)
                for a in range(lo, hi, 64):
                    b = min(a + 64, hi)
                    ts(R("SE", 16 * a, 16 * b), R("GE", 16 * a, 16 * b), 0.0, None, OP.max)
                terms = [("selp", "SE")]
            if hi == b1 and turned:
                mm(whole, R("EQ", b0, b1), R("idbig"), False, False)
            elif hi == b1:
                mm(whole, R("idbig"), R("EQ", b0, b1), False, False)
            sums(key, lo, hi, terms, ends, turned)
            lo = hi
        if turned:
            leaders(keys, R("P0", 400, 424), R("m16"), mid)
        else:
            winners(keys, "KT", "KS", I, R("P0", 400, 424), R("mi", 0, 24), R("mh", 0, 24), R("m16"), mid)
        first[0] = CFG["m1"]
        ts(R("m1", 24, 48), R("P0", 400, 424), 0.5, mid / 2.0 + 1099.75, OP.mult, OP.add)
        ts(R("m1", 48, 72), R("m1", 24, 48), 4.0, 1.0 - 4400.0 - mid, OP.mult, OP.add)
        tt(R("m1", 0, 24), R("m1", 48, 72), R("P0", 400, 424), OP.subtract)
        first[0] = 0.0

    def old_lists(t):
        ph, n, o = t % PH, paired(t) // 2, DW * t
        if t == 0 and n == 0:
            cp(R("d16", 2, I + 2), lanes("der_i", 0))
            return
        terms = [("wlo", "whi", "idf", "W"), ("tlo", "thi", "trin", "NEQ")]
        if CFG["dv"] or (t == PH and not CFG["again"]):
            terms = [("wlo", "whi", "idf", "Dv")]
        bank = CFG["obank"] if t else "P2"
        mm(R(bank, 0, I + 2), R("zer"), R("oneb", 0, I + 2), True, False)
        for k, (lo, hi, both, src) in enumerate(terms):
            even, odd = R(src, ph, 2 * PH * n, 2 * PH), R(src, ph + PH, 2 * PH * n, 2 * PH)
            steps = [(1, lo, odd), (0, hi, even), (n + 2, lo, even), (n + 2, hi, odd)] if n else []
            steps += [(2 * n + 2, both, lanes(src, ph, 2 * n, I))] if 2 * n < I else []
            for j, (a, s, r) in enumerate(steps):
                mm(R(bank, a, a + size(r)), R(s), r, False, k + 1 == len(terms) and j + 1 == len(steps))
        if len(terms) == 1:
            cp(R("d16", o, o + I + 2), R(bank, 0, I + 2))
        else:
            ts(R("d16", o, o + I + 2), R(bank, 0, I + 2), col("pw", 7), P - 1.0, OP.add, OP.min)

    def old_tops(t):
        m, o = paired(t), DW * t
        n, lo, one = m // 2, 0, m
        for who, w in CFG["old"][t]:
            if who == "2":
                hi = lo + w // 2
                act(R("GA", 8 + 16 * lo, 8 + 16 * hi), at(MO, R("d16", o + n + 2 + lo, o + n + 2 + hi)))
                end = hi + (hi == n)
                b = R("GD", 16 * lo, 16 * end)
                tt(b, at(MO, R("d16", o + lo, o + end)), R("GA", 16 * lo, 16 * end), OP.max)
                fold(R("SD", 16 * lo, 16 * end), b, "rmask8")
                lo = hi
            else:
                a = 16 + 16 * w * (one // w % 2)
                copy(who, R("GA", a, a + 16 * w), at(MO, R("d16", o + one + 2, o + one + w + 2)))
                fold(R("SD", a, a + 16 * w), R("GA", a, a + 16 * w))
                mm(R("P2", one, one + w), R("idb"), R("SD", a + 15, a + 16 * w, 16), True, False)
                mm(R("P2", one, one + w), R("idn"), lanes("meas", t % PH, one, one + w), False, True)
                one += w
        if m:
            mm(R("P2", 0, m), R("idb"), R("SD", 15, 8 * m + 8, 8), True, False)
            mm(R("P2", 0, m), R("idn"), lanes("meas", t % PH, 0, m), False, True)
        act(R("AD", 0, I), R("P2", 0, I), AF.Abs)

    def single(t):
        return sum(w for who, w in CFG["new"][t] if who == "2")

    def tops(t, a, b):
        if a >= single(t):
            return R("SE", 16 * a + 15, 16 * b, 16)
        return R("SE", 8 * a + 15, 8 * b + 8, 8)

    def new_lists(t):
        one = single(t)
        cp(R("e16", one + 2, I + 2), R("Ea", one, I))
        if one:
            n = one // 2
            ts(R("Eh", 0, one), R("Ea", 0, one), -P / 2.0, None, OP.add)
            even, odd = R("Eh", 0, one, 2), R("Eh", 1, one, 2)
            mm(R("P3", 0, one + 2), R("zer"), R("oneb", 0, one + 2), True, False)
            for j, (a, s, r) in enumerate(((1, "blo", odd), (0, "bhi", even), (n + 2, "blo", even), (n + 2, "bhi", odd))):
                mm(R("P3", a, a + n), R(s), r, False, j == 3)
            ts(R("e16", 0, one + 2), R("P3", 0, one + 2), P / 2.0, None, OP.add)

    def new_tops(t, cut):
        a, lo = 0, single(t)
        one, n = lo, lo // 2
        for who, w in CFG["new"][t]:
            if who == "2":
                b = a + w // 2
                act(R("GE", 8 + 16 * a, 8 + 16 * b), at(MO, R("e16", n + 2 + a, n + 2 + b)))
                end = b + (b == n)
                both = R("GE", 16 * (n + 1 + a), 16 * (n + 1 + end))
                tt(both, at(MO, R("e16", a, end)), R("GE", 16 * a, 16 * end), OP.max)
                fold(R("SE", 16 * a, 16 * end), both, "rmask8")
                a = b
            else:
                hi = lo + w
                got = R("GE", 16 * lo + 32, 16 * hi + 32)
                copy(who, got, at(MO, R("e16", lo + 2, hi + 2)))
                fold(R("SE", 16 * lo, 16 * hi), got)
                lo = hi
        for a, b in ((0, min(one, cut)), (one, cut)):
            if a < b:
                mm(R("P3", a, b), R("idb"), tops(t, a, b), a == 0, False)
        mm(R("P3", 0, cut), R("idn"), lanes("meas", t % PH, 0, cut), False, True)
        act(R("AE", 0, cut), R("P3", 0, cut), AF.Abs)
        late.append(lambda: act(R("UQ", 0, I), at(R("qk%d" % t), cls(t))))
        while late:
            if CFG["late"]:
                F["behind"]()
            late.pop()()

    def decide(who, out, gain, count=None):
        if who == "v":
            ts(out, gain, col("mg"), None, OP.is_gt)
        else:
            act(out, gain, AF.Sigmoid, bias=col("mg", 1), scale=256.0, accum=count)

    def morphs(t):
        o = R("P4", 320, 344)
        mm(o, R("idf"), ch("i8", t, 24), True, False)
        for x in range(16):
            mm(o, sk("selo", x), R("non", x, I, 16), False, x == 15)
        ts(R("zw"), o, 0.5, None, OP.mult)
        n = 24 // CFG["ms"][t]
        for a in range(0, 24, n):
            cp(at(R("morph"), R("zw", a, a + n)), lanes("meas", t % PH, 16 * a, 16 * (a + n)))

    def lists(t, banks):
        ph, non, x = t % PH, R("non", 0, I), R("XD")
        old, base, dn = (R(b, 0, I) for b in banks)
        mm(old, R("idK2"), non, False, True)
        if CFG["patch"][t]:
            tt(x, old, R("Ea", 0, I), OP.max)
            mm(base, R("idKn"), non, True, False)
            mm(base, R("idf"), x, False, True)
            if t + 1 < RO:
                tt(lanes("NEQ", ph), base, lanes("Bf", ph), OP.not_equal)
            act(lanes("Dv", ph), base)
            if t + 1 < RO:
                for k, (s, r) in enumerate((("cst", R("oneb", 0, I)), ("idKn", non), ("idf", x), ("tri", lanes("NEQ", ph)))):
                    mm(dn, R(s), r, k == 0, k == 3)
                if not CFG["wlate"]:
                    copy(CFG["wev"], lanes("W", ph), dn)
            return
        mm(base, R("idK"), non, False, True)
        tt(x, old, R("Ea", 0, I), OP.max)
        tt(lanes("NEQ", ph), base, x, OP.not_equal)
        for k, (s, r) in enumerate((("cst", R("oneb", 0, I)), ("idKn", non), ("idf", x), ("tri", lanes("NEQ", ph)))):
            mm(dn, R(s), r, k == 0, k == 3)
        copy(CFG["wev"], lanes("W", ph), dn)
        if not CFG["again"]:
            mm(base, R("idKn"), non, True, False)
            mm(base, R("idf"), x, False, True)
            act(lanes("Dv", ph), base)

    def settled():
        for ph, bank in ((1, "P0"), (2, "P7")):
            p = R(bank, 0, I)
            for k, (s, r) in enumerate((("idf", lanes("W", ph)), ("trin", lanes("NEQ", ph)), ("cstn", R("oneb", 0, I)))):
                mm(p, R(s), r, k == 0, k == 2)
            act(lanes("Dv", ph), p)

    def counts():
        o = R("P4", 344, 345)
        for k in range(PH):
            mm(o, ch("non", k, 128), col("oneb"), k == 0, k == PH - 1)
        act(col("cnt"), o)

    def dist(t):
        ph = t % PH
        half, kd, non = R("P5", 0, I), R("P7", 0, I), R("non", 0, I)
        us = R("USE", 37 * t, 37 * t + I)
        first[1] = CFG["mu"]
        if t:
            dma("s", R("morc"), MO)
        old_tops(t)
        if not t:
            dma("s", R("morc"), MO)
            dma("s", R("meas", V, VX), T.mea[:, 0:VX - V])
            dma("s", R("bas_i", V, VX), T.bas[:, 0:VX - V])
            if any(CFG["mz"]):
                dma("s", R("morph", P, 8 * IX), T.mor[:, 0:8 * CAP])
        ea = R("Ea", 0, I)
        tt(ea, at(WV, R("m16")), lanes("bas_i", ph), OP.max)
        ts(ea, ea, 4095, None, OP.bitwise_and)
        new_lists(t)
        if t == 1:
            F["behind"]()
            later(2)
        if t + 1 < RO:
            first[0] = CFG["olds"]
            old_lists(t + 1)
            first[0] = 0.0
        cut = CFG["cut"]
        xc = R("P7", I, 2 * I - cut) if CFG["xcut"] else lanes("meas", ph, cut, I)
        if CFG["xcut"]:
            mm(xc, R("idb"), lanes("meas", ph, cut, I), True, True)
        first[0] = CFG["m1"]
        mm(kd, R("idK"), R("dg", t, t + I), True, False)
        for x in range(16):
            mm(R("P7", x, I, 16), ch("cyc", t - 1, 128) if t else R("idb"), R("m1", 0, 24), False, False)
        mm(R("P6", 0, I), R("idKn"), R("dg", t, t + I), True, False)
        mm(R("P6", 0, I), R("idH"), R("oneb", 0, I), False, False)
        terms = (("idf", lanes("W", ph)), ("trin", lanes("NEQ", ph)), ("cs2", R("oneb", 0, I)))
        if CFG["dv"] or (t == PH and not CFG["again"]):
            terms = (("idf", lanes("Dv", ph)), ("idKn", R("oneb", 0, I)))
        for k, (s, r) in enumerate(terms):
            mm(R("P1", 0, I), R(s), r, k == 0, False)
        first[0] = 0.0
        new_tops(t, cut)
        mm(R("P5", 0, cut), R("blkn"), R("AD", 0, cut), True, False)
        mm(R("P5", 0, cut), R("blk"), R("AE", 0, cut), False, True)
        if cut < I:
            o, top, x, me = R("P5", cut, I), tops(t, cut, I), lanes("meas", ph, cut, I), R("SQ", 0, I - cut)
            tt(me, top, xc, OP.min)
            for k, (s, r) in enumerate((("blkn", R("AD", cut, I)), ("blk", x), ("blk", top), ("blk2n", me))):
                mm(o, R(s), r, k == 0, k == 3)
        first[0], first[1] = CFG["chain"], CFG["muy"][t]
        summed = CFG["non"][0] == "a" and CFG["patch"][t] and t + 1 < RO
        decide(CFG["non"][0], non, half, col("cnt") if summed else None)
        scan(R("cum", 1, IX), R("non", 1, IX), R("non", 0, IX - 1), OP.add, OP.add, col("non"))
        for n in range(6):
            act(ch("junk", n % 2, IX // 2), R("cum", 1, IX, 2), AF.Sign, bias=col("cb", n), accum=col("acc", n))
        first[0] = CFG["use"][t]
        mm(R("P6", 0, I), R("idKn"), non, False, True)
        mm(kd, R("idK"), non, False, True)
        tt(R("LXg"), R("P6", 0, I), R("use_i", 0, I) if CFG["use0"] and not t else us, OP.max)
        tt(us, kd, R("LXg"), OP.min)
        first[0] = 0.0
        if t + 1 < RO:
            offer(t + 1, R("qk%d" % (t + 1)), R("USE"), "rk%d" % (t + 1))
        else:
            dma("s", T.yu[:], R("USE"))
        if not CFG["mor"][t]:
            morphs(t)
        if CFG["patch"][t]:
            lists(t, ("P1", "P6", "P1"))
            if CFG["again"]:
                settled()
        else:
            first[0] = CFG["olds"]
            mm(R("P6", 0, I), R("idf"), lanes("Bf", ph), True, False)
            first[0] = 0.0

    def ask(t):
        ph, patch = t % PH, CFG["patch"][t]
        s6, v6, acc = R("s16", 0, 6), R("sv16", 0, 6), R("acc", 0, 6)
        zs = R("Z", 0, 16 * CAP, 16)
        first[0] = CFG["chain"]
        ts(v6, acc, -3.0, 3.0 * IX / 2 + ph, OP.mult, OP.add)
        ts(s6, acc, -1.0, IX / 2.0, OP.mult, OP.add)
        copy(CFG["zs"], zs, at(R("meas"), v6))
        cp(R("uq16"), at(R("UQ"), s6))
        act(R("Bs"), at(R("bas_i"), v6))
        act(R("AD2"), at(R("AD"), s6))
        first[0] = 0.0
        spots(t)
        first[0] = CFG["chain"]
        ts(R("U2"), R("uq16"), -V / 2.0, None, OP.add)
        turned = CFG["turned"] > 1
        if turned:
            mm(R("P4", 0, 128) + (0, CAP), R("U2"), R("idb"), True, False)
        else:
            mm(R("P4", 0, CAP), R("idb"), R("U2"), True, False)
        lo, qm, nb = 0, R("qm%d" % t), 0
        for k, (who, n) in enumerate(CFG["ask1"][t]):
            hi = lo + n
            key, gq = R("P4", 0, 128) + (lo, hi) if turned else R("P4", lo, hi), R("GQ", 16 * lo, 16 * hi)
            if who == "p":
                for a in range(lo, hi, 32):
                    b, bank = min(a + 32, hi), CFG["abank"][nb]
                    nb += 1
                    w = 16 * (b - a)
                    act(R("GQ", 16 * a, 16 * b), at(qm, R("uq16", a, b)))
                    for j in range(16):
                        mm(R(bank, j, w, 16), R("idb"), R("Z", 16 * a, 16 * b, 16), j == 0, False)
                    mm(R(bank, 0, w), R("idn"), R("GQ", 16 * a, 16 * b), False, True)
                    act(R("SQ", 16 * a, 16 * b), R(bank, 0, w), AF.Abs)
                terms = [("selk", "SQ")]
            else:
                fold(R("RQ", 16 * lo, 16 * hi), R("Z", 16 * lo, 16 * hi))
                if who == "q":
                    for a in range(lo, hi, 32):
                        b, bank = min(a + 32, hi), CFG["abank"][nb]
                        nb += 1
                        w = 16 * (b - a)
                        act(R("GQ", 16 * a, 16 * b), at(qm, R("uq16", a, b)))
                        mm(R(bank, 0, w), R("idb"), R("RQ", 16 * a, 16 * b), True, False)
                        mm(R(bank, 0, w), R("idn"), R("GQ", 16 * a, 16 * b), False, True)
                        act(R("SQ", 16 * a, 16 * b), R(bank, 0, w), AF.Abs)
                    terms = [("selk", "SQ")]
                elif who == "r":
                    act(gq, at(qm, R("uq16", lo, hi)))
                    sums(key, lo, hi, [("selk", "GQ")], False, turned)
                    head = R("GQ", 16 * lo, 16 * hi, 16)
                    tt(head, head, R("Z", 16 * lo, 16 * hi, 16), OP.min)
                    scan(R("SQ", 16 * lo, 16 * hi), R("RQ", 16 * lo, 16 * hi), gq, OP.max, OP.min)
                    terms = [("selm", "SQ")]
                else:
                    tt(gq, at(qm, R("uq16", lo, hi)), R("RQ", 16 * lo, 16 * hi), OP.subtract)
                    if who == "t":
                        act(R("SQ", 16 * lo, 16 * hi), gq, AF.Abs)
                        terms = [("selk", "SQ")]
                    else:
                        ts(R("SQ", 16 * lo, 16 * hi), gq, 0.0, None, OP.max)
                        terms = [("seln", "GQ"), ("selp", "SQ")]
            kinds = [w if w in "sr" else "" for w, _ in CFG["ask1"][t]]
            if CFG["join"][t]:
                if kinds[k + 1:k + 2] == [kinds[k]]:
                    lo = hi
                    continue
                lo = sum(m for w, m in CFG["ask1"][t][:min(j for j in range(k + 1) if len(set(kinds[j:k + 1])) == 1)])
            key = R("P4", 0, 128) + (lo, hi) if turned else R("P4", lo, hi)
            sums(key, lo, hi, terms, hi == CAP, turned)
            lo = hi
        if turned:
            answers()
        else:
            winners([(R("P4", 0, CAP), 0, CAP)], "KT2", "KS2", CAP, R("P4", 100, 106), R("mi", 24, 30), R("mh", 24, 30), R("n16", 0, 6))
        if CFG["mor"][t]:
            first[0] = 0.0
            morphs(t)
            first[0] = CFG["chain"]
        tt(R("E2"), at(R("qw%d" % t), R("n16", 0, 6)), R("Bs"), OP.max)
        ts(R("E2"), R("E2"), 4095, None, OP.bitwise_and)
        cp(R("e216"), R("E2"))
        if patch and t + 1 < RO and CFG["wlate"]:
            F["behind"]()
            copy(CFG["wev"], lanes("W", ph), R("P1", 0, I))
        lo = 0
        for who, n in CFG["ask2"][t]:
            copy(who, R("GQ", 16 * lo, 16 * (lo + n)), at(R("morc"), R("e216", lo, lo + n)))
            fold(R("SQ", 16 * lo, 16 * (lo + n)), R("GQ", 16 * lo, 16 * (lo + n)))
            lo += n
        first[0] = 0.0
        if not patch:
            cp(at(R("Ea"), s6), R("E2"))
        elif t + 1 < RO:
            tt(R("NE2"), R("E2"), R("Bs"), OP.not_equal)
            w2 = R("P4", 410, 410 + CAP)
            mm(w2, R("cst"), R("oneb", 0, CAP), True, False)
            mm(w2, R("tri"), R("NE2"), False, True)
            tt(R("W2"), w2, R("E2"), OP.add)
            if patch == 2:
                tt(R("Wd"), at(R("W", 0, VX), v6), R("W2"), OP.subtract)
        elif patch == 2:
            cp(R("W2"), R("E2"))
            tt(R("Wd"), at(R("Dv", 0, VX), v6), R("W2"), OP.subtract)
        if CFG["mz"][t]:
            tt(R("dxs"), at(R("morph", 0, 8 * IX), R("z16", 0, 6)), zs, OP.subtract)
        first[0] = CFG["chain"]
        top, two = R("SQ", 15, 16 * CAP, 16), twice(t)
        tt(R("MM2"), top, zs, OP.min)
        terms = (("blkn", R("AD2")), ("blk", zs), ("blk", top), ("blk2n", R("MM2")))
        for k, (s, r) in enumerate(terms):
            for h in range(two):
                mm(R("P4", 128 + CAP * h, 128 + CAP * (h + 1)), R(s), r, k + h == 0, k == 3 and h + 1 == two)
        summed = CFG["non"][1] == "a" and patch and t + 1 < RO and two == 1
        decide(CFG["non"][1], R("adb", 0, two * CAP), R("P4", 128, 128 + two * CAP), col("cnt", 1) if summed else None)
        if patch and t + 1 < RO and not summed:
            first[0] = 0.0
            act(R("junk", 0, CAP), R("adb", 0, CAP), accum=col("cnt", 1))
        first[0] = 0.0

    def far(t):
        return not CFG["mz"][t], CFG["patch"][t] == 1 or (CFG["patch"][t] == 2 and t + 1 < RO)

    def twice(t):
        return 2 if all(far(t)) else 1

    def spots(t):
        y = R(CFG["ybank"], 0, 6)
        mm(y, R("idb"), ch("tz", t, 6), True, False)
        for x in range(16):
            mm(y, sk("selz", x), R("Z", 16 * x, 16 * CAP, 256), False, x == 15)
        ts(R("r2", 0, 6), y, 16 * ROUND, 16 * ROUND, OP.add, OP.subtract)
        tt(R("z2", 0, 6), y, R("r2", 0, 6), OP.subtract)
        if CFG["mz"][t]:
            mm(y, R("id16n"), R("acc", 0, 6), True, False)
            mm(y, R("idb"), R("z2", 0, 6), False, True)
            ts(R("z16", 0, 6), y, 0.5, 4.0 * IX + 3.5, OP.mult, OP.add)

    def close(t):
        ph, patch, two = t % PH, CFG["patch"][t], twice(t)
        s6, v6, acc, zs, adb = R("s16", 0, 6), R("sv16", 0, 6), R("acc", 0, 6), R("Z", 0, 16 * CAP, 16), R("adb", 0, CAP)
        bank, (fz, fw) = "P6" if patch else "P5", far(t)
        zo, wo = R(bank, 0, 6), R(bank, 6 * (two - 1), 6 * two)
        if fz:
            mm(zo, R("id16n"), acc, True, False)
            mm(zo, R("idb"), R("z2", 0, 6), False, False)
        if fw:
            mm(wo, R("id12n"), acc, not fz, False)
        first[0] = CFG["end"]
        if patch == 2:
            tt(R("Wd"), adb, R("Wd"), OP.mult)
            tt(at(R("W" if t + 1 < RO else "Dv", 0, VX), v6), R("W2"), R("Wd"), OP.add)
        if not fz:
            tt(R("dxs"), adb, R("dxs"), OP.mult)
            tt(at(R("morph", 0, 8 * IX), R("z16", 0, 6)), zs, R("dxs"), OP.add)
        if not patch:
            cp(at(R("non"), s6), adb)
        for x in range(16 * (fz or fw)):
            mm(R(bank, 0, 6 * two), sk("selo", x), R("adb", x, two * CAP, 16), False, x == 15)
        if fw:
            ts(R("z16", 8, 14), wo, 0.25, 3.0 * IX / 2 + ph, OP.mult, OP.add)
            if patch == 1 and t + 1 < RO:
                cp(at(R("W"), R("z16", 8, 14)), R("W2"))
        if fz:
            ts(R("z16", 0, 6), zo, 0.5, 4.0 * IX + 3.5, OP.mult, OP.add)
        if fw and t + 1 == RO:
            cp(at(R("Dv"), R("z16", 8, 14)), R("E2"))
        if t + 1 == RO:
            dma("s", T.yd[:], DV)
        if fz:
            cp(at(R("morph"), R("z16", 0, 6)), zs)
        first[0] = 0.0
        if t + 1 == RO:
            dma("a", T.ym[:], MO)
            return
        if patch:
            offer_lists(t + 1)
            cp(at(R("Dv"), R("z16", 8, 14)), R("E2"))
        else:
            lists(t, ("P1", "P6", CFG["wbank"]))
            offer_lists(t + 1)
        if CFG["non"][0] == "v" or not CFG["patch"][t]:
            counts()
        a = R("P4", 400, 401)
        terms = (2, 0, 1) if CFG["patch"][t] else (2, 0)
        for k in terms:
            mm(a, R("oalln"), col("cnt", k), k == terms[0], k == terms[-1])
        ts(col("mg", 2), a, 128 * ROUND, 128 * ROUND, OP.add, OP.subtract)
        ts(col("mg"), col("mg", 2), a, -64.0, OP.subtract, OP.add)
        if "a" in CFG["non"]:
            act(col("mg", 1), col("mg"), scale=-256.0)

    spread(0)
    hand(R("qm0"), [R("qm%d" % t) for t in range(RO)], MS, "rm0")
    if CFG["use0"]:
        F["behind"]()
        offer(0, R("qk0"), R("use_i"), "rk0")
    search(0)
    if CFG["use0"]:
        cp(R("USE", I, C), R("use_i", I, C))
    else:
        cp(R("USE"), R("use_i"))
        offer(0, R("qk0"), R("USE"), "rk0")
    first[0] = CFG["d16"]
    old_lists(0)
    first[0] = 0.0
    tables()
    offer_lists(0)
    first[0] = CFG["later"]
    targets()
    later(1)
    first[0] = 0.0
    for t in range(RO):
        dist(t)
        if t + 1 < RO:
            spread(t + 1)
            turns(t + 1)
        ask(t)
        if t + 1 < RO:
            search(t + 1)
        close(t)
    come = []
    for t in range(RO):
        a, b = len(topo.engines(asked[t], core)), len(topo.engines(helper(topo, T.cores, asked[t]), core))
        come += [(R("qm%d" % t), "rm%d" % t, b), (R("qk%d" % t), "rk%d" % t, a), (R("qw%d" % t, 0, CFG["straight"][t]), "rw%d" % t, a)]
        come += [(R("qw%d" % t, CFG["straight"][t], V), "rh%d" % t, b)] * (CFG["straight"][t] < V)
    F["issue"](come)
